import numpy as np
import ml_dtypes


def mxq(x, axis, fmt="e4m3"):
    dtype, down = {"e4m3": (ml_dtypes.float8_e4m3fn, 7), "e5m2": (ml_dtypes.float8_e5m2, 14)}[fmt]
    v = np.moveaxis(np.asarray(x, np.float32).astype(ml_dtypes.bfloat16).astype(np.float64), axis, -1)
    blocks = v.reshape(v.shape[:-1] + (-1, 32))
    amax = np.abs(blocks).max(-1, keepdims=True)
    byte = np.maximum(np.where(amax > 0, np.frexp(amax)[1] - 1 + 127, 0) - down, 1)
    scale = np.exp2(byte - 127.0)
    codes = (blocks / scale).astype(np.float32).astype(dtype).astype(np.float64)
    return np.moveaxis((codes * scale).reshape(v.shape), -1, axis)


WIDE = False


def mx_kscale(k):
    if not WIDE:
        return np.ones(k)
    levels = np.array([10, -10, 5, -5, 0])
    if k % 512:
        return np.exp2(np.random.permutation(np.resize(levels, k // 32))).repeat(32)
    a = np.empty((k // 512, 16))
    for p in range(k // 512):
        a[p, :8] = np.random.permutation(np.resize(levels, 8))
        for g in range(8):
            far = levels[np.abs(levels - a[p, g]) >= 10]
            a[p, g + 8] = far[np.random.randint(len(far))]
    return np.exp2(a.ravel()).repeat(32)


BF16 = ml_dtypes.bfloat16


def bf(x):
    return np.asarray(x, np.float32).astype(BF16)


def f64(x):
    return np.asarray(x).astype(np.float64)


N, D, K = 2048, 1024, 512


def scale_rows(gain, m):
    return gain[:, None] * m


def draw0():
    s = mx_kscale(D)
    u = mx_kscale(N)
    return {
        "x": bf(np.random.standard_normal((N, D)) * s),
        "p": bf(np.random.standard_normal((D, D)) / np.sqrt(D) / s[:, None]),
        "beta": bf(np.random.standard_normal((D, K)) / np.sqrt(D) / s[:, None]),
        "r": bf(np.random.uniform(0.5, 1.5, N) * u),
        "t": bf((1.0 + 0.3 * np.random.standard_normal(N)) / u),
        "v": bf(np.random.standard_normal((D, K)) / np.sqrt(D)),
        "psi": bf(np.random.uniform(0.05, 0.2, D)),
    }


def core(x, p, beta, r, t, v, psi):
    n_cases = x.shape[0]
    xq = mxq(f64(x), 1, "e4m3")
    e0 = xq @ mxq(f64(p), 0, "e4m3")
    e = scale_rows(f64(r), e0)
    z0 = xq @ mxq(f64(beta), 0, "e4m3")
    z = scale_rows(f64(t), z0)
    c = mxq(e, 0, "e4m3").T @ mxq(z, 0, "e4m3")
    return (c / n_cases - f64(v)) / f64(psi)[:, None]


def e4m3fn_bytes(y):
    return np.clip(np.asarray(y, np.float64), -448.0, 448.0).astype(np.float32).astype(ml_dtypes.float8_e4m3fn).view(np.uint8)


def e4m3fn_values(b):
    return np.asarray(b, np.uint8).view(ml_dtypes.float8_e4m3fn).astype(np.float64)


def setup_inputs():
    d = draw0()
    x0 = np.asarray(d['x']).astype(np.float64)
    s = (np.max(np.abs(x0), axis=(0,), keepdims=True) / 448.0).astype(np.float32)
    out = {}
    for k, v in d.items():
        if k == 'x':
            out['x_bytes'] = e4m3fn_bytes(x0 / s.astype(np.float64))
            out['x_scale'] = s
        else:
            out[k] = v
    return out


def reference(x_bytes, x_scale, p, beta, r, t, v, psi):
    return core(e4m3fn_values(x_bytes) * x_scale.astype(np.float64), p, beta, r, t, v, psi)

@@ -1,0 +1,312 @@
+from contextlib import ExitStack
+
+import concourse.mybir as mybir
+from concourse.masks import make_identity
+
+N, D, K = 2048, 1024, 512
+
+FLOPS = 2 * N * D * D + 2 * N * D * K + 2 * N * D * K
+
+F32 = mybir.dt.float32
+BF16 = mybir.dt.bfloat16
+U32 = mybir.dt.uint32
+U8 = mybir.dt.uint8
+FP8 = mybir.dt.float8_e4m3fn
+FP8X4 = mybir.dt.float8_e4m3fn_x4
+MULT = mybir.AluOpType.mult
+SUBTRACT = mybir.AluOpType.subtract
+COPY = mybir.ActivationFunctionType.Copy
+
+P = 128
+PACK = 4
+K_PASS = P * PACK
+PASSES = D // K_PASS
+GROUPS = N // K_PASS
+UNITS = N // P
+WIDTH = 512
+BLOCKS = (D + K) // WIDTH
+Z = BLOCKS - 1
+D_BLOCKS = D // P
+WIDE_BUFS = 12
+FLAT_BUFS = 2
+FIRST_SCALED_V = 4
+KINDS = ["factors","accumulate","multiply","x_quantize","wz_group","turn","finish","empty","prepare_v","y_quantize","w_quantize","y_group","w_group","x_group","product","psi"]
+W_AT = {(0, 0): -59, (0, 1): -56, (Z, 0): -37, (Z, 1): -26, (1, 0): -6, (1, 1): 4}
+WQ_AT = {(0, 0): -36, (0, 1): -11, (Z, 0): 1, (Z, 1): 1, (1, 0): 3, (1, 1): 5}
+P_AT, P_STEP, T_AT, T_STEP, Q_LAG = -14, 1.5, -11, 1.5, 7
+I_LAG, Y_LAG, C_LAG, F_AT, V_AT, V_STEP, PSI_AT = 10, 8, 43, 199, 4, 15, -8
+
+
+def tile_factoranalysisemloadinggradient_kernel(
+    tc, x_bytes, x_scale, p, beta, r, t, v, psi, out
+):
+    nc = tc.nc
+    with ExitStack() as ctx:
+        keep = ctx.enter_context(tc.tile_pool(name="keep", bufs=1))
+        work = ctx.enter_context(tc.tile_pool(name="work", bufs=3))
+        sums = ctx.enter_context(tc.psum_pool(name="sums", bufs=1))
+        banks = ctx.enter_context(tc.psum_pool(name="banks", bufs=4))
+        ctx.enter_context(tc.manual_schedule())
+
+        warm = keep.tile([P, 1], F32, name="warm")
+        nc.vector.memset(warm[:], 0.0)
+        nc.scalar.activation(out=warm[:], in_=warm[:], func=COPY)
+        identity = keep.tile([P, P], F32, name="identity")
+        make_identity(nc, identity[:])
+        identity16 = keep.tile([P, P], BF16, name="identity16")
+        nc.gpsimd.tensor_copy(out=identity16[:], in_=identity[:])
+        psi_rows = keep.tile([P, P], BF16, name="psi_rows")
+        nc.gpsimd.memset(psi_rows[:], 0.0)
+
+        scale_cols = keep.tile([P, D // P], F32, name="scale_cols")
+        nc.sync.dma_start(out=scale_cols[:], in_=x_scale.rearrange("o (p m) -> p (o m)", p=P))
+        r16 = keep.tile([P, GROUPS, PACK], BF16, name="r16")
+        nc.scalar.dma_start(out=r16[:], in_=r.rearrange("(g p t) -> p g t", p=P, t=PACK))
+        t16 = keep.tile([P, GROUPS, PACK], BF16, name="t16")
+        nc.scalar.dma_start(out=t16[:], in_=t.rearrange("(g p t) -> p g t", p=P, t=PACK))
+
+        x_view = x_bytes.rearrange("(g p t) f -> g p t f", p=P, t=PACK)
+        p_view = p.rearrange("(g p j) d -> g p j d", p=P, j=PACK)
+        beta_view = beta.rearrange("(g p j) d -> g p j d", p=P, j=PACK)
+        x_raw = []
+        for g in range(GROUPS):
+            raw = keep.tile([P, PACK, D], U8, name=f"x_raw{g}")
+            x_raw.append(raw)
+        w_raw = {}
+        for b in range(BLOCKS):
+            for g in range(PASSES):
+                raw = keep.tile([P, PACK, WIDTH], BF16, name=f"w_raw{b}{g}")
+                w_raw[b, g] = raw
+
+        def load_x(g, a, b):
+            nc.sync.dma_start(out=x_raw[g][:, a:b, :], in_=x_view[g][:, a:b, :])
+
+        def load_w(b, g):
+            if b == Z:
+                src = beta_view[g]
+            else:
+                src = p_view[g][:, :, b * WIDTH : (b + 1) * WIDTH]
+            nc.sync.dma_start(out=w_raw[b, g][:], in_=src)
+
+        load_w(0, 0)
+        load_x(0, 0, 2)
+        load_w(0, 1)
+        load_x(0, 2, 4)
+        nc.sync.dma_start(out=psi_rows[0:D_BLOCKS, :], in_=psi.rearrange("(b p) -> b p", p=P))
+        load_w(Z, 0)
+        load_w(Z, 1)
+        load_x(1, 0, 4)
+        load_w(1, 0)
+        load_w(1, 1)
+        load_x(2, 0, 4)
+        load_x(3, 0, 4)
+        v_raw = keep.tile([P, D_BLOCKS, K], BF16, name="v_raw")
+        nc.sync.dma_start(out=v_raw[:], in_=v.rearrange("(b p) k -> p b k", p=P))
+
+        scale = keep.tile([P, D], F32, name="scale")
+        w_codes = keep.tile([P, BLOCKS, PASSES, WIDTH], U32, name="w_codes", align_bytes=256)
+        w_planes = keep.tile([P, BLOCKS, PASSES, WIDTH], U8, name="w_planes", align_bytes=256)
+        x_codes = keep.tile([P, UNITS, PASSES, P], U32, name="x_codes", align_bytes=256)
+        x_planes = keep.tile([P, UNITS, PASSES, P], U8, name="x_planes", align_bytes=256)
+        y_codes = keep.tile([P, GROUPS, BLOCKS, WIDTH], U32, name="y_codes", align_bytes=256)
+        y_planes = keep.tile([P, GROUPS, BLOCKS, WIDTH], U8, name="y_planes", align_bytes=256)
+        factor_r = keep.tile([P, UNITS], F32, name="factor_r")
+        factor_t = keep.tile([P, UNITS], F32, name="factor_t")
+        v_scaled = keep.tile([P, D_BLOCKS - FIRST_SCALED_V, K], F32, name="v_scaled")
+        psi_inv_mean = keep.tile([P, D_BLOCKS], F32, name="psi_inv_mean")
+        psi_inv = keep.tile([P, D_BLOCKS], F32, name="psi_inv")
+
+        w_grouped, wide, turned, x_grouped = {}, {}, {}, {}
+        y_bank, y_flat, y_grouped, c_bank = {}, {}, {}, {}
+
+        def spread_scale():
+            view = scale[:].rearrange("p (n q m) -> p q n m", q=2, m=4)
+            for q, copy in ((0, nc.vector.tensor_copy), (1, nc.scalar.copy)):
+                bank = banks.tile([P, 4, P], F32, name="bank")
+                for m in range(4):
+                    col = scale_cols[:, 4 * q + m : 4 * q + m + 1]
+                    nc.tensor.transpose(bank[:, m, :], col.to_broadcast([P, P]), identity[:])
+                copy(out=view[:, q], in_=bank[:].rearrange("p m n -> p n m"))
+
+        def w_group(b, g, copy):
+            tile = work.tile([P, WIDTH, PACK], BF16, name="w_grouped_tile", align_bytes=256)
+            copy(out=tile[:], in_=w_raw[b, g][:].rearrange("p j c -> p c j"))
+            w_grouped[b, g] = tile
+
+        def w_quantize(b, g):
+            nc.vector.quantize_mx(
+                out=w_codes[:, b, g, :].bitcast(FP8X4),
+                scales=w_planes[:, b, g, :],
+                in_=w_grouped[b, g][:].rearrange("p c j -> p (c j)"),
+            )
+
+        def product(i):
+            tile = work.tile([P, D], BF16, name="wide_tile", bufs=WIDE_BUFS)
+            nc.vector.tensor_tensor(
+                out=tile[:],
+                in0=x_raw[i // PACK][:, i % PACK, :].bitcast(FP8),
+                in1=scale[:],
+                op=MULT,
+            )
+            wide[i] = tile
+
+        def turn(i):
+            bank = banks.tile([P, PASSES, 2, P], F32, name="bank")
+            words = wide[i][:].bitcast(F32)
+            for g in range(PASSES):
+                for u in range(2):
+                    nc.tensor.transpose(
+                        bank[:, g, u, :], words[:, 256 * g + u : 256 * (g + 1) : 2], identity[:]
+                    )
+            turned[i] = bank
+
+        def x_group(i):
+            tile = work.tile([P, PASSES * P * PACK], BF16, name="x_grouped_tile", bufs=6, align_bytes=256)
+            nc.scalar.copy(
+                out=tile[:].bitcast(F32).rearrange("p (g c u) -> p g c u", g=PASSES, u=2),
+                in_=turned[i][:].rearrange("p g u c -> p g c u"),
+            )
+            x_grouped[i] = tile
+
+        def x_quantize(i):
+            nc.vector.quantize_mx(
+                out=x_codes[:, i].rearrange("p g c -> p (g c)").bitcast(FP8X4),
+                scales=x_planes[:, i].rearrange("p g c -> p (g c)"),
+                in_=x_grouped[i][:],
+            )
+
+        def multiply(i, b):
+            bank = banks.tile([P, WIDTH], F32, name="bank")
+            for g in range(PASSES):
+                nc.tensor.matmul_mx(
+                    out=bank[:],
+                    lhsT=x_codes[:, i, g, :].bitcast(FP8X4),
+                    lhsT_scale=x_planes[:, i, g, :],
+                    rhs=w_codes[:, b, g, :].bitcast(FP8X4),
+                    rhs_scale=w_planes[:, b, g, :],
+                    start=(g == 0),
+                    stop=(g == PASSES - 1),
+                )
+            y_bank[i, b] = bank
+
+        def empty(i, b):
+            group, j = i // PACK, i % PACK
+            if j == 0:
+                tile = work.tile([P, PACK, WIDTH], BF16, name=f"y_flat_tile{b}", bufs=FLAT_BUFS)
+                y_flat[group, b] = tile
+            factor = factor_t if b == Z else factor_r
+            nc.scalar.activation(
+                out=y_flat[group, b][:, j, :], in_=y_bank[i, b][:], func=COPY, scale=factor[:, i : i + 1]
+            )
+
+        def y_group(group, b):
+            tile = work.tile([P, WIDTH, PACK], BF16, name="y_grouped_tile", align_bytes=256)
+            nc.vector.tensor_copy(out=tile[:], in_=y_flat[group, b][:].rearrange("p j c -> p c j"))
+            y_grouped[group, b] = tile
+
+        def y_quantize(group, b):
+            nc.vector.quantize_mx(
+                out=y_codes[:, group, b, :].bitcast(FP8X4),
+                scales=y_planes[:, group, b, :],
+                in_=y_grouped[group, b][:].rearrange("p c j -> p (c j)"),
+            )
+
+        def accumulate(group, d):
+            if group == 0:
+                if d < 4:
+                    bank = sums.tile([P, K], F32, name=f"c{d}")
+                else:
+                    bank = banks.tile([P, K], F32, name="bank")
+                c_bank[d] = bank
+            cols = slice(d % 4 * P, (d % 4 + 1) * P)
+            nc.tensor.matmul_mx(
+                out=c_bank[d][:],
+                lhsT=y_codes[:, group, d // 4, cols].bitcast(FP8X4),
+                lhsT_scale=y_planes[:, group, d // 4, cols],
+                rhs=y_codes[:, group, Z, :].bitcast(FP8X4),
+                rhs_scale=y_planes[:, group, Z, :],
+                start=(group == 0),
+                stop=(group == GROUPS - 1),
+            )
+
+        def prepare_psi():
+            bank = banks.tile([P, P], BF16, name="bank")
+            nc.tensor.transpose(bank[:], psi_rows[:], identity16[:])
+            nc.vector.reciprocal(out=psi_inv[:], in_=bank[:, 0:D_BLOCKS])
+            nc.vector.tensor_scalar(
+                out=psi_inv_mean[:], in0=psi_inv[:], scalar1=1.0 / N, scalar2=None, op0=MULT
+            )
+
+        def prepare_v(d):
+            nc.scalar.activation(
+                out=v_scaled[:, d - FIRST_SCALED_V, :], in_=v_raw[:, d, :], func=COPY, scale=psi_inv[:, d : d + 1]
+            )
+
+        def finish(d):
+            tile = work.tile([P, K], F32, name="result", bufs=4)
+            if d < FIRST_SCALED_V:
+                nc.vector.scalar_tensor_tensor(
+                    out=tile[:], in0=c_bank[d][:], scalar=1.0 / N, in1=v_raw[:, d, :], op0=MULT, op1=SUBTRACT
+                )
+                nc.scalar.activation(out=tile[:], in_=tile[:], func=COPY, scale=psi_inv[:, d : d + 1])
+            else:
+                nc.vector.scalar_tensor_tensor(
+                    out=tile[:],
+                    in0=c_bank[d][:],
+                    scalar=psi_inv_mean[:, d : d + 1],
+                    in1=v_scaled[:, d - FIRST_SCALED_V, :],
+                    op0=MULT,
+                    op1=SUBTRACT,
+                )
+            nc.sync.dma_start(out=out[d * P : (d + 1) * P, :], in_=tile[:])
+
+        vector_copy = nc.vector.tensor_copy
+        scalar_copy = nc.scalar.copy
+
+        def factors():
+            nc.vector.tensor_copy(out=factor_r[:], in_=r16[:].rearrange("p g t -> p (g t)"))
+            nc.vector.tensor_copy(out=factor_t[:], in_=t16[:].rearrange("p g t -> p (g t)"))
+
+        calls = []
+
+        def at(tick, kind, f, *args):
+            calls.append((tick, KINDS.index(kind), len(calls), f, args))
+
+        order = (0, Z, 1)
+        place = {}
+        for g in range(GROUPS):
+            for b in order:
+                for j in range(PACK):
+                    place[g * PACK + j, b] = len(place)
+        for (b, g, copy) in ((0, 0, vector_copy), (0, 1, vector_copy), (Z, 0, scalar_copy), (Z, 1, scalar_copy), (1, 0, scalar_copy), (1, 1, scalar_copy)):
+            at(W_AT[b, g], "w_group" if b != Z else "wz_group", w_group, b, g, copy)
+            at(WQ_AT[b, g], "w_quantize", w_quantize, b, g)
+        for i in range(UNITS):
+            at(P_AT + P_STEP * i, "product", product, i)
+            at(T_AT + T_STEP * i, "turn", turn, i)
+            at(T_AT + T_STEP * i, "x_group", x_group, i)
+            at(T_AT + T_STEP * i + Q_LAG, "x_quantize", x_quantize, i)
+        for (i, b), n in place.items():
+            at(n, "multiply", multiply, i, b)
+            at(n, "empty", empty, i, b)
+        for g in range(GROUPS):
+            for b in order:
+                n = place[g * PACK + PACK - 1, b] + I_LAG
+                at(n, "y_group", y_group, g, b)
+                at(n + Y_LAG, "y_quantize", y_quantize, g, b)
+            n = place[g * PACK + PACK - 1, Z] + I_LAG + Y_LAG + C_LAG
+            for d in range(4):
+                at(n + 0.25 * d, "accumulate", accumulate, g, d)
+        for d in range(4):
+            at(F_AT + d, "finish", finish, d)
+        for d in range(4, 8):
+            for g in range(GROUPS - 1):
+                at(200 + d + 0.1 * g, "accumulate", accumulate, g, d)
+            at(210 + d, "accumulate", accumulate, GROUPS - 1, d)
+            at(210 + d, "finish", finish, d)
+            at(V_AT + V_STEP * d, "prepare_v", prepare_v, d)
+        at(PSI_AT, "psi", prepare_psi)
+        at(-99, "factors", factors)
+        spread_scale()
+        for tick, kind, n, f, args in sorted(calls, key=lambda c: c[:3]):
+            f(*args)

@@ -24,17 +24,11 @@ PASSES = D // K_PASS
 GROUPS = N // K_PASS
 UNITS = N // P
 WIDTH = 512
-BLOCKS = (D + K) // WIDTH
-Z = BLOCKS - 1
-D_BLOCKS = D // P
-WIDE_BUFS = 12
-FLAT_BUFS = 2
-FIRST_SCALED_V = 4
-KINDS = ["factors","accumulate","multiply","x_quantize","wz_group","turn","finish","empty","prepare_v","y_quantize","w_quantize","y_group","w_group","x_group","product","psi"]
-W_AT = {(0, 0): -59, (0, 1): -56, (Z, 0): -37, (Z, 1): -26, (1, 0): -6, (1, 1): 4}
-WQ_AT = {(0, 0): -36, (0, 1): -11, (Z, 0): 1, (Z, 1): 1, (1, 0): 3, (1, 1): 5}
-P_AT, P_STEP, T_AT, T_STEP, Q_LAG = -14, 1.5, -11, 1.5, 7
-I_LAG, Y_LAG, C_LAG, F_AT, V_AT, V_STEP, PSI_AT = 10, 8, 43, 199, 4, 15, -8
+Z = 2
+BANDS = D // P
+BANKS = 8
+RUN = 4
+RINGS = {"bank": BANKS, "wide": 8, "x_grouped": 3, "flat": 9, "grouped_v": 3, "grouped_s": 3}
 
 
 def tile_factoranalysisemloadinggradient_kernel(
@@ -43,270 +37,311 @@ def tile_factoranalysisemloadinggradient_kernel(
     nc = tc.nc
     with ExitStack() as ctx:
         keep = ctx.enter_context(tc.tile_pool(name="keep", bufs=1))
-        work = ctx.enter_context(tc.tile_pool(name="work", bufs=3))
-        sums = ctx.enter_context(tc.psum_pool(name="sums", bufs=1))
-        banks = ctx.enter_context(tc.psum_pool(name="banks", bufs=4))
+        psum = ctx.enter_context(tc.psum_pool(name="psum", bufs=1))
         ctx.enter_context(tc.manual_schedule())
 
-        warm = keep.tile([P, 1], F32, name="warm")
-        nc.vector.memset(warm[:], 0.0)
-        nc.scalar.activation(out=warm[:], in_=warm[:], func=COPY)
         identity = keep.tile([P, P], F32, name="identity")
         make_identity(nc, identity[:])
-        identity16 = keep.tile([P, P], BF16, name="identity16")
-        nc.gpsimd.tensor_copy(out=identity16[:], in_=identity[:])
-        psi_rows = keep.tile([P, P], BF16, name="psi_rows")
-        nc.gpsimd.memset(psi_rows[:], 0.0)
+
+        x_view = x_bytes.rearrange("(g q j) f -> g q j f", q=P, j=PACK)
+        p_view = p.rearrange("(g q j) d -> g q j d", q=P, j=PACK)
+        beta_view = beta.rearrange("(g q j) d -> g q j d", q=P, j=PACK)
+        x_raw, w_raw = {}, {}
+
+        def load_x(first, count):
+            raw = keep.tile([P, count, D], U8, name=f"x_raw{first}")
+            j = first % PACK
+            nc.sync.dma_start(out=raw[:], in_=x_view[first // PACK][:, j : j + count, :])
+            for n in range(count):
+                x_raw[first + n] = raw[:, n, :]
+
+        def load_beta(g):
+            raw = keep.tile([P, PACK, K], BF16, name=f"beta_raw{g}")
+            nc.sync.dma_start(out=raw[:], in_=beta_view[g])
+            w_raw[Z, g] = raw[:]
+
+        def load_p(b, g):
+            raw = keep.tile([P, PACK, WIDTH], BF16, name=f"p_raw{b}{g}")
+            nc.sync.dma_start(out=raw[:], in_=p_view[g][:, :, b * WIDTH : (b + 1) * WIDTH])
+            w_raw[b, g] = raw[:]
 
         scale_cols = keep.tile([P, D // P], F32, name="scale_cols")
-        nc.sync.dma_start(out=scale_cols[:], in_=x_scale.rearrange("o (p m) -> p (o m)", p=P))
         r16 = keep.tile([P, GROUPS, PACK], BF16, name="r16")
-        nc.scalar.dma_start(out=r16[:], in_=r.rearrange("(g p t) -> p g t", p=P, t=PACK))
         t16 = keep.tile([P, GROUPS, PACK], BF16, name="t16")
-        nc.scalar.dma_start(out=t16[:], in_=t.rearrange("(g p t) -> p g t", p=P, t=PACK))
-
-        x_view = x_bytes.rearrange("(g p t) f -> g p t f", p=P, t=PACK)
-        p_view = p.rearrange("(g p j) d -> g p j d", p=P, j=PACK)
-        beta_view = beta.rearrange("(g p j) d -> g p j d", p=P, j=PACK)
-        x_raw = []
-        for g in range(GROUPS):
-            raw = keep.tile([P, PACK, D], U8, name=f"x_raw{g}")
-            x_raw.append(raw)
-        w_raw = {}
-        for b in range(BLOCKS):
-            for g in range(PASSES):
-                raw = keep.tile([P, PACK, WIDTH], BF16, name=f"w_raw{b}{g}")
-                w_raw[b, g] = raw
-
-        def load_x(g, a, b):
-            nc.sync.dma_start(out=x_raw[g][:, a:b, :], in_=x_view[g][:, a:b, :])
-
-        def load_w(b, g):
-            if b == Z:
-                src = beta_view[g]
-            else:
-                src = p_view[g][:, :, b * WIDTH : (b + 1) * WIDTH]
-            nc.sync.dma_start(out=w_raw[b, g][:], in_=src)
-
-        load_w(0, 0)
-        load_x(0, 0, 2)
-        load_w(0, 1)
-        load_x(0, 2, 4)
-        nc.sync.dma_start(out=psi_rows[0:D_BLOCKS, :], in_=psi.rearrange("(b p) -> b p", p=P))
-        load_w(Z, 0)
-        load_w(Z, 1)
-        load_x(1, 0, 4)
-        load_w(1, 0)
-        load_w(1, 1)
-        load_x(2, 0, 4)
-        load_x(3, 0, 4)
-        v_raw = keep.tile([P, D_BLOCKS, K], BF16, name="v_raw")
-        nc.sync.dma_start(out=v_raw[:], in_=v.rearrange("(b p) k -> p b k", p=P))
+        v_raw = keep.tile([P, BANDS, K], BF16, name="v_raw")
+        psi16 = keep.tile([P, BANDS, 2], BF16, name="psi16")
+        nc.sync.dma_start(out=scale_cols[:], in_=x_scale.rearrange("o (q m) -> q (o m)", q=P))
+        load_beta(0)
+        load_x(0, 2)
+        load_beta(1)
+        load_x(2, 2)
+        load_p(0, 0)
+        load_x(4, 4)
+        load_p(0, 1)
+        nc.sync.dma_start(out=t16[:], in_=t.rearrange("(g q j) -> q g j", q=P, j=PACK))
+        nc.sync.dma_start(out=r16[:], in_=r.rearrange("(g q j) -> q g j", q=P, j=PACK))
+        load_p(1, 0)
+        load_x(8, 4)
+        load_p(1, 1)
+        load_x(12, 4)
+        nc.sync.dma_start(out=v_raw[:], in_=v.rearrange("(b q) k -> q b k", q=P))
+        with nc.allow_non_contiguous_dma(reason="one noise variance for each partition and band"):
+            nc.sync.dma_start(out=psi16[:, :, 0], in_=psi.rearrange("(b q) -> q b", q=P))
 
         scale = keep.tile([P, D], F32, name="scale")
-        w_codes = keep.tile([P, BLOCKS, PASSES, WIDTH], U32, name="w_codes", align_bytes=256)
-        w_planes = keep.tile([P, BLOCKS, PASSES, WIDTH], U8, name="w_planes", align_bytes=256)
-        x_codes = keep.tile([P, UNITS, PASSES, P], U32, name="x_codes", align_bytes=256)
-        x_planes = keep.tile([P, UNITS, PASSES, P], U8, name="x_planes", align_bytes=256)
-        y_codes = keep.tile([P, GROUPS, BLOCKS, WIDTH], U32, name="y_codes", align_bytes=256)
-        y_planes = keep.tile([P, GROUPS, BLOCKS, WIDTH], U8, name="y_planes", align_bytes=256)
-        factor_r = keep.tile([P, UNITS], F32, name="factor_r")
-        factor_t = keep.tile([P, UNITS], F32, name="factor_t")
-        v_scaled = keep.tile([P, D_BLOCKS - FIRST_SCALED_V, K], F32, name="v_scaled")
-        psi_inv_mean = keep.tile([P, D_BLOCKS], F32, name="psi_inv_mean")
-        psi_inv = keep.tile([P, D_BLOCKS], F32, name="psi_inv")
+        factor = {b: keep.tile([P, UNITS], F32, name=f"factor{b}") for b in (0, Z)}
+        factor[1] = factor[0]
+        psi_inv = keep.tile([P, BANDS], F32, name="psi_inv")
+        tiles, taken = {}, {ring: 0 for ring in RINGS}
 
-        w_grouped, wide, turned, x_grouped = {}, {}, {}, {}
-        y_bank, y_flat, y_grouped, c_bank = {}, {}, {}, {}
+        def take(ring, shape, dtype):
+            pool = psum if ring == "bank" else keep
+            name = f"{ring}{taken[ring] % RINGS[ring]}"
+            taken[ring] = taken[ring] + 1
+            if ring == "bank":
+                return pool.tile(shape, dtype, name=name)
+            return pool.tile(shape, dtype, name=name, align_bytes=256)
 
-        def spread_scale():
-            view = scale[:].rearrange("p (n q m) -> p q n m", q=2, m=4)
-            for q, copy in ((0, nc.vector.tensor_copy), (1, nc.scalar.copy)):
-                bank = banks.tile([P, 4, P], F32, name="bank")
-                for m in range(4):
-                    col = scale_cols[:, 4 * q + m : 4 * q + m + 1]
-                    nc.tensor.transpose(bank[:, m, :], col.to_broadcast([P, P]), identity[:])
-                copy(out=view[:, q], in_=bank[:].rearrange("p m n -> p n m"))
+        def mx_tiles(key, width):
+            name = "_".join(str(part) for part in key)
+            codes = keep.tile([P, width], U32, name=f"codes_{name}", align_bytes=256)
+            scales = keep.tile([P, width], U8, name=f"scales_{name}", align_bytes=256)
+            tiles[key] = (codes, scales)
+            return codes, scales
 
-        def w_group(b, g, copy):
-            tile = work.tile([P, WIDTH, PACK], BF16, name="w_grouped_tile", align_bytes=256)
-            copy(out=tile[:], in_=w_raw[b, g][:].rearrange("p j c -> p c j"))
-            w_grouped[b, g] = tile
+        def spread_turn(h):
+            bank = take("bank", [P, 4, P], F32)
+            for m in range(4):
+                col = scale_cols[:, 4 * h + m : 4 * h + m + 1]
+                nc.tensor.transpose(bank[:, m, :], col.to_broadcast([P, P]), identity[:])
+            tiles["spread_turn", h] = bank
 
-        def w_quantize(b, g):
+        def spread_copy(h):
+            view = scale[:].rearrange("q (n h m) -> q h n m", h=2, m=4)
+            nc.scalar.copy(out=view[:, h], in_=tiles["spread_turn", h][:].rearrange("q m n -> q n m"))
+
+        def widen_factor(b):
+            source = t16 if b == Z else r16
+            nc.vector.tensor_copy(out=factor[b][:], in_=source[:].rearrange("q g j -> q (g j)"))
+
+        def invert_psi():
+            nc.vector.reciprocal(out=psi_inv[:], in_=psi16[:, :, 0])
+
+        def interleave(kind, engine, a, b):
+            source = w_raw[a, b] if kind == "w" else tiles["flat", a, b][:]
+            tile = take("grouped_" + engine, [P, WIDTH, PACK], BF16)
+            copy = nc.vector.tensor_copy if engine == "v" else nc.scalar.copy
+            copy(
+                out=tile[:].rearrange("q (c i) j -> q c j i", i=RUN),
+                in_=source.rearrange("q j (c i) -> q c j i", i=RUN),
+            )
+            tiles["grouped", kind, a, b] = tile
+
+        def quantize(kind, a, b):
+            codes, scales = mx_tiles((kind, a, b), WIDTH)
+            source = tiles["grouped", kind, a, b]
             nc.vector.quantize_mx(
-                out=w_codes[:, b, g, :].bitcast(FP8X4),
-                scales=w_planes[:, b, g, :],
-                in_=w_grouped[b, g][:].rearrange("p c j -> p (c j)"),
+                out=codes[:].bitcast(FP8X4), scales=scales[:], in_=source[:].rearrange("q c j -> q (c j)")
             )
 
         def product(i):
-            tile = work.tile([P, D], BF16, name="wide_tile", bufs=WIDE_BUFS)
-            nc.vector.tensor_tensor(
-                out=tile[:],
-                in0=x_raw[i // PACK][:, i % PACK, :].bitcast(FP8),
-                in1=scale[:],
-                op=MULT,
-            )
-            wide[i] = tile
+            tile = take("wide", [P, D], BF16)
+            nc.vector.tensor_tensor(out=tile[:], in0=x_raw[i].bitcast(FP8), in1=scale[:], op=MULT)
+            tiles["wide", i] = tile
 
         def turn(i):
-            bank = banks.tile([P, PASSES, 2, P], F32, name="bank")
-            words = wide[i][:].bitcast(F32)
+            bank = take("bank", [P, PASSES, 2, P], F32)
+            words = tiles["wide", i][:].bitcast(F32)
             for g in range(PASSES):
                 for u in range(2):
                     nc.tensor.transpose(
                         bank[:, g, u, :], words[:, 256 * g + u : 256 * (g + 1) : 2], identity[:]
                     )
-            turned[i] = bank
+            tiles["turn", i] = bank
 
         def x_group(i):
-            tile = work.tile([P, PASSES * P * PACK], BF16, name="x_grouped_tile", bufs=6, align_bytes=256)
+            if i % 2 == 0:
+                tiles["x_grouped", i // 2] = take("x_grouped", [P, 2 * D], BF16)
+            half = tiles["x_grouped", i // 2][:, i % 2 * D : (i % 2 + 1) * D]
             nc.scalar.copy(
-                out=tile[:].bitcast(F32).rearrange("p (g c u) -> p g c u", g=PASSES, u=2),
-                in_=turned[i][:].rearrange("p g u c -> p g c u"),
+                out=half.bitcast(F32).rearrange("q (g c u) -> q g c u", g=PASSES, u=2),
+                in_=tiles["turn", i][:].rearrange("q g u c -> q g c u"),
             )
-            x_grouped[i] = tile
 
-        def x_quantize(i):
+        def x_quantize(pair):
+            codes, scales = mx_tiles(("x", pair), 2 * PASSES * P)
             nc.vector.quantize_mx(
-                out=x_codes[:, i].rearrange("p g c -> p (g c)").bitcast(FP8X4),
-                scales=x_planes[:, i].rearrange("p g c -> p (g c)"),
-                in_=x_grouped[i][:],
+                out=codes[:].bitcast(FP8X4), scales=scales[:], in_=tiles["x_grouped", pair][:]
             )
 
         def multiply(i, b):
-            bank = banks.tile([P, WIDTH], F32, name="bank")
+            bank = take("bank", [P, WIDTH], F32)
+            x_codes, x_scales = tiles["x", i // 2]
             for g in range(PASSES):
+                cols = slice((i % 2 * PASSES + g) * P, (i % 2 * PASSES + g + 1) * P)
+                w_codes, w_scales = tiles["w", b, g]
                 nc.tensor.matmul_mx(
                     out=bank[:],
-                    lhsT=x_codes[:, i, g, :].bitcast(FP8X4),
-                    lhsT_scale=x_planes[:, i, g, :],
-                    rhs=w_codes[:, b, g, :].bitcast(FP8X4),
-                    rhs_scale=w_planes[:, b, g, :],
+                    lhsT=x_codes[:, cols].bitcast(FP8X4),
+                    lhsT_scale=x_scales[:, cols],
+                    rhs=w_codes[:].bitcast(FP8X4),
+                    rhs_scale=w_scales[:],
                     start=(g == 0),
                     stop=(g == PASSES - 1),
                 )
-            y_bank[i, b] = bank
+            tiles["multiply", i, b] = bank
 
         def empty(i, b):
-            group, j = i // PACK, i % PACK
+            group, j = divmod(i, PACK)
             if j == 0:
-                tile = work.tile([P, PACK, WIDTH], BF16, name=f"y_flat_tile{b}", bufs=FLAT_BUFS)
-                y_flat[group, b] = tile
-            factor = factor_t if b == Z else factor_r
+                tiles["flat", group, b] = take("flat", [P, PACK, WIDTH], BF16)
             nc.scalar.activation(
-                out=y_flat[group, b][:, j, :], in_=y_bank[i, b][:], func=COPY, scale=factor[:, i : i + 1]
-            )
-
-        def y_group(group, b):
-            tile = work.tile([P, WIDTH, PACK], BF16, name="y_grouped_tile", align_bytes=256)
-            nc.vector.tensor_copy(out=tile[:], in_=y_flat[group, b][:].rearrange("p j c -> p c j"))
-            y_grouped[group, b] = tile
-
-        def y_quantize(group, b):
-            nc.vector.quantize_mx(
-                out=y_codes[:, group, b, :].bitcast(FP8X4),
-                scales=y_planes[:, group, b, :],
-                in_=y_grouped[group, b][:].rearrange("p c j -> p (c j)"),
+                out=tiles["flat", group, b][:, j, :],
+                in_=tiles["multiply", i, b][:],
+                func=COPY,
+                scale=factor[b][:, i : i + 1],
             )
 
         def accumulate(group, d):
             if group == 0:
-                if d < 4:
-                    bank = sums.tile([P, K], F32, name=f"c{d}")
-                else:
-                    bank = banks.tile([P, K], F32, name="bank")
-                c_bank[d] = bank
+                tiles["sum", d] = take("bank", [P, K], F32)
             cols = slice(d % 4 * P, (d % 4 + 1) * P)
+            e_codes, e_scales = tiles["y", group, d // 4]
+            z_codes, z_scales = tiles["y", group, Z]
             nc.tensor.matmul_mx(
-                out=c_bank[d][:],
-                lhsT=y_codes[:, group, d // 4, cols].bitcast(FP8X4),
-                lhsT_scale=y_planes[:, group, d // 4, cols],
-                rhs=y_codes[:, group, Z, :].bitcast(FP8X4),
-                rhs_scale=y_planes[:, group, Z, :],
+                out=tiles["sum", d][:],
+                lhsT=e_codes[:, cols].bitcast(FP8X4),
+                lhsT_scale=e_scales[:, cols],
+                rhs=z_codes[:].bitcast(FP8X4),
+                rhs_scale=z_scales[:],
                 start=(group == 0),
                 stop=(group == GROUPS - 1),
             )
 
-        def prepare_psi():
-            bank = banks.tile([P, P], BF16, name="bank")
-            nc.tensor.transpose(bank[:], psi_rows[:], identity16[:])
-            nc.vector.reciprocal(out=psi_inv[:], in_=bank[:, 0:D_BLOCKS])
-            nc.vector.tensor_scalar(
-                out=psi_inv_mean[:], in0=psi_inv[:], scalar1=1.0 / N, scalar2=None, op0=MULT
+        def subtract(d):
+            tile = keep.tile([P, K], F32, name=f"result{d}")
+            nc.vector.scalar_tensor_tensor(
+                out=tile[:], in0=tiles["sum", d][:], scalar=1.0 / N, in1=v_raw[:, d, :], op0=MULT, op1=SUBTRACT
             )
+            tiles["result", d] = tile
 
-        def prepare_v(d):
-            nc.scalar.activation(
-                out=v_scaled[:, d - FIRST_SCALED_V, :], in_=v_raw[:, d, :], func=COPY, scale=psi_inv[:, d : d + 1]
-            )
-
-        def finish(d):
-            tile = work.tile([P, K], F32, name="result", bufs=4)
-            if d < FIRST_SCALED_V:
-                nc.vector.scalar_tensor_tensor(
-                    out=tile[:], in0=c_bank[d][:], scalar=1.0 / N, in1=v_raw[:, d, :], op0=MULT, op1=SUBTRACT
-                )
-                nc.scalar.activation(out=tile[:], in_=tile[:], func=COPY, scale=psi_inv[:, d : d + 1])
-            else:
-                nc.vector.scalar_tensor_tensor(
-                    out=tile[:],
-                    in0=c_bank[d][:],
-                    scalar=psi_inv_mean[:, d : d + 1],
-                    in1=v_scaled[:, d - FIRST_SCALED_V, :],
-                    op0=MULT,
-                    op1=SUBTRACT,
-                )
+        def store(d):
+            tile = tiles["result", d]
+            nc.scalar.activation(out=tile[:], in_=tile[:], func=COPY, scale=psi_inv[:, d : d + 1])
             nc.sync.dma_start(out=out[d * P : (d + 1) * P, :], in_=tile[:])
 
-        vector_copy = nc.vector.tensor_copy
-        scalar_copy = nc.scalar.copy
+        def needs(step):
+            name, args = step[0], step[1:]
+            if name is spread_copy:
+                return [(spread_turn, *args)]
+            if name is product:
+                return [(spread_copy, 0), (spread_copy, 1)]
+            if name is turn:
+                return [(product, *args)]
+            if name is x_group:
+                return [(turn, *args)]
+            if name is x_quantize:
+                return [(x_group, 2 * args[0]), (x_group, 2 * args[0] + 1)]
+            if name is interleave and args[0] == "y":
+                return [(empty, PACK * args[2] + j, args[3]) for j in range(PACK)]
+            if name is quantize:
+                return [(interleave, args[0], engine_of[args], *args[1:])]
+            if name is multiply:
+                return [(x_quantize, args[0] // 2)] + [(quantize, "w", args[1], g) for g in range(PASSES)]
+            if name is empty:
+                return [(multiply, *args), (widen_factor, Z if args[1] == Z else 0)]
+            if name is accumulate:
+                return [(quantize, "y", args[0], args[1] // 4), (quantize, "y", args[0], Z)]
+            if name is subtract:
+                return [(accumulate, GROUPS - 1, *args)]
+            if name is store:
+                return [(subtract, *args), (invert_psi,)]
+            return []
 
-        def factors():
-            nc.vector.tensor_copy(out=factor_r[:], in_=r16[:].rearrange("p g t -> p (g t)"))
-            nc.vector.tensor_copy(out=factor_t[:], in_=t16[:].rearrange("p g t -> p (g t)"))
+        def claims(step):
+            name, args = step[0], step[1:]
+            if name is spread_turn:
+                return "bank", (spread_copy, *args)
+            if name is turn:
+                return "bank", (x_group, *args)
+            if name is multiply:
+                return "bank", (empty, *args)
+            if name is accumulate and args[0] == 0:
+                return "bank", (subtract, args[1])
+            if name is product:
+                return "wide", (turn, *args)
+            if name is x_group and args[0] % 2 == 0:
+                return "x_grouped", (x_quantize, args[0] // 2)
+            if name is empty and args[0] % PACK == 0:
+                key = ("y", args[0] // PACK, args[1])
+                return "flat", (interleave, "y", engine_of[key], *key[1:])
+            if name is interleave:
+                return "grouped_" + args[1], (quantize, args[0], *args[2:])
+            return None, None
 
-        calls = []
+        engine_of = {("w", b, g): "v" for b in (0, 1, Z) for g in range(PASSES)}
+        engine_of.update({("y", g, b): "v" for b in (0, 1, Z) for g in range(GROUPS)})
+        for key in (("w", Z, 1), ("w", 0, 0), ("w", 0, 1), ("y", 3, 1)):
+            engine_of[key] = "s"
 
-        def at(tick, kind, f, *args):
-            calls.append((tick, KINDS.index(kind), len(calls), f, args))
+        def I(*key):
+            return (interleave, key[0], engine_of[key], *key[1:])
 
-        order = (0, Z, 1)
-        place = {}
+        def Q(*key):
+            return (quantize, *key)
+
+        def PR(i):
+            return (product, i)
+
+        def QX(i):
+            return (x_quantize, i)
+
+        def T(k):
+            return [(turn, 2 * k), (turn, 2 * k + 1)]
+
+        def M(g, b, js=range(PACK)):
+            return [(multiply, PACK * g + j, b) for j in js]
+
+        first = T(0) + T(1) + M(0, Z) + T(2) + T(3) + M(0, 0) + M(1, Z) + T(4) + M(1, 0) + T(5) + M(0, 1) + T(6) + M(2, Z) + T(7) + M(2, 0) + M(1, 1) + M(3, Z) + M(3, 0) + M(2, 1) + M(3, 1)
+        tensor = [(spread_turn, 0), (spread_turn, 1)] + first
         for g in range(GROUPS):
-            for b in order:
-                for j in range(PACK):
-                    place[g * PACK + j, b] = len(place)
-        for (b, g, copy) in ((0, 0, vector_copy), (0, 1, vector_copy), (Z, 0, scalar_copy), (Z, 1, scalar_copy), (1, 0, scalar_copy), (1, 1, scalar_copy)):
-            at(W_AT[b, g], "w_group" if b != Z else "wz_group", w_group, b, g, copy)
-            at(WQ_AT[b, g], "w_quantize", w_quantize, b, g)
-        for i in range(UNITS):
-            at(P_AT + P_STEP * i, "product", product, i)
-            at(T_AT + T_STEP * i, "turn", turn, i)
-            at(T_AT + T_STEP * i, "x_group", x_group, i)
-            at(T_AT + T_STEP * i + Q_LAG, "x_quantize", x_quantize, i)
-        for (i, b), n in place.items():
-            at(n, "multiply", multiply, i, b)
-            at(n, "empty", empty, i, b)
-        for g in range(GROUPS):
-            for b in order:
-                n = place[g * PACK + PACK - 1, b] + I_LAG
-                at(n, "y_group", y_group, g, b)
-                at(n + Y_LAG, "y_quantize", y_quantize, g, b)
-            n = place[g * PACK + PACK - 1, Z] + I_LAG + Y_LAG + C_LAG
-            for d in range(4):
-                at(n + 0.25 * d, "accumulate", accumulate, g, d)
-        for d in range(4):
-            at(F_AT + d, "finish", finish, d)
-        for d in range(4, 8):
-            for g in range(GROUPS - 1):
-                at(200 + d + 0.1 * g, "accumulate", accumulate, g, d)
-            at(210 + d, "accumulate", accumulate, GROUPS - 1, d)
-            at(210 + d, "finish", finish, d)
-            at(V_AT + V_STEP * d, "prepare_v", prepare_v, d)
-        at(PSI_AT, "psi", prepare_psi)
-        at(-99, "factors", factors)
-        spread_scale()
-        for tick, kind, n, f, args in sorted(calls, key=lambda c: c[:3]):
-            f(*args)
+            tensor.extend((accumulate, g, d) for d in range(4))
+        for d in range(4, BANDS):
+            tensor.extend((accumulate, g, d) for g in range(GROUPS))
+        scalar = [((x_group if step[0] is turn else empty), *step[1:]) for step in first]
+        scalar[4:4] = [I("w", 0, 1)]
+        scalar[2:2] = [I("w", 0, 0)]
+        scalar = [(spread_copy, 0), (spread_copy, 1), I("w", Z, 1)] + scalar
+        scalar.append(I("y", 3, 1))
+        scalar.extend((store, d) for d in range(BANDS))
+
+        vector = [I("w", Z, 0), PR(0), PR(1), Q("w", Z, 0), PR(2), PR(3), QX(0), Q("w", Z, 1), (widen_factor, Z), PR(4), PR(5), QX(1), PR(6), (widen_factor, 0), Q("w", 0, 0), PR(7), Q("w", 0, 1), I("w", 1, 0), PR(8), QX(2), PR(9), QX(3), I("w", 1, 1), Q("w", 1, 0), PR(10), Q("w", 1, 1), PR(11), QX(4)]
+        vector += [PR(12), PR(13), QX(5), PR(14), PR(15), I("y", 0, Z), (invert_psi,), I("y", 0, 0), Q("y", 0, Z), QX(6), I("y", 1, Z), Q("y", 0, 0), I("y", 1, 0), Q("y", 1, Z), QX(7)]
+        order = [(0, 1), (2, Z), (2, 0), (1, 1), (3, Z), (3, 0), (2, 1)]
+        last = (1, 0)
+        for key in order:
+            vector += [I("y", *key), Q("y", *last)]
+            last = key
+        vector += [Q("y", 2, 1), (subtract, 0), Q("y", 3, 1)]
+        vector += [(subtract, d) for d in range(1, 8)]
+
+        queues = [vector, scalar, tensor]
+        written, readers = set(), {ring: [] for ring in RINGS}
+        while any(queues):
+            progress = False
+            for queue in queues:
+                while queue:
+                    step = queue[0]
+                    ring, reader = claims(step)
+                    waits = needs(step)
+                    if ring is not None and len(readers[ring]) >= RINGS[ring]:
+                        waits = waits + [readers[ring][-RINGS[ring]]]
+                    if not all(wait in written for wait in waits):
+                        break
+                    step[0](*step[1:])
+                    written.add(step)
+                    if ring is not None:
+                        readers[ring].append(reader)
+                    queue.remove(step)
+                    progress = True
+            assert progress

@@ -14,6 +14,7 @@ U8 = mybir.dt.uint8
 FP8 = mybir.dt.float8_e4m3fn
 FP8X4 = mybir.dt.float8_e4m3fn_x4
 MULT = mybir.AluOpType.mult
+ADD = mybir.AluOpType.add
 SUBTRACT = mybir.AluOpType.subtract
 COPY = mybir.ActivationFunctionType.Copy
 
@@ -27,8 +28,10 @@ WIDTH = 512
 Z = 2
 BANDS = D // P
 BANKS = 8
+SPLIT = 28
+LATE = [("y", 3, 1)]
 RUN = 4
-RINGS = {"bank": BANKS, "wide": 8, "x_grouped": 3, "flat": 9, "grouped_v": 3, "grouped_s": 3}
+RINGS = {"wide": 4, "flat": 10, "grouped_v": 3, "grouped_s": 1, "shared0": 1, "shared1": 1, "shared2": 1, **{f"bank{n}": 1 for n in range(BANKS)}}
 
 
 def tile_factoranalysisemloadinggradient_kernel(
@@ -52,8 +55,8 @@ def tile_factoranalysisemloadinggradient_kernel(
             raw = keep.tile([P, count, D], U8, name=f"x_raw{first}")
             j = first % PACK
             nc.sync.dma_start(out=raw[:], in_=x_view[first // PACK][:, j : j + count, :])
-            for n in range(count):
-                x_raw[first + n] = raw[:, n, :]
+            for n in range(0, count, 2):
+                x_raw[(first + n) // 2] = raw[:, n : n + 2, :].rearrange("q j f -> q (j f)")
 
         def load_beta(g):
             raw = keep.tile([P, PACK, K], BF16, name=f"beta_raw{g}")
@@ -65,19 +68,20 @@ def tile_factoranalysisemloadinggradient_kernel(
             nc.sync.dma_start(out=raw[:], in_=p_view[g][:, :, b * WIDTH : (b + 1) * WIDTH])
             w_raw[b, g] = raw[:]
 
-        scale_cols = keep.tile([P, D // P], F32, name="scale_cols")
+        scale = keep.tile([P, PASSES, PACK], F32, name="scale")
         r16 = keep.tile([P, GROUPS, PACK], BF16, name="r16")
         t16 = keep.tile([P, GROUPS, PACK], BF16, name="t16")
         v_raw = keep.tile([P, BANDS, K], BF16, name="v_raw")
         psi16 = keep.tile([P, BANDS, 2], BF16, name="psi16")
-        nc.sync.dma_start(out=scale_cols[:], in_=x_scale.rearrange("o (q m) -> q (o m)", q=P))
-        load_beta(0)
         load_x(0, 2)
-        load_beta(1)
+        load_beta(0)
+        nc.sync.dma_start(out=scale[:], in_=x_scale.rearrange("o (g q j) -> q (o g) j", q=P, j=PACK))
         load_x(2, 2)
+        load_beta(1)
+        load_x(4, 2)
         load_p(0, 0)
-        load_x(4, 4)
         load_p(0, 1)
+        load_x(6, 2)
         nc.sync.dma_start(out=t16[:], in_=t.rearrange("(g q j) -> q g j", q=P, j=PACK))
         nc.sync.dma_start(out=r16[:], in_=r.rearrange("(g q j) -> q g j", q=P, j=PACK))
         load_p(1, 0)
@@ -88,108 +92,111 @@ def tile_factoranalysisemloadinggradient_kernel(
         with nc.allow_non_contiguous_dma(reason="one noise variance for each partition and band"):
             nc.sync.dma_start(out=psi16[:, :, 0], in_=psi.rearrange("(b q) -> q b", q=P))
 
-        scale = keep.tile([P, D], F32, name="scale")
         factor = {b: keep.tile([P, UNITS], F32, name=f"factor{b}") for b in (0, Z)}
         factor[1] = factor[0]
         psi_inv = keep.tile([P, BANDS], F32, name="psi_inv")
         tiles, taken = {}, {ring: 0 for ring in RINGS}
 
         def take(ring, shape, dtype):
-            pool = psum if ring == "bank" else keep
-            name = f"{ring}{taken[ring] % RINGS[ring]}"
+            name = f"{ring}_{taken[ring] % RINGS[ring]}"
             taken[ring] = taken[ring] + 1
-            if ring == "bank":
-                return pool.tile(shape, dtype, name=name)
-            return pool.tile(shape, dtype, name=name, align_bytes=256)
+            if ring.startswith("bank"):
+                return psum.tile(shape, dtype, name=name)
+            return keep.tile(shape, dtype, name=name, align_bytes=256)
 
-        def mx_tiles(key, width):
-            name = "_".join(str(part) for part in key)
-            codes = keep.tile([P, width], U32, name=f"codes_{name}", align_bytes=256)
-            scales = keep.tile([P, width], U8, name=f"scales_{name}", align_bytes=256)
-            tiles[key] = (codes, scales)
-            return codes, scales
-
-        def spread_turn(h):
-            bank = take("bank", [P, 4, P], F32)
-            for m in range(4):
-                col = scale_cols[:, 4 * h + m : 4 * h + m + 1]
-                nc.tensor.transpose(bank[:, m, :], col.to_broadcast([P, P]), identity[:])
-            tiles["spread_turn", h] = bank
-
-        def spread_copy(h):
-            view = scale[:].rearrange("q (n h m) -> q h n m", h=2, m=4)
-            nc.scalar.copy(out=view[:, h], in_=tiles["spread_turn", h][:].rearrange("q m n -> q n m"))
+        def mx_tiles(key):
+            if key not in tiles:
+                name = "_".join(str(part) for part in key)
+                codes = keep.tile([P, WIDTH], U32, name=f"codes_{name}", align_bytes=256)
+                scales = keep.tile([P, WIDTH], U8, name=f"scales_{name}", align_bytes=256)
+                tiles[key] = (codes, scales)
+            return tiles[key]
 
         def widen_factor(b):
             source = t16 if b == Z else r16
-            nc.vector.tensor_copy(out=factor[b][:], in_=source[:].rearrange("q g j -> q (g j)"))
+            nc.scalar.copy(out=factor[b][:], in_=source[:].rearrange("q g j -> q (g j)"))
 
         def invert_psi():
             nc.vector.reciprocal(out=psi_inv[:], in_=psi16[:, :, 0])
 
-        def interleave(kind, engine, a, b):
-            source = w_raw[a, b] if kind == "w" else tiles["flat", a, b][:]
-            tile = take("grouped_" + engine, [P, WIDTH, PACK], BF16)
-            copy = nc.vector.tensor_copy if engine == "v" else nc.scalar.copy
-            copy(
-                out=tile[:].rearrange("q (c i) j -> q c j i", i=RUN),
-                in_=source.rearrange("q j (c i) -> q c j i", i=RUN),
-            )
-            tiles["grouped", kind, a, b] = tile
+        def interleave(key, n):
+            kind, a, b = key
+            engine, ring, first, last = pieces[key][n]
+            source = (w_raw[a, b] if kind == "w" else tiles["flat", a, b][:])[:, :, first:last]
+            tile = take(ring, [P, last - first, PACK], BF16)
+            if engine == "g":
+                nc.gpsimd.tensor_scalar(
+                    out=tile[:], in0=source.rearrange("q j c -> q c j"), scalar1=1.0, scalar2=0.0, op0=MULT, op1=ADD
+                )
+            else:
+                copy = nc.vector.tensor_copy if engine == "v" else nc.scalar.copy
+                copy(
+                    out=tile[:].rearrange("q (c i) j -> q c j i", i=RUN),
+                    in_=source.rearrange("q j (c i) -> q c j i", i=RUN),
+                )
+            tiles["grouped", key, n] = tile
 
-        def quantize(kind, a, b):
-            codes, scales = mx_tiles((kind, a, b), WIDTH)
-            source = tiles["grouped", kind, a, b]
+        def quantize(key, n):
+            codes, scales = mx_tiles(key)
+            first, last = pieces[key][n][2:]
             nc.vector.quantize_mx(
-                out=codes[:].bitcast(FP8X4), scales=scales[:], in_=source[:].rearrange("q c j -> q (c j)")
+                out=codes[:, first:last].bitcast(FP8X4),
+                scales=scales[:, first:last],
+                in_=tiles["grouped", key, n][:].rearrange("q c j -> q (c j)"),
             )
 
-        def product(i):
-            tile = take("wide", [P, D], BF16)
-            nc.vector.tensor_tensor(out=tile[:], in0=x_raw[i].bitcast(FP8), in1=scale[:], op=MULT)
-            tiles["wide", i] = tile
+        def widen(pair):
+            tile = take("wide", [P, 2 * D], BF16)
+            nc.scalar.copy(out=tile[:], in_=x_raw[pair].bitcast(FP8))
+            tiles["wide", pair] = tile
 
-        def turn(i):
-            bank = take("bank", [P, PASSES, 2, P], F32)
-            words = tiles["wide", i][:].bitcast(F32)
-            for g in range(PASSES):
+        def turn(pair, g):
+            bank = take(bank_of[turn, pair, g], [P, 2, 2 * P], F32)
+            words = tiles["wide", pair][:].bitcast(F32)
+            for unit in range(2):
+                first = unit * D // 2 + g * K_PASS // 2
                 for u in range(2):
                     nc.tensor.transpose(
-                        bank[:, g, u, :], words[:, 256 * g + u : 256 * (g + 1) : 2], identity[:]
+                        bank[:, u, unit * P : (unit + 1) * P],
+                        words[:, first + u : first + K_PASS // 2 : 2],
+                        identity[:],
                     )
-            tiles["turn", i] = bank
+            tiles["turn", pair, g] = bank
 
-        def x_group(i):
-            if i % 2 == 0:
-                tiles["x_grouped", i // 2] = take("x_grouped", [P, 2 * D], BF16)
-            half = tiles["x_grouped", i // 2][:, i % 2 * D : (i % 2 + 1) * D]
-            nc.scalar.copy(
-                out=half.bitcast(F32).rearrange("q (g c u) -> q g c u", g=PASSES, u=2),
-                in_=tiles["turn", i][:].rearrange("q g u c -> q g c u"),
+        def product(pair, g):
+            if g == 0:
+                tiles["x_grouped", pair] = take(f"shared{pair % 2}", [P, PASSES, 2 * P, 2, 2], BF16)
+            values = tiles["turn", pair, g][:].bitcast(BF16).rearrange("q u (c e) -> q c u e", e=2)
+            scales = scale[:, g, :].rearrange("q (o u e) -> q o u e", o=1, u=2)
+            nc.vector.tensor_tensor(
+                out=tiles["x_grouped", pair][:, g], in0=values, in1=scales.to_broadcast([P, 2 * P, 2, 2]), op=MULT
             )
 
-        def x_quantize(pair):
-            codes, scales = mx_tiles(("x", pair), 2 * PASSES * P)
+        def x_quantize(pair, first, count):
+            codes, scales = mx_tiles(("x", pair))
+            cols = slice(first * 2 * P, (first + count) * 2 * P)
+            source = tiles["x_grouped", pair][:, first : first + count]
             nc.vector.quantize_mx(
-                out=codes[:].bitcast(FP8X4), scales=scales[:], in_=tiles["x_grouped", pair][:]
+                out=codes[:, cols].bitcast(FP8X4),
+                scales=scales[:, cols],
+                in_=source.rearrange("q g c u e -> q (g c u e)"),
             )
 
-        def multiply(i, b):
-            bank = take("bank", [P, WIDTH], F32)
+        def multiply(i, b, g):
+            if g == 0:
+                tiles["multiply", i, b] = take(bank_of[multiply, i, b, g], [P, WIDTH], F32)
             x_codes, x_scales = tiles["x", i // 2]
-            for g in range(PASSES):
-                cols = slice((i % 2 * PASSES + g) * P, (i % 2 * PASSES + g + 1) * P)
-                w_codes, w_scales = tiles["w", b, g]
-                nc.tensor.matmul_mx(
-                    out=bank[:],
-                    lhsT=x_codes[:, cols].bitcast(FP8X4),
-                    lhsT_scale=x_scales[:, cols],
-                    rhs=w_codes[:].bitcast(FP8X4),
-                    rhs_scale=w_scales[:],
-                    start=(g == 0),
-                    stop=(g == PASSES - 1),
-                )
-            tiles["multiply", i, b] = bank
+            cols = slice((2 * g + i % 2) * P, (2 * g + i % 2 + 1) * P)
+            w_codes, w_scales = tiles["w", b, g]
+            nc.tensor.matmul_mx(
+                out=tiles["multiply", i, b][:],
+                lhsT=x_codes[:, cols].bitcast(FP8X4),
+                lhsT_scale=x_scales[:, cols],
+                rhs=w_codes[:].bitcast(FP8X4),
+                rhs_scale=w_scales[:],
+                start=(g == 0),
+                stop=(g == PASSES - 1),
+            )
 
         def empty(i, b):
             group, j = divmod(i, PACK)
@@ -204,7 +211,7 @@ def tile_factoranalysisemloadinggradient_kernel(
 
         def accumulate(group, d):
             if group == 0:
-                tiles["sum", d] = take("bank", [P, K], F32)
+                tiles["sum", d] = take(bank_of[accumulate, group, d], [P, K], F32)
             cols = slice(d % 4 * P, (d % 4 + 1) * P)
             e_codes, e_scales = tiles["y", group, d // 4]
             z_codes, z_scales = tiles["y", group, Z]
@@ -230,28 +237,27 @@ def tile_factoranalysisemloadinggradient_kernel(
             nc.scalar.activation(out=tile[:], in_=tile[:], func=COPY, scale=psi_inv[:, d : d + 1])
             nc.sync.dma_start(out=out[d * P : (d + 1) * P, :], in_=tile[:])
 
+        def each_piece(name, key):
+            return [(name, key, n) for n in range(len(pieces[key]))]
+
         def needs(step):
             name, args = step[0], step[1:]
-            if name is spread_copy:
-                return [(spread_turn, *args)]
-            if name is product:
-                return [(spread_copy, 0), (spread_copy, 1)]
             if name is turn:
-                return [(product, *args)]
-            if name is x_group:
+                return [(widen, args[0])]
+            if name is product:
                 return [(turn, *args)]
             if name is x_quantize:
-                return [(x_group, 2 * args[0]), (x_group, 2 * args[0] + 1)]
-            if name is interleave and args[0] == "y":
-                return [(empty, PACK * args[2] + j, args[3]) for j in range(PACK)]
+                return [(product, args[0], g) for g in range(args[1], args[1] + args[2])]
+            if name is interleave and args[0][0] == "y":
+                return [(empty, PACK * args[0][1] + j, args[0][2]) for j in range(PACK)]
             if name is quantize:
-                return [(interleave, args[0], engine_of[args], *args[1:])]
+                return [(interleave, *args)]
             if name is multiply:
-                return [(x_quantize, args[0] // 2)] + [(quantize, "w", args[1], g) for g in range(PASSES)]
+                return [QX(args[0] // 2, args[2])] + each_piece(quantize, ("w", *args[1:]))
             if name is empty:
-                return [(multiply, *args), (widen_factor, Z if args[1] == Z else 0)]
+                return [(multiply, *args, PASSES - 1), (widen_factor, Z if args[1] == Z else 0)]
             if name is accumulate:
-                return [(quantize, "y", args[0], args[1] // 4), (quantize, "y", args[0], Z)]
+                return each_piece(quantize, ("y", args[0], args[1] // 4)) + each_piece(quantize, ("y", args[0], Z))
             if name is subtract:
                 return [(accumulate, GROUPS - 1, *args)]
             if name is store:
@@ -260,72 +266,109 @@ def tile_factoranalysisemloadinggradient_kernel(
 
         def claims(step):
             name, args = step[0], step[1:]
-            if name is spread_turn:
-                return "bank", (spread_copy, *args)
             if name is turn:
-                return "bank", (x_group, *args)
-            if name is multiply:
-                return "bank", (empty, *args)
+                return bank_of[step], [(product, *args)]
+            if name is multiply and args[2] == 0:
+                return bank_of[step], [(empty, *args[:2])]
             if name is accumulate and args[0] == 0:
-                return "bank", (subtract, args[1])
-            if name is product:
-                return "wide", (turn, *args)
-            if name is x_group and args[0] % 2 == 0:
-                return "x_grouped", (x_quantize, args[0] // 2)
+                return bank_of[step], [(subtract, args[1])]
+            if name is widen:
+                return "wide", [(turn, args[0], PASSES - 1)]
+            if name is product and args[1] == 0:
+                return f"shared{args[0] % 2}", [QX(args[0], g) for g in range(PASSES)]
             if name is empty and args[0] % PACK == 0:
-                key = ("y", args[0] // PACK, args[1])
-                return "flat", (interleave, "y", engine_of[key], *key[1:])
+                return "flat", each_piece(interleave, ("y", args[0] // PACK, args[1]))
             if name is interleave:
-                return "grouped_" + args[1], (quantize, args[0], *args[2:])
+                return pieces[args[0]][args[1]][1], [(quantize, *args)]
             return None, None
 
-        engine_of = {("w", b, g): "v" for b in (0, 1, Z) for g in range(PASSES)}
-        engine_of.update({("y", g, b): "v" for b in (0, 1, Z) for g in range(GROUPS)})
-        for key in (("w", Z, 1), ("w", 0, 0), ("w", 0, 1), ("y", 3, 1)):
-            engine_of[key] = "s"
+        def I(kind, a, b, n=0):
+            return (interleave, (kind, a, b), n)
 
-        def I(*key):
-            return (interleave, key[0], engine_of[key], *key[1:])
+        def Q(kind, a, b, n=0):
+            return (quantize, (kind, a, b), n)
 
-        def Q(*key):
-            return (quantize, *key)
+        def PR(k):
+            return [(product, k, 0), (product, k, 1)]
 
-        def PR(i):
-            return (product, i)
-
-        def QX(i):
-            return (x_quantize, i)
+        def QX(k, g=0):
+            return (x_quantize, k, g, 1) if k == 0 else (x_quantize, k, 0, PASSES)
 
         def T(k):
-            return [(turn, 2 * k), (turn, 2 * k + 1)]
+            return [(turn, k, 0), (turn, k, 1)]
 
         def M(g, b, js=range(PACK)):
-            return [(multiply, PACK * g + j, b) for j in js]
+            return [(multiply, PACK * g + j, b, h) for j in js for h in range(PASSES)]
 
-        first = T(0) + T(1) + M(0, Z) + T(2) + T(3) + M(0, 0) + M(1, Z) + T(4) + M(1, 0) + T(5) + M(0, 1) + T(6) + M(2, Z) + T(7) + M(2, 0) + M(1, 1) + M(3, Z) + M(3, 0) + M(2, 1) + M(3, 1)
-        tensor = [(spread_turn, 0), (spread_turn, 1)] + first
+        def E(g, b, js=range(PACK)):
+            return [(empty, PACK * g + j, b) for j in js]
+
+        def W(k):
+            return [(widen, k)]
+
+        keys = [("w", b, g) for b in (0, 1, Z) for g in range(PASSES)]
+        keys += [("y", g, b) for b in (0, 1, Z) for g in range(GROUPS)]
+        pieces = {key: [("v", "grouped_v", 0, WIDTH)] for key in keys}
+        H = WIDTH // 2
+        pieces["w", Z, 0] = [("v", "shared2", 0, WIDTH)]
+        pieces["w", Z, 1] = [("g", "shared2", 0, H), ("s", "grouped_s", H, WIDTH)]
+        pieces["w", 0, 0] = [("s", "shared2", 0, WIDTH)]
+        pieces["w", 0, 1] = [("g", "shared0", 0, H), ("v", "grouped_v", H, WIDTH)]
+        pieces["w", 1, 0] = [("g", "shared2", 0, H), ("g", "shared0", H, WIDTH)]
+        pieces["w", 1, 1] = [("g", "shared1", 0, H), ("g", "shared0", H, WIDTH)]
+        pieces["y", 0, Z] = [("g", "shared1", 0, H), ("g", "shared0", H, WIDTH)]
+        for key in LATE:
+            pieces[key] = [("s", "shared2", 0, WIDTH)] if key == ("y", 3, 1) else [("s", "grouped_s", 0, WIDTH)]
+        gpsimd = [I("w", Z, 1, 0), I("w", 0, 1, 0), I("w", 1, 0, 0), I("w", 1, 0, 1), I("w", 1, 1, 0), I("w", 1, 1, 1), I("y", 0, Z, 0), I("y", 0, Z, 1)]
+        behind = {I("w", Z, 1, 0): [Q("w", Z, 0)], I("w", 0, 0): [Q("w", Z, 1, 0)], I("w", 1, 0, 0): [Q("w", 0, 0)], I("y", 3, 1): [Q("w", 1, 0, 0)]}
+        for n, step in enumerate(step for step in gpsimd[1:] if step[0] is interleave):
+            if n != 1:
+                behind[step] = [QX(n, 1)]
+                behind[product, n + 2, 0] = [(quantize, *step[1:])]
+        tensor = T(0) + T(1) + [(multiply, j, Z, 0) for j in range(2)] + T(2) + [(multiply, j, Z, 1) for j in range(2)] + M(0, Z, (2, 3)) + T(3) + M(0, 0)
+        for k in range(2, 6):
+            js = (0, 1) if k % 2 == 0 else (2, 3)
+            tensor += T(k + 2) + M(k // 2, Z, js) + M(k // 2, 0, js)
+        tensor += M(0, 1) + M(1, 1) + M(3, Z) + M(3, 0) + M(2, 1) + M(3, 1)
+        scalar = W(0) + W(1) + [I("w", Z, 1, 1)] + W(2) + [I("w", 0, 0)] + W(3)
+        for step in tensor:
+            if step[0] is multiply:
+                if step[1] == 0 and step[2] != 1 and step[3] == 1:
+                    scalar.append((widen_factor, step[2]))
+                if step[3] == 1:
+                    scalar.append((empty, *step[1:3]))
+            elif step[2] == 0 and 3 <= step[1] < 7:
+                scalar += W(step[1] + 1)
         for g in range(GROUPS):
             tensor.extend((accumulate, g, d) for d in range(4))
+        for g in range(2):
+            tensor.extend((accumulate, g, d) for d in range(4, BANDS))
         for d in range(4, BANDS):
-            tensor.extend((accumulate, g, d) for g in range(GROUPS))
-        scalar = [((x_group if step[0] is turn else empty), *step[1:]) for step in first]
-        scalar[4:4] = [I("w", 0, 1)]
-        scalar[2:2] = [I("w", 0, 0)]
-        scalar = [(spread_copy, 0), (spread_copy, 1), I("w", Z, 1)] + scalar
-        scalar.append(I("y", 3, 1))
+            tensor.extend((accumulate, g, d) for g in range(2, GROUPS))
+        bank_of, turns, sums = {}, 0, 0
+        for step in tensor:
+            if step[0] is turn:
+                bank_of[step] = f"bank{turns % 4}"
+                turns = turns + 1
+            elif step[-1] == 0 and step[0] is multiply or step[0] is accumulate and step[1] == 0:
+                bank_of[step] = f"bank{4 + sums % 4}" if sums < SPLIT else f"bank{(sums - SPLIT) % 8}"
+                sums = sums + 1
+        scalar += [I(*key) for key in LATE]
         scalar.extend((store, d) for d in range(BANDS))
 
-        vector = [I("w", Z, 0), PR(0), PR(1), Q("w", Z, 0), PR(2), PR(3), QX(0), Q("w", Z, 1), (widen_factor, Z), PR(4), PR(5), QX(1), PR(6), (widen_factor, 0), Q("w", 0, 0), PR(7), Q("w", 0, 1), I("w", 1, 0), PR(8), QX(2), PR(9), QX(3), I("w", 1, 1), Q("w", 1, 0), PR(10), Q("w", 1, 1), PR(11), QX(4)]
-        vector += [PR(12), PR(13), QX(5), PR(14), PR(15), I("y", 0, Z), (invert_psi,), I("y", 0, 0), Q("y", 0, Z), QX(6), I("y", 1, Z), Q("y", 0, 0), I("y", 1, 0), Q("y", 1, Z), QX(7)]
-        order = [(0, 1), (2, Z), (2, 0), (1, 1), (3, Z), (3, 0), (2, 1)]
+        vector = [I("w", Z, 0), Q("w", Z, 0), (product, 0, 0), (product, 0, 1), QX(0, 0), Q("w", Z, 1, 0), Q("w", Z, 1, 1), QX(0, 1), *PR(1), I("w", 0, 1, 1), QX(1), Q("w", 0, 1, 1), Q("w", 0, 1, 0), Q("w", 0, 0)]
+        vector += [*PR(2), Q("w", 1, 0, 0), QX(2), *PR(3), Q("w", 1, 0, 1), QX(3), *PR(4), I("y", 0, 0), Q("w", 1, 1, 0), QX(4), *PR(5), Q("y", 0, 0), Q("w", 1, 1, 1), QX(5)]
+        vector += [*PR(6), I("y", 1, Z), (invert_psi,), Q("y", 0, Z, 0), QX(6), *PR(7), Q("y", 1, Z), Q("y", 0, Z, 1), QX(7), I("y", 1, 0)]
+        order = [(2, Z), (2, 0), (3, Z), (3, 0), (0, 1), (1, 1), (2, 1)]
         last = (1, 0)
         for key in order:
-            vector += [I("y", *key), Q("y", *last)]
-            last = key
-        vector += [Q("y", 2, 1), (subtract, 0), Q("y", 3, 1)]
-        vector += [(subtract, d) for d in range(1, 8)]
+            if ("y", *key) not in LATE:
+                vector += [I("y", *key), Q("y", *last)]
+                last = key
+        vector += [(subtract, 0), Q("y", *last)] + [Q(*key) for key in LATE] + [(subtract, 1)]
+        vector += [(subtract, d) for d in range(2, 8)]
 
-        queues = [vector, scalar, tensor]
+        queues = [vector, scalar, tensor, gpsimd]
         written, readers = set(), {ring: [] for ring in RINGS}
         while any(queues):
             progress = False
@@ -333,9 +376,9 @@ def tile_factoranalysisemloadinggradient_kernel(
                 while queue:
                     step = queue[0]
                     ring, reader = claims(step)
-                    waits = needs(step)
+                    waits = needs(step) + behind.get(step, [])
                     if ring is not None and len(readers[ring]) >= RINGS[ring]:
-                        waits = waits + [readers[ring][-RINGS[ring]]]
+                        waits = waits + readers[ring][-RINGS[ring]]
                     if not all(wait in written for wait in waits):
                         break
                     step[0](*step[1:])
@@ -344,4 +387,4 @@ def tile_factoranalysisemloadinggradient_kernel(
                         readers[ring].append(reader)
                     queue.remove(step)
                     progress = True
-            assert progress
+            assert progress, [(queue[0][0], queue[0][1:]) for queue in queues if queue]

@@ -29,9 +29,14 @@ Z = 2
 BANDS = D // P
 BANKS = 8
 SPLIT = 28
-LATE = [("y", 3, 1)]
+PREPARED = (7,)
+GM = 0
+GA = 2
+VDIV = (1,)
+WARM = ()
+LATE = "s"
 RUN = 4
-RINGS = {"wide": 4, "flat": 10, "grouped_v": 3, "grouped_s": 1, "shared0": 1, "shared1": 1, "shared2": 1, **{f"bank{n}": 1 for n in range(BANKS)}}
+RINGS = {"wide": 4, "flat": 10, "grouped_v": 3, "grouped_s": 2, "shared0": 1, "shared1": 1, "shared2": 1, "shared3": 1, **{f"bank{n}": 1 for n in range(BANKS)}}
 
 
 def tile_factoranalysisemloadinggradient_kernel(
@@ -43,6 +48,9 @@ def tile_factoranalysisemloadinggradient_kernel(
         psum = ctx.enter_context(tc.psum_pool(name="psum", bufs=1))
         ctx.enter_context(tc.manual_schedule())
 
+        if WARM:
+            zeros = keep.tile([P, 2 * P], F32, name="zeros")
+            nc.vector.memset(zeros[:], 0.0)
         identity = keep.tile([P, P], F32, name="identity")
         make_identity(nc, identity[:])
 
@@ -80,12 +88,12 @@ def tile_factoranalysisemloadinggradient_kernel(
         load_beta(1)
         load_x(4, 2)
         load_p(0, 0)
-        load_p(0, 1)
         load_x(6, 2)
+        load_p(0, 1)
         nc.sync.dma_start(out=t16[:], in_=t.rearrange("(g q j) -> q g j", q=P, j=PACK))
-        nc.sync.dma_start(out=r16[:], in_=r.rearrange("(g q j) -> q g j", q=P, j=PACK))
         load_p(1, 0)
         load_x(8, 4)
+        nc.sync.dma_start(out=r16[:], in_=r.rearrange("(g q j) -> q g j", q=P, j=PACK))
         load_p(1, 1)
         load_x(12, 4)
         nc.sync.dma_start(out=v_raw[:], in_=v.rearrange("(b q) k -> q b k", q=P))
@@ -95,6 +103,7 @@ def tile_factoranalysisemloadinggradient_kernel(
         factor = {b: keep.tile([P, UNITS], F32, name=f"factor{b}") for b in (0, Z)}
         factor[1] = factor[0]
         psi_inv = keep.tile([P, BANDS], F32, name="psi_inv")
+        psi_inv_mean = keep.tile([P, BANDS], F32, name="psi_inv_mean")
         tiles, taken = {}, {ring: 0 for ring in RINGS}
 
         def take(ring, shape, dtype):
@@ -118,6 +127,9 @@ def tile_factoranalysisemloadinggradient_kernel(
 
         def invert_psi():
             nc.vector.reciprocal(out=psi_inv[:], in_=psi16[:, :, 0])
+
+        def mean_psi():
+            nc.vector.tensor_scalar(out=psi_inv_mean[:], in0=psi_inv[:], scalar1=1.0 / N, scalar2=None, op0=MULT)
 
         def interleave(key, n):
             kind, a, b = key
@@ -225,17 +237,35 @@ def tile_factoranalysisemloadinggradient_kernel(
                 stop=(group == GROUPS - 1),
             )
 
+        def prepare(d):
+            tile = keep.tile([P, K], F32, name=f"v_over_psi{d}")
+            nc.scalar.activation(out=tile[:], in_=v_raw[:, d, :], func=COPY, scale=psi_inv[:, d : d + 1])
+            tiles["prepared", d] = tile
+
         def subtract(d):
             tile = keep.tile([P, K], F32, name=f"result{d}")
+            if d in PREPARED:
+                mean, other = psi_inv_mean[:, d : d + 1], tiles["prepared", d][:]
+            else:
+                mean, other = 1.0 / N, v_raw[:, d, :]
             nc.vector.scalar_tensor_tensor(
-                out=tile[:], in0=tiles["sum", d][:], scalar=1.0 / N, in1=v_raw[:, d, :], op0=MULT, op1=SUBTRACT
+                out=tile[:], in0=tiles["sum", d][:], scalar=mean, in1=other, op0=MULT, op1=SUBTRACT
             )
             tiles["result", d] = tile
 
-        def store(d):
+        def divide(d):
             tile = tiles["result", d]
-            nc.scalar.activation(out=tile[:], in_=tile[:], func=COPY, scale=psi_inv[:, d : d + 1])
-            nc.sync.dma_start(out=out[d * P : (d + 1) * P, :], in_=tile[:])
+            if d in VDIV:
+                nc.vector.tensor_scalar(out=tile[:], in0=tile[:], scalar1=psi_inv[:, d : d + 1], scalar2=None, op0=MULT)
+            else:
+                nc.scalar.activation(out=tile[:], in_=tile[:], func=COPY, scale=psi_inv[:, d : d + 1])
+
+        def store(d):
+            nc.sync.dma_start(out=out[d * P : (d + 1) * P, :], in_=tiles["result", d][:])
+
+        def warm(n):
+            bank = psum.tile([P, 2 * P], F32, name="bank7_0")
+            nc.tensor.matmul(bank[:], lhsT=zeros[:, :P], rhs=zeros[:], start=True, stop=True)
 
         def each_piece(name, key):
             return [(name, key, n) for n in range(len(pieces[key]))]
@@ -257,11 +287,18 @@ def tile_factoranalysisemloadinggradient_kernel(
             if name is empty:
                 return [(multiply, *args, PASSES - 1), (widen_factor, Z if args[1] == Z else 0)]
             if name is accumulate:
-                return each_piece(quantize, ("y", args[0], args[1] // 4)) + each_piece(quantize, ("y", args[0], Z))
+                key = ("y", args[0], args[1] // 4)
+                mine = [step for step in each_piece(quantize, key) if pieces[key][step[2]][3] > args[1] % 4 * P]
+                return mine[:1] + each_piece(quantize, ("y", args[0], Z))
             if name is subtract:
-                return [(accumulate, GROUPS - 1, *args)]
-            if name is store:
+                prepared = [(prepare, *args), (mean_psi,)] if args[0] in PREPARED else []
+                return [(accumulate, GROUPS - 1, *args)] + prepared
+            if name is prepare or name is mean_psi:
+                return [(invert_psi,)]
+            if name is divide:
                 return [(subtract, *args), (invert_psi,)]
+            if name is store:
+                return [(subtract if args[0] in PREPARED else divide, *args)]
             return []
 
         def claims(step):
@@ -310,41 +347,48 @@ def tile_factoranalysisemloadinggradient_kernel(
         keys += [("y", g, b) for b in (0, 1, Z) for g in range(GROUPS)]
         pieces = {key: [("v", "grouped_v", 0, WIDTH)] for key in keys}
         H = WIDTH // 2
-        pieces["w", Z, 0] = [("v", "shared2", 0, WIDTH)]
+        pieces["w", Z, 0] = [("v", "grouped_v", 0, H), ("s", "shared2", H, WIDTH)]
         pieces["w", Z, 1] = [("g", "shared2", 0, H), ("s", "grouped_s", H, WIDTH)]
-        pieces["w", 0, 0] = [("s", "shared2", 0, WIDTH)]
-        pieces["w", 0, 1] = [("g", "shared0", 0, H), ("v", "grouped_v", H, WIDTH)]
-        pieces["w", 1, 0] = [("g", "shared2", 0, H), ("g", "shared0", H, WIDTH)]
+        pieces["w", 0, 0] = [("s", "shared3", 0, H), ("g", "shared0", H, WIDTH)]
+        pieces["w", 0, 1] = [("v", "grouped_v", 0, H), ("s", "grouped_s", H, WIDTH)]
+        pieces["y", 0, 0] = [("v", "grouped_v", 0, H), ("v", "grouped_v", H, WIDTH)]
+        pieces["w", 1, 0] = [("g", "shared3", 0, H), ("g", "shared3", H, WIDTH)]
         pieces["w", 1, 1] = [("g", "shared1", 0, H), ("g", "shared0", H, WIDTH)]
         pieces["y", 0, Z] = [("g", "shared1", 0, H), ("g", "shared0", H, WIDTH)]
-        for key in LATE:
-            pieces[key] = [("s", "shared2", 0, WIDTH)] if key == ("y", 3, 1) else [("s", "grouped_s", 0, WIDTH)]
-        gpsimd = [I("w", Z, 1, 0), I("w", 0, 1, 0), I("w", 1, 0, 0), I("w", 1, 0, 1), I("w", 1, 1, 0), I("w", 1, 1, 1), I("y", 0, Z, 0), I("y", 0, Z, 1)]
-        behind = {I("w", Z, 1, 0): [Q("w", Z, 0)], I("w", 0, 0): [Q("w", Z, 1, 0)], I("w", 1, 0, 0): [Q("w", 0, 0)], I("y", 3, 1): [Q("w", 1, 0, 0)]}
-        for n, step in enumerate(step for step in gpsimd[1:] if step[0] is interleave):
-            if n != 1:
+        pieces["y", 2, 1] = [("s", "grouped_s", 0, H), (LATE, "grouped_" + LATE, H, WIDTH)]
+        pieces["y", 3, 1] = [("s", "shared2", 0, H), ("s", "grouped_s", H, WIDTH)]
+        gpsimd = [I("w", Z, 1, 0), I("w", 0, 0, 1), I("w", 1, 0, 0), I("w", 1, 0, 1), I("w", 1, 1, 0), I("w", 1, 1, 1), I("y", 0, Z, 0), I("y", 0, Z, 1)]
+        behind = {I("w", Z, 1, 0): [Q("w", Z, 0, 1)], I("w", 1, 0, 0): [Q("w", 0, 0)], I("y", 3, 1, 0): [Q("w", Z, 1, 0)]}
+        for n, step in enumerate(gpsimd[1:]):
+            if n not in (1, 2):
                 behind[step] = [QX(n, 1)]
                 behind[product, n + 2, 0] = [(quantize, *step[1:])]
-        tensor = T(0) + T(1) + [(multiply, j, Z, 0) for j in range(2)] + T(2) + [(multiply, j, Z, 1) for j in range(2)] + M(0, Z, (2, 3)) + T(3) + M(0, 0)
+        tensor = T(0) + T(1) + [(multiply, j, Z, 0) for j in range(2)] + T(2) + [(multiply, j, Z, 1) for j in range(2)] + T(3) + M(0, Z, (2, 3)) + M(0, 0)
         for k in range(2, 6):
             js = (0, 1) if k % 2 == 0 else (2, 3)
             tensor += T(k + 2) + M(k // 2, Z, js) + M(k // 2, 0, js)
         tensor += M(0, 1) + M(1, 1) + M(3, Z) + M(3, 0) + M(2, 1) + M(3, 1)
-        scalar = W(0) + W(1) + [I("w", Z, 1, 1)] + W(2) + [I("w", 0, 0)] + W(3)
+        scalar = W(0) + [I("w", Z, 0, 1)] + W(1) + [I("w", Z, 1, 1)] + W(2) + [I("w", 0, 0, 0)] + W(3) + [I("w", 0, 1, 1)]
         for step in tensor:
             if step[0] is multiply:
                 if step[1] == 0 and step[2] != 1 and step[3] == 1:
                     scalar.append((widen_factor, step[2]))
                 if step[3] == 1:
                     scalar.append((empty, *step[1:3]))
-            elif step[2] == 0 and 3 <= step[1] < 7:
+                if step[1:] == (3, Z, 1):
+                    scalar += W(4)
+            elif step[2] == 0 and 4 <= step[1] < 7:
                 scalar += W(step[1] + 1)
-        for g in range(GROUPS):
+            elif step[1:] == (7, 0):
+                scalar += [(prepare, d) for d in PREPARED]
+        for g in range(GA):
             tensor.extend((accumulate, g, d) for d in range(4))
-        for g in range(2):
+        for d in range(4):
+            tensor.extend((accumulate, g, d) for g in range(GA, GROUPS))
+        for g in range(GM):
             tensor.extend((accumulate, g, d) for d in range(4, BANDS))
         for d in range(4, BANDS):
-            tensor.extend((accumulate, g, d) for g in range(2, GROUPS))
+            tensor.extend((accumulate, g, d) for g in range(GM, GROUPS))
         bank_of, turns, sums = {}, 0, 0
         for step in tensor:
             if step[0] is turn:
@@ -353,22 +397,23 @@ def tile_factoranalysisemloadinggradient_kernel(
             elif step[-1] == 0 and step[0] is multiply or step[0] is accumulate and step[1] == 0:
                 bank_of[step] = f"bank{4 + sums % 4}" if sums < SPLIT else f"bank{(sums - SPLIT) % 8}"
                 sums = sums + 1
-        scalar += [I(*key) for key in LATE]
-        scalar.extend((store, d) for d in range(BANDS))
+        for n, place in enumerate(reversed(WARM)):
+            tensor.insert(place, (warm, n))
+        scalar += [I("y", 2, 1, 0), I("y", 3, 1, 0), (divide, 0)] + [I("y", 2, 1, 1)] * (LATE == "s") + [I("y", 3, 1, 1)]
+        scalar.extend((divide, d) for d in range(1, BANDS) if d not in PREPARED and d not in VDIV)
 
-        vector = [I("w", Z, 0), Q("w", Z, 0), (product, 0, 0), (product, 0, 1), QX(0, 0), Q("w", Z, 1, 0), Q("w", Z, 1, 1), QX(0, 1), *PR(1), I("w", 0, 1, 1), QX(1), Q("w", 0, 1, 1), Q("w", 0, 1, 0), Q("w", 0, 0)]
-        vector += [*PR(2), Q("w", 1, 0, 0), QX(2), *PR(3), Q("w", 1, 0, 1), QX(3), *PR(4), I("y", 0, 0), Q("w", 1, 1, 0), QX(4), *PR(5), Q("y", 0, 0), Q("w", 1, 1, 1), QX(5)]
-        vector += [*PR(6), I("y", 1, Z), (invert_psi,), Q("y", 0, Z, 0), QX(6), *PR(7), Q("y", 1, Z), Q("y", 0, Z, 1), QX(7), I("y", 1, 0)]
-        order = [(2, Z), (2, 0), (3, Z), (3, 0), (0, 1), (1, 1), (2, 1)]
+        vector = [I("w", Z, 0), Q("w", Z, 0), Q("w", Z, 0, 1), (product, 0, 0), (product, 0, 1), QX(0, 0), Q("w", Z, 1, 0), Q("w", Z, 1, 1), QX(0, 1), *PR(1), I("w", 0, 1, 0), QX(1), Q("w", 0, 1, 0), Q("w", 0, 0, 1), Q("w", 0, 1, 1), Q("w", 0, 0, 0)]
+        vector += [*PR(2), QX(2), Q("w", 1, 0, 0), *PR(3), I("y", 0, 0, 0), Q("w", 1, 0, 1), QX(3), *PR(4), I("y", 0, 0, 1), Q("y", 0, 0, 0), Q("w", 1, 1, 0), (invert_psi,), QX(4), *PR(5), Q("y", 0, 0, 1), Q("w", 1, 1, 1), (mean_psi,), QX(5)]
+        vector += [*PR(6), I("y", 1, Z), Q("y", 0, Z, 0), QX(6), *PR(7), Q("y", 1, Z), Q("y", 0, Z, 1), QX(7), I("y", 1, 0)]
+        order = [(2, Z), (2, 0), (3, Z), (3, 0), (0, 1), (1, 1)]
         last = (1, 0)
         for key in order:
-            if ("y", *key) not in LATE:
-                vector += [I("y", *key), Q("y", *last)]
-                last = key
-        vector += [(subtract, 0), Q("y", *last)] + [Q(*key) for key in LATE] + [(subtract, 1)]
-        vector += [(subtract, d) for d in range(2, 8)]
+            vector += [I("y", *key), Q("y", *last)]
+            last = key
+        vector += [(subtract, 0), Q("y", 1, 1), Q("y", 2, 1, 0), Q("y", 3, 1, 0), (subtract, 1)] + [I("y", 2, 1, 1)] * (LATE == "v") + [(subtract, 2)] + [(divide, 1)] * (1 in VDIV) + [Q("y", 2, 1, 1)] + [(divide, 2)] * (2 in VDIV) + [(subtract, 3), Q("y", 3, 1, 1)] + [(divide, 3)] * (3 in VDIV)
+        vector += [(subtract, d) for d in range(4, 8)]
 
-        queues = [vector, scalar, tensor, gpsimd]
+        queues = [vector, scalar, tensor, gpsimd, [(store, d) for d in range(BANDS)]]
         written, readers = set(), {ring: [] for ring in RINGS}
         while any(queues):
             progress = False

@@ -28,15 +28,21 @@ WIDTH = 512
 Z = 2
 BANDS = D // P
 BANKS = 8
-SPLIT = 28
+SPLIT = 32
 PREPARED = (7,)
 GM = 0
-GA = 2
-VDIV = (1,)
+GA = 1
+VPREP = ()
+ORDER = [(2, Z), (2, 0), (3, Z), (3, 0), (0, 1), (1, 1)]
+VEXIT = ()
+VAT = 2
+FILL = (3, 4)
+GC = 304
+VDIV = (0, 1)
 WARM = ()
 LATE = "s"
 RUN = 4
-RINGS = {"wide": 4, "flat": 10, "grouped_v": 3, "grouped_s": 2, "shared0": 1, "shared1": 1, "shared2": 1, "shared3": 1, **{f"bank{n}": 1 for n in range(BANKS)}}
+RINGS = {"wide": 4, "flat": 10, "grouped_v": 3, "grouped_s": 2, "shared0": 1, "shared1": 1, "shared2": 1, "shared3": 1, "shared4": 1, **{f"bank{n}": 1 for n in range(BANKS)}}
 
 
 def tile_factoranalysisemloadinggradient_kernel(
@@ -92,8 +98,8 @@ def tile_factoranalysisemloadinggradient_kernel(
         load_p(0, 1)
         nc.sync.dma_start(out=t16[:], in_=t.rearrange("(g q j) -> q g j", q=P, j=PACK))
         load_p(1, 0)
-        load_x(8, 4)
         nc.sync.dma_start(out=r16[:], in_=r.rearrange("(g q j) -> q g j", q=P, j=PACK))
+        load_x(8, 4)
         load_p(1, 1)
         load_x(12, 4)
         nc.sync.dma_start(out=v_raw[:], in_=v.rearrange("(b q) k -> q b k", q=P))
@@ -135,26 +141,32 @@ def tile_factoranalysisemloadinggradient_kernel(
             kind, a, b = key
             engine, ring, first, last = pieces[key][n]
             source = (w_raw[a, b] if kind == "w" else tiles["flat", a, b][:])[:, :, first:last]
-            tile = take(ring, [P, last - first, PACK], BF16)
+            if key in joint:
+                if n == 0:
+                    tiles["joint", key] = take(ring, [P, WIDTH, PACK], BF16)
+                tile = tiles["joint", key][:, first:last, :]
+            else:
+                tile = take(ring, [P, last - first, PACK], BF16)[:]
             if engine == "g":
                 nc.gpsimd.tensor_scalar(
-                    out=tile[:], in0=source.rearrange("q j c -> q c j"), scalar1=1.0, scalar2=0.0, op0=MULT, op1=ADD
+                    out=tile, in0=source.rearrange("q j c -> q c j"), scalar1=1.0, scalar2=0.0, op0=MULT, op1=ADD
                 )
             else:
                 copy = nc.vector.tensor_copy if engine == "v" else nc.scalar.copy
                 copy(
-                    out=tile[:].rearrange("q (c i) j -> q c j i", i=RUN),
+                    out=tile.rearrange("q (c i) j -> q c j i", i=RUN),
                     in_=source.rearrange("q j (c i) -> q c j i", i=RUN),
                 )
             tiles["grouped", key, n] = tile
 
         def quantize(key, n):
             codes, scales = mx_tiles(key)
-            first, last = pieces[key][n][2:]
+            first, last = (0, WIDTH) if key in joint else pieces[key][n][2:]
+            source = tiles["joint", key][:] if key in joint else tiles["grouped", key, n]
             nc.vector.quantize_mx(
                 out=codes[:, first:last].bitcast(FP8X4),
                 scales=scales[:, first:last],
-                in_=tiles["grouped", key, n][:].rearrange("q c j -> q (c j)"),
+                in_=source.rearrange("q c j -> q (c j)"),
             )
 
         def widen(pair):
@@ -214,12 +226,11 @@ def tile_factoranalysisemloadinggradient_kernel(
             group, j = divmod(i, PACK)
             if j == 0:
                 tiles["flat", group, b] = take("flat", [P, PACK, WIDTH], BF16)
-            nc.scalar.activation(
-                out=tiles["flat", group, b][:, j, :],
-                in_=tiles["multiply", i, b][:],
-                func=COPY,
-                scale=factor[b][:, i : i + 1],
-            )
+            row, bank, gain = tiles["flat", group, b][:, j, :], tiles["multiply", i, b][:], factor[b][:, i : i + 1]
+            if (i, b) in VEXIT:
+                nc.vector.tensor_scalar(out=row, in0=bank, scalar1=gain, scalar2=None, op0=MULT)
+            else:
+                nc.scalar.activation(out=row, in_=bank, func=COPY, scale=gain)
 
         def accumulate(group, d):
             if group == 0:
@@ -239,7 +250,10 @@ def tile_factoranalysisemloadinggradient_kernel(
 
         def prepare(d):
             tile = keep.tile([P, K], F32, name=f"v_over_psi{d}")
-            nc.scalar.activation(out=tile[:], in_=v_raw[:, d, :], func=COPY, scale=psi_inv[:, d : d + 1])
+            if d in VPREP:
+                nc.vector.tensor_scalar(out=tile[:], in0=v_raw[:, d, :], scalar1=psi_inv[:, d : d + 1], scalar2=None, op0=MULT)
+            else:
+                nc.scalar.activation(out=tile[:], in_=v_raw[:, d, :], func=COPY, scale=psi_inv[:, d : d + 1])
             tiles["prepared", d] = tile
 
         def subtract(d):
@@ -268,7 +282,8 @@ def tile_factoranalysisemloadinggradient_kernel(
             nc.tensor.matmul(bank[:], lhsT=zeros[:, :P], rhs=zeros[:], start=True, stop=True)
 
         def each_piece(name, key):
-            return [(name, key, n) for n in range(len(pieces[key]))]
+            count = 1 if name is quantize and key in joint else len(pieces[key])
+            return [(name, key, n) for n in range(count)]
 
         def needs(step):
             name, args = step[0], step[1:]
@@ -278,17 +293,20 @@ def tile_factoranalysisemloadinggradient_kernel(
                 return [(turn, *args)]
             if name is x_quantize:
                 return [(product, args[0], g) for g in range(args[1], args[1] + args[2])]
-            if name is interleave and args[0][0] == "y":
-                return [(empty, PACK * args[0][1] + j, args[0][2]) for j in range(PACK)]
+            if name is interleave and args[0][0] == "w":
+                return [(interleave, args[0], 0)] if args[0] in joint and args[1] > 0 else []
+            if name is interleave:
+                return ([(interleave, args[0], 0)] if args[0] in joint and args[1] > 0 else []) + [(empty, PACK * args[0][1] + j, args[0][2]) for j in range(PACK)]
             if name is quantize:
-                return [(interleave, *args)]
+                return each_piece(interleave, args[0]) if args[0] in joint else [(interleave, *args)]
             if name is multiply:
                 return [QX(args[0] // 2, args[2])] + each_piece(quantize, ("w", *args[1:]))
             if name is empty:
-                return [(multiply, *args, PASSES - 1), (widen_factor, Z if args[1] == Z else 0)]
+                first = [(empty, args[0] // PACK * PACK, args[1])] if args[0] % PACK else []
+                return first + [(multiply, *args, PASSES - 1), (widen_factor, Z if args[1] == Z else 0)]
             if name is accumulate:
                 key = ("y", args[0], args[1] // 4)
-                mine = [step for step in each_piece(quantize, key) if pieces[key][step[2]][3] > args[1] % 4 * P]
+                mine = [step for step in each_piece(quantize, key) if key in joint or pieces[key][step[2]][3] > args[1] % 4 * P]
                 return mine[:1] + each_piece(quantize, ("y", args[0], Z))
             if name is subtract:
                 prepared = [(prepare, *args), (mean_psi,)] if args[0] in PREPARED else []
@@ -315,7 +333,7 @@ def tile_factoranalysisemloadinggradient_kernel(
                 return f"shared{args[0] % 2}", [QX(args[0], g) for g in range(PASSES)]
             if name is empty and args[0] % PACK == 0:
                 return "flat", each_piece(interleave, ("y", args[0] // PACK, args[1]))
-            if name is interleave:
+            if name is interleave and not (args[0] in joint and args[1] > 0):
                 return pieces[args[0]][args[1]][1], [(quantize, *args)]
             return None, None
 
@@ -347,48 +365,45 @@ def tile_factoranalysisemloadinggradient_kernel(
         keys += [("y", g, b) for b in (0, 1, Z) for g in range(GROUPS)]
         pieces = {key: [("v", "grouped_v", 0, WIDTH)] for key in keys}
         H = WIDTH // 2
+        joint = [("w", 1, 0), ("w", 1, 1), ("y", 0, Z), ("y", 0, 0), ("y", 1, Z), ("y", 1, 0)]
+        for key in joint:
+            pieces[key] = [("g", "shared3", 0, GC), ("v", "shared3", GC, WIDTH)]
         pieces["w", Z, 0] = [("v", "grouped_v", 0, H), ("s", "shared2", H, WIDTH)]
         pieces["w", Z, 1] = [("g", "shared2", 0, H), ("s", "grouped_s", H, WIDTH)]
         pieces["w", 0, 0] = [("s", "shared3", 0, H), ("g", "shared0", H, WIDTH)]
         pieces["w", 0, 1] = [("v", "grouped_v", 0, H), ("s", "grouped_s", H, WIDTH)]
-        pieces["y", 0, 0] = [("v", "grouped_v", 0, H), ("v", "grouped_v", H, WIDTH)]
-        pieces["w", 1, 0] = [("g", "shared3", 0, H), ("g", "shared3", H, WIDTH)]
-        pieces["w", 1, 1] = [("g", "shared1", 0, H), ("g", "shared0", H, WIDTH)]
-        pieces["y", 0, Z] = [("g", "shared1", 0, H), ("g", "shared0", H, WIDTH)]
         pieces["y", 2, 1] = [("s", "grouped_s", 0, H), (LATE, "grouped_" + LATE, H, WIDTH)]
         pieces["y", 3, 1] = [("s", "shared2", 0, H), ("s", "grouped_s", H, WIDTH)]
-        gpsimd = [I("w", Z, 1, 0), I("w", 0, 0, 1), I("w", 1, 0, 0), I("w", 1, 0, 1), I("w", 1, 1, 0), I("w", 1, 1, 1), I("y", 0, Z, 0), I("y", 0, Z, 1)]
-        behind = {I("w", Z, 1, 0): [Q("w", Z, 0, 1)], I("w", 1, 0, 0): [Q("w", 0, 0)], I("y", 3, 1, 0): [Q("w", Z, 1, 0)]}
-        for n, step in enumerate(gpsimd[1:]):
-            if n not in (1, 2):
-                behind[step] = [QX(n, 1)]
-                behind[product, n + 2, 0] = [(quantize, *step[1:])]
+        gpsimd = [I("w", Z, 1, 0), I("w", 0, 0, 1)] + [I(*key) for key in joint]
+        behind = {I("w", Z, 1, 0): [Q("w", Z, 0, 1)], I("w", 0, 0, 1): [QX(0, 1)], (product, 2, 0): [Q("w", 0, 0, 1)], I("w", 1, 0, 0): [Q("w", 0, 0, 0)], I("y", 3, 1, 0): [Q("w", Z, 1, 0)]}
         tensor = T(0) + T(1) + [(multiply, j, Z, 0) for j in range(2)] + T(2) + [(multiply, j, Z, 1) for j in range(2)] + T(3) + M(0, Z, (2, 3)) + M(0, 0)
         for k in range(2, 6):
             js = (0, 1) if k % 2 == 0 else (2, 3)
             tensor += T(k + 2) + M(k // 2, Z, js) + M(k // 2, 0, js)
-        tensor += M(0, 1) + M(1, 1) + M(3, Z) + M(3, 0) + M(2, 1) + M(3, 1)
+            if k in FILL:
+                tensor += M(0, 1, (0, 1) if k == FILL[0] else (2, 3))
+        tensor += M(0, 1) * (not FILL) + M(1, 1) + M(3, Z) + M(3, 0) + M(2, 1) + M(3, 1)
         scalar = W(0) + [I("w", Z, 0, 1)] + W(1) + [I("w", Z, 1, 1)] + W(2) + [I("w", 0, 0, 0)] + W(3) + [I("w", 0, 1, 1)]
         for step in tensor:
             if step[0] is multiply:
-                if step[1] == 0 and step[2] != 1 and step[3] == 1:
-                    scalar.append((widen_factor, step[2]))
-                if step[3] == 1:
+                if step[1:] == (0, Z, 1):
+                    scalar.append((widen_factor, Z))
+                if step[1:] == (2, Z, 1):
+                    scalar.append((widen_factor, 0))
+                if step[3] == 1 and step[1:3] not in VEXIT:
                     scalar.append((empty, *step[1:3]))
                 if step[1:] == (3, Z, 1):
                     scalar += W(4)
             elif step[2] == 0 and 4 <= step[1] < 7:
                 scalar += W(step[1] + 1)
             elif step[1:] == (7, 0):
-                scalar += [(prepare, d) for d in PREPARED]
+                scalar += [(prepare, d) for d in PREPARED if d not in VPREP]
         for g in range(GA):
             tensor.extend((accumulate, g, d) for d in range(4))
         for d in range(4):
             tensor.extend((accumulate, g, d) for g in range(GA, GROUPS))
-        for g in range(GM):
-            tensor.extend((accumulate, g, d) for d in range(4, BANDS))
         for d in range(4, BANDS):
-            tensor.extend((accumulate, g, d) for g in range(GM, GROUPS))
+            tensor.extend((accumulate, g, d) for g in range(GROUPS))
         bank_of, turns, sums = {}, 0, 0
         for step in tensor:
             if step[0] is turn:
@@ -399,18 +414,19 @@ def tile_factoranalysisemloadinggradient_kernel(
                 sums = sums + 1
         for n, place in enumerate(reversed(WARM)):
             tensor.insert(place, (warm, n))
-        scalar += [I("y", 2, 1, 0), I("y", 3, 1, 0), (divide, 0)] + [I("y", 2, 1, 1)] * (LATE == "s") + [I("y", 3, 1, 1)]
-        scalar.extend((divide, d) for d in range(1, BANDS) if d not in PREPARED and d not in VDIV)
+        scalar += [I("y", 2, 1, 0), I("y", 3, 1, 0), I("y", 2, 1, 1), I("y", 3, 1, 1)]
+        scalar.extend((divide, d) for d in range(BANDS) if d not in PREPARED and d not in VDIV)
 
-        vector = [I("w", Z, 0), Q("w", Z, 0), Q("w", Z, 0, 1), (product, 0, 0), (product, 0, 1), QX(0, 0), Q("w", Z, 1, 0), Q("w", Z, 1, 1), QX(0, 1), *PR(1), I("w", 0, 1, 0), QX(1), Q("w", 0, 1, 0), Q("w", 0, 0, 1), Q("w", 0, 1, 1), Q("w", 0, 0, 0)]
-        vector += [*PR(2), QX(2), Q("w", 1, 0, 0), *PR(3), I("y", 0, 0, 0), Q("w", 1, 0, 1), QX(3), *PR(4), I("y", 0, 0, 1), Q("y", 0, 0, 0), Q("w", 1, 1, 0), (invert_psi,), QX(4), *PR(5), Q("y", 0, 0, 1), Q("w", 1, 1, 1), (mean_psi,), QX(5)]
-        vector += [*PR(6), I("y", 1, Z), Q("y", 0, Z, 0), QX(6), *PR(7), Q("y", 1, Z), Q("y", 0, Z, 1), QX(7), I("y", 1, 0)]
-        order = [(2, Z), (2, 0), (3, Z), (3, 0), (0, 1), (1, 1)]
-        last = (1, 0)
-        for key in order:
+        vector = [I("w", Z, 0), Q("w", Z, 0), Q("w", Z, 0, 1), *PR(0), QX(0, 0), Q("w", Z, 1, 0), Q("w", Z, 1, 1), QX(0, 1), *PR(1), I("w", 0, 1, 0), QX(1), Q("w", 0, 1, 0), Q("w", 0, 0, 1), Q("w", 0, 1, 1), Q("w", 0, 0, 0)]
+        for k in range(2, 8):
+            vector += [*PR(k), I(*joint[k - 2], 1)] + [(invert_psi,)] * (k == 4) + [(mean_psi,)] * (k == 5) + [QX(k), Q(*joint[k - 2])]
+        order = ORDER
+        vector += [I("y", *order[0])]
+        for last, key in zip(order, order[1:]):
+            if key == order[VAT]:
+                vector += [(empty, *unit) for unit in VEXIT] + [(prepare, d) for d in VPREP]
             vector += [I("y", *key), Q("y", *last)]
-            last = key
-        vector += [(subtract, 0), Q("y", 1, 1), Q("y", 2, 1, 0), Q("y", 3, 1, 0), (subtract, 1)] + [I("y", 2, 1, 1)] * (LATE == "v") + [(subtract, 2)] + [(divide, 1)] * (1 in VDIV) + [Q("y", 2, 1, 1)] + [(divide, 2)] * (2 in VDIV) + [(subtract, 3), Q("y", 3, 1, 1)] + [(divide, 3)] * (3 in VDIV)
+        vector += [(subtract, 0), Q("y", 1, 1), Q("y", 2, 1, 0), (divide, 0), Q("y", 3, 1, 0), (subtract, 1), (subtract, 2)] + [(divide, 1)] * (1 in VDIV) + [Q("y", 2, 1, 1), (subtract, 3)] + [(divide, 2)] * (2 in VDIV) + [Q("y", 3, 1, 1)]
         vector += [(subtract, d) for d in range(4, 8)]
 
         queues = [vector, scalar, tensor, gpsimd, [(store, d) for d in range(BANDS)]]

@@ -37,11 +37,11 @@ ORDER = [(2, Z), (2, 0), (3, Z), (3, 0), (0, 1), (1, 1)]
 VEXIT = ()
 VAT = 2
 FILL = (3, 4)
-GC = 304
+GC = 288
 VDIV = (0, 1)
 WARM = ()
 LATE = "s"
-RUN = 4
+RUN = 8
 RINGS = {"wide": 4, "flat": 10, "grouped_v": 3, "grouped_s": 2, "shared0": 1, "shared1": 1, "shared2": 1, "shared3": 1, "shared4": 1, **{f"bank{n}": 1 for n in range(BANKS)}}
 
 
@@ -96,10 +96,11 @@ def tile_factoranalysisemloadinggradient_kernel(
         load_p(0, 0)
         load_x(6, 2)
         load_p(0, 1)
+        load_x(8, 2)
         nc.sync.dma_start(out=t16[:], in_=t.rearrange("(g q j) -> q g j", q=P, j=PACK))
         load_p(1, 0)
         nc.sync.dma_start(out=r16[:], in_=r.rearrange("(g q j) -> q g j", q=P, j=PACK))
-        load_x(8, 4)
+        load_x(10, 2)
         load_p(1, 1)
         load_x(12, 4)
         nc.sync.dma_start(out=v_raw[:], in_=v.rearrange("(b q) k -> q b k", q=P))
@@ -383,7 +384,7 @@ def tile_factoranalysisemloadinggradient_kernel(
             if k in FILL:
                 tensor += M(0, 1, (0, 1) if k == FILL[0] else (2, 3))
         tensor += M(0, 1) * (not FILL) + M(1, 1) + M(3, Z) + M(3, 0) + M(2, 1) + M(3, 1)
-        scalar = W(0) + [I("w", Z, 0, 1)] + W(1) + [I("w", Z, 1, 1)] + W(2) + [I("w", 0, 0, 0)] + W(3) + [I("w", 0, 1, 1)]
+        scalar = W(0) + [I("w", Z, 0, 1)] + W(1) + [I("w", Z, 1, 1)] + W(2) + [I("w", 0, 0, 0)] + W(3) + [I("w", 0, 1, 1)] + W(4)
         for step in tensor:
             if step[0] is multiply:
                 if step[1:] == (0, Z, 1):
@@ -392,8 +393,6 @@ def tile_factoranalysisemloadinggradient_kernel(
                     scalar.append((widen_factor, 0))
                 if step[3] == 1 and step[1:3] not in VEXIT:
                     scalar.append((empty, *step[1:3]))
-                if step[1:] == (3, Z, 1):
-                    scalar += W(4)
             elif step[2] == 0 and 4 <= step[1] < 7:
                 scalar += W(step[1] + 1)
             elif step[1:] == (7, 0):

@@ -41,7 +41,7 @@ GC = 288
 VDIV = (0, 1)
 WARM = ()
 LATE = "s"
-RUN = 8
+RUN = 4
 RINGS = {"wide": 4, "flat": 10, "grouped_v": 3, "grouped_s": 2, "shared0": 1, "shared1": 1, "shared2": 1, "shared3": 1, "shared4": 1, **{f"bank{n}": 1 for n in range(BANKS)}}
 
 

@@ -37,12 +37,12 @@ ORDER = [(2, Z), (2, 0), (3, Z), (3, 0), (0, 1), (1, 1)]
 VEXIT = ()
 VAT = 2
 FILL = (3, 4)
-GC = 288
+GC = 320
 VDIV = (0, 1)
 WARM = ()
 LATE = "s"
 RUN = 4
-RINGS = {"wide": 4, "flat": 10, "grouped_v": 3, "grouped_s": 2, "shared0": 1, "shared1": 1, "shared2": 1, "shared3": 1, "shared4": 1, **{f"bank{n}": 1 for n in range(BANKS)}}
+RINGS = {"wide": 3, "flat": 10, "grouped_v": 3, "grouped_s": 2, "shared0": 1, "shared1": 1, "shared2": 1, "shared3": 1, "shared4": 1, **{f"bank{n}": 1 for n in range(BANKS)}}
 
 
 def tile_factoranalysisemloadinggradient_kernel(
@@ -170,22 +170,26 @@ def tile_factoranalysisemloadinggradient_kernel(
                 in_=source.rearrange("q c j -> q (c j)"),
             )
 
-        def widen(pair):
-            tile = take("wide", [P, 2 * D], BF16)
-            nc.scalar.copy(out=tile[:], in_=x_raw[pair].bitcast(FP8))
-            tiles["wide", pair] = tile
+        def widen(pair, g):
+            if pair == 0:
+                tile = keep.tile([P, D], BF16, name=f"first_wide{g}", align_bytes=256)
+                for unit in range(2):
+                    source = x_raw[0][:, unit * D + g * K_PASS : unit * D + (g + 1) * K_PASS]
+                    nc.scalar.copy(out=tile[:, unit * K_PASS : (unit + 1) * K_PASS], in_=source.bitcast(FP8))
+                tiles["wide", 0, g] = [tile[:, unit * K_PASS : (unit + 1) * K_PASS] for unit in range(2)]
+            else:
+                tile = take("wide", [P, 2 * D], BF16)
+                nc.scalar.copy(out=tile[:], in_=x_raw[pair].bitcast(FP8))
+                for h in range(PASSES):
+                    starts = [unit * D + h * K_PASS for unit in range(2)]
+                    tiles["wide", pair, h] = [tile[:, start : start + K_PASS] for start in starts]
 
         def turn(pair, g):
             bank = take(bank_of[turn, pair, g], [P, 2, 2 * P], F32)
-            words = tiles["wide", pair][:].bitcast(F32)
             for unit in range(2):
-                first = unit * D // 2 + g * K_PASS // 2
+                words = tiles["wide", pair, g][unit].bitcast(F32)
                 for u in range(2):
-                    nc.tensor.transpose(
-                        bank[:, u, unit * P : (unit + 1) * P],
-                        words[:, first + u : first + K_PASS // 2 : 2],
-                        identity[:],
-                    )
+                    nc.tensor.transpose(bank[:, u, unit * P : (unit + 1) * P], words[:, u::2], identity[:])
             tiles["turn", pair, g] = bank
 
         def product(pair, g):
@@ -289,7 +293,7 @@ def tile_factoranalysisemloadinggradient_kernel(
         def needs(step):
             name, args = step[0], step[1:]
             if name is turn:
-                return [(widen, args[0])]
+                return [(widen, args[0], args[1] if args[0] == 0 else 0)]
             if name is product:
                 return [(turn, *args)]
             if name is x_quantize:
@@ -328,7 +332,7 @@ def tile_factoranalysisemloadinggradient_kernel(
                 return bank_of[step], [(empty, *args[:2])]
             if name is accumulate and args[0] == 0:
                 return bank_of[step], [(subtract, args[1])]
-            if name is widen:
+            if name is widen and args[0] > 0:
                 return "wide", [(turn, args[0], PASSES - 1)]
             if name is product and args[1] == 0:
                 return f"shared{args[0] % 2}", [QX(args[0], g) for g in range(PASSES)]
@@ -360,23 +364,23 @@ def tile_factoranalysisemloadinggradient_kernel(
             return [(empty, PACK * g + j, b) for j in js]
 
         def W(k):
-            return [(widen, k)]
+            return [(widen, k, 0)]
 
         keys = [("w", b, g) for b in (0, 1, Z) for g in range(PASSES)]
         keys += [("y", g, b) for b in (0, 1, Z) for g in range(GROUPS)]
         pieces = {key: [("v", "grouped_v", 0, WIDTH)] for key in keys}
         H = WIDTH // 2
-        joint = [("w", 1, 0), ("w", 1, 1), ("y", 0, Z), ("y", 0, 0), ("y", 1, Z), ("y", 1, 0)]
+        joint = [("w", 1, 0), ("w", 1, 1), ("y", 0, Z), ("y", 0, 0), ("y", 1, Z)]
         for key in joint:
             pieces[key] = [("g", "shared3", 0, GC), ("v", "shared3", GC, WIDTH)]
         pieces["w", Z, 0] = [("v", "grouped_v", 0, H), ("s", "shared2", H, WIDTH)]
-        pieces["w", Z, 1] = [("g", "shared2", 0, H), ("s", "grouped_s", H, WIDTH)]
-        pieces["w", 0, 0] = [("s", "shared3", 0, H), ("g", "shared0", H, WIDTH)]
+        pieces["w", Z, 1] = [("g", "shared2", 0, H), ("s", "shared4", H, WIDTH)]
+        pieces["w", 0, 0] = [("s", "shared3", 0, H), ("g", "shared4", H, WIDTH)]
         pieces["w", 0, 1] = [("v", "grouped_v", 0, H), ("s", "grouped_s", H, WIDTH)]
         pieces["y", 2, 1] = [("s", "grouped_s", 0, H), (LATE, "grouped_" + LATE, H, WIDTH)]
         pieces["y", 3, 1] = [("s", "shared2", 0, H), ("s", "grouped_s", H, WIDTH)]
         gpsimd = [I("w", Z, 1, 0), I("w", 0, 0, 1)] + [I(*key) for key in joint]
-        behind = {I("w", Z, 1, 0): [Q("w", Z, 0, 1)], I("w", 0, 0, 1): [QX(0, 1)], (product, 2, 0): [Q("w", 0, 0, 1)], I("w", 1, 0, 0): [Q("w", 0, 0, 0)], I("y", 3, 1, 0): [Q("w", Z, 1, 0)]}
+        behind = {I("w", Z, 1, 0): [Q("w", Z, 0, 1)], I("w", 0, 0, 1): [Q("w", Z, 1, 1)], I("w", 1, 0, 0): [Q("w", 0, 0, 0)], I("y", 3, 1, 0): [Q("w", Z, 1, 0)]}
         tensor = T(0) + T(1) + [(multiply, j, Z, 0) for j in range(2)] + T(2) + [(multiply, j, Z, 1) for j in range(2)] + T(3) + M(0, Z, (2, 3)) + M(0, 0)
         for k in range(2, 6):
             js = (0, 1) if k % 2 == 0 else (2, 3)
@@ -384,7 +388,7 @@ def tile_factoranalysisemloadinggradient_kernel(
             if k in FILL:
                 tensor += M(0, 1, (0, 1) if k == FILL[0] else (2, 3))
         tensor += M(0, 1) * (not FILL) + M(1, 1) + M(3, Z) + M(3, 0) + M(2, 1) + M(3, 1)
-        scalar = W(0) + [I("w", Z, 0, 1)] + W(1) + [I("w", Z, 1, 1)] + W(2) + [I("w", 0, 0, 0)] + W(3) + [I("w", 0, 1, 1)] + W(4)
+        scalar = W(0) + [(widen, 0, 1), I("w", Z, 0, 1)] + W(1) + [I("w", Z, 1, 1)] + W(2) + [I("w", 0, 0, 0)] + W(3) + [I("w", 0, 1, 1)] + W(4)
         for step in tensor:
             if step[0] is multiply:
                 if step[1:] == (0, Z, 1):
@@ -416,11 +420,15 @@ def tile_factoranalysisemloadinggradient_kernel(
         scalar += [I("y", 2, 1, 0), I("y", 3, 1, 0), I("y", 2, 1, 1), I("y", 3, 1, 1)]
         scalar.extend((divide, d) for d in range(BANDS) if d not in PREPARED and d not in VDIV)
 
-        vector = [I("w", Z, 0), Q("w", Z, 0), Q("w", Z, 0, 1), *PR(0), QX(0, 0), Q("w", Z, 1, 0), Q("w", Z, 1, 1), QX(0, 1), *PR(1), I("w", 0, 1, 0), QX(1), Q("w", 0, 1, 0), Q("w", 0, 0, 1), Q("w", 0, 1, 1), Q("w", 0, 0, 0)]
-        for k in range(2, 8):
-            vector += [*PR(k), I(*joint[k - 2], 1)] + [(invert_psi,)] * (k == 4) + [(mean_psi,)] * (k == 5) + [QX(k), Q(*joint[k - 2])]
+        vector = [I("w", Z, 0), (product, 0, 0), Q("w", Z, 0), QX(0, 0), Q("w", Z, 0, 1)]
+        after = {0: [QX(0, 1), Q("w", Z, 1, 0), Q("w", Z, 1, 1)], 1: [QX(1), I("w", 0, 1, 0), Q("w", 0, 0, 1), Q("w", 0, 1, 1), Q("w", 0, 1, 0), Q("w", 0, 0, 0)]}
+        for k in range(2, 7):
+            after[k] = [I(*joint[k - 2], 1)] + [(invert_psi,)] * (k == 4) + [(mean_psi,)] * (k == 5) + [QX(k), Q(*joint[k - 2])]
+        after[7] = [I("y", 1, 0), QX(7)]
+        for k in range(8):
+            vector += [(product, k, 1)] + [(product, k + 1, 0)] * (k < 7) + after[k]
         order = ORDER
-        vector += [I("y", *order[0])]
+        vector += [I("y", *order[0]), Q("y", 1, 0)]
         for last, key in zip(order, order[1:]):
             if key == order[VAT]:
                 vector += [(empty, *unit) for unit in VEXIT] + [(prepare, d) for d in VPREP]

@@ -29,15 +29,16 @@ Z = 2
 BANDS = D // P
 BANKS = 8
 SPLIT = 32
-PREPARED = (7,)
+PREPARED = (6, 7)
 GM = 0
 GA = 1
 VPREP = ()
+GPREP = (6,)
 ORDER = [(2, Z), (2, 0), (3, Z), (3, 0), (0, 1), (1, 1)]
 VEXIT = ()
 VAT = 2
 FILL = (3, 4)
-GC = 320
+GC = 352
 VDIV = (0, 1)
 WARM = ()
 LATE = "s"
@@ -88,8 +89,8 @@ def tile_factoranalysisemloadinggradient_kernel(
         v_raw = keep.tile([P, BANDS, K], BF16, name="v_raw")
         psi16 = keep.tile([P, BANDS, 2], BF16, name="psi16")
         load_x(0, 2)
+        nc.scalar.dma_start(out=scale[:], in_=x_scale.rearrange("o (g q j) -> q (o g) j", q=P, j=PACK))
         load_beta(0)
-        nc.sync.dma_start(out=scale[:], in_=x_scale.rearrange("o (g q j) -> q (o g) j", q=P, j=PACK))
         load_x(2, 2)
         load_beta(1)
         load_x(4, 2)
@@ -150,7 +151,12 @@ def tile_factoranalysisemloadinggradient_kernel(
                 tile = take(ring, [P, last - first, PACK], BF16)[:]
             if engine == "g":
                 nc.gpsimd.tensor_scalar(
-                    out=tile, in0=source.rearrange("q j c -> q c j"), scalar1=1.0, scalar2=0.0, op0=MULT, op1=ADD
+                    out=tile.rearrange("q (c i) j -> q c j i", i=RUN),
+                    in0=source.rearrange("q j (c i) -> q c j i", i=RUN),
+                    scalar1=1.0,
+                    scalar2=0.0,
+                    op0=MULT,
+                    op1=ADD,
                 )
             else:
                 copy = nc.vector.tensor_copy if engine == "v" else nc.scalar.copy
@@ -254,8 +260,10 @@ def tile_factoranalysisemloadinggradient_kernel(
             )
 
         def prepare(d):
-            tile = keep.tile([P, K], F32, name=f"v_over_psi{d}")
-            if d in VPREP:
+            tile = take("shared3", [P, K], F32) if d in GPREP else keep.tile([P, K], F32, name=f"v_over_psi{d}")
+            if d in GPREP:
+                nc.gpsimd.tensor_scalar(out=tile[:], in0=v_raw[:, d, :], scalar1=psi_inv[:, d : d + 1], scalar2=0.0, op0=MULT, op1=ADD)
+            elif d in VPREP:
                 nc.vector.tensor_scalar(out=tile[:], in0=v_raw[:, d, :], scalar1=psi_inv[:, d : d + 1], scalar2=None, op0=MULT)
             else:
                 nc.scalar.activation(out=tile[:], in_=v_raw[:, d, :], func=COPY, scale=psi_inv[:, d : d + 1])
@@ -332,6 +340,8 @@ def tile_factoranalysisemloadinggradient_kernel(
                 return bank_of[step], [(empty, *args[:2])]
             if name is accumulate and args[0] == 0:
                 return bank_of[step], [(subtract, args[1])]
+            if name is prepare and args[0] in GPREP:
+                return "shared3", [(subtract, *args)]
             if name is widen and args[0] > 0:
                 return "wide", [(turn, args[0], PASSES - 1)]
             if name is product and args[1] == 0:
@@ -381,6 +391,8 @@ def tile_factoranalysisemloadinggradient_kernel(
         pieces["y", 3, 1] = [("s", "shared2", 0, H), ("s", "grouped_s", H, WIDTH)]
         gpsimd = [I("w", Z, 1, 0), I("w", 0, 0, 1)] + [I(*key) for key in joint]
         behind = {I("w", Z, 1, 0): [Q("w", Z, 0, 1)], I("w", 0, 0, 1): [Q("w", Z, 1, 1)], I("w", 1, 0, 0): [Q("w", 0, 0, 0)], I("y", 3, 1, 0): [Q("w", Z, 1, 0)]}
+        gpsimd += [(prepare, d) for d in GPREP]
+        behind.update({(prepare, d): [Q(*joint[-1])] for d in GPREP})
         tensor = T(0) + T(1) + [(multiply, j, Z, 0) for j in range(2)] + T(2) + [(multiply, j, Z, 1) for j in range(2)] + T(3) + M(0, Z, (2, 3)) + M(0, 0)
         for k in range(2, 6):
             js = (0, 1) if k % 2 == 0 else (2, 3)
@@ -393,14 +405,14 @@ def tile_factoranalysisemloadinggradient_kernel(
             if step[0] is multiply:
                 if step[1:] == (0, Z, 1):
                     scalar.append((widen_factor, Z))
-                if step[1:] == (2, Z, 1):
+                if step[1:] == (3, Z, 1):
                     scalar.append((widen_factor, 0))
                 if step[3] == 1 and step[1:3] not in VEXIT:
                     scalar.append((empty, *step[1:3]))
             elif step[2] == 0 and 4 <= step[1] < 7:
                 scalar += W(step[1] + 1)
             elif step[1:] == (7, 0):
-                scalar += [(prepare, d) for d in PREPARED if d not in VPREP]
+                scalar += [(prepare, d) for d in PREPARED if d not in VPREP and d not in GPREP]
         for g in range(GA):
             tensor.extend((accumulate, g, d) for d in range(4))
         for d in range(4):

@@ -38,7 +38,7 @@ ORDER = [(2, Z), (2, 0), (3, Z), (3, 0), (0, 1), (1, 1)]
 VEXIT = ()
 VAT = 2
 FILL = (3, 4)
-GC = 352
+GC = 400
 VDIV = (0, 1)
 WARM = ()
 LATE = "s"
@@ -362,7 +362,7 @@ def tile_factoranalysisemloadinggradient_kernel(
             return [(product, k, 0), (product, k, 1)]
 
         def QX(k, g=0):
-            return (x_quantize, k, g, 1) if k == 0 else (x_quantize, k, 0, PASSES)
+            return (x_quantize, k, g, 1) if k < 7 else (x_quantize, k, 0, PASSES)
 
         def T(k):
             return [(turn, k, 0), (turn, k, 1)]
@@ -432,10 +432,10 @@ def tile_factoranalysisemloadinggradient_kernel(
         scalar += [I("y", 2, 1, 0), I("y", 3, 1, 0), I("y", 2, 1, 1), I("y", 3, 1, 1)]
         scalar.extend((divide, d) for d in range(BANDS) if d not in PREPARED and d not in VDIV)
 
-        vector = [I("w", Z, 0), (product, 0, 0), Q("w", Z, 0), QX(0, 0), Q("w", Z, 0, 1)]
-        after = {0: [QX(0, 1), Q("w", Z, 1, 0), Q("w", Z, 1, 1)], 1: [QX(1), I("w", 0, 1, 0), Q("w", 0, 0, 1), Q("w", 0, 1, 1), Q("w", 0, 1, 0), Q("w", 0, 0, 0)]}
+        vector = [I("w", Z, 0), (product, 0, 0), Q("w", Z, 0), Q("w", Z, 0, 1), QX(0, 0)]
+        after = {0: [QX(0, 1), Q("w", Z, 1, 1), Q("w", Z, 1, 0)], 1: [QX(1, 0), QX(1, 1), I("w", 0, 1, 0), Q("w", 0, 0, 1), Q("w", 0, 1, 1), Q("w", 0, 0, 0), Q("w", 0, 1, 0)]}
         for k in range(2, 7):
-            after[k] = [I(*joint[k - 2], 1)] + [(invert_psi,)] * (k == 4) + [(mean_psi,)] * (k == 5) + [QX(k), Q(*joint[k - 2])]
+            after[k] = [I(*joint[k - 2], 1)] + [(invert_psi,)] * (k == 4) + [(mean_psi,)] * (k == 5) + [QX(k, 0), Q(*joint[k - 2]), QX(k, 1)]
         after[7] = [I("y", 1, 0), QX(7)]
         for k in range(8):
             vector += [(product, k, 1)] + [(product, k + 1, 0)] * (k < 7) + after[k]

@@ -24,26 +24,32 @@ K_PASS = P * PACK
 PASSES = D // K_PASS
 GROUPS = N // K_PASS
 UNITS = N // P
+PAIRS = UNITS // 2
 WIDTH = 512
+HALF = WIDTH // 2
+QUARTER = WIDTH // 4
 Z = 2
 BANDS = D // P
+BLOCK_BANDS = WIDTH // P
 BANKS = 8
-SPLIT = 32
-PREPARED = (6, 7)
-GM = 0
-GA = 1
-VPREP = ()
-GPREP = (6,)
-ORDER = [(2, Z), (2, 0), (3, Z), (3, 0), (0, 1), (1, 1)]
-VEXIT = ()
-VAT = 2
-FILL = (3, 4)
-GC = 400
-VDIV = (0, 1)
-WARM = ()
-LATE = "s"
+TURN_BANKS = 4
 RUN = 4
-RINGS = {"wide": 3, "flat": 10, "grouped_v": 3, "grouped_s": 2, "shared0": 1, "shared1": 1, "shared2": 1, "shared3": 1, "shared4": 1, **{f"bank{n}": 1 for n in range(BANKS)}}
+GPSIMD_COLUMNS = 400
+VECTOR_DIVIDES = (0, 1)
+LAST_BAND = BANDS - 1
+
+RINGS = {
+    "wide": 3,
+    "flat": 10,
+    "by_vector": 3,
+    "by_scalar": 2,
+    "x_even": 1,
+    "x_odd": 1,
+    "gate_a": 1,
+    "gate_b": 1,
+    "gate_c": 1,
+    **{f"bank{n}": 1 for n in range(BANKS)},
+}
 
 
 def tile_factoranalysisemloadinggradient_kernel(
@@ -55,9 +61,6 @@ def tile_factoranalysisemloadinggradient_kernel(
         psum = ctx.enter_context(tc.psum_pool(name="psum", bufs=1))
         ctx.enter_context(tc.manual_schedule())
 
-        if WARM:
-            zeros = keep.tile([P, 2 * P], F32, name="zeros")
-            nc.vector.memset(zeros[:], 0.0)
         identity = keep.tile([P, P], F32, name="identity")
         make_identity(nc, identity[:])
 
@@ -66,49 +69,45 @@ def tile_factoranalysisemloadinggradient_kernel(
         beta_view = beta.rearrange("(g q j) d -> g q j d", q=P, j=PACK)
         x_raw, w_raw = {}, {}
 
-        def load_x(first, count):
-            raw = keep.tile([P, count, D], U8, name=f"x_raw{first}")
-            j = first % PACK
-            nc.sync.dma_start(out=raw[:], in_=x_view[first // PACK][:, j : j + count, :])
-            for n in range(0, count, 2):
-                x_raw[(first + n) // 2] = raw[:, n : n + 2, :].rearrange("q j f -> q (j f)")
+        def load_x(first_pair, pairs):
+            raw = keep.tile([P, 2 * pairs, D], U8, name=f"x_raw{first_pair}")
+            group, j = divmod(2 * first_pair, PACK)
+            nc.sync.dma_start(out=raw[:], in_=x_view[group][:, j : j + 2 * pairs, :])
+            for n in range(pairs):
+                x_raw[first_pair + n] = raw[:, 2 * n : 2 * n + 2, :].rearrange("q j f -> q (j f)")
 
-        def load_beta(g):
-            raw = keep.tile([P, PACK, K], BF16, name=f"beta_raw{g}")
-            nc.sync.dma_start(out=raw[:], in_=beta_view[g])
-            w_raw[Z, g] = raw[:]
-
-        def load_p(b, g):
-            raw = keep.tile([P, PACK, WIDTH], BF16, name=f"p_raw{b}{g}")
-            nc.sync.dma_start(out=raw[:], in_=p_view[g][:, :, b * WIDTH : (b + 1) * WIDTH])
-            w_raw[b, g] = raw[:]
+        def load_w(block, g):
+            raw = keep.tile([P, PACK, WIDTH], BF16, name=f"w_raw{block}{g}")
+            rows = beta_view[g] if block == Z else p_view[g][:, :, block * WIDTH : (block + 1) * WIDTH]
+            nc.sync.dma_start(out=raw[:], in_=rows)
+            w_raw[block, g] = raw[:]
 
         scale = keep.tile([P, PASSES, PACK], F32, name="scale")
         r16 = keep.tile([P, GROUPS, PACK], BF16, name="r16")
         t16 = keep.tile([P, GROUPS, PACK], BF16, name="t16")
         v_raw = keep.tile([P, BANDS, K], BF16, name="v_raw")
         psi16 = keep.tile([P, BANDS, 2], BF16, name="psi16")
-        load_x(0, 2)
+        load_x(0, 1)
         nc.scalar.dma_start(out=scale[:], in_=x_scale.rearrange("o (g q j) -> q (o g) j", q=P, j=PACK))
-        load_beta(0)
-        load_x(2, 2)
-        load_beta(1)
-        load_x(4, 2)
-        load_p(0, 0)
-        load_x(6, 2)
-        load_p(0, 1)
-        load_x(8, 2)
+        load_w(Z, 0)
+        load_x(1, 1)
+        load_w(Z, 1)
+        load_x(2, 1)
+        load_w(0, 0)
+        load_x(3, 1)
+        load_w(0, 1)
+        load_x(4, 1)
         nc.sync.dma_start(out=t16[:], in_=t.rearrange("(g q j) -> q g j", q=P, j=PACK))
-        load_p(1, 0)
+        load_w(1, 0)
         nc.sync.dma_start(out=r16[:], in_=r.rearrange("(g q j) -> q g j", q=P, j=PACK))
-        load_x(10, 2)
-        load_p(1, 1)
-        load_x(12, 4)
+        load_x(5, 1)
+        load_w(1, 1)
+        load_x(6, 2)
         nc.sync.dma_start(out=v_raw[:], in_=v.rearrange("(b q) k -> q b k", q=P))
         with nc.allow_non_contiguous_dma(reason="one noise variance for each partition and band"):
             nc.sync.dma_start(out=psi16[:, :, 0], in_=psi.rearrange("(b q) -> q b", q=P))
 
-        factor = {b: keep.tile([P, UNITS], F32, name=f"factor{b}") for b in (0, Z)}
+        factor = {block: keep.tile([P, UNITS], F32, name=f"factor{block}") for block in (0, Z)}
         factor[1] = factor[0]
         psi_inv = keep.tile([P, BANDS], F32, name="psi_inv")
         psi_inv_mean = keep.tile([P, BANDS], F32, name="psi_inv_mean")
@@ -129,9 +128,12 @@ def tile_factoranalysisemloadinggradient_kernel(
                 tiles[key] = (codes, scales)
             return tiles[key]
 
-        def widen_factor(b):
-            source = t16 if b == Z else r16
-            nc.scalar.copy(out=factor[b][:], in_=source[:].rearrange("q g j -> q (g j)"))
+        def x_ring(pair):
+            return "x_odd" if pair % 2 else "x_even"
+
+        def widen_factor(block):
+            source = t16 if block == Z else r16
+            nc.scalar.copy(out=factor[block][:], in_=source[:].rearrange("q g j -> q (g j)"))
 
         def invert_psi():
             nc.vector.reciprocal(out=psi_inv[:], in_=psi16[:, :, 0])
@@ -139,56 +141,49 @@ def tile_factoranalysisemloadinggradient_kernel(
         def mean_psi():
             nc.vector.tensor_scalar(out=psi_inv_mean[:], in0=psi_inv[:], scalar1=1.0 / N, scalar2=None, op0=MULT)
 
-        def interleave(key, n):
-            kind, a, b = key
-            engine, ring, first, last = pieces[key][n]
+        def interleave(slab, n):
+            kind, a, b = slab
+            engine, ring, first, last = pieces[slab][n]
             source = (w_raw[a, b] if kind == "w" else tiles["flat", a, b][:])[:, :, first:last]
-            if key in joint:
+            if slab in shared:
                 if n == 0:
-                    tiles["joint", key] = take(ring, [P, WIDTH, PACK], BF16)
-                tile = tiles["joint", key][:, first:last, :]
+                    tiles["grouped", slab] = take(ring, [P, WIDTH, PACK], BF16)
+                tile = tiles["grouped", slab][:, first:last, :]
             else:
                 tile = take(ring, [P, last - first, PACK], BF16)[:]
-            if engine == "g":
-                nc.gpsimd.tensor_scalar(
-                    out=tile.rearrange("q (c i) j -> q c j i", i=RUN),
-                    in0=source.rearrange("q j (c i) -> q c j i", i=RUN),
-                    scalar1=1.0,
-                    scalar2=0.0,
-                    op0=MULT,
-                    op1=ADD,
-                )
+                tiles["grouped", slab, n] = tile
+            target = tile.rearrange("q (c i) j -> q c j i", i=RUN)
+            source = source.rearrange("q j (c i) -> q c j i", i=RUN)
+            if engine == "gpsimd":
+                nc.gpsimd.tensor_scalar(out=target, in0=source, scalar1=1.0, scalar2=0.0, op0=MULT, op1=ADD)
+            elif engine == "vector":
+                nc.vector.tensor_copy(out=target, in_=source)
             else:
-                copy = nc.vector.tensor_copy if engine == "v" else nc.scalar.copy
-                copy(
-                    out=tile.rearrange("q (c i) j -> q c j i", i=RUN),
-                    in_=source.rearrange("q j (c i) -> q c j i", i=RUN),
-                )
-            tiles["grouped", key, n] = tile
+                nc.scalar.copy(out=target, in_=source)
 
-        def quantize(key, n):
-            codes, scales = mx_tiles(key)
-            first, last = (0, WIDTH) if key in joint else pieces[key][n][2:]
-            source = tiles["joint", key][:] if key in joint else tiles["grouped", key, n]
+        def quantize(slab, n):
+            codes, scales = mx_tiles(slab)
+            first, last = (0, WIDTH) if slab in shared else pieces[slab][n][2:]
+            source = tiles["grouped", slab][:] if slab in shared else tiles["grouped", slab, n]
             nc.vector.quantize_mx(
                 out=codes[:, first:last].bitcast(FP8X4),
                 scales=scales[:, first:last],
                 in_=source.rearrange("q c j -> q (c j)"),
             )
 
-        def widen(pair, g):
-            if pair == 0:
-                tile = keep.tile([P, D], BF16, name=f"first_wide{g}", align_bytes=256)
-                for unit in range(2):
-                    source = x_raw[0][:, unit * D + g * K_PASS : unit * D + (g + 1) * K_PASS]
-                    nc.scalar.copy(out=tile[:, unit * K_PASS : (unit + 1) * K_PASS], in_=source.bitcast(FP8))
-                tiles["wide", 0, g] = [tile[:, unit * K_PASS : (unit + 1) * K_PASS] for unit in range(2)]
-            else:
-                tile = take("wide", [P, 2 * D], BF16)
-                nc.scalar.copy(out=tile[:], in_=x_raw[pair].bitcast(FP8))
-                for h in range(PASSES):
-                    starts = [unit * D + h * K_PASS for unit in range(2)]
-                    tiles["wide", pair, h] = [tile[:, start : start + K_PASS] for start in starts]
+        def widen_first(g):
+            tile = keep.tile([P, 2 * K_PASS], BF16, name=f"first_wide{g}", align_bytes=256)
+            for unit in range(2):
+                source = x_raw[0][:, unit * D + g * K_PASS : unit * D + (g + 1) * K_PASS]
+                nc.scalar.copy(out=tile[:, unit * K_PASS : (unit + 1) * K_PASS], in_=source.bitcast(FP8))
+            tiles["wide", 0, g] = [tile[:, unit * K_PASS : (unit + 1) * K_PASS] for unit in range(2)]
+
+        def widen(pair):
+            tile = take("wide", [P, 2 * D], BF16)
+            nc.scalar.copy(out=tile[:], in_=x_raw[pair].bitcast(FP8))
+            for g in range(PASSES):
+                starts = [unit * D + g * K_PASS for unit in range(2)]
+                tiles["wide", pair, g] = [tile[:, start : start + K_PASS] for start in starts]
 
         def turn(pair, g):
             bank = take(bank_of[turn, pair, g], [P, 2, 2 * P], F32)
@@ -196,35 +191,34 @@ def tile_factoranalysisemloadinggradient_kernel(
                 words = tiles["wide", pair, g][unit].bitcast(F32)
                 for u in range(2):
                     nc.tensor.transpose(bank[:, u, unit * P : (unit + 1) * P], words[:, u::2], identity[:])
-            tiles["turn", pair, g] = bank
+            tiles["turned", pair, g] = bank
 
         def product(pair, g):
             if g == 0:
-                tiles["x_grouped", pair] = take(f"shared{pair % 2}", [P, PASSES, 2 * P, 2, 2], BF16)
-            values = tiles["turn", pair, g][:].bitcast(BF16).rearrange("q u (c e) -> q c u e", e=2)
+                tiles["x_grouped", pair] = take(x_ring(pair), [P, PASSES, 2 * P, 2, 2], BF16)
+            values = tiles["turned", pair, g][:].bitcast(BF16).rearrange("q u (c e) -> q c u e", e=2)
             scales = scale[:, g, :].rearrange("q (o u e) -> q o u e", o=1, u=2)
             nc.vector.tensor_tensor(
                 out=tiles["x_grouped", pair][:, g], in0=values, in1=scales.to_broadcast([P, 2 * P, 2, 2]), op=MULT
             )
 
-        def x_quantize(pair, first, count):
+        def x_quantize(pair, g):
             codes, scales = mx_tiles(("x", pair))
-            cols = slice(first * 2 * P, (first + count) * 2 * P)
-            source = tiles["x_grouped", pair][:, first : first + count]
+            cols = slice(g * 2 * P, (g + 1) * 2 * P)
             nc.vector.quantize_mx(
                 out=codes[:, cols].bitcast(FP8X4),
                 scales=scales[:, cols],
-                in_=source.rearrange("q g c u e -> q (g c u e)"),
+                in_=tiles["x_grouped", pair][:, g : g + 1].rearrange("q g c u e -> q (g c u e)"),
             )
 
-        def multiply(i, b, g):
+        def multiply(unit, block, g):
             if g == 0:
-                tiles["multiply", i, b] = take(bank_of[multiply, i, b, g], [P, WIDTH], F32)
-            x_codes, x_scales = tiles["x", i // 2]
-            cols = slice((2 * g + i % 2) * P, (2 * g + i % 2 + 1) * P)
-            w_codes, w_scales = tiles["w", b, g]
+                tiles["first", unit, block] = take(bank_of[multiply, unit, block, g], [P, WIDTH], F32)
+            x_codes, x_scales = tiles["x", unit // 2]
+            cols = slice((2 * g + unit % 2) * P, (2 * g + unit % 2 + 1) * P)
+            w_codes, w_scales = tiles["w", block, g]
             nc.tensor.matmul_mx(
-                out=tiles["multiply", i, b][:],
+                out=tiles["first", unit, block][:],
                 lhsT=x_codes[:, cols].bitcast(FP8X4),
                 lhsT_scale=x_scales[:, cols],
                 rhs=w_codes[:].bitcast(FP8X4),
@@ -233,24 +227,26 @@ def tile_factoranalysisemloadinggradient_kernel(
                 stop=(g == PASSES - 1),
             )
 
-        def empty(i, b):
-            group, j = divmod(i, PACK)
+        def empty(unit, block):
+            group, j = divmod(unit, PACK)
             if j == 0:
-                tiles["flat", group, b] = take("flat", [P, PACK, WIDTH], BF16)
-            row, bank, gain = tiles["flat", group, b][:, j, :], tiles["multiply", i, b][:], factor[b][:, i : i + 1]
-            if (i, b) in VEXIT:
-                nc.vector.tensor_scalar(out=row, in0=bank, scalar1=gain, scalar2=None, op0=MULT)
-            else:
-                nc.scalar.activation(out=row, in_=bank, func=COPY, scale=gain)
+                tiles["flat", group, block] = take("flat", [P, PACK, WIDTH], BF16)
+            nc.scalar.activation(
+                out=tiles["flat", group, block][:, j, :],
+                in_=tiles["first", unit, block][:],
+                func=COPY,
+                scale=factor[block][:, unit : unit + 1],
+            )
 
-        def accumulate(group, d):
+        def accumulate(group, band):
             if group == 0:
-                tiles["sum", d] = take(bank_of[accumulate, group, d], [P, K], F32)
-            cols = slice(d % 4 * P, (d % 4 + 1) * P)
-            e_codes, e_scales = tiles["y", group, d // 4]
+                tiles["sum", band] = take(bank_of[accumulate, group, band], [P, K], F32)
+            block, place = divmod(band, BLOCK_BANDS)
+            cols = slice(place * P, (place + 1) * P)
+            e_codes, e_scales = tiles["y", group, block]
             z_codes, z_scales = tiles["y", group, Z]
             nc.tensor.matmul_mx(
-                out=tiles["sum", d][:],
+                out=tiles["sum", band][:],
                 lhsT=e_codes[:, cols].bitcast(FP8X4),
                 lhsT_scale=e_scales[:, cols],
                 rhs=z_codes[:].bitcast(FP8X4),
@@ -259,77 +255,172 @@ def tile_factoranalysisemloadinggradient_kernel(
                 stop=(group == GROUPS - 1),
             )
 
-        def prepare(d):
-            tile = take("shared3", [P, K], F32) if d in GPREP else keep.tile([P, K], F32, name=f"v_over_psi{d}")
-            if d in GPREP:
-                nc.gpsimd.tensor_scalar(out=tile[:], in0=v_raw[:, d, :], scalar1=psi_inv[:, d : d + 1], scalar2=0.0, op0=MULT, op1=ADD)
-            elif d in VPREP:
-                nc.vector.tensor_scalar(out=tile[:], in0=v_raw[:, d, :], scalar1=psi_inv[:, d : d + 1], scalar2=None, op0=MULT)
-            else:
-                nc.scalar.activation(out=tile[:], in_=v_raw[:, d, :], func=COPY, scale=psi_inv[:, d : d + 1])
-            tiles["prepared", d] = tile
-
-        def subtract(d):
-            tile = keep.tile([P, K], F32, name=f"result{d}")
-            if d in PREPARED:
-                mean, other = psi_inv_mean[:, d : d + 1], tiles["prepared", d][:]
-            else:
-                mean, other = 1.0 / N, v_raw[:, d, :]
-            nc.vector.scalar_tensor_tensor(
-                out=tile[:], in0=tiles["sum", d][:], scalar=mean, in1=other, op0=MULT, op1=SUBTRACT
+        def prepare_last():
+            tiles["v_over_psi"] = keep.tile([P, K], F32, name="v_over_psi")
+            nc.scalar.activation(
+                out=tiles["v_over_psi"][:],
+                in_=v_raw[:, LAST_BAND, :],
+                func=COPY,
+                scale=psi_inv[:, LAST_BAND : LAST_BAND + 1],
             )
-            tiles["result", d] = tile
 
-        def divide(d):
-            tile = tiles["result", d]
-            if d in VDIV:
-                nc.vector.tensor_scalar(out=tile[:], in0=tile[:], scalar1=psi_inv[:, d : d + 1], scalar2=None, op0=MULT)
+        def subtract(band):
+            tile = keep.tile([P, K], F32, name=f"result{band}")
+            if band == LAST_BAND:
+                mean, other = psi_inv_mean[:, band : band + 1], tiles["v_over_psi"][:]
             else:
-                nc.scalar.activation(out=tile[:], in_=tile[:], func=COPY, scale=psi_inv[:, d : d + 1])
+                mean, other = 1.0 / N, v_raw[:, band, :]
+            nc.vector.scalar_tensor_tensor(
+                out=tile[:], in0=tiles["sum", band][:], scalar=mean, in1=other, op0=MULT, op1=SUBTRACT
+            )
+            tiles["result", band] = tile
 
-        def store(d):
-            nc.sync.dma_start(out=out[d * P : (d + 1) * P, :], in_=tiles["result", d][:])
+        def divide(band):
+            tile, inverse = tiles["result", band], psi_inv[:, band : band + 1]
+            if band in VECTOR_DIVIDES:
+                nc.vector.tensor_scalar(out=tile[:], in0=tile[:], scalar1=inverse, scalar2=None, op0=MULT)
+            else:
+                nc.scalar.activation(out=tile[:], in_=tile[:], func=COPY, scale=inverse)
 
-        def warm(n):
-            bank = psum.tile([P, 2 * P], F32, name="bank7_0")
-            nc.tensor.matmul(bank[:], lhsT=zeros[:, :P], rhs=zeros[:], start=True, stop=True)
+        def store(band):
+            nc.sync.dma_start(out=out[band * P : (band + 1) * P, :], in_=tiles["result", band][:])
 
-        def each_piece(name, key):
-            count = 1 if name is quantize and key in joint else len(pieces[key])
-            return [(name, key, n) for n in range(count)]
+        slabs = [("w", block, g) for block in (0, 1, Z) for g in range(PASSES)]
+        slabs += [("y", group, block) for block in (0, 1, Z) for group in range(GROUPS)]
+        pieces = {slab: [("vector", "by_vector", 0, WIDTH)] for slab in slabs}
+        shared = [("w", 1, 0), ("w", 1, 1), ("y", 0, Z), ("y", 0, 0), ("y", 1, Z), ("y", 1, 0)]
+        for slab in shared:
+            pieces[slab] = [("gpsimd", "gate_b", 0, GPSIMD_COLUMNS), ("vector", "gate_b", GPSIMD_COLUMNS, WIDTH)]
+        pieces["w", Z, 0] = [("vector", "by_vector", 0, HALF), ("scalar", "gate_a", HALF, WIDTH)]
+        pieces["w", Z, 1] = [("gpsimd", "gate_a", 0, WIDTH - QUARTER), ("scalar", "gate_c", WIDTH - QUARTER, WIDTH)]
+        pieces["w", 0, 0] = [
+            ("scalar", "gate_b", 0, HALF),
+            ("gpsimd", "gate_c", HALF, WIDTH - QUARTER),
+            ("vector", "by_vector", WIDTH - QUARTER, WIDTH),
+        ]
+        pieces["w", 0, 1] = [("vector", "by_vector", 0, HALF), ("scalar", "by_scalar", HALF, WIDTH)]
+        pieces["y", 2, 1] = [("scalar", "by_scalar", 0, HALF), ("scalar", "by_scalar", HALF, WIDTH)]
+        pieces["y", 3, 1] = [("scalar", "gate_a", 0, HALF), ("scalar", "by_scalar", HALF, WIDTH)]
+
+        def mix(kind, a, b, n=0):
+            return (interleave, (kind, a, b), n)
+
+        def quant(kind, a, b, n=0):
+            return (quantize, (kind, a, b), n)
+
+        def both(step, pair):
+            return [(step, pair, g) for g in range(PASSES)]
+
+        def first_stage(group, block, rows=range(PACK)):
+            return [(multiply, PACK * group + j, block, g) for j in rows for g in range(PASSES)]
+
+        def each_piece(step, slab):
+            count = 1 if step is quantize and slab in shared else len(pieces[slab])
+            return [(step, slab, n) for n in range(count)]
+
+        gpsimd = [mix("w", Z, 1, 0), mix("w", 0, 0, 1)] + [mix(*slab) for slab in shared]
+
+        tensor = both(turn, 0) + both(turn, 1) + [(multiply, unit, Z, 0) for unit in range(2)]
+        tensor += both(turn, 2) + [(multiply, unit, Z, 1) for unit in range(2)]
+        tensor += both(turn, 3) + first_stage(0, Z, (2, 3)) + first_stage(0, 0)
+        for pair in range(2, PAIRS - 2):
+            group, rows = pair // 2, (2, 3) if pair % 2 else (0, 1)
+            tensor += both(turn, pair + 2) + first_stage(group, Z, rows) + first_stage(group, 0, rows)
+            if pair in (3, 4):
+                tensor += first_stage(0, 1, (0, 1) if pair == 3 else (2, 3))
+        for group, block in ((1, 1), (3, Z), (3, 0), (2, 1), (3, 1)):
+            tensor += first_stage(group, block)
+
+        scalar = [(widen_first, 0), (widen_first, 1), mix("w", Z, 0, 1), (widen, 1), mix("w", Z, 1, 1), (widen, 2)]
+        scalar += [mix("w", 0, 0, 0), (widen, 3), mix("w", 0, 1, 1), (widen, 4)]
+        for step in tensor:
+            if step == (multiply, 0, Z, 1):
+                scalar.append((widen_factor, Z))
+            if step == (multiply, 3, Z, 1):
+                scalar.append((widen_factor, 0))
+            if step[0] is multiply and step[3] == PASSES - 1:
+                scalar.append((empty, *step[1:3]))
+            if step[0] is turn and step[2] == 0 and step[1] >= 4:
+                scalar.append((widen, step[1] + 1) if step[1] + 1 < PAIRS else (prepare_last,))
+        scalar += [mix("y", group, 1, n) for n in range(2) for group in (2, 3)]
+        scalar += [(divide, band) for band in range(LAST_BAND) if band not in VECTOR_DIVIDES]
+
+        tensor += [(accumulate, 0, band) for band in range(BLOCK_BANDS)]
+        tensor += [(accumulate, group, band) for band in range(BLOCK_BANDS) for group in range(1, GROUPS)]
+        tensor += [(accumulate, group, band) for band in range(BLOCK_BANDS, BANDS) for group in range(GROUPS)]
+
+        bank_of, turns, sums, freed = {}, 0, 0, None
+        for step in tensor:
+            if step == (multiply, PACK * (GROUPS - 1), Z, 0):
+                freed = sums
+            if step[0] is turn:
+                bank_of[step] = f"bank{turns % TURN_BANKS}"
+                turns = turns + 1
+            elif (step[0] is multiply and step[3] == 0) or (step[0] is accumulate and step[1] == 0):
+                if freed is None:
+                    bank_of[step] = f"bank{TURN_BANKS + sums % (BANKS - TURN_BANKS)}"
+                else:
+                    bank_of[step] = f"bank{(sums - freed) % BANKS}"
+                sums = sums + 1
+
+        vector = [mix("w", Z, 0), (product, 0, 0), quant("w", Z, 0), quant("w", Z, 0, 1), (x_quantize, 0, 0)]
+        vector += [(product, 0, 1), (product, 1, 0), (x_quantize, 0, 1), quant("w", Z, 1, 1), quant("w", Z, 1, 0)]
+        vector += [(product, 1, 1), (x_quantize, 1, 0), mix("w", 0, 1, 0), (x_quantize, 1, 1), mix("w", 0, 0, 2)]
+        vector += [quant("w", 0, 0, 1), quant("w", 0, 1, 1), quant("w", 0, 0, 2), quant("w", 0, 0, 0), quant("w", 0, 1, 0)]
+        small = {4: [(invert_psi,)], 5: [(mean_psi,)]}
+        for pair in range(2, PAIRS):
+            slab = shared[pair - 2]
+            vector += both(product, pair) + [mix(*slab, 1)] + small.get(pair, [])
+            vector += [(x_quantize, pair, 0), quant(*slab), (x_quantize, pair, 1)]
+        piled = [(2, Z), (2, 0), (3, Z), (3, 0), (0, 1), (1, 1)]
+        vector.append(mix("y", *piled[0]))
+        for before, panel in zip(piled, piled[1:]):
+            vector += [mix("y", *panel), quant("y", *before)]
+        vector += [(subtract, 0), quant("y", 1, 1), quant("y", 2, 1, 0), (divide, 0), quant("y", 3, 1, 0)]
+        vector += [(subtract, 1), (subtract, 2), (divide, 1), quant("y", 2, 1, 1), (subtract, 3), quant("y", 3, 1, 1)]
+        vector += [(subtract, band) for band in range(BLOCK_BANDS, BANDS)]
+
+        sync = [(store, band) for band in range(BANDS)]
+
+        behind = {
+            mix("w", Z, 1, 0): [quant("w", Z, 0, 1)],
+            mix("w", 0, 0, 1): [quant("w", Z, 1, 1)],
+            mix("w", 1, 0, 0): [quant("w", 0, 0, 0)],
+            mix("y", 3, 1, 0): [quant("w", Z, 1, 0)],
+        }
 
         def needs(step):
             name, args = step[0], step[1:]
             if name is turn:
-                return [(widen, args[0], args[1] if args[0] == 0 else 0)]
+                return [(widen, args[0]) if args[0] else (widen_first, args[1])]
             if name is product:
                 return [(turn, *args)]
             if name is x_quantize:
-                return [(product, args[0], g) for g in range(args[1], args[1] + args[2])]
-            if name is interleave and args[0][0] == "w":
-                return [(interleave, args[0], 0)] if args[0] in joint and args[1] > 0 else []
+                return [(product, *args)]
             if name is interleave:
-                return ([(interleave, args[0], 0)] if args[0] in joint and args[1] > 0 else []) + [(empty, PACK * args[0][1] + j, args[0][2]) for j in range(PACK)]
+                (kind, a, b), n = args
+                buffer = [(interleave, args[0], 0)] if args[0] in shared and n > 0 else []
+                return buffer + ([(empty, PACK * a + j, b) for j in range(PACK)] if kind == "y" else [])
             if name is quantize:
-                return each_piece(interleave, args[0]) if args[0] in joint else [(interleave, *args)]
+                return each_piece(interleave, args[0]) if args[0] in shared else [(interleave, *args)]
             if name is multiply:
-                return [QX(args[0] // 2, args[2])] + each_piece(quantize, ("w", *args[1:]))
+                return [(x_quantize, args[0] // 2, args[2])] + each_piece(quantize, ("w", *args[1:]))
             if name is empty:
-                first = [(empty, args[0] // PACK * PACK, args[1])] if args[0] % PACK else []
-                return first + [(multiply, *args, PASSES - 1), (widen_factor, Z if args[1] == Z else 0)]
+                return [(multiply, *args, PASSES - 1), (widen_factor, Z if args[1] == Z else 0)]
             if name is accumulate:
-                key = ("y", args[0], args[1] // 4)
-                mine = [step for step in each_piece(quantize, key) if key in joint or pieces[key][step[2]][3] > args[1] % 4 * P]
-                return mine[:1] + each_piece(quantize, ("y", args[0], Z))
+                block, place = divmod(args[1], BLOCK_BANDS)
+                slab = ("y", args[0], block)
+                n = 0 if slab in shared else [piece[3] > place * P for piece in pieces[slab]].index(True)
+                return [(quantize, slab, n)] + each_piece(quantize, ("y", args[0], Z))
             if name is subtract:
-                prepared = [(prepare, *args), (mean_psi,)] if args[0] in PREPARED else []
-                return [(accumulate, GROUPS - 1, *args)] + prepared
-            if name is prepare or name is mean_psi:
+                last = [(prepare_last,), (mean_psi,)] if args[0] == LAST_BAND else []
+                return [(accumulate, GROUPS - 1, *args)] + last
+            if name is prepare_last or name is mean_psi:
                 return [(invert_psi,)]
             if name is divide:
                 return [(subtract, *args), (invert_psi,)]
             if name is store:
-                return [(subtract if args[0] in PREPARED else divide, *args)]
+                return [(subtract if args[0] == LAST_BAND else divide, *args)]
             return []
 
         def claims(step):
@@ -340,115 +431,17 @@ def tile_factoranalysisemloadinggradient_kernel(
                 return bank_of[step], [(empty, *args[:2])]
             if name is accumulate and args[0] == 0:
                 return bank_of[step], [(subtract, args[1])]
-            if name is prepare and args[0] in GPREP:
-                return "shared3", [(subtract, *args)]
-            if name is widen and args[0] > 0:
-                return "wide", [(turn, args[0], PASSES - 1)]
+            if name is widen:
+                return "wide", both(turn, args[0])
             if name is product and args[1] == 0:
-                return f"shared{args[0] % 2}", [QX(args[0], g) for g in range(PASSES)]
+                return x_ring(args[0]), both(x_quantize, args[0])
             if name is empty and args[0] % PACK == 0:
                 return "flat", each_piece(interleave, ("y", args[0] // PACK, args[1]))
-            if name is interleave and not (args[0] in joint and args[1] > 0):
+            if name is interleave and not (args[0] in shared and args[1] > 0):
                 return pieces[args[0]][args[1]][1], [(quantize, *args)]
             return None, None
 
-        def I(kind, a, b, n=0):
-            return (interleave, (kind, a, b), n)
-
-        def Q(kind, a, b, n=0):
-            return (quantize, (kind, a, b), n)
-
-        def PR(k):
-            return [(product, k, 0), (product, k, 1)]
-
-        def QX(k, g=0):
-            return (x_quantize, k, g, 1) if k < 7 else (x_quantize, k, 0, PASSES)
-
-        def T(k):
-            return [(turn, k, 0), (turn, k, 1)]
-
-        def M(g, b, js=range(PACK)):
-            return [(multiply, PACK * g + j, b, h) for j in js for h in range(PASSES)]
-
-        def E(g, b, js=range(PACK)):
-            return [(empty, PACK * g + j, b) for j in js]
-
-        def W(k):
-            return [(widen, k, 0)]
-
-        keys = [("w", b, g) for b in (0, 1, Z) for g in range(PASSES)]
-        keys += [("y", g, b) for b in (0, 1, Z) for g in range(GROUPS)]
-        pieces = {key: [("v", "grouped_v", 0, WIDTH)] for key in keys}
-        H = WIDTH // 2
-        joint = [("w", 1, 0), ("w", 1, 1), ("y", 0, Z), ("y", 0, 0), ("y", 1, Z)]
-        for key in joint:
-            pieces[key] = [("g", "shared3", 0, GC), ("v", "shared3", GC, WIDTH)]
-        pieces["w", Z, 0] = [("v", "grouped_v", 0, H), ("s", "shared2", H, WIDTH)]
-        pieces["w", Z, 1] = [("g", "shared2", 0, H), ("s", "shared4", H, WIDTH)]
-        pieces["w", 0, 0] = [("s", "shared3", 0, H), ("g", "shared4", H, WIDTH)]
-        pieces["w", 0, 1] = [("v", "grouped_v", 0, H), ("s", "grouped_s", H, WIDTH)]
-        pieces["y", 2, 1] = [("s", "grouped_s", 0, H), (LATE, "grouped_" + LATE, H, WIDTH)]
-        pieces["y", 3, 1] = [("s", "shared2", 0, H), ("s", "grouped_s", H, WIDTH)]
-        gpsimd = [I("w", Z, 1, 0), I("w", 0, 0, 1)] + [I(*key) for key in joint]
-        behind = {I("w", Z, 1, 0): [Q("w", Z, 0, 1)], I("w", 0, 0, 1): [Q("w", Z, 1, 1)], I("w", 1, 0, 0): [Q("w", 0, 0, 0)], I("y", 3, 1, 0): [Q("w", Z, 1, 0)]}
-        gpsimd += [(prepare, d) for d in GPREP]
-        behind.update({(prepare, d): [Q(*joint[-1])] for d in GPREP})
-        tensor = T(0) + T(1) + [(multiply, j, Z, 0) for j in range(2)] + T(2) + [(multiply, j, Z, 1) for j in range(2)] + T(3) + M(0, Z, (2, 3)) + M(0, 0)
-        for k in range(2, 6):
-            js = (0, 1) if k % 2 == 0 else (2, 3)
-            tensor += T(k + 2) + M(k // 2, Z, js) + M(k // 2, 0, js)
-            if k in FILL:
-                tensor += M(0, 1, (0, 1) if k == FILL[0] else (2, 3))
-        tensor += M(0, 1) * (not FILL) + M(1, 1) + M(3, Z) + M(3, 0) + M(2, 1) + M(3, 1)
-        scalar = W(0) + [(widen, 0, 1), I("w", Z, 0, 1)] + W(1) + [I("w", Z, 1, 1)] + W(2) + [I("w", 0, 0, 0)] + W(3) + [I("w", 0, 1, 1)] + W(4)
-        for step in tensor:
-            if step[0] is multiply:
-                if step[1:] == (0, Z, 1):
-                    scalar.append((widen_factor, Z))
-                if step[1:] == (3, Z, 1):
-                    scalar.append((widen_factor, 0))
-                if step[3] == 1 and step[1:3] not in VEXIT:
-                    scalar.append((empty, *step[1:3]))
-            elif step[2] == 0 and 4 <= step[1] < 7:
-                scalar += W(step[1] + 1)
-            elif step[1:] == (7, 0):
-                scalar += [(prepare, d) for d in PREPARED if d not in VPREP and d not in GPREP]
-        for g in range(GA):
-            tensor.extend((accumulate, g, d) for d in range(4))
-        for d in range(4):
-            tensor.extend((accumulate, g, d) for g in range(GA, GROUPS))
-        for d in range(4, BANDS):
-            tensor.extend((accumulate, g, d) for g in range(GROUPS))
-        bank_of, turns, sums = {}, 0, 0
-        for step in tensor:
-            if step[0] is turn:
-                bank_of[step] = f"bank{turns % 4}"
-                turns = turns + 1
-            elif step[-1] == 0 and step[0] is multiply or step[0] is accumulate and step[1] == 0:
-                bank_of[step] = f"bank{4 + sums % 4}" if sums < SPLIT else f"bank{(sums - SPLIT) % 8}"
-                sums = sums + 1
-        for n, place in enumerate(reversed(WARM)):
-            tensor.insert(place, (warm, n))
-        scalar += [I("y", 2, 1, 0), I("y", 3, 1, 0), I("y", 2, 1, 1), I("y", 3, 1, 1)]
-        scalar.extend((divide, d) for d in range(BANDS) if d not in PREPARED and d not in VDIV)
-
-        vector = [I("w", Z, 0), (product, 0, 0), Q("w", Z, 0), Q("w", Z, 0, 1), QX(0, 0)]
-        after = {0: [QX(0, 1), Q("w", Z, 1, 1), Q("w", Z, 1, 0)], 1: [QX(1, 0), QX(1, 1), I("w", 0, 1, 0), Q("w", 0, 0, 1), Q("w", 0, 1, 1), Q("w", 0, 0, 0), Q("w", 0, 1, 0)]}
-        for k in range(2, 7):
-            after[k] = [I(*joint[k - 2], 1)] + [(invert_psi,)] * (k == 4) + [(mean_psi,)] * (k == 5) + [QX(k, 0), Q(*joint[k - 2]), QX(k, 1)]
-        after[7] = [I("y", 1, 0), QX(7)]
-        for k in range(8):
-            vector += [(product, k, 1)] + [(product, k + 1, 0)] * (k < 7) + after[k]
-        order = ORDER
-        vector += [I("y", *order[0]), Q("y", 1, 0)]
-        for last, key in zip(order, order[1:]):
-            if key == order[VAT]:
-                vector += [(empty, *unit) for unit in VEXIT] + [(prepare, d) for d in VPREP]
-            vector += [I("y", *key), Q("y", *last)]
-        vector += [(subtract, 0), Q("y", 1, 1), Q("y", 2, 1, 0), (divide, 0), Q("y", 3, 1, 0), (subtract, 1), (subtract, 2)] + [(divide, 1)] * (1 in VDIV) + [Q("y", 2, 1, 1), (subtract, 3)] + [(divide, 2)] * (2 in VDIV) + [Q("y", 3, 1, 1)]
-        vector += [(subtract, d) for d in range(4, 8)]
-
-        queues = [vector, scalar, tensor, gpsimd, [(store, d) for d in range(BANDS)]]
+        queues = [vector, scalar, tensor, gpsimd, sync]
         written, readers = set(), {ring: [] for ring in RINGS}
         while any(queues):
             progress = False
@@ -467,4 +460,4 @@ def tile_factoranalysisemloadinggradient_kernel(
                         readers[ring].append(reader)
                     queue.remove(step)
                     progress = True
-            assert progress, [(queue[0][0], queue[0][1:]) for queue in queues if queue]
+            assert progress

@@ -34,7 +34,7 @@ BLOCK_BANDS = WIDTH // P
 BANKS = 8
 TURN_BANKS = 4
 RUN = 4
-GPSIMD_COLUMNS = 400
+GPSIMD_COLUMNS = 384
 VECTOR_DIVIDES = (0, 1)
 LAST_BAND = BANDS - 1
 
@@ -371,7 +371,10 @@ def tile_factoranalysisemloadinggradient_kernel(
         for pair in range(2, PAIRS):
             slab = shared[pair - 2]
             vector += both(product, pair) + [mix(*slab, 1)] + small.get(pair, [])
-            vector += [(x_quantize, pair, 0), quant(*slab), (x_quantize, pair, 1)]
+            if pair < PAIRS - 1:
+                vector += [(x_quantize, pair, 0), quant(*slab), (x_quantize, pair, 1)]
+            else:
+                vector += both(x_quantize, pair) + [quant(*slab)]
         piled = [(2, Z), (2, 0), (3, Z), (3, 0), (0, 1), (1, 1)]
         vector.append(mix("y", *piled[0]))
         for before, panel in zip(piled, piled[1:]):

@@ -31,25 +31,18 @@ QUARTER = WIDTH // 4
 Z = 2
 BANDS = D // P
 BLOCK_BANDS = WIDTH // P
+STRIPS = WIDTH // P
 BANKS = 8
-TURN_BANKS = 4
 RUN = 4
-GPSIMD_COLUMNS = 384
-VECTOR_DIVIDES = (0, 1)
-LAST_BAND = BANDS - 1
-
-RINGS = {
-    "wide": 3,
-    "flat": 10,
-    "by_vector": 3,
-    "by_scalar": 2,
-    "x_even": 1,
-    "x_odd": 1,
-    "gate_a": 1,
-    "gate_b": 1,
-    "gate_c": 1,
-    **{f"bank{n}": 1 for n in range(BANKS)},
-}
+VECTOR_WIDENS = ((0, 0), (1, None))
+PREPARED = (0, 1, 2, 3, 4, 5, 6, 7)
+STRIP_RUN = 4
+GC = 384
+HEAD_BANKS = {("turned", 2, 0): 4, ("turned", 2, 1): 5, ("first", 0, 2): 6, ("first", 1, 2): 7, ("turned", 3, 0): 0, ("turned", 3, 1): 1,
+  ("first", 2, 2): 2, ("first", 3, 2): 3, ("turned", 4, 0): 6, ("turned", 4, 1): 7, ("turned", 0, 0): 0, ("turned", 0, 1): 1, ("turned", 1, 0): 2, ("turned", 1, 1): 3}
+TURN_RING = (0, 1, 6, 7)
+SUM_RING = (2, 3, 4, 5)
+FREED_RING = (6, 7, 0, 1, 2, 3, 4, 5)
 
 
 def tile_factoranalysisemloadinggradient_kernel(
@@ -63,6 +56,8 @@ def tile_factoranalysisemloadinggradient_kernel(
 
         identity = keep.tile([P, P], F32, name="identity")
         make_identity(nc, identity[:])
+        one = keep.tile([P, 1], F32, name="one")
+        nc.vector.memset(one[:], 1.0)
 
         x_view = x_bytes.rearrange("(g q j) f -> g q j f", q=P, j=PACK)
         p_view = p.rearrange("(g q j) d -> g q j d", q=P, j=PACK)
@@ -87,49 +82,61 @@ def tile_factoranalysisemloadinggradient_kernel(
         t16 = keep.tile([P, GROUPS, PACK], BF16, name="t16")
         v_raw = keep.tile([P, BANDS, K], BF16, name="v_raw")
         psi16 = keep.tile([P, BANDS, 2], BF16, name="psi16")
+
+        def load_scale():
+            nc.scalar.dma_start(out=scale[:], in_=x_scale.rearrange("o (g q j) -> q (o g) j", q=P, j=PACK))
+
+        def load_factor(tile, source):
+            nc.sync.dma_start(out=tile[:], in_=source.rearrange("(g q j) -> q g j", q=P, j=PACK))
+
+        def load_end():
+            nc.sync.dma_start(out=v_raw[:], in_=v.rearrange("(b q) k -> q b k", q=P))
+            with nc.allow_non_contiguous_dma(reason="one noise variance for each partition and band"):
+                nc.sync.dma_start(out=psi16[:, :, 0], in_=psi.rearrange("(b q) -> q b", q=P))
+
         load_x(0, 1)
-        nc.scalar.dma_start(out=scale[:], in_=x_scale.rearrange("o (g q j) -> q (o g) j", q=P, j=PACK))
-        load_w(Z, 0)
+        load_scale()
         load_x(1, 1)
-        load_w(Z, 1)
+        load_w(Z, 0)
         load_x(2, 1)
-        load_w(0, 0)
+        load_w(Z, 1)
         load_x(3, 1)
+        load_w(0, 0)
         load_w(0, 1)
+        load_factor(t16, t)
         load_x(4, 1)
-        nc.sync.dma_start(out=t16[:], in_=t.rearrange("(g q j) -> q g j", q=P, j=PACK))
+        load_factor(r16, r)
         load_w(1, 0)
-        nc.sync.dma_start(out=r16[:], in_=r.rearrange("(g q j) -> q g j", q=P, j=PACK))
         load_x(5, 1)
         load_w(1, 1)
         load_x(6, 2)
-        nc.sync.dma_start(out=v_raw[:], in_=v.rearrange("(b q) k -> q b k", q=P))
-        with nc.allow_non_contiguous_dma(reason="one noise variance for each partition and band"):
-            nc.sync.dma_start(out=psi16[:, :, 0], in_=psi.rearrange("(b q) -> q b", q=P))
+        load_end()
 
         factor = {block: keep.tile([P, UNITS], F32, name=f"factor{block}") for block in (0, Z)}
         factor[1] = factor[0]
         psi_inv = keep.tile([P, BANDS], F32, name="psi_inv")
         psi_inv_mean = keep.tile([P, BANDS], F32, name="psi_inv_mean")
-        tiles, taken = {}, {ring: 0 for ring in RINGS}
+        tiles, buffer_of = {}, {}
 
-        def take(ring, shape, dtype):
-            name = f"{ring}_{taken[ring] % RINGS[ring]}"
-            taken[ring] = taken[ring] + 1
-            if ring.startswith("bank"):
-                return psum.tile(shape, dtype, name=name)
-            return keep.tile(shape, dtype, name=name, align_bytes=256)
-
-        def mx_tiles(key):
+        def tile_of(key, shape, dtype):
             if key not in tiles:
-                name = "_".join(str(part) for part in key)
-                codes = keep.tile([P, WIDTH], U32, name=f"codes_{name}", align_bytes=256)
-                scales = keep.tile([P, WIDTH], U8, name=f"scales_{name}", align_bytes=256)
-                tiles[key] = (codes, scales)
+                name = buffer_of.get(key) or "_".join(str(part) for part in key)
+                if name.startswith("bank"):
+                    tiles[key] = psum.tile(shape, dtype, name=name)
+                else:
+                    tiles[key] = keep.tile(shape, dtype, name=name, align_bytes=256)
             return tiles[key]
 
-        def x_ring(pair):
-            return "x_odd" if pair % 2 else "x_even"
+        def mx_tiles(key):
+            return tile_of(("codes", *key), [P, WIDTH], U32), tile_of(("scales", *key), [P, WIDTH], U8)
+
+        def piece_of(slab, column):
+            edges = cuts.get(slab, (0, WIDTH))
+            return [(a, b) for a, b in zip(edges, edges[1:]) if column < b][0]
+
+        def grouped(slab, first, last):
+            a, b = piece_of(slab, first)
+            return tile_of(("grouped", *slab, a), [P, b - a, PACK], BF16)[:, first - a : last - a, :]
 
         def widen_factor(block):
             source = t16 if block == Z else r16
@@ -141,18 +148,10 @@ def tile_factoranalysisemloadinggradient_kernel(
         def mean_psi():
             nc.vector.tensor_scalar(out=psi_inv_mean[:], in0=psi_inv[:], scalar1=1.0 / N, scalar2=None, op0=MULT)
 
-        def interleave(slab, n):
+        def interleave(slab, engine, first, last):
             kind, a, b = slab
-            engine, ring, first, last = pieces[slab][n]
             source = (w_raw[a, b] if kind == "w" else tiles["flat", a, b][:])[:, :, first:last]
-            if slab in shared:
-                if n == 0:
-                    tiles["grouped", slab] = take(ring, [P, WIDTH, PACK], BF16)
-                tile = tiles["grouped", slab][:, first:last, :]
-            else:
-                tile = take(ring, [P, last - first, PACK], BF16)[:]
-                tiles["grouped", slab, n] = tile
-            target = tile.rearrange("q (c i) j -> q c j i", i=RUN)
+            target = grouped(slab, first, last).rearrange("q (c i) j -> q c j i", i=RUN)
             source = source.rearrange("q j (c i) -> q c j i", i=RUN)
             if engine == "gpsimd":
                 nc.gpsimd.tensor_scalar(out=target, in0=source, scalar1=1.0, scalar2=0.0, op0=MULT, op1=ADD)
@@ -161,46 +160,53 @@ def tile_factoranalysisemloadinggradient_kernel(
             else:
                 nc.scalar.copy(out=target, in_=source)
 
-        def quantize(slab, n):
+        def quantize(slab, first, last):
             codes, scales = mx_tiles(slab)
-            first, last = (0, WIDTH) if slab in shared else pieces[slab][n][2:]
-            source = tiles["grouped", slab][:] if slab in shared else tiles["grouped", slab, n]
             nc.vector.quantize_mx(
                 out=codes[:, first:last].bitcast(FP8X4),
                 scales=scales[:, first:last],
-                in_=source.rearrange("q c j -> q (c j)"),
+                in_=grouped(slab, first, last).rearrange("q c j -> q (c j)"),
             )
 
-        def widen_first(g):
-            tile = keep.tile([P, 2 * K_PASS], BF16, name=f"first_wide{g}", align_bytes=256)
-            for unit in range(2):
-                source = x_raw[0][:, unit * D + g * K_PASS : unit * D + (g + 1) * K_PASS]
-                nc.scalar.copy(out=tile[:, unit * K_PASS : (unit + 1) * K_PASS], in_=source.bitcast(FP8))
-            tiles["wide", 0, g] = [tile[:, unit * K_PASS : (unit + 1) * K_PASS] for unit in range(2)]
-
-        def widen(pair):
-            tile = take("wide", [P, 2 * D], BF16)
-            nc.scalar.copy(out=tile[:], in_=x_raw[pair].bitcast(FP8))
-            for g in range(PASSES):
-                starts = [unit * D + g * K_PASS for unit in range(2)]
-                tiles["wide", pair, g] = [tile[:, start : start + K_PASS] for start in starts]
+        def widen(pair, g):
+            passes = range(PASSES) if g is None else [g]
+            tile = tile_of(("wide", pair, g), [P, 2 * len(passes) * K_PASS], BF16)
+            runs = [(0, 0, 2 * D)] if g is None else [(unit * K_PASS, unit * D + g * K_PASS, K_PASS) for unit in range(2)]
+            for place, first, count in runs:
+                source = x_raw[pair][:, first : first + count].bitcast(FP8)
+                if (pair, g) in VECTOR_WIDENS:
+                    target = tile[:].rearrange("p (u w e) -> p w u e", u=2, e=2)
+                    nc.vector.tensor_scalar(
+                        out=target[:, place // PACK : (place + count) // PACK],
+                        in0=source.rearrange("p (w u e) -> p w u e", u=2, e=2),
+                        scalar1=one[:],
+                        scalar2=None,
+                        op0=MULT,
+                    )
+                else:
+                    nc.scalar.copy(out=tile[:, place : place + count], in_=source)
+            words = tile[:].bitcast(F32)
+            for n, (unit, h) in enumerate((unit, h) for unit in range(2) for h in passes):
+                for u in range(2):
+                    if (pair, g) in VECTOR_WIDENS:
+                        first = (2 * len(passes) * u + n) * P
+                        tiles["words", pair, h, unit, u] = words[:, first : first + P]
+                    else:
+                        tiles["words", pair, h, unit, u] = words[:, 2 * n * P + u : 2 * (n + 1) * P : 2]
 
         def turn(pair, g):
-            bank = take(bank_of[turn, pair, g], [P, 2, 2 * P], F32)
+            bank = tile_of(("turned", pair, g), [P, 2, 2 * P], F32)
             for unit in range(2):
-                words = tiles["wide", pair, g][unit].bitcast(F32)
                 for u in range(2):
-                    nc.tensor.transpose(bank[:, u, unit * P : (unit + 1) * P], words[:, u::2], identity[:])
-            tiles["turned", pair, g] = bank
+                    nc.tensor.transpose(
+                        bank[:, u, unit * P : (unit + 1) * P], tiles["words", pair, g, unit, u], identity[:]
+                    )
 
         def product(pair, g):
-            if g == 0:
-                tiles["x_grouped", pair] = take(x_ring(pair), [P, PASSES, 2 * P, 2, 2], BF16)
+            target = tile_of(("x_grouped", pair, g), [P, 2 * P, 2, 2], BF16)
             values = tiles["turned", pair, g][:].bitcast(BF16).rearrange("q u (c e) -> q c u e", e=2)
             scales = scale[:, g, :].rearrange("q (o u e) -> q o u e", o=1, u=2)
-            nc.vector.tensor_tensor(
-                out=tiles["x_grouped", pair][:, g], in0=values, in1=scales.to_broadcast([P, 2 * P, 2, 2]), op=MULT
-            )
+            nc.vector.tensor_tensor(out=target[:], in0=values, in1=scales.to_broadcast([P, 2 * P, 2, 2]), op=MULT)
 
         def x_quantize(pair, g):
             codes, scales = mx_tiles(("x", pair))
@@ -208,105 +214,99 @@ def tile_factoranalysisemloadinggradient_kernel(
             nc.vector.quantize_mx(
                 out=codes[:, cols].bitcast(FP8X4),
                 scales=scales[:, cols],
-                in_=tiles["x_grouped", pair][:, g : g + 1].rearrange("q g c u e -> q (g c u e)"),
+                in_=tiles["x_grouped", pair, g][:].rearrange("q c u e -> q (c u e)"),
             )
 
-        def multiply(unit, block, g):
-            if g == 0:
-                tiles["first", unit, block] = take(bank_of[multiply, unit, block, g], [P, WIDTH], F32)
-            x_codes, x_scales = tiles["x", unit // 2]
+        def first_pass(target, unit, block, g, w_cols):
+            x_codes, x_scales = mx_tiles(("x", unit // 2))
             cols = slice((2 * g + unit % 2) * P, (2 * g + unit % 2 + 1) * P)
-            w_codes, w_scales = tiles["w", block, g]
+            w_codes, w_scales = mx_tiles(("w", block, g))
             nc.tensor.matmul_mx(
-                out=tiles["first", unit, block][:],
+                out=target,
                 lhsT=x_codes[:, cols].bitcast(FP8X4),
                 lhsT_scale=x_scales[:, cols],
-                rhs=w_codes[:].bitcast(FP8X4),
-                rhs_scale=w_scales[:],
+                rhs=w_codes[:, w_cols].bitcast(FP8X4),
+                rhs_scale=w_scales[:, w_cols],
                 start=(g == 0),
                 stop=(g == PASSES - 1),
             )
 
+        def multiply(unit, block, g):
+            first_pass(tile_of(("first", unit, block), [P, WIDTH], F32)[:], unit, block, g, slice(0, WIDTH))
+
+        def multiply_strip(group, block, strip):
+            bank = tile_of(("strip", group, block, strip), [P, PACK, P], F32)
+            for j in range(PACK):
+                for g in range(PASSES):
+                    first_pass(bank[:, j, :], PACK * group + j, block, g, slice(strip * P, (strip + 1) * P))
+
         def empty(unit, block):
             group, j = divmod(unit, PACK)
-            if j == 0:
-                tiles["flat", group, block] = take("flat", [P, PACK, WIDTH], BF16)
             nc.scalar.activation(
-                out=tiles["flat", group, block][:, j, :],
+                out=tile_of(("flat", group, block), [P, PACK, WIDTH], BF16)[:, j, :],
                 in_=tiles["first", unit, block][:],
                 func=COPY,
                 scale=factor[block][:, unit : unit + 1],
             )
 
+        def empty_strip(group, block, strip):
+            target = grouped(("y", group, block), strip * P, (strip + 1) * P)
+            factors = factor[block][:, PACK * group : PACK * (group + 1)].rearrange("q (a j b) -> q a j b", a=1, b=1)
+            nc.vector.tensor_tensor(
+                out=target.rearrange("q (c i) j -> q c j i", i=STRIP_RUN),
+                in0=tiles["strip", group, block, strip][:].rearrange("q j (c i) -> q c j i", i=STRIP_RUN),
+                in1=factors.to_broadcast([P, P // STRIP_RUN, PACK, STRIP_RUN]),
+                op=MULT,
+            )
+
         def accumulate(group, band):
-            if group == 0:
-                tiles["sum", band] = take(bank_of[accumulate, group, band], [P, K], F32)
             block, place = divmod(band, BLOCK_BANDS)
             cols = slice(place * P, (place + 1) * P)
-            e_codes, e_scales = tiles["y", group, block]
-            z_codes, z_scales = tiles["y", group, Z]
+            e_codes, e_scales = mx_tiles(("y", group, block))
+            z_codes, z_scales = mx_tiles(("y", group, Z))
             nc.tensor.matmul_mx(
-                out=tiles["sum", band][:],
+                out=tile_of(("sum", band), [P, K], F32)[:],
                 lhsT=e_codes[:, cols].bitcast(FP8X4),
                 lhsT_scale=e_scales[:, cols],
                 rhs=z_codes[:].bitcast(FP8X4),
                 rhs_scale=z_scales[:],
-                start=(group == 0),
-                stop=(group == GROUPS - 1),
+                start=(group == group_order[band][0]),
+                stop=(group == group_order[band][-1]),
             )
 
-        def prepare_last():
-            tiles["v_over_psi"] = keep.tile([P, K], F32, name="v_over_psi")
+        def prepare(band):
             nc.scalar.activation(
-                out=tiles["v_over_psi"][:],
-                in_=v_raw[:, LAST_BAND, :],
+                out=tile_of(("result", band), [P, K], F32)[:],
+                in_=v_raw[:, band, :],
                 func=COPY,
-                scale=psi_inv[:, LAST_BAND : LAST_BAND + 1],
+                scale=psi_inv[:, band : band + 1],
             )
 
-        def subtract(band):
-            tile = keep.tile([P, K], F32, name=f"result{band}")
-            if band == LAST_BAND:
-                mean, other = psi_inv_mean[:, band : band + 1], tiles["v_over_psi"][:]
+        def subtract(band, first, last):
+            tile = tile_of(("result", band), [P, K], F32)[:, first:last]
+            if band in PREPARED:
+                mean, other = psi_inv_mean[:, band : band + 1], tile
             else:
-                mean, other = 1.0 / N, v_raw[:, band, :]
+                mean, other = 1.0 / N, v_raw[:, band, first:last]
             nc.vector.scalar_tensor_tensor(
-                out=tile[:], in0=tiles["sum", band][:], scalar=mean, in1=other, op0=MULT, op1=SUBTRACT
+                out=tile, in0=tiles["sum", band][:, first:last], scalar=mean, in1=other, op0=MULT, op1=SUBTRACT
             )
-            tiles["result", band] = tile
 
-        def divide(band):
+        def divide(band, engine):
             tile, inverse = tiles["result", band], psi_inv[:, band : band + 1]
-            if band in VECTOR_DIVIDES:
+            if engine == "vector":
                 nc.vector.tensor_scalar(out=tile[:], in0=tile[:], scalar1=inverse, scalar2=None, op0=MULT)
             else:
                 nc.scalar.activation(out=tile[:], in_=tile[:], func=COPY, scale=inverse)
 
-        def store(band):
-            nc.sync.dma_start(out=out[band * P : (band + 1) * P, :], in_=tiles["result", band][:])
+        def store(band, first, last):
+            nc.sync.dma_start(out=out[band * P : (band + 1) * P, first:last], in_=tiles["result", band][:, first:last])
 
-        slabs = [("w", block, g) for block in (0, 1, Z) for g in range(PASSES)]
-        slabs += [("y", group, block) for block in (0, 1, Z) for group in range(GROUPS)]
-        pieces = {slab: [("vector", "by_vector", 0, WIDTH)] for slab in slabs}
-        shared = [("w", 1, 0), ("w", 1, 1), ("y", 0, Z), ("y", 0, 0), ("y", 1, Z), ("y", 1, 0)]
-        for slab in shared:
-            pieces[slab] = [("gpsimd", "gate_b", 0, GPSIMD_COLUMNS), ("vector", "gate_b", GPSIMD_COLUMNS, WIDTH)]
-        pieces["w", Z, 0] = [("vector", "by_vector", 0, HALF), ("scalar", "gate_a", HALF, WIDTH)]
-        pieces["w", Z, 1] = [("gpsimd", "gate_a", 0, WIDTH - QUARTER), ("scalar", "gate_c", WIDTH - QUARTER, WIDTH)]
-        pieces["w", 0, 0] = [
-            ("scalar", "gate_b", 0, HALF),
-            ("gpsimd", "gate_c", HALF, WIDTH - QUARTER),
-            ("vector", "by_vector", WIDTH - QUARTER, WIDTH),
-        ]
-        pieces["w", 0, 1] = [("vector", "by_vector", 0, HALF), ("scalar", "by_scalar", HALF, WIDTH)]
-        pieces["y", 2, 1] = [("scalar", "by_scalar", 0, HALF), ("scalar", "by_scalar", HALF, WIDTH)]
-        pieces["y", 3, 1] = [("scalar", "gate_a", 0, HALF), ("scalar", "by_scalar", HALF, WIDTH)]
+        def mix(slab, engine, first=0, last=WIDTH):
+            return (interleave, slab, engine, first, last)
 
-        def mix(kind, a, b, n=0):
-            return (interleave, (kind, a, b), n)
-
-        def quant(kind, a, b, n=0):
-            return (quantize, (kind, a, b), n)
+        def quant(slab, first=0, last=WIDTH):
+            return (quantize, slab, first, last)
 
         def both(step, pair):
             return [(step, pair, g) for g in range(PASSES)]
@@ -314,25 +314,50 @@ def tile_factoranalysisemloadinggradient_kernel(
         def first_stage(group, block, rows=range(PACK)):
             return [(multiply, PACK * group + j, block, g) for j in rows for g in range(PASSES)]
 
-        def each_piece(step, slab):
-            count = 1 if step is quantize and slab in shared else len(pieces[slab])
-            return [(step, slab, n) for n in range(count)]
+        def strips(step, group, block, which=range(STRIPS)):
+            return [(step, group, block, strip) for strip in which]
 
-        gpsimd = [mix("w", Z, 1, 0), mix("w", 0, 0, 1)] + [mix(*slab) for slab in shared]
 
-        tensor = both(turn, 0) + both(turn, 1) + [(multiply, unit, Z, 0) for unit in range(2)]
-        tensor += both(turn, 2) + [(multiply, unit, Z, 1) for unit in range(2)]
-        tensor += both(turn, 3) + first_stage(0, Z, (2, 3)) + first_stage(0, 0)
-        for pair in range(2, PAIRS - 2):
-            group, rows = pair // 2, (2, 3) if pair % 2 else (0, 1)
-            tensor += both(turn, pair + 2) + first_stage(group, Z, rows) + first_stage(group, 0, rows)
-            if pair in (3, 4):
-                tensor += first_stage(0, 1, (0, 1) if pair == 3 else (2, 3))
-        for group, block in ((1, 1), (3, Z), (3, 0), (2, 1), (3, 1)):
-            tensor += first_stage(group, block)
+        def rotate(name, count, keys):
+            for n, key in enumerate(keys):
+                tenants.setdefault(f"{name}{n % count}", []).append(key)
 
-        scalar = [(widen_first, 0), (widen_first, 1), mix("w", Z, 0, 1), (widen, 1), mix("w", Z, 1, 1), (widen, 2)]
-        scalar += [mix("w", 0, 0, 0), (widen, 3), mix("w", 0, 1, 1), (widen, 4)]
+        def sub(band, first=0, last=WIDTH):
+            return (subtract, band, first, last)
+
+        def y(group, block):
+            return ("y", group, block)
+
+        tenants, cuts = {}, {}
+        wz0, wz1, w00, w01, w10, w11 = [("w", block, g) for block in (Z, 0, 1) for g in range(PASSES)]
+
+        shared = [w10, w11, y(0, Z), y(0, 0), y(1, Z), y(1, 0)]
+        gpsimd = [mix(s, "gpsimd", 0, GC) for s in [wz0, w00] + shared] + [mix(y(0, 1), "gpsimd", 0, GC), mix(y(3, 0), "gpsimd", 0, GC)]
+        for s in (wz0, w00, w01):
+            cuts[s] = (0, GC, WIDTH)
+
+        def rest(s):
+            return mix(s, "scalar", GC, WIDTH)
+
+        def q2(s):
+            return [quant(s, GC, WIDTH), quant(s, 0, GC)]
+
+        def pair_stage(pair, blocks=(Z, 0)):
+            return [step for block in blocks for step in first_stage(pair // 2, block, (2, 3) if pair % 2 else (0, 1))]
+
+        tensor = both(turn, 0) + both(turn, 1) + both(turn, 2) + [(multiply, unit, Z, 0) for unit in range(2)]
+        tensor += both(turn, 3) + [(multiply, unit, Z, 1) for unit in range(2)] + first_stage(0, Z, (2, 3))
+        tensor += both(turn, 4) + first_stage(0, 0) + pair_stage(2)
+        tensor += both(turn, 5) + pair_stage(3) + pair_stage(0, (1,))
+        tensor += both(turn, 6) + pair_stage(4)
+        tensor += both(turn, 7) + pair_stage(1, (1,)) + pair_stage(5) + pair_stage(2, (1,)) + pair_stage(6)
+        tensor += strips(multiply_strip, 2, 1) + pair_stage(7) + pair_stage(3, (1,)) + strips(multiply_strip, 3, 1)
+        FREED = (multiply_strip, 2, 1, 0)
+
+        scalar = [(widen, 0, 1), rest(wz0), (widen, 2, None), mix(wz1, "scalar"), (widen, 3, None)]
+        scalar += [rest(w00), rest(w01), (widen, 4, None)]
+        extra = {(empty, 3, Z): [(widen, 5, None)], (empty, 5, 0): [(widen, 6, None)], (empty, 1, 1): [(widen, 7, None)],
+                 (empty, 9, 0): [(prepare, 7)], (empty, 13, 0): [mix(y(2, 0), "scalar")]}
         for step in tensor:
             if step == (multiply, 0, Z, 1):
                 scalar.append((widen_factor, Z))
@@ -340,127 +365,138 @@ def tile_factoranalysisemloadinggradient_kernel(
                 scalar.append((widen_factor, 0))
             if step[0] is multiply and step[3] == PASSES - 1:
                 scalar.append((empty, *step[1:3]))
-            if step[0] is turn and step[2] == 0 and step[1] >= 4:
-                scalar.append((widen, step[1] + 1) if step[1] + 1 < PAIRS else (prepare_last,))
-        scalar += [mix("y", group, 1, n) for n in range(2) for group in (2, 3)]
-        scalar += [(divide, band) for band in range(LAST_BAND) if band not in VECTOR_DIVIDES]
+                scalar += extra.get(scalar[-1], [])
+        scalar += [mix(y(3, Z), "scalar"), mix(y(1, 1), "scalar")]
+        scalar += [(prepare, band) for band in range(7)]
 
-        tensor += [(accumulate, 0, band) for band in range(BLOCK_BANDS)]
-        tensor += [(accumulate, group, band) for band in range(BLOCK_BANDS) for group in range(1, GROUPS)]
-        tensor += [(accumulate, group, band) for band in range(BLOCK_BANDS, BANDS) for group in range(GROUPS)]
+        tensor += [(accumulate, group, band) for group in range(3) for band in range(BLOCK_BANDS)]
+        tensor += [(accumulate, 3, band) for band in range(BLOCK_BANDS)]
+        tensor += [(accumulate, group, band) for band in range(BLOCK_BANDS, BANDS) for group in (0, 2, 3, 1)]
+        group_order = {band: [step[1] for step in tensor if step[0] is accumulate and step[2] == band] for band in range(BANDS)}
 
-        bank_of, turns, sums, freed = {}, 0, 0, None
-        for step in tensor:
-            if step == (multiply, PACK * (GROUPS - 1), Z, 0):
-                freed = sums
+        def made(step):
             if step[0] is turn:
-                bank_of[step] = f"bank{turns % TURN_BANKS}"
-                turns = turns + 1
-            elif (step[0] is multiply and step[3] == 0) or (step[0] is accumulate and step[1] == 0):
-                if freed is None:
-                    bank_of[step] = f"bank{TURN_BANKS + sums % (BANKS - TURN_BANKS)}"
-                else:
-                    bank_of[step] = f"bank{(sums - freed) % BANKS}"
-                sums = sums + 1
+                return ("turned", *step[1:])
+            if step[0] is multiply and step[3] == 0:
+                return ("first", *step[1:3])
+            if step[0] is multiply_strip:
+                return ("strip", *step[1:])
+            if step[0] is accumulate and step[1] == group_order[step[2]][0]:
+                return ("sum", step[2])
+            return None
 
-        vector = [mix("w", Z, 0), (product, 0, 0), quant("w", Z, 0), quant("w", Z, 0, 1), (x_quantize, 0, 0)]
-        vector += [(product, 0, 1), (product, 1, 0), (x_quantize, 0, 1), quant("w", Z, 1, 1), quant("w", Z, 1, 0)]
-        vector += [(product, 1, 1), (x_quantize, 1, 0), mix("w", 0, 1, 0), (x_quantize, 1, 1), mix("w", 0, 0, 2)]
-        vector += [quant("w", 0, 0, 1), quant("w", 0, 1, 1), quant("w", 0, 0, 2), quant("w", 0, 0, 0), quant("w", 0, 1, 0)]
+        ring = {"turned": list(TURN_RING), "sums": list(SUM_RING)}
+        for step in tensor:
+            if step == FREED:
+                ring["sums"] = list(FREED_RING)
+            key = made(step)
+            if key is not None:
+                banks = ring["turned" if key[0] == "turned" else "sums"]
+                if key in HEAD_BANKS:
+                    bank = HEAD_BANKS[key]
+                else:
+                    bank = banks[0]
+                    banks.remove(bank)
+                    banks.append(bank)
+                tenants.setdefault(f"bank{bank}", []).append(key)
+
+        vector = [(widen, 0, 0), (widen, 1, None)] + both(product, 0) + [(x_quantize, 0, 0)] + q2(wz0) + [(x_quantize, 0, 1)]
+        vector += both(product, 1) + [quant(wz1), (x_quantize, 1, 0), (x_quantize, 1, 1), mix(w01, "vector", 0, GC), quant(w01, GC, WIDTH)] + q2(w00) + [quant(w01, 0, GC)]
         small = {4: [(invert_psi,)], 5: [(mean_psi,)]}
         for pair in range(2, PAIRS):
             slab = shared[pair - 2]
-            vector += both(product, pair) + [mix(*slab, 1)] + small.get(pair, [])
-            if pair < PAIRS - 1:
-                vector += [(x_quantize, pair, 0), quant(*slab), (x_quantize, pair, 1)]
-            else:
-                vector += both(x_quantize, pair) + [quant(*slab)]
-        piled = [(2, Z), (2, 0), (3, Z), (3, 0), (0, 1), (1, 1)]
-        vector.append(mix("y", *piled[0]))
-        for before, panel in zip(piled, piled[1:]):
-            vector += [mix("y", *panel), quant("y", *before)]
-        vector += [(subtract, 0), quant("y", 1, 1), quant("y", 2, 1, 0), (divide, 0), quant("y", 3, 1, 0)]
-        vector += [(subtract, 1), (subtract, 2), (divide, 1), quant("y", 2, 1, 1), (subtract, 3), quant("y", 3, 1, 1)]
-        vector += [(subtract, band) for band in range(BLOCK_BANDS, BANDS)]
+            vector += both(product, pair) + [mix(slab, "vector", GC, WIDTH)] + small.get(pair, [])
+            vector += both(x_quantize, pair) + [quant(slab)]
+        vector += [mix(y(2, Z), "vector")]
+        vector += strips(empty_strip, 2, 1) + [mix(y(0, 1), "vector", GC, WIDTH), quant(y(2, Z)), quant(y(2, 1)), quant(y(0, 1)), quant(y(2, 0))]
+        vector += strips(empty_strip, 3, 1) + [mix(y(3, 0), "vector", GC, WIDTH), quant(y(3, Z)), quant(y(3, 0)), quant(y(3, 1)), sub(0), quant(y(1, 1)), sub(1)]
+        vector += [sub(band) for band in range(2, 7)] + [sub(7, 0, HALF), sub(7, HALF, WIDTH)]
+        sync = [(store, band, 0, WIDTH) for band in range(7)] + [(store, 7, 0, HALF), (store, 7, HALF, WIDTH)]
 
-        sync = [(store, band) for band in range(BANDS)]
-
-        behind = {
-            mix("w", Z, 1, 0): [quant("w", Z, 0, 1)],
-            mix("w", 0, 0, 1): [quant("w", Z, 1, 1)],
-            mix("w", 1, 0, 0): [quant("w", 0, 0, 0)],
-            mix("y", 3, 1, 0): [quant("w", Z, 1, 0)],
-        }
-
-        def needs(step):
-            name, args = step[0], step[1:]
-            if name is turn:
-                return [(widen, args[0]) if args[0] else (widen_first, args[1])]
-            if name is product:
-                return [(turn, *args)]
-            if name is x_quantize:
-                return [(product, *args)]
-            if name is interleave:
-                (kind, a, b), n = args
-                buffer = [(interleave, args[0], 0)] if args[0] in shared and n > 0 else []
-                return buffer + ([(empty, PACK * a + j, b) for j in range(PACK)] if kind == "y" else [])
-            if name is quantize:
-                return each_piece(interleave, args[0]) if args[0] in shared else [(interleave, *args)]
-            if name is multiply:
-                return [(x_quantize, args[0] // 2, args[2])] + each_piece(quantize, ("w", *args[1:]))
-            if name is empty:
-                return [(multiply, *args, PASSES - 1), (widen_factor, Z if args[1] == Z else 0)]
-            if name is accumulate:
-                block, place = divmod(args[1], BLOCK_BANDS)
-                slab = ("y", args[0], block)
-                n = 0 if slab in shared else [piece[3] > place * P for piece in pieces[slab]].index(True)
-                return [(quantize, slab, n)] + each_piece(quantize, ("y", args[0], Z))
-            if name is subtract:
-                last = [(prepare_last,), (mean_psi,)] if args[0] == LAST_BAND else []
-                return [(accumulate, GROUPS - 1, *args)] + last
-            if name is prepare_last or name is mean_psi:
-                return [(invert_psi,)]
-            if name is divide:
-                return [(subtract, *args), (invert_psi,)]
-            if name is store:
-                return [(subtract if args[0] == LAST_BAND else divide, *args)]
-            return []
-
-        def claims(step):
-            name, args = step[0], step[1:]
-            if name is turn:
-                return bank_of[step], [(product, *args)]
-            if name is multiply and args[2] == 0:
-                return bank_of[step], [(empty, *args[:2])]
-            if name is accumulate and args[0] == 0:
-                return bank_of[step], [(subtract, args[1])]
-            if name is widen:
-                return "wide", both(turn, args[0])
-            if name is product and args[1] == 0:
-                return x_ring(args[0]), both(x_quantize, args[0])
-            if name is empty and args[0] % PACK == 0:
-                return "flat", each_piece(interleave, ("y", args[0] // PACK, args[1]))
-            if name is interleave and not (args[0] in shared and args[1] > 0):
-                return pieces[args[0]][args[1]][1], [(quantize, *args)]
-            return None, None
+        rotate("wide", 3, [("wide", pair, None) for pair in range(1, PAIRS)])
+        rotate("xg", 2, [("x_grouped", pair, 0) for pair in range(PAIRS)])
+        rotate("flat", 8, [("flat", step[1] // PACK, step[2]) for step in scalar if step[0] is empty and step[1] % PACK == 0])
+        tenants["gate_h"] = [("grouped", *s, 0) for s in [wz0, w00, w10, y(2, Z), y(3, Z)]]
+        tenants["gate_a"] = [("x_grouped", 0, 1), ("x_grouped", 2, 1), ("grouped", *w11, 0), ("x_grouped", 4, 1), ("grouped", *y(0, 0), 0), ("x_grouped", 6, 1), ("grouped", *y(1, 0), 0), ("grouped", *y(0, 1), 0), ("grouped", *y(3, 0), 0)]
+        tenants["gate_b"] = [("x_grouped", 1, 1), ("x_grouped", 3, 1), ("grouped", *y(0, Z), 0), ("x_grouped", 5, 1), ("grouped", *y(1, Z), 0), ("x_grouped", 7, 1), ("grouped", *y(1, 1), 0)]
+        rotate("other", 3, [("grouped", *s, 0) for s in [wz1, w01, y(2, 0), y(2, 1), y(3, 1)]])
 
         queues = [vector, scalar, tensor, gpsimd, sync]
-        written, readers = set(), {ring: [] for ring in RINGS}
+        tenant_before = {}
+        for buffer, keys in tenants.items():
+            for before, key in zip([None] + keys, keys):
+                buffer_of[key], tenant_before[key] = buffer, before
+
+        group_order = {band: [step[1] for step in tensor if step[0] is accumulate and step[2] == band] for band in range(BANDS)}
+        def touches(step):
+            name, args = step[0], step[1:]
+            whole = (0, WIDTH)
+            if name is widen:
+                return [], [(("wide", *args), *whole)]
+            if name is turn:
+                return [(("wide", args[0], None), *whole), (("wide", *args), *whole)], [(("turned", *args), *whole)]
+            if name is product:
+                return [(("turned", *args), *whole)], [(("x_grouped", *args), *whole)]
+            if name is x_quantize:
+                return [(("x_grouped", *args), *whole)], [(("x", *args), *whole)]
+            if name is interleave:
+                slab, first, last = args[0], args[2], args[3]
+                source = [(("flat", *slab[1:]), *whole)] if slab[0] == "y" else []
+                return source, [(("grouped", *slab, piece_of(slab, first)[0]), first, last)]
+            if name is quantize:
+                return [(("grouped", *args[0], piece_of(*args[:2])[0]), *args[1:])], [args]
+            if name is multiply:
+                unit, block, g = args
+                before = [(("first", unit, block), 0, g)] if g else []
+                return before + [(("x", unit // 2, g), *whole), (("w", block, g), *whole)], [(("first", unit, block), g, g + 1)]
+            if name is multiply_strip:
+                group, block = args[:2]
+                x_keys = [("x", 2 * group + n, g) for n in range(2) for g in range(PASSES)]
+                w_keys = [("w", block, g) for g in range(PASSES)]
+                return [(key, *whole) for key in x_keys + w_keys], [(("strip", *args), *whole)]
+            if name is empty:
+                return [(("first", *args), *whole), (("factor", args[1] == Z), *whole)], [(("flat", args[0] // PACK, args[1]), *whole)]
+            if name is empty_strip:
+                group, block, strip = args
+                return [(("strip", *args), *whole), (("factor", block == Z), *whole)], [(("grouped", "y", group, block, piece_of(("y", group, block), strip * P)[0]), strip * P, (strip + 1) * P)]
+            if name is widen_factor:
+                return [], [(("factor", args[0] == Z), *whole)]
+            if name is accumulate:
+                group, band = args
+                block, place = divmod(band, BLOCK_BANDS)
+                n = group_order[band].index(group)
+                before = [(("sum", band), 0, n)] if n else []
+                return before + [(("y", group, block), place * P, (place + 1) * P), (("y", group, Z), *whole)], [(("sum", band), n, n + 1)]
+            if name is invert_psi:
+                return [], [(("psi_inv",), *whole)]
+            if name is mean_psi:
+                return [(("psi_inv",), *whole)], [(("psi_inv_mean",), *whole)]
+            if name is prepare:
+                return [(("psi_inv",), *whole)], [(("prepared", args[0]), *whole)]
+            if name is subtract:
+                band = args[0]
+                made = [(("prepared", band), *whole), (("psi_inv_mean",), *whole)] if band in PREPARED else []
+                return [(("sum", band), *whole)] + made, [(("result" if band in PREPARED else "difference", band), *args[1:])]
+            if name is divide:
+                return [(("difference", args[0]), *whole), (("psi_inv",), *whole)], [(("result", args[0]), *whole)]
+            return [(("result", args[0]), *args[1:])], []
+
+        steps = [step for queue in queues for step in queue]
+        waits = {step: set() for step in steps}
+        for step in steps:
+            read, written = touches(step)
+            for other in steps:
+                other_read, other_written = touches(other)
+                for key, first, last in read:
+                    if any(key == k and first < b and a < last for k, a, b in other_written):
+                        waits[step].add(other)
+                for key, first, last in written:
+                    if any(k == tenant_before.get(key) for k, a, b in other_read + other_written):
+                        waits[step].add(other)
+        done = set()
         while any(queues):
-            progress = False
-            for queue in queues:
-                while queue:
-                    step = queue[0]
-                    ring, reader = claims(step)
-                    waits = needs(step) + behind.get(step, [])
-                    if ring is not None and len(readers[ring]) >= RINGS[ring]:
-                        waits = waits + readers[ring][-RINGS[ring]]
-                    if not all(wait in written for wait in waits):
-                        break
-                    step[0](*step[1:])
-                    written.add(step)
-                    if ring is not None:
-                        readers[ring].append(reader)
-                    queue.remove(step)
-                    progress = True
-            assert progress
+            ready = [queue for queue in queues if queue and all(wait in done for wait in waits[queue[0]])]
+            step = ready[0][0]
+            step[0](*step[1:])
+            done.add(step)
+            ready[0].remove(step)

@@ -36,13 +36,14 @@ BANKS = 8
 RUN = 4
 VECTOR_WIDENS = ((0, 0), (1, None))
 PREPARED = (0, 1, 2, 3, 4, 5, 6, 7)
-STRIP_RUN = 4
+STRIP_RUN = 1
 GC = 384
-HEAD_BANKS = {("turned", 2, 0): 4, ("turned", 2, 1): 5, ("first", 0, 2): 6, ("first", 1, 2): 7, ("turned", 3, 0): 0, ("turned", 3, 1): 1,
-  ("first", 2, 2): 2, ("first", 3, 2): 3, ("turned", 4, 0): 6, ("turned", 4, 1): 7, ("turned", 0, 0): 0, ("turned", 0, 1): 1, ("turned", 1, 0): 2, ("turned", 1, 1): 3}
+HEAD_BANKS = {("warm", 0): 6, ("warm", 1): 7, ("warm", 2): 6, ("warm", 3): 7, ("warm", 4): 7, ("warm", 5): 2, ("turned", 2, 0): 4, ("turned", 2, 1): 5, ("first", 0, 2): 6, ("first", 1, 2): 7, ("turned", 3, 0): 0, ("turned", 3, 1): 1,
+  ("first", 2, 2): 2, ("first", 3, 2): 3, ("turned", 4, 0): 6, ("turned", 4, 1): 7, ("first", 0, 0): 2, ("first", 1, 0): 3, ("first", 2, 0): 4, ("first", 3, 0): 2, ("turned", 0, 0): 0, ("turned", 0, 1): 1, ("turned", 1, 0): 2, ("turned", 1, 1): 3}
 TURN_RING = (0, 1, 6, 7)
-SUM_RING = (2, 3, 4, 5)
-FREED_RING = (6, 7, 0, 1, 2, 3, 4, 5)
+SUM_RING = (3, 5, 4, 2)
+FREED_RING = (6, 3, 7, 5, 4, 2)
+WARM = False
 
 
 def tile_factoranalysisemloadinggradient_kernel(
@@ -54,6 +55,8 @@ def tile_factoranalysisemloadinggradient_kernel(
         psum = ctx.enter_context(tc.psum_pool(name="psum", bufs=1))
         ctx.enter_context(tc.manual_schedule())
 
+        zeros = keep.tile([P, HALF], F32, name="zeros")
+        nc.vector.memset(zeros[:], 0.0)
         identity = keep.tile([P, P], F32, name="identity")
         make_identity(nc, identity[:])
         one = keep.tile([P, 1], F32, name="one")
@@ -202,6 +205,11 @@ def tile_factoranalysisemloadinggradient_kernel(
                         bank[:, u, unit * P : (unit + 1) * P], tiles["words", pair, g, unit, u], identity[:]
                     )
 
+        def warm(n):
+            nc.tensor.matmul(
+                out=tile_of(("warm", n), [P, HALF], F32)[:], lhsT=zeros[:, :P], rhs=zeros[:], start=True, stop=True
+            )
+
         def product(pair, g):
             target = tile_of(("x_grouped", pair, g), [P, 2 * P, 2, 2], BF16)
             values = tiles["turned", pair, g][:].bitcast(BF16).rearrange("q u (c e) -> q c u e", e=2)
@@ -259,17 +267,17 @@ def tile_factoranalysisemloadinggradient_kernel(
                 op=MULT,
             )
 
-        def accumulate(group, band):
+        def accumulate(group, band, first=0, last=K):
             block, place = divmod(band, BLOCK_BANDS)
             cols = slice(place * P, (place + 1) * P)
             e_codes, e_scales = mx_tiles(("y", group, block))
             z_codes, z_scales = mx_tiles(("y", group, Z))
             nc.tensor.matmul_mx(
-                out=tile_of(("sum", band), [P, K], F32)[:],
+                out=tile_of(("sum", band, first), [P, last - first], F32)[:],
                 lhsT=e_codes[:, cols].bitcast(FP8X4),
                 lhsT_scale=e_scales[:, cols],
-                rhs=z_codes[:].bitcast(FP8X4),
-                rhs_scale=z_scales[:],
+                rhs=z_codes[:, first:last].bitcast(FP8X4),
+                rhs_scale=z_scales[:, first:last],
                 start=(group == group_order[band][0]),
                 stop=(group == group_order[band][-1]),
             )
@@ -289,7 +297,7 @@ def tile_factoranalysisemloadinggradient_kernel(
             else:
                 mean, other = 1.0 / N, v_raw[:, band, first:last]
             nc.vector.scalar_tensor_tensor(
-                out=tile, in0=tiles["sum", band][:, first:last], scalar=mean, in1=other, op0=MULT, op1=SUBTRACT
+                out=tile, in0=tiles["sum", band, first][:], scalar=mean, in1=other, op0=MULT, op1=SUBTRACT
             )
 
         def divide(band, engine):
@@ -331,13 +339,13 @@ def tile_factoranalysisemloadinggradient_kernel(
         tenants, cuts = {}, {}
         wz0, wz1, w00, w01, w10, w11 = [("w", block, g) for block in (Z, 0, 1) for g in range(PASSES)]
 
-        shared = [w10, w11, y(0, Z), y(0, 0), y(1, Z), y(1, 0)]
-        gpsimd = [mix(s, "gpsimd", 0, GC) for s in [wz0, w00] + shared] + [mix(y(0, 1), "gpsimd", 0, GC), mix(y(3, 0), "gpsimd", 0, GC)]
-        for s in (wz0, w00, w01):
+        full = [y(0, Z), y(0, 0), y(1, 0), y(2, Z)]
+        gpsimd = [mix(s, "gpsimd", 0, GC) for s in [wz0, w00, w10, w11]] + [mix(s, "gpsimd") for s in full] + [mix(s, "gpsimd", 0, GC) for s in (y(2, 0), y(3, 0))]
+        for s in (wz0, w00, w01, w10, y(2, 0), y(3, 0)):
             cuts[s] = (0, GC, WIDTH)
 
-        def rest(s):
-            return mix(s, "scalar", GC, WIDTH)
+        def rest(s, engine="scalar"):
+            return mix(s, engine, GC, WIDTH)
 
         def q2(s):
             return [quant(s, GC, WIDTH), quant(s, 0, GC)]
@@ -345,50 +353,61 @@ def tile_factoranalysisemloadinggradient_kernel(
         def pair_stage(pair, blocks=(Z, 0)):
             return [step for block in blocks for step in first_stage(pair // 2, block, (2, 3) if pair % 2 else (0, 1))]
 
-        tensor = both(turn, 0) + both(turn, 1) + both(turn, 2) + [(multiply, unit, Z, 0) for unit in range(2)]
+        def by_pass(pair, block):
+            return [(multiply, 2 * pair + n, block, g) for g in range(PASSES) for n in range(2)]
+
+        def acc(group, band, first=0, last=K):
+            return (accumulate, group, band, first, last)
+
+        def w(n):
+            return [(warm, n)] if WARM else []
+
+        tensor = w(0) + w(1) + both(turn, 0) + w(2) + both(turn, 1) + w(3) + both(turn, 2) + w(4) + [(multiply, unit, Z, 0) for unit in range(2)] + w(5)
         tensor += both(turn, 3) + [(multiply, unit, Z, 1) for unit in range(2)] + first_stage(0, Z, (2, 3))
-        tensor += both(turn, 4) + first_stage(0, 0) + pair_stage(2)
-        tensor += both(turn, 5) + pair_stage(3) + pair_stage(0, (1,))
-        tensor += both(turn, 6) + pair_stage(4)
-        tensor += both(turn, 7) + pair_stage(1, (1,)) + pair_stage(5) + pair_stage(2, (1,)) + pair_stage(6)
-        tensor += strips(multiply_strip, 2, 1) + pair_stage(7) + pair_stage(3, (1,)) + strips(multiply_strip, 3, 1)
-        FREED = (multiply_strip, 2, 1, 0)
+        tensor += both(turn, 4) + first_stage(0, 0) + by_pass(2, Z) + pair_stage(2, (0,))
+        tensor += both(turn, 5) + pair_stage(3) + strips(multiply_strip, 0, 1, (0,)) + pair_stage(2, (1,))
+        tensor += both(turn, 6) + pair_stage(4, (Z,)) + strips(multiply_strip, 0, 1, (1,)) + pair_stage(4, (0,))
+        tensor += both(turn, 7) + pair_stage(5, (Z,)) + strips(multiply_strip, 0, 1, (2,)) + pair_stage(5, (0,)) + pair_stage(3, (1,)) + pair_stage(6, (Z,)) + strips(multiply_strip, 0, 1, (3,)) + pair_stage(6, (0,))
+        tensor += strips(multiply_strip, 2, 1) + pair_stage(7) + strips(multiply_strip, 3, 1)
 
         scalar = [(widen, 0, 1), rest(wz0), (widen, 2, None), mix(wz1, "scalar"), (widen, 3, None)]
-        scalar += [rest(w00), rest(w01), (widen, 4, None)]
-        extra = {(empty, 3, Z): [(widen, 5, None)], (empty, 5, 0): [(widen, 6, None)], (empty, 1, 1): [(widen, 7, None)],
-                 (empty, 9, 0): [(prepare, 7)], (empty, 13, 0): [mix(y(2, 0), "scalar")]}
+        scalar += [rest(w00), rest(w01), (widen_factor, Z), (widen, 4, None)]
+        extra = {(empty, 3, Z): [rest(w10)], (empty, 3, 0): [(widen, 5, None)], (empty, 5, 0): [(widen, 6, None)], (empty, 5, 1): [(widen, 7, None)],
+                 (empty, 9, Z): [mix(y(1, Z), "scalar", 0, QUARTER)], (empty, 9, 0): [mix(y(1, Z), "scalar", QUARTER, WIDTH - QUARTER)], (empty, 11, Z): [mix(y(1, Z), "scalar", WIDTH - QUARTER, WIDTH)], (empty, 13, Z): [rest(y(2, 0))], (empty, 13, 0): [mix(y(1, 1), "scalar")]}
         for step in tensor:
-            if step == (multiply, 0, Z, 1):
-                scalar.append((widen_factor, Z))
             if step == (multiply, 3, Z, 1):
                 scalar.append((widen_factor, 0))
             if step[0] is multiply and step[3] == PASSES - 1:
                 scalar.append((empty, *step[1:3]))
                 scalar += extra.get(scalar[-1], [])
-        scalar += [mix(y(3, Z), "scalar"), mix(y(1, 1), "scalar")]
-        scalar += [(prepare, band) for band in range(7)]
+        scalar += [mix(y(3, Z), "scalar"), rest(y(3, 0))]
+        scalar += [(prepare, band) for band in range(8)]
 
-        tensor += [(accumulate, group, band) for group in range(3) for band in range(BLOCK_BANDS)]
-        tensor += [(accumulate, 3, band) for band in range(BLOCK_BANDS)]
-        tensor += [(accumulate, group, band) for band in range(BLOCK_BANDS, BANDS) for group in (0, 2, 3, 1)]
-        group_order = {band: [step[1] for step in tensor if step[0] is accumulate and step[2] == band] for band in range(BANDS)}
+        tensor += [acc(group, band) for group in range(3) for band in range(BLOCK_BANDS)]
+        tensor += [acc(3, band) for band in range(BLOCK_BANDS)]
+        tensor += [acc(group, band) for band in (4, 5, 6) for group in (0, 2, 1, 3)]
+        tensor += [acc(group, 7, first, first + HALF) for first in (0, HALF) for group in (0, 2, 1, 3)]
+        freed = {(multiply, 10, 0, 0): [6], (multiply, 7, 1, 0): [7], (multiply, 13, 0, 0): [0], (multiply_strip, 2, 1, 1): [1]}
+        hold = {("strip", 0, 1, 1): 1}
+        group_order = {band: [step[1] for step in tensor if step[0] is accumulate and step[2:4] == (band, 0)] for band in range(BANDS)}
 
         def made(step):
             if step[0] is turn:
                 return ("turned", *step[1:])
+            if step[0] is warm:
+                return ("warm", step[1])
             if step[0] is multiply and step[3] == 0:
                 return ("first", *step[1:3])
             if step[0] is multiply_strip:
                 return ("strip", *step[1:])
             if step[0] is accumulate and step[1] == group_order[step[2]][0]:
-                return ("sum", step[2])
+                return ("sum", *step[2:4])
             return None
 
         ring = {"turned": list(TURN_RING), "sums": list(SUM_RING)}
+        held = []
         for step in tensor:
-            if step == FREED:
-                ring["sums"] = list(FREED_RING)
+            ring["sums"] = freed.get(step, []) + ring["sums"]
             key = made(step)
             if key is not None:
                 banks = ring["turned" if key[0] == "turned" else "sums"]
@@ -397,29 +416,38 @@ def tile_factoranalysisemloadinggradient_kernel(
                 else:
                     bank = banks[0]
                     banks.remove(bank)
-                    banks.append(bank)
+                    held.append([bank, hold.get(key, 0), banks])
+                    for entry in list(held):
+                        if entry[1] == 0:
+                            entry[2].append(entry[0])
+                            held.remove(entry)
+                        entry[1] = entry[1] - 1
                 tenants.setdefault(f"bank{bank}", []).append(key)
 
         vector = [(widen, 0, 0), (widen, 1, None)] + both(product, 0) + [(x_quantize, 0, 0)] + q2(wz0) + [(x_quantize, 0, 1)]
         vector += both(product, 1) + [quant(wz1), (x_quantize, 1, 0), (x_quantize, 1, 1), mix(w01, "vector", 0, GC), quant(w01, GC, WIDTH)] + q2(w00) + [quant(w01, 0, GC)]
-        small = {4: [(invert_psi,)], 5: [(mean_psi,)]}
-        for pair in range(2, PAIRS):
-            slab = shared[pair - 2]
-            vector += both(product, pair) + [mix(slab, "vector", GC, WIDTH)] + small.get(pair, [])
-            vector += both(x_quantize, pair) + [quant(slab)]
-        vector += [mix(y(2, Z), "vector")]
-        vector += strips(empty_strip, 2, 1) + [mix(y(0, 1), "vector", GC, WIDTH), quant(y(2, Z)), quant(y(2, 1)), quant(y(0, 1)), quant(y(2, 0))]
-        vector += strips(empty_strip, 3, 1) + [mix(y(3, 0), "vector", GC, WIDTH), quant(y(3, Z)), quant(y(3, 0)), quant(y(3, 1)), sub(0), quant(y(1, 1)), sub(1)]
-        vector += [sub(band) for band in range(2, 7)] + [sub(7, 0, HALF), sub(7, HALF, WIDTH)]
+        vector += both(product, 2) + both(x_quantize, 2)
+        vector += both(product, 3) + both(x_quantize, 3) + [rest(w11, "vector"), (invert_psi,)] + q2(w10) + [quant(w11)]
+        for pair in range(4, PAIRS):
+            strip = strips(empty_strip, 0, 1, (pair - 4,))
+            vector += both(product, pair) + strip + ([(mean_psi,)] if pair == 4 else [])
+            vector += both(x_quantize, pair) + [quant(full[pair - 4])]
+        vector += strips(empty_strip, 2, 1) + [quant(y(1, Z))] + q2(y(2, 0)) + [quant(y(1, 1)), quant(y(2, 1))]
+        vector += strips(empty_strip, 3, 1) + [quant(y(3, Z))] + q2(y(3, 0))[::-1] + [quant(y(0, 1)), quant(y(3, 1))]
+        vector += [sub(band) for band in range(7)] + [sub(7, 0, HALF), sub(7, HALF, WIDTH)]
         sync = [(store, band, 0, WIDTH) for band in range(7)] + [(store, 7, 0, HALF), (store, 7, HALF, WIDTH)]
 
+        def g(s, first=0):
+            return ("grouped", *s, first)
+
         rotate("wide", 3, [("wide", pair, None) for pair in range(1, PAIRS)])
-        rotate("xg", 2, [("x_grouped", pair, 0) for pair in range(PAIRS)])
-        rotate("flat", 8, [("flat", step[1] // PACK, step[2]) for step in scalar if step[0] is empty and step[1] % PACK == 0])
-        tenants["gate_h"] = [("grouped", *s, 0) for s in [wz0, w00, w10, y(2, Z), y(3, Z)]]
-        tenants["gate_a"] = [("x_grouped", 0, 1), ("x_grouped", 2, 1), ("grouped", *w11, 0), ("x_grouped", 4, 1), ("grouped", *y(0, 0), 0), ("x_grouped", 6, 1), ("grouped", *y(1, 0), 0), ("grouped", *y(0, 1), 0), ("grouped", *y(3, 0), 0)]
-        tenants["gate_b"] = [("x_grouped", 1, 1), ("x_grouped", 3, 1), ("grouped", *y(0, Z), 0), ("x_grouped", 5, 1), ("grouped", *y(1, Z), 0), ("x_grouped", 7, 1), ("grouped", *y(1, 1), 0)]
-        rotate("other", 3, [("grouped", *s, 0) for s in [wz1, w01, y(2, 0), y(2, 1), y(3, 1)]])
+        rotate("flat", 7, [("flat", step[1] // PACK, step[2]) for step in scalar if step[0] is empty and step[1] % PACK == 0])
+        tenants["xg0"] = [("x_grouped", pair, 0) for pair in (0, 1, 3, 4, 5, 6, 7)]
+        tenants["xg1"] = [("x_grouped", pair, 1) for pair in (0, 1, 2, 3)]
+        tenants["gate_h"] = [g(wz0), g(w00), g(w10), g(y(0, Z)), ("x_grouped", 5, 1), g(y(1, 0)), ("x_grouped", 7, 1), g(y(2, 0))]
+        tenants["gate_a"] = [("x_grouped", 2, 0), g(w11), ("x_grouped", 4, 1), g(y(0, 0)), ("x_grouped", 6, 1), g(y(2, Z)), g(y(3, Z))]
+        tenants["gate_b"] = [g(y(1, 1)), g(y(3, 0))]
+        rotate("other", 4, [g(s) for s in [wz1, w01, y(0, 1), y(2, 1), y(1, Z), y(3, 1)]])
 
         queues = [vector, scalar, tensor, gpsimd, sync]
         tenant_before = {}
@@ -433,6 +461,8 @@ def tile_factoranalysisemloadinggradient_kernel(
             whole = (0, WIDTH)
             if name is widen:
                 return [], [(("wide", *args), *whole)]
+            if name is warm:
+                return [], [(("warm", *args), *whole)]
             if name is turn:
                 return [(("wide", args[0], None), *whole), (("wide", *args), *whole)], [(("turned", *args), *whole)]
             if name is product:
@@ -462,11 +492,11 @@ def tile_factoranalysisemloadinggradient_kernel(
             if name is widen_factor:
                 return [], [(("factor", args[0] == Z), *whole)]
             if name is accumulate:
-                group, band = args
+                group, band, first = args[:3]
                 block, place = divmod(band, BLOCK_BANDS)
                 n = group_order[band].index(group)
-                before = [(("sum", band), 0, n)] if n else []
-                return before + [(("y", group, block), place * P, (place + 1) * P), (("y", group, Z), *whole)], [(("sum", band), n, n + 1)]
+                before = [(("sum", band, first), 0, n)] if n else []
+                return before + [(("y", group, block), place * P, (place + 1) * P), (("y", group, Z), *whole)], [(("sum", band, first), n, n + 1)]
             if name is invert_psi:
                 return [], [(("psi_inv",), *whole)]
             if name is mean_psi:
@@ -476,7 +506,7 @@ def tile_factoranalysisemloadinggradient_kernel(
             if name is subtract:
                 band = args[0]
                 made = [(("prepared", band), *whole), (("psi_inv_mean",), *whole)] if band in PREPARED else []
-                return [(("sum", band), *whole)] + made, [(("result" if band in PREPARED else "difference", band), *args[1:])]
+                return [(("sum", band, args[1]), *whole)] + made, [(("result" if band in PREPARED else "difference", band), *args[1:])]
             if name is divide:
                 return [(("difference", args[0]), *whole), (("psi_inv",), *whole)], [(("result", args[0]), *whole)]
             return [(("result", args[0]), *args[1:])], []

@@ -43,7 +43,7 @@ HEAD_BANKS = {("warm", 0): 6, ("warm", 1): 7, ("warm", 2): 6, ("warm", 3): 7, ("
 TURN_RING = (0, 1, 6, 7)
 SUM_RING = (3, 5, 4, 2)
 FREED_RING = (6, 3, 7, 5, 4, 2)
-WARM = False
+WARM = True
 
 
 def tile_factoranalysisemloadinggradient_kernel(

@@ -36,7 +36,7 @@ BANKS = 8
 RUN = 4
 VECTOR_WIDENS = ((0, 0), (1, None))
 PREPARED = (0, 1, 2, 3, 4, 5, 6, 7)
-STRIP_RUN = 1
+STRIP_RUN = 4
 GC = 384
 HEAD_BANKS = {("warm", 0): 6, ("warm", 1): 7, ("warm", 2): 6, ("warm", 3): 7, ("warm", 4): 7, ("warm", 5): 2, ("turned", 2, 0): 4, ("turned", 2, 1): 5, ("first", 0, 2): 6, ("first", 1, 2): 7, ("turned", 3, 0): 0, ("turned", 3, 1): 1,
   ("first", 2, 2): 2, ("first", 3, 2): 3, ("turned", 4, 0): 6, ("turned", 4, 1): 7, ("first", 0, 0): 2, ("first", 1, 0): 3, ("first", 2, 0): 4, ("first", 3, 0): 2, ("turned", 0, 0): 0, ("turned", 0, 1): 1, ("turned", 1, 0): 2, ("turned", 1, 1): 3}

@@ -34,7 +34,7 @@ BLOCK_BANDS = WIDTH // P
 STRIPS = WIDTH // P
 BANKS = 8
 RUN = 4
-VECTOR_WIDENS = ((0, 0), (1, None))
+VECTOR_WIDENS = ((0, 0),)
 PREPARED = (0, 1, 2, 3, 4, 5, 6, 7)
 STRIP_RUN = 4
 GC = 384
@@ -44,6 +44,7 @@ TURN_RING = (0, 1, 6, 7)
 SUM_RING = (3, 5, 4, 2)
 FREED_RING = (6, 3, 7, 5, 4, 2)
 WARM = True
+G0 = 320
 
 
 def tile_factoranalysisemloadinggradient_kernel(
@@ -225,7 +226,7 @@ def tile_factoranalysisemloadinggradient_kernel(
                 in_=tiles["x_grouped", pair, g][:].rearrange("q c u e -> q (c u e)"),
             )
 
-        def first_pass(target, unit, block, g, w_cols):
+        def first_pass(target, unit, block, g, w_cols, start, stop):
             x_codes, x_scales = mx_tiles(("x", unit // 2))
             cols = slice((2 * g + unit % 2) * P, (2 * g + unit % 2 + 1) * P)
             w_codes, w_scales = mx_tiles(("w", block, g))
@@ -235,18 +236,19 @@ def tile_factoranalysisemloadinggradient_kernel(
                 lhsT_scale=x_scales[:, cols],
                 rhs=w_codes[:, w_cols].bitcast(FP8X4),
                 rhs_scale=w_scales[:, w_cols],
-                start=(g == 0),
-                stop=(g == PASSES - 1),
+                start=start,
+                stop=stop,
             )
 
         def multiply(unit, block, g):
-            first_pass(tile_of(("first", unit, block), [P, WIDTH], F32)[:], unit, block, g, slice(0, WIDTH))
+            first_pass(tile_of(("first", unit, block), [P, WIDTH], F32)[:], unit, block, g, slice(0, WIDTH), g == 0, g == PASSES - 1)
 
         def multiply_strip(group, block, strip):
             bank = tile_of(("strip", group, block, strip), [P, PACK, P], F32)
-            for j in range(PACK):
-                for g in range(PASSES):
-                    first_pass(bank[:, j, :], PACK * group + j, block, g, slice(strip * P, (strip + 1) * P))
+            order = [(g, j) for g in range(PASSES) for j in range(PACK)]
+            for g, j in order:
+                cols = slice(strip * P, (strip + 1) * P)
+                first_pass(bank[:, j, :], PACK * group + j, block, g, cols, (g, j) == order[0], (g, j) == order[-1])
 
         def empty(unit, block):
             group, j = divmod(unit, PACK)
@@ -340,8 +342,8 @@ def tile_factoranalysisemloadinggradient_kernel(
         wz0, wz1, w00, w01, w10, w11 = [("w", block, g) for block in (Z, 0, 1) for g in range(PASSES)]
 
         full = [y(0, Z), y(0, 0), y(1, 0), y(2, Z)]
-        gpsimd = [mix(s, "gpsimd", 0, GC) for s in [wz0, w00, w10, w11]] + [mix(s, "gpsimd") for s in full] + [mix(s, "gpsimd", 0, GC) for s in (y(2, 0), y(3, 0))]
-        for s in (wz0, w00, w01, w10, y(2, 0), y(3, 0)):
+        gpsimd = [mix(wz0, "gpsimd", 0, G0)] + [mix(s, "gpsimd", 0, GC) for s in [w00, w10, w11]] + [mix(s, "gpsimd") for s in full] + [mix(s, "gpsimd", 0, GC) for s in (y(2, 0), y(3, 0))]
+        for s in (w00, w01, w10, y(2, 0), y(3, 0)):
             cuts[s] = (0, GC, WIDTH)
 
         def rest(s, engine="scalar"):
@@ -370,7 +372,7 @@ def tile_factoranalysisemloadinggradient_kernel(
         tensor += both(turn, 7) + pair_stage(5, (Z,)) + strips(multiply_strip, 0, 1, (2,)) + pair_stage(5, (0,)) + pair_stage(3, (1,)) + pair_stage(6, (Z,)) + strips(multiply_strip, 0, 1, (3,)) + pair_stage(6, (0,))
         tensor += strips(multiply_strip, 2, 1) + pair_stage(7) + strips(multiply_strip, 3, 1)
 
-        scalar = [(widen, 0, 1), rest(wz0), (widen, 2, None), mix(wz1, "scalar"), (widen, 3, None)]
+        scalar = [(widen, 0, 1), (widen, 1, None), mix(wz0, "scalar", G0, WIDTH), (widen, 2, None), mix(wz1, "scalar"), (widen, 3, None)]
         scalar += [rest(w00), rest(w01), (widen_factor, Z), (widen, 4, None)]
         extra = {(empty, 3, Z): [rest(w10)], (empty, 3, 0): [(widen, 5, None)], (empty, 5, 0): [(widen, 6, None)], (empty, 5, 1): [(widen, 7, None)],
                  (empty, 9, Z): [mix(y(1, Z), "scalar", 0, QUARTER)], (empty, 9, 0): [mix(y(1, Z), "scalar", QUARTER, WIDTH - QUARTER)], (empty, 11, Z): [mix(y(1, Z), "scalar", WIDTH - QUARTER, WIDTH)], (empty, 13, Z): [rest(y(2, 0))], (empty, 13, 0): [mix(y(1, 1), "scalar")]}
@@ -424,7 +426,7 @@ def tile_factoranalysisemloadinggradient_kernel(
                         entry[1] = entry[1] - 1
                 tenants.setdefault(f"bank{bank}", []).append(key)
 
-        vector = [(widen, 0, 0), (widen, 1, None)] + both(product, 0) + [(x_quantize, 0, 0)] + q2(wz0) + [(x_quantize, 0, 1)]
+        vector = [(widen, 0, 0)] + both(product, 0) + [(x_quantize, 0, 0)] + [quant(wz0)] + [(x_quantize, 0, 1)]
         vector += both(product, 1) + [quant(wz1), (x_quantize, 1, 0), (x_quantize, 1, 1), mix(w01, "vector", 0, GC), quant(w01, GC, WIDTH)] + q2(w00) + [quant(w01, 0, GC)]
         vector += both(product, 2) + both(x_quantize, 2)
         vector += both(product, 3) + both(x_quantize, 3) + [rest(w11, "vector"), (invert_psi,)] + q2(w10) + [quant(w11)]

@@ -45,6 +45,7 @@ SUM_RING = (3, 5, 4, 2)
 FREED_RING = (6, 3, 7, 5, 4, 2)
 WARM = True
 G0 = 320
+SHARED_ENDS = ()
 
 
 def tile_factoranalysisemloadinggradient_kernel(
@@ -302,6 +303,19 @@ def tile_factoranalysisemloadinggradient_kernel(
                 out=tile, in0=tiles["sum", band, first][:], scalar=mean, in1=other, op0=MULT, op1=SUBTRACT
             )
 
+        def scale_sum(band):
+            nc.scalar.activation(
+                out=tile_of(("scaled", band), [P, K], F32)[:],
+                in_=tiles["sum", band, 0][:],
+                func=COPY,
+                scale=psi_inv_mean[:, band : band + 1],
+            )
+
+        def take_away(band):
+            before = tiles["result", band]
+            tiles["result", band] = tile_of(("ended", band), [P, K], F32)
+            nc.gpsimd.tensor_tensor(out=tiles["result", band][:], in0=tiles["scaled", band][:], in1=before[:], op=SUBTRACT)
+
         def divide(band, engine):
             tile, inverse = tiles["result", band], psi_inv[:, band : band + 1]
             if engine == "vector":
@@ -342,8 +356,8 @@ def tile_factoranalysisemloadinggradient_kernel(
         wz0, wz1, w00, w01, w10, w11 = [("w", block, g) for block in (Z, 0, 1) for g in range(PASSES)]
 
         full = [y(0, Z), y(0, 0), y(1, 0), y(2, Z)]
-        gpsimd = [mix(wz0, "gpsimd", 0, G0)] + [mix(s, "gpsimd", 0, GC) for s in [w00, w10, w11]] + [mix(s, "gpsimd") for s in full] + [mix(s, "gpsimd", 0, GC) for s in (y(2, 0), y(3, 0))]
-        for s in (w00, w01, w10, y(2, 0), y(3, 0)):
+        gpsimd = [mix(wz0, "gpsimd", 0, G0)] + [mix(s, "gpsimd", 0, GC) for s in [wz1, w10, w11]] + [mix(s, "gpsimd") for s in full] + [mix(s, "gpsimd", 0, GC) for s in (y(2, 0), y(3, 0))]
+        for s in (wz1, y(2, 0), y(3, 0)):
             cuts[s] = (0, GC, WIDTH)
 
         def rest(s, engine="scalar"):
@@ -372,9 +386,9 @@ def tile_factoranalysisemloadinggradient_kernel(
         tensor += both(turn, 7) + pair_stage(5, (Z,)) + strips(multiply_strip, 0, 1, (2,)) + pair_stage(5, (0,)) + pair_stage(3, (1,)) + pair_stage(6, (Z,)) + strips(multiply_strip, 0, 1, (3,)) + pair_stage(6, (0,))
         tensor += strips(multiply_strip, 2, 1) + pair_stage(7) + strips(multiply_strip, 3, 1)
 
-        scalar = [(widen, 0, 1), (widen, 1, None), mix(wz0, "scalar", G0, WIDTH), (widen, 2, None), mix(wz1, "scalar"), (widen, 3, None)]
-        scalar += [rest(w00), rest(w01), (widen_factor, Z), (widen, 4, None)]
-        extra = {(empty, 3, Z): [rest(w10)], (empty, 3, 0): [(widen, 5, None)], (empty, 5, 0): [(widen, 6, None)], (empty, 5, 1): [(widen, 7, None)],
+        scalar = [(widen, 0, 1), (widen, 1, None), mix(wz0, "scalar", G0, WIDTH), (widen, 2, None), rest(wz1), (widen, 3, None)]
+        scalar += [mix(w00, "scalar"), (widen_factor, Z), (widen, 4, None)]
+        extra = {(empty, 3, 0): [(widen, 5, None)], (empty, 5, 0): [(widen, 6, 0)], (empty, 7, 0): [(widen, 6, 1)], (empty, 5, 1): [(widen, 7, None)],
                  (empty, 9, Z): [mix(y(1, Z), "scalar", 0, QUARTER)], (empty, 9, 0): [mix(y(1, Z), "scalar", QUARTER, WIDTH - QUARTER)], (empty, 11, Z): [mix(y(1, Z), "scalar", WIDTH - QUARTER, WIDTH)], (empty, 13, Z): [rest(y(2, 0))], (empty, 13, 0): [mix(y(1, 1), "scalar")]}
         for step in tensor:
             if step == (multiply, 3, Z, 1):
@@ -427,9 +441,9 @@ def tile_factoranalysisemloadinggradient_kernel(
                 tenants.setdefault(f"bank{bank}", []).append(key)
 
         vector = [(widen, 0, 0)] + both(product, 0) + [(x_quantize, 0, 0)] + [quant(wz0)] + [(x_quantize, 0, 1)]
-        vector += both(product, 1) + [quant(wz1), (x_quantize, 1, 0), (x_quantize, 1, 1), mix(w01, "vector", 0, GC), quant(w01, GC, WIDTH)] + q2(w00) + [quant(w01, 0, GC)]
+        vector += both(product, 1) + q2(wz1) + [(x_quantize, 1, 0), (x_quantize, 1, 1), mix(w01, "vector"), quant(w00), quant(w01)]
         vector += both(product, 2) + both(x_quantize, 2)
-        vector += both(product, 3) + both(x_quantize, 3) + [rest(w11, "vector"), (invert_psi,)] + q2(w10) + [quant(w11)]
+        vector += both(product, 3) + both(x_quantize, 3) + [rest(w10, "vector"), rest(w11, "vector"), (invert_psi,), quant(w10), quant(w11)]
         for pair in range(4, PAIRS):
             strip = strips(empty_strip, 0, 1, (pair - 4,))
             vector += both(product, pair) + strip + ([(mean_psi,)] if pair == 4 else [])
@@ -442,15 +456,21 @@ def tile_factoranalysisemloadinggradient_kernel(
         def g(s, first=0):
             return ("grouped", *s, first)
 
-        rotate("wide", 3, [("wide", pair, None) for pair in range(1, PAIRS)])
+        rotate("wide", 3, [("wide", pair, None) for pair in range(1, PAIRS) if pair != 6])
         rotate("flat", 7, [("flat", step[1] // PACK, step[2]) for step in scalar if step[0] is empty and step[1] % PACK == 0])
         tenants["xg0"] = [("x_grouped", pair, 0) for pair in (0, 1, 3, 4, 5, 6, 7)]
         tenants["xg1"] = [("x_grouped", pair, 1) for pair in (0, 1, 2, 3)]
-        tenants["gate_h"] = [g(wz0), g(w00), g(w10), g(y(0, Z)), ("x_grouped", 5, 1), g(y(1, 0)), ("x_grouped", 7, 1), g(y(2, 0))]
+        tenants["gate_h"] = [g(wz0), g(wz1)]
+        tenants["gate_w"] = [g(w00), g(w10), g(y(0, Z)), ("x_grouped", 5, 1), g(y(1, 0)), ("x_grouped", 7, 1), g(y(2, 0))]
         tenants["gate_a"] = [("x_grouped", 2, 0), g(w11), ("x_grouped", 4, 1), g(y(0, 0)), ("x_grouped", 6, 1), g(y(2, Z)), g(y(3, Z))]
         tenants["gate_b"] = [g(y(1, 1)), g(y(3, 0))]
-        rotate("other", 4, [g(s) for s in [wz1, w01, y(0, 1), y(2, 1), y(1, Z), y(3, 1)]])
+        rotate("other", 4, [g(s) for s in [w01, y(0, 1), y(2, 1), y(1, Z), y(3, 1)]])
 
+        for pair in (0, 6):
+            for h in range(PASSES):
+                tenants[f"wide_pass{pair}{h}"] = [("wide", pair, h)]
+        for band, buffer in enumerate(name for name in sorted(tenants) if name.startswith("wide")):
+            tenants[buffer].append(("result", band))
         queues = [vector, scalar, tensor, gpsimd, sync]
         tenant_before = {}
         for buffer, keys in tenants.items():
@@ -504,11 +524,15 @@ def tile_factoranalysisemloadinggradient_kernel(
             if name is mean_psi:
                 return [(("psi_inv",), *whole)], [(("psi_inv_mean",), *whole)]
             if name is prepare:
-                return [(("psi_inv",), *whole)], [(("prepared", args[0]), *whole)]
+                return [(("psi_inv",), *whole)], [(("prepared", args[0]), *whole), (("result", args[0]), 0, 0)]
             if name is subtract:
                 band = args[0]
                 made = [(("prepared", band), *whole), (("psi_inv_mean",), *whole)] if band in PREPARED else []
                 return [(("sum", band, args[1]), *whole)] + made, [(("result" if band in PREPARED else "difference", band), *args[1:])]
+            if name is scale_sum:
+                return [(("sum", args[0], 0), *whole), (("psi_inv_mean",), *whole)], [(("scaled", args[0]), *whole)]
+            if name is take_away:
+                return [(("scaled", args[0]), *whole), (("prepared", args[0]), *whole)], [(("result", args[0]), *whole), (("ended", args[0]), *whole)]
             if name is divide:
                 return [(("difference", args[0]), *whole), (("psi_inv",), *whole)], [(("result", args[0]), *whole)]
             return [(("result", args[0]), *args[1:])], []

@@ -443,10 +443,10 @@ def tile_factoranalysisemloadinggradient_kernel(
         vector = [(widen, 0, 0)] + both(product, 0) + [(x_quantize, 0, 0)] + [quant(wz0)] + [(x_quantize, 0, 1)]
         vector += both(product, 1) + q2(wz1) + [(x_quantize, 1, 0), (x_quantize, 1, 1), mix(w01, "vector"), quant(w00), quant(w01)]
         vector += both(product, 2) + both(x_quantize, 2)
-        vector += both(product, 3) + both(x_quantize, 3) + [rest(w10, "vector"), rest(w11, "vector"), (invert_psi,), quant(w10), quant(w11)]
+        vector += both(product, 3) + both(x_quantize, 3) + [rest(w10, "vector"), rest(w11, "vector"), quant(w10), quant(w11)]
         for pair in range(4, PAIRS):
             strip = strips(empty_strip, 0, 1, (pair - 4,))
-            vector += both(product, pair) + strip + ([(mean_psi,)] if pair == 4 else [])
+            vector += both(product, pair) + strip + {6: [(invert_psi,)], 7: [(mean_psi,)]}.get(pair, [])
             vector += both(x_quantize, pair) + [quant(full[pair - 4])]
         vector += strips(empty_strip, 2, 1) + [quant(y(1, Z))] + q2(y(2, 0)) + [quant(y(1, 1)), quant(y(2, 1))]
         vector += strips(empty_strip, 3, 1) + [quant(y(3, Z))] + q2(y(3, 0))[::-1] + [quant(y(0, 1)), quant(y(3, 1))]

@@ -34,6 +34,7 @@ BLOCK_BANDS = WIDTH // P
 STRIPS = WIDTH // P
 BANKS = 8
 RUN = 4
+BLOCK = 16
 VECTOR_WIDENS = ((0, 0),)
 PREPARED = (0, 1, 2, 3, 4, 5, 6, 7)
 STRIP_RUN = 4
@@ -82,17 +83,17 @@ def tile_factoranalysisemloadinggradient_kernel(
             nc.sync.dma_start(out=raw[:], in_=rows)
             w_raw[block, g] = raw[:]
 
-        scale = keep.tile([P, PASSES, PACK], F32, name="scale")
-        r16 = keep.tile([P, GROUPS, PACK], BF16, name="r16")
-        t16 = keep.tile([P, GROUPS, PACK], BF16, name="t16")
+        scale = [keep.tile([P, PACK], F32, name=f"scale{g}") for g in range(PASSES)]
+        r16 = keep.tile([P, GROUPS, BLOCK], BF16, name="r16")
+        t16 = keep.tile([P, GROUPS, BLOCK], BF16, name="t16")
         v_raw = keep.tile([P, BANDS, K], BF16, name="v_raw")
-        psi16 = keep.tile([P, BANDS, 2], BF16, name="psi16")
+        psi16 = keep.tile([P, BANDS, BLOCK], BF16, name="psi16")
 
-        def load_scale():
-            nc.scalar.dma_start(out=scale[:], in_=x_scale.rearrange("o (g q j) -> q (o g) j", q=P, j=PACK))
+        def load_scale(g):
+            nc.scalar.dma_start(out=scale[g][:], in_=x_scale.rearrange("o (g q j) -> (o g) q j", q=P, j=PACK)[g])
 
         def load_factor(tile, source):
-            nc.sync.dma_start(out=tile[:], in_=source.rearrange("(g q j) -> q g j", q=P, j=PACK))
+            nc.sync.dma_start(out=tile[:, :, :PACK], in_=source.rearrange("(g q j) -> q g j", q=P, j=PACK))
 
         def load_end():
             nc.sync.dma_start(out=v_raw[:], in_=v.rearrange("(b q) k -> q b k", q=P))
@@ -100,15 +101,16 @@ def tile_factoranalysisemloadinggradient_kernel(
                 nc.sync.dma_start(out=psi16[:, :, 0], in_=psi.rearrange("(b q) -> q b", q=P))
 
         load_x(0, 1)
-        load_scale()
+        load_scale(0)
         load_x(1, 1)
+        load_scale(1)
         load_w(Z, 0)
         load_x(2, 1)
         load_w(Z, 1)
         load_x(3, 1)
         load_w(0, 0)
-        load_w(0, 1)
         load_factor(t16, t)
+        load_w(0, 1)
         load_x(4, 1)
         load_factor(r16, r)
         load_w(1, 0)
@@ -145,7 +147,7 @@ def tile_factoranalysisemloadinggradient_kernel(
 
         def widen_factor(block):
             source = t16 if block == Z else r16
-            nc.scalar.copy(out=factor[block][:], in_=source[:].rearrange("q g j -> q (g j)"))
+            nc.scalar.copy(out=factor[block][:].rearrange("q (g j) -> q g j", j=PACK), in_=source[:, :, :PACK])
 
         def invert_psi():
             nc.vector.reciprocal(out=psi_inv[:], in_=psi16[:, :, 0])
@@ -215,7 +217,7 @@ def tile_factoranalysisemloadinggradient_kernel(
         def product(pair, g):
             target = tile_of(("x_grouped", pair, g), [P, 2 * P, 2, 2], BF16)
             values = tiles["turned", pair, g][:].bitcast(BF16).rearrange("q u (c e) -> q c u e", e=2)
-            scales = scale[:, g, :].rearrange("q (o u e) -> q o u e", o=1, u=2)
+            scales = scale[g][:].rearrange("q (o u e) -> q o u e", o=1, u=2)
             nc.vector.tensor_tensor(out=target[:], in0=values, in1=scales.to_broadcast([P, 2 * P, 2, 2]), op=MULT)
 
         def x_quantize(pair, g):
@@ -357,7 +359,7 @@ def tile_factoranalysisemloadinggradient_kernel(
 
         full = [y(0, Z), y(0, 0), y(1, 0), y(2, Z)]
         gpsimd = [mix(wz0, "gpsimd", 0, G0)] + [mix(s, "gpsimd", 0, GC) for s in [wz1, w10, w11]] + [mix(s, "gpsimd") for s in full] + [mix(s, "gpsimd", 0, GC) for s in (y(2, 0), y(3, 0))]
-        for s in (wz1, y(2, 0), y(3, 0)):
+        for s in (wz1, w01, w10, y(2, 0), y(3, 0)):
             cuts[s] = (0, GC, WIDTH)
 
         def rest(s, engine="scalar"):
@@ -387,8 +389,8 @@ def tile_factoranalysisemloadinggradient_kernel(
         tensor += strips(multiply_strip, 2, 1) + pair_stage(7) + strips(multiply_strip, 3, 1)
 
         scalar = [(widen, 0, 1), (widen, 1, None), mix(wz0, "scalar", G0, WIDTH), (widen, 2, None), rest(wz1), (widen, 3, None)]
-        scalar += [mix(w00, "scalar"), (widen_factor, Z), (widen, 4, None)]
-        extra = {(empty, 3, 0): [(widen, 5, None)], (empty, 5, 0): [(widen, 6, 0)], (empty, 7, 0): [(widen, 6, 1)], (empty, 5, 1): [(widen, 7, None)],
+        scalar += [mix(w00, "scalar"), rest(w01), (widen_factor, Z), (widen, 4, None)]
+        extra = {(empty, 3, Z): [rest(w10)], (empty, 3, 0): [(widen, 5, None)], (empty, 5, 0): [(widen, 6, 0)], (empty, 7, 0): [(widen, 6, 1)], (empty, 5, 1): [(widen, 7, None)],
                  (empty, 9, Z): [mix(y(1, Z), "scalar", 0, QUARTER)], (empty, 9, 0): [mix(y(1, Z), "scalar", QUARTER, WIDTH - QUARTER)], (empty, 11, Z): [mix(y(1, Z), "scalar", WIDTH - QUARTER, WIDTH)], (empty, 13, Z): [rest(y(2, 0))], (empty, 13, 0): [mix(y(1, 1), "scalar")]}
         for step in tensor:
             if step == (multiply, 3, Z, 1):
@@ -441,9 +443,9 @@ def tile_factoranalysisemloadinggradient_kernel(
                 tenants.setdefault(f"bank{bank}", []).append(key)
 
         vector = [(widen, 0, 0)] + both(product, 0) + [(x_quantize, 0, 0)] + [quant(wz0)] + [(x_quantize, 0, 1)]
-        vector += both(product, 1) + q2(wz1) + [(x_quantize, 1, 0), (x_quantize, 1, 1), mix(w01, "vector"), quant(w00), quant(w01)]
+        vector += both(product, 1) + q2(wz1) + [(x_quantize, 1, 0), (x_quantize, 1, 1), mix(w01, "vector", 0, GC), quant(w01, GC, WIDTH), quant(w00), quant(w01, 0, GC)]
         vector += both(product, 2) + both(x_quantize, 2)
-        vector += both(product, 3) + both(x_quantize, 3) + [rest(w10, "vector"), rest(w11, "vector"), quant(w10), quant(w11)]
+        vector += both(product, 3) + both(x_quantize, 3) + [rest(w11, "vector"), ] + q2(w10) + [quant(w11)]
         for pair in range(4, PAIRS):
             strip = strips(empty_strip, 0, 1, (pair - 4,))
             vector += both(product, pair) + strip + {6: [(invert_psi,)], 7: [(mean_psi,)]}.get(pair, [])

@@ -35,7 +35,7 @@ STRIPS = WIDTH // P
 BANKS = 8
 RUN = 4
 BLOCK = 16
-VECTOR_WIDENS = ((0, 0),)
+VECTOR_WIDENS = ((0, 0), (1, 0),)
 PREPARED = (0, 1, 2, 3, 4, 5, 6, 7)
 STRIP_RUN = 4
 GC = 384
@@ -44,9 +44,9 @@ HEAD_BANKS = {("warm", 0): 6, ("warm", 1): 7, ("warm", 2): 6, ("warm", 3): 7, ("
 TURN_RING = (0, 1, 6, 7)
 SUM_RING = (3, 5, 4, 2)
 FREED_RING = (6, 3, 7, 5, 4, 2)
-WARM = True
+WARM = (0, 1, 2, 3, 4,)
 G0 = 320
-SHARED_ENDS = ()
+WARM_WIDTH = 272
 
 
 def tile_factoranalysisemloadinggradient_kernel(
@@ -58,7 +58,7 @@ def tile_factoranalysisemloadinggradient_kernel(
         psum = ctx.enter_context(tc.psum_pool(name="psum", bufs=1))
         ctx.enter_context(tc.manual_schedule())
 
-        zeros = keep.tile([P, HALF], F32, name="zeros")
+        zeros = keep.tile([P, WARM_WIDTH], F32, name="zeros")
         nc.vector.memset(zeros[:], 0.0)
         identity = keep.tile([P, P], F32, name="identity")
         make_identity(nc, identity[:])
@@ -211,7 +211,7 @@ def tile_factoranalysisemloadinggradient_kernel(
 
         def warm(n):
             nc.tensor.matmul(
-                out=tile_of(("warm", n), [P, HALF], F32)[:], lhsT=zeros[:, :P], rhs=zeros[:], start=True, stop=True
+                out=tile_of(("warm", n), [P, WARM_WIDTH], F32)[:], lhsT=zeros[:, :P], rhs=zeros[:], start=True, stop=True
             )
 
         def product(pair, g):
@@ -357,11 +357,6 @@ def tile_factoranalysisemloadinggradient_kernel(
         tenants, cuts = {}, {}
         wz0, wz1, w00, w01, w10, w11 = [("w", block, g) for block in (Z, 0, 1) for g in range(PASSES)]
 
-        full = [y(0, Z), y(0, 0), y(1, 0), y(2, Z)]
-        gpsimd = [mix(wz0, "gpsimd", 0, G0)] + [mix(s, "gpsimd", 0, GC) for s in [wz1, w10, w11]] + [mix(s, "gpsimd") for s in full] + [mix(s, "gpsimd", 0, GC) for s in (y(2, 0), y(3, 0))]
-        for s in (wz1, w01, w10, y(2, 0), y(3, 0)):
-            cuts[s] = (0, GC, WIDTH)
-
         def rest(s, engine="scalar"):
             return mix(s, engine, GC, WIDTH)
 
@@ -378,19 +373,30 @@ def tile_factoranalysisemloadinggradient_kernel(
             return (accumulate, group, band, first, last)
 
         def w(n):
-            return [(warm, n)] if WARM else []
+            return [(warm, n)] if n in WARM else []
 
-        tensor = w(0) + w(1) + both(turn, 0) + w(2) + both(turn, 1) + w(3) + both(turn, 2) + w(4) + [(multiply, unit, Z, 0) for unit in range(2)] + w(5)
-        tensor += both(turn, 3) + [(multiply, unit, Z, 1) for unit in range(2)] + first_stage(0, Z, (2, 3))
+        def g(s, first=0):
+            return ("grouped", *s, first)
+
+        def xg(pair, h):
+            return ("x_grouped", pair, h)
+
+        full = [y(0, Z), y(0, 0), y(1, 0), y(2, Z)]
+        gpsimd = [mix(wz0, "gpsimd", 0, G0)] + [mix(s, "gpsimd", 0, GC) for s in [wz1, w10, w11]] + [mix(s, "gpsimd") for s in full] + [mix(s, "gpsimd", 0, GC) for s in (y(2, 0), y(3, 0))]
+        for s in [wz1, y(2, 0), y(3, 0)]:
+            cuts[s] = (0, GC, WIDTH)
+
+        tensor = w(0) + w(1) + both(turn, 0) + w(2) + both(turn, 1) + w(3) + both(turn, 2) + w(4) + both(turn, 3) + w(5) + [(multiply, unit, Z, 0) for unit in range(2)]
+        tensor += [(multiply, unit, Z, 1) for unit in range(2)] + first_stage(0, Z, (2, 3))
         tensor += both(turn, 4) + first_stage(0, 0) + by_pass(2, Z) + pair_stage(2, (0,))
         tensor += both(turn, 5) + pair_stage(3) + strips(multiply_strip, 0, 1, (0,)) + pair_stage(2, (1,))
         tensor += both(turn, 6) + pair_stage(4, (Z,)) + strips(multiply_strip, 0, 1, (1,)) + pair_stage(4, (0,))
         tensor += both(turn, 7) + pair_stage(5, (Z,)) + strips(multiply_strip, 0, 1, (2,)) + pair_stage(5, (0,)) + pair_stage(3, (1,)) + pair_stage(6, (Z,)) + strips(multiply_strip, 0, 1, (3,)) + pair_stage(6, (0,))
         tensor += strips(multiply_strip, 2, 1) + pair_stage(7) + strips(multiply_strip, 3, 1)
 
-        scalar = [(widen, 0, 1), (widen, 1, None), mix(wz0, "scalar", G0, WIDTH), (widen, 2, None), rest(wz1), (widen, 3, None)]
-        scalar += [mix(w00, "scalar"), rest(w01), (widen_factor, Z), (widen, 4, None)]
-        extra = {(empty, 3, Z): [rest(w10)], (empty, 3, 0): [(widen, 5, None)], (empty, 5, 0): [(widen, 6, 0)], (empty, 7, 0): [(widen, 6, 1)], (empty, 5, 1): [(widen, 7, None)],
+        scalar = [(widen, 0, 1), (widen, 1, 1), mix(wz0, "scalar", G0, WIDTH), (widen, 2, None), rest(wz1), (widen, 3, None)]
+        scalar += [mix(w00, "scalar"), (widen_factor, Z), (widen, 4, None)]
+        extra = {(empty, 3, 0): [(widen, 5, None)], (empty, 5, 0): [(widen, 6, 0)], (empty, 7, 0): [(widen, 6, 1)], (empty, 5, 1): [(widen, 7, None)],
                  (empty, 9, Z): [mix(y(1, Z), "scalar", 0, QUARTER)], (empty, 9, 0): [mix(y(1, Z), "scalar", QUARTER, WIDTH - QUARTER)], (empty, 11, Z): [mix(y(1, Z), "scalar", WIDTH - QUARTER, WIDTH)], (empty, 13, Z): [rest(y(2, 0))], (empty, 13, 0): [mix(y(1, 1), "scalar")]}
         for step in tensor:
             if step == (multiply, 3, Z, 1):
@@ -401,10 +407,9 @@ def tile_factoranalysisemloadinggradient_kernel(
         scalar += [mix(y(3, Z), "scalar"), rest(y(3, 0))]
         scalar += [(prepare, band) for band in range(8)]
 
-        tensor += [acc(group, band) for group in range(3) for band in range(BLOCK_BANDS)]
-        tensor += [acc(3, band) for band in range(BLOCK_BANDS)]
-        tensor += [acc(group, band) for band in (4, 5, 6) for group in (0, 2, 1, 3)]
-        tensor += [acc(group, 7, first, first + HALF) for first in (0, HALF) for group in (0, 2, 1, 3)]
+        tensor += [acc(group, band) for group in range(GROUPS) for band in range(BLOCK_BANDS)]
+        tensor += [acc(group, band) for band in (4, 5, 6) for group in (1, 2, 0, 3)]
+        tensor += [acc(group, 7, first, first + HALF) for first in (0, HALF) for group in range(4)]
         freed = {(multiply, 10, 0, 0): [6], (multiply, 7, 1, 0): [7], (multiply, 13, 0, 0): [0], (multiply_strip, 2, 1, 1): [1]}
         hold = {("strip", 0, 1, 1): 1}
         group_order = {band: [step[1] for step in tensor if step[0] is accumulate and step[2:4] == (band, 0)] for band in range(BANDS)}
@@ -442,37 +447,48 @@ def tile_factoranalysisemloadinggradient_kernel(
                         entry[1] = entry[1] - 1
                 tenants.setdefault(f"bank{bank}", []).append(key)
 
-        vector = [(widen, 0, 0)] + both(product, 0) + [(x_quantize, 0, 0)] + [quant(wz0)] + [(x_quantize, 0, 1)]
-        vector += both(product, 1) + q2(wz1) + [(x_quantize, 1, 0), (x_quantize, 1, 1), mix(w01, "vector", 0, GC), quant(w01, GC, WIDTH), quant(w00), quant(w01, 0, GC)]
+        vector = [(widen, 0, 0), (widen, 1, 0)] + both(product, 0) + [(x_quantize, 0, 0), quant(wz0), (x_quantize, 0, 1)]
+        vector += both(product, 1) + q2(wz1) + both(x_quantize, 1) + [mix(w01, "vector"), quant(w00), quant(w01)]
         vector += both(product, 2) + both(x_quantize, 2)
-        vector += both(product, 3) + both(x_quantize, 3) + [rest(w11, "vector"), ] + q2(w10) + [quant(w11)]
+        vector += both(product, 3) + both(x_quantize, 3) + [rest(w10, "vector"), rest(w11, "vector"), quant(w10), quant(w11)]
+        tail = {4: [quant(full[0])] + [], 5: [quant(full[1])], 6: [quant(full[2])], 7: [quant(full[3])]}
+        gates = {}
         for pair in range(4, PAIRS):
-            strip = strips(empty_strip, 0, 1, (pair - 4,))
-            vector += both(product, pair) + strip + {6: [(invert_psi,)], 7: [(mean_psi,)]}.get(pair, [])
-            vector += both(x_quantize, pair) + [quant(full[pair - 4])]
+            steps = both(x_quantize, pair) + tail[pair]
+            if steps[-2][0] is widen:
+                steps = [steps[0], steps[-2]] + steps[1:-2] + steps[-1:]
+            gates[pair] = xg(*steps[-2][1:]) if steps[-2][0] is x_quantize else None
+            vector += both(product, pair) + strips(empty_strip, 0, 1, (pair - 4,)) + {6: [(invert_psi,)], 7: [(mean_psi,)]}.get(pair, []) + steps
         vector += strips(empty_strip, 2, 1) + [quant(y(1, Z))] + q2(y(2, 0)) + [quant(y(1, 1)), quant(y(2, 1))]
         vector += strips(empty_strip, 3, 1) + [quant(y(3, Z))] + q2(y(3, 0))[::-1] + [quant(y(0, 1)), quant(y(3, 1))]
-        vector += [sub(band) for band in range(7)] + [sub(7, 0, HALF), sub(7, HALF, WIDTH)]
+        vector += [sub(band) for band in range(7)]
+        vector += [sub(7, 0, HALF), sub(7, HALF, WIDTH)]
         sync = [(store, band, 0, WIDTH) for band in range(7)] + [(store, 7, 0, HALF), (store, 7, HALF, WIDTH)]
 
-        def g(s, first=0):
-            return ("grouped", *s, first)
-
-        rotate("wide", 3, [("wide", pair, None) for pair in range(1, PAIRS) if pair != 6])
-        rotate("flat", 7, [("flat", step[1] // PACK, step[2]) for step in scalar if step[0] is empty and step[1] % PACK == 0])
-        tenants["xg0"] = [("x_grouped", pair, 0) for pair in (0, 1, 3, 4, 5, 6, 7)]
-        tenants["xg1"] = [("x_grouped", pair, 1) for pair in (0, 1, 2, 3)]
-        tenants["gate_h"] = [g(wz0), g(wz1)]
-        tenants["gate_w"] = [g(w00), g(w10), g(y(0, Z)), ("x_grouped", 5, 1), g(y(1, 0)), ("x_grouped", 7, 1), g(y(2, 0))]
-        tenants["gate_a"] = [("x_grouped", 2, 0), g(w11), ("x_grouped", 4, 1), g(y(0, 0)), ("x_grouped", 6, 1), g(y(2, Z)), g(y(3, Z))]
-        tenants["gate_b"] = [g(y(1, 1)), g(y(3, 0))]
-        rotate("other", 4, [g(s) for s in [w01, y(0, 1), y(2, 1), y(1, Z), y(3, 1)]])
-
-        for pair in (0, 6):
-            for h in range(PASSES):
-                tenants[f"wide_pass{pair}{h}"] = [("wide", pair, h)]
-        for band, buffer in enumerate(name for name in sorted(tenants) if name.startswith("wide")):
+        whole_pairs = [step[1:] for step in scalar + vector if step[0] is widen and step[2] is None]
+        rotate("wide", 3, [("wide", *key) for key in sorted(whole_pairs)])
+        for step in scalar + vector:
+            if step[0] is widen and step[2] is not None:
+                tenants[f"wide_pass{step[1]}{step[2]}"] = [("wide", *step[1:])]
+        for band, buffer in zip(range(BANDS), sorted(name for name in tenants if name.startswith("wide"))):
             tenants[buffer].append(("result", band))
+        rotate("flat", 6, [("flat", step[1] // PACK, step[2]) for step in scalar if step[0] is empty and step[1] % PACK == 0])
+        after = dict(zip(range(4, PAIRS), full[1:] + [y(2, 0)]))
+        tenants["gate_z"] = [g(wz0), g(wz1), g(y(3, Z))]
+        tenants["gate_w"] = [g(w00), g(w10), g(y(0, Z))] + ([] if gates[4] else [g(after[4])])
+        tenants["gate_2"] = [xg(2, 0), g(w11)]
+        for pair in range(4, PAIRS):
+            if gates[pair]:
+                tenants[f"gate_{pair}"] = [gates[pair], g(after[pair])]
+        tenants["gate_y"] = tenants.get("gate_y", [g(y(1, 1))]) + [g(y(3, 0))]
+        tenants["late"] = [g(w01), g(y(0, 1))]
+        tenants["gate_2"].append(g(y(1, Z)))
+        tenants["gate_w"].append(g(y(2, 1)))
+        tenants["gate_4"].append(g(y(3, 1)))
+        used = [xg(2, 0)] + list(gates.values())
+        for h in range(PASSES):
+            tenants[f"xg{h}"] = [xg(pair, h) for pair in range(PAIRS) if xg(pair, h) not in used]
+
         queues = [vector, scalar, tensor, gpsimd, sync]
         tenant_before = {}
         for buffer, keys in tenants.items():

@@ -30,23 +30,17 @@ HALF = WIDTH // 2
 QUARTER = WIDTH // 4
 Z = 2
 BANDS = D // P
-BLOCK_BANDS = WIDTH // P
-STRIPS = WIDTH // P
-BANKS = 8
+SIDE_BANDS = WIDTH // P
+LAST_BAND = BANDS - 1
+DUOS = 4
 RUN = 4
-BLOCK = 16
-VECTOR_WIDENS = ((0, 0), (1, 0),)
-PREPARED = (0, 1, 2, 3, 4, 5, 6, 7)
-STRIP_RUN = 4
-GC = 384
-HEAD_BANKS = {("warm", 0): 6, ("warm", 1): 7, ("warm", 2): 6, ("warm", 3): 7, ("warm", 4): 7, ("warm", 5): 2, ("turned", 2, 0): 4, ("turned", 2, 1): 5, ("first", 0, 2): 6, ("first", 1, 2): 7, ("turned", 3, 0): 0, ("turned", 3, 1): 1,
-  ("first", 2, 2): 2, ("first", 3, 2): 3, ("turned", 4, 0): 6, ("turned", 4, 1): 7, ("first", 0, 0): 2, ("first", 1, 0): 3, ("first", 2, 0): 4, ("first", 3, 0): 2, ("turned", 0, 0): 0, ("turned", 0, 1): 1, ("turned", 1, 0): 2, ("turned", 1, 1): 3}
-TURN_RING = (0, 1, 6, 7)
-SUM_RING = (3, 5, 4, 2)
-FREED_RING = (6, 3, 7, 5, 4, 2)
-WARM = (0, 1, 2, 3, 4,)
-G0 = 320
+ROW = 16
+GPSIMD_COLUMNS = 384
+GPSIMD_FIRST_COLUMNS = 320
+VECTOR_WIDENS = ((0, 0), (1, 0))
 WARM_WIDTH = 272
+WIDE_BUFFERS = 3
+FLAT_BUFFERS = 6
 
 
 def tile_factoranalysisemloadinggradient_kernel(
@@ -68,62 +62,59 @@ def tile_factoranalysisemloadinggradient_kernel(
         x_view = x_bytes.rearrange("(g q j) f -> g q j f", q=P, j=PACK)
         p_view = p.rearrange("(g q j) d -> g q j d", q=P, j=PACK)
         beta_view = beta.rearrange("(g q j) d -> g q j d", q=P, j=PACK)
+        scale_view = x_scale.rearrange("o (g q j) -> (o g) q j", q=P, j=PACK)
         x_raw, w_raw = {}, {}
 
-        def load_x(first_pair, pairs):
+        def load_x(first_pair, pairs=1):
             raw = keep.tile([P, 2 * pairs, D], U8, name=f"x_raw{first_pair}")
             group, j = divmod(2 * first_pair, PACK)
             nc.sync.dma_start(out=raw[:], in_=x_view[group][:, j : j + 2 * pairs, :])
             for n in range(pairs):
                 x_raw[first_pair + n] = raw[:, 2 * n : 2 * n + 2, :].rearrange("q j f -> q (j f)")
 
-        def load_w(block, g):
-            raw = keep.tile([P, PACK, WIDTH], BF16, name=f"w_raw{block}{g}")
-            rows = beta_view[g] if block == Z else p_view[g][:, :, block * WIDTH : (block + 1) * WIDTH]
+        def load_w(side, g):
+            raw = keep.tile([P, PACK, WIDTH], BF16, name=f"w_raw{side}{g}")
+            rows = beta_view[g] if side == Z else p_view[g][:, :, side * WIDTH : (side + 1) * WIDTH]
             nc.sync.dma_start(out=raw[:], in_=rows)
-            w_raw[block, g] = raw[:]
-
-        scale = [keep.tile([P, PACK], F32, name=f"scale{g}") for g in range(PASSES)]
-        r16 = keep.tile([P, GROUPS, BLOCK], BF16, name="r16")
-        t16 = keep.tile([P, GROUPS, BLOCK], BF16, name="t16")
-        v_raw = keep.tile([P, BANDS, K], BF16, name="v_raw")
-        psi16 = keep.tile([P, BANDS, BLOCK], BF16, name="psi16")
+            w_raw[side, g] = raw[:]
 
         def load_scale(g):
-            nc.scalar.dma_start(out=scale[g][:], in_=x_scale.rearrange("o (g q j) -> (o g) q j", q=P, j=PACK)[g])
+            nc.scalar.dma_start(out=scale[g][:], in_=scale_view[g])
 
         def load_factor(tile, source):
             nc.sync.dma_start(out=tile[:, :, :PACK], in_=source.rearrange("(g q j) -> q g j", q=P, j=PACK))
 
-        def load_end():
-            nc.sync.dma_start(out=v_raw[:], in_=v.rearrange("(b q) k -> q b k", q=P))
-            with nc.allow_non_contiguous_dma(reason="one noise variance for each partition and band"):
-                nc.sync.dma_start(out=psi16[:, :, 0], in_=psi.rearrange("(b q) -> q b", q=P))
-
-        load_x(0, 1)
+        scale = [keep.tile([P, PACK], F32, name=f"scale{g}") for g in range(PASSES)]
+        r16 = keep.tile([P, GROUPS, ROW], BF16, name="r16")
+        t16 = keep.tile([P, GROUPS, ROW], BF16, name="t16")
+        v_raw = keep.tile([P, BANDS, K], BF16, name="v_raw")
+        psi16 = keep.tile([P, BANDS, ROW], BF16, name="psi16")
+        load_x(0)
         load_scale(0)
-        load_x(1, 1)
+        load_x(1)
         load_scale(1)
         load_w(Z, 0)
-        load_x(2, 1)
+        load_x(2)
         load_w(Z, 1)
-        load_x(3, 1)
+        load_x(3)
         load_w(0, 0)
         load_factor(t16, t)
         load_w(0, 1)
-        load_x(4, 1)
+        load_x(4)
         load_factor(r16, r)
         load_w(1, 0)
-        load_x(5, 1)
+        load_x(5)
         load_w(1, 1)
-        load_x(6, 2)
-        load_end()
+        load_x(6, pairs=2)
+        nc.sync.dma_start(out=v_raw[:], in_=v.rearrange("(b q) k -> q b k", q=P))
+        with nc.allow_non_contiguous_dma(reason="one noise variance for each partition and band"):
+            nc.sync.dma_start(out=psi16[:, :, 0], in_=psi.rearrange("(b q) -> q b", q=P))
 
-        factor = {block: keep.tile([P, UNITS], F32, name=f"factor{block}") for block in (0, Z)}
+        factor = {side: keep.tile([P, UNITS], F32, name=f"factor{side}") for side in (0, Z)}
         factor[1] = factor[0]
         psi_inv = keep.tile([P, BANDS], F32, name="psi_inv")
         psi_inv_mean = keep.tile([P, BANDS], F32, name="psi_inv_mean")
-        tiles, buffer_of = {}, {}
+        tiles, buffer_of, cut = {}, {}, set()
 
         def tile_of(key, shape, dtype):
             if key not in tiles:
@@ -137,17 +128,22 @@ def tile_factoranalysisemloadinggradient_kernel(
         def mx_tiles(key):
             return tile_of(("codes", *key), [P, WIDTH], U32), tile_of(("scales", *key), [P, WIDTH], U8)
 
-        def piece_of(slab, column):
-            edges = cuts.get(slab, (0, WIDTH))
-            return [(a, b) for a, b in zip(edges, edges[1:]) if column < b][0]
+        def grouped_key(slab, column=0):
+            return ("grouped", *slab, GPSIMD_COLUMNS if slab in cut and column >= GPSIMD_COLUMNS else 0)
 
         def grouped(slab, first, last):
-            a, b = piece_of(slab, first)
-            return tile_of(("grouped", *slab, a), [P, b - a, PACK], BF16)[:, first - a : last - a, :]
+            key = grouped_key(slab, first)
+            end = GPSIMD_COLUMNS if slab in cut and key[-1] == 0 else WIDTH
+            return tile_of(key, [P, end - key[-1], PACK], BF16)[:, first - key[-1] : last - key[-1], :]
 
-        def widen_factor(block):
-            source = t16 if block == Z else r16
-            nc.scalar.copy(out=factor[block][:].rearrange("q (g j) -> q g j", j=PACK), in_=source[:, :, :PACK])
+        def warm(n):
+            nc.tensor.matmul(
+                out=tile_of(("warm", n), [P, WARM_WIDTH], F32)[:], lhsT=zeros[:, :P], rhs=zeros[:], start=True, stop=True
+            )
+
+        def widen_factor(side):
+            source = t16 if side == Z else r16
+            nc.scalar.copy(out=factor[side][:].rearrange("q (g j) -> q g j", j=PACK), in_=source[:, :, :PACK])
 
         def invert_psi():
             nc.vector.reciprocal(out=psi_inv[:], in_=psi16[:, :, 0])
@@ -178,8 +174,9 @@ def tile_factoranalysisemloadinggradient_kernel(
         def widen(pair, g):
             passes = range(PASSES) if g is None else [g]
             tile = tile_of(("wide", pair, g), [P, 2 * len(passes) * K_PASS], BF16)
-            runs = [(0, 0, 2 * D)] if g is None else [(unit * K_PASS, unit * D + g * K_PASS, K_PASS) for unit in range(2)]
-            for place, first, count in runs:
+            whole = [(0, 0, 2 * D)]
+            by_unit = [(unit * K_PASS, unit * D + passes[0] * K_PASS, K_PASS) for unit in range(2)]
+            for place, first, count in whole if g is None else by_unit:
                 source = x_raw[pair][:, first : first + count].bitcast(FP8)
                 if (pair, g) in VECTOR_WIDENS:
                     target = tile[:].rearrange("p (u w e) -> p w u e", u=2, e=2)
@@ -196,8 +193,7 @@ def tile_factoranalysisemloadinggradient_kernel(
             for n, (unit, h) in enumerate((unit, h) for unit in range(2) for h in passes):
                 for u in range(2):
                     if (pair, g) in VECTOR_WIDENS:
-                        first = (2 * len(passes) * u + n) * P
-                        tiles["words", pair, h, unit, u] = words[:, first : first + P]
+                        tiles["words", pair, h, unit, u] = words[:, (2 * u + n) * P : (2 * u + n + 1) * P]
                     else:
                         tiles["words", pair, h, unit, u] = words[:, 2 * n * P + u : 2 * (n + 1) * P : 2]
 
@@ -208,11 +204,6 @@ def tile_factoranalysisemloadinggradient_kernel(
                     nc.tensor.transpose(
                         bank[:, u, unit * P : (unit + 1) * P], tiles["words", pair, g, unit, u], identity[:]
                     )
-
-        def warm(n):
-            nc.tensor.matmul(
-                out=tile_of(("warm", n), [P, WARM_WIDTH], F32)[:], lhsT=zeros[:, :P], rhs=zeros[:], start=True, stop=True
-            )
 
         def product(pair, g):
             target = tile_of(("x_grouped", pair, g), [P, 2 * P, 2, 2], BF16)
@@ -229,53 +220,67 @@ def tile_factoranalysisemloadinggradient_kernel(
                 in_=tiles["x_grouped", pair, g][:].rearrange("q c u e -> q (c u e)"),
             )
 
-        def first_pass(target, unit, block, g, w_cols, start, stop):
+        def first_pass(target, unit, side, g, w_cols):
             x_codes, x_scales = mx_tiles(("x", unit // 2))
             cols = slice((2 * g + unit % 2) * P, (2 * g + unit % 2 + 1) * P)
-            w_codes, w_scales = mx_tiles(("w", block, g))
+            w_codes, w_scales = mx_tiles(("w", side, g))
             nc.tensor.matmul_mx(
                 out=target,
                 lhsT=x_codes[:, cols].bitcast(FP8X4),
                 lhsT_scale=x_scales[:, cols],
                 rhs=w_codes[:, w_cols].bitcast(FP8X4),
                 rhs_scale=w_scales[:, w_cols],
-                start=start,
-                stop=stop,
+                start=(g == 0),
+                stop=(g == PASSES - 1),
             )
 
-        def multiply(unit, block, g):
-            first_pass(tile_of(("first", unit, block), [P, WIDTH], F32)[:], unit, block, g, slice(0, WIDTH), g == 0, g == PASSES - 1)
+        def multiply(unit, side, g):
+            first_pass(tile_of(("first", unit, side), [P, WIDTH], F32)[:], unit, side, g, slice(0, WIDTH))
 
-        def multiply_strip(group, block, strip):
-            bank = tile_of(("strip", group, block, strip), [P, PACK, P], F32)
-            order = [(g, j) for g in range(PASSES) for j in range(PACK)]
-            for g, j in order:
-                cols = slice(strip * P, (strip + 1) * P)
-                first_pass(bank[:, j, :], PACK * group + j, block, g, cols, (g, j) == order[0], (g, j) == order[-1])
+        def multiply_duo(group, side, duo):
+            half, u = divmod(duo, 2)
+            bank = tile_of(("duo", group, side, duo), [P, 2, HALF], F32)
+            for e in range(2):
+                for g in range(PASSES):
+                    first_pass(bank[:, e, :], PACK * group + 2 * u + e, side, g, slice(half * HALF, (half + 1) * HALF))
 
-        def empty(unit, block):
+        def empty(unit, side):
             group, j = divmod(unit, PACK)
             nc.scalar.activation(
-                out=tile_of(("flat", group, block), [P, PACK, WIDTH], BF16)[:, j, :],
-                in_=tiles["first", unit, block][:],
+                out=tile_of(("flat", group, side), [P, PACK, WIDTH], BF16)[:, j, :],
+                in_=tiles["first", unit, side][:],
                 func=COPY,
-                scale=factor[block][:, unit : unit + 1],
+                scale=factor[side][:, unit : unit + 1],
             )
 
-        def empty_strip(group, block, strip):
-            target = grouped(("y", group, block), strip * P, (strip + 1) * P)
-            factors = factor[block][:, PACK * group : PACK * (group + 1)].rearrange("q (a j b) -> q a j b", a=1, b=1)
+        def empty_duo(group, side, duo):
+            half, u = divmod(duo, 2)
+            first = PACK * group + 2 * u
+            factors = factor[side][:, first : first + 2].rearrange("q (o e) -> q o e", o=1)
             nc.vector.tensor_tensor(
-                out=target.rearrange("q (c i) j -> q c j i", i=STRIP_RUN),
-                in0=tiles["strip", group, block, strip][:].rearrange("q j (c i) -> q c j i", i=STRIP_RUN),
-                in1=factors.to_broadcast([P, P // STRIP_RUN, PACK, STRIP_RUN]),
+                out=tile_of(("paired", group, side, half), [P, 2, HALF, 2], BF16)[:, u],
+                in0=tiles["duo", group, side, duo][:].rearrange("q e c -> q c e"),
+                in1=factors.to_broadcast([P, HALF, 2]),
                 op=MULT,
             )
 
-        def accumulate(group, band, first=0, last=K):
-            block, place = divmod(band, BLOCK_BANDS)
+        def join(group, side, half, engine):
+            target = grouped(("y", group, side), half * HALF, (half + 1) * HALF)
+            source = tiles["paired", group, side, half][:]
+            if engine == "vector":
+                nc.vector.tensor_copy(
+                    out=target.rearrange("q c (u e) -> q c u e", e=2), in_=source.rearrange("q u c e -> q c u e")
+                )
+            else:
+                nc.scalar.copy(
+                    out=target.rearrange("q c j -> q (c j)").bitcast(U32).rearrange("q (c u) -> q c u", u=2),
+                    in_=source.rearrange("q u c e -> q u (c e)").bitcast(U32).rearrange("q u c -> q c u"),
+                )
+
+        def accumulate(group, band, first, last):
+            side, place = divmod(band, SIDE_BANDS)
             cols = slice(place * P, (place + 1) * P)
-            e_codes, e_scales = mx_tiles(("y", group, block))
+            e_codes, e_scales = mx_tiles(("y", group, side))
             z_codes, z_scales = mx_tiles(("y", group, Z))
             nc.tensor.matmul_mx(
                 out=tile_of(("sum", band, first), [P, last - first], F32)[:],
@@ -295,214 +300,182 @@ def tile_factoranalysisemloadinggradient_kernel(
                 scale=psi_inv[:, band : band + 1],
             )
 
-        def subtract(band, first, last):
-            tile = tile_of(("result", band), [P, K], F32)[:, first:last]
-            if band in PREPARED:
-                mean, other = psi_inv_mean[:, band : band + 1], tile
-            else:
-                mean, other = 1.0 / N, v_raw[:, band, first:last]
+        def finish(band, first, last):
+            tile = tiles["result", band][:, first:last]
             nc.vector.scalar_tensor_tensor(
-                out=tile, in0=tiles["sum", band, first][:], scalar=mean, in1=other, op0=MULT, op1=SUBTRACT
+                out=tile,
+                in0=tiles["sum", band, first][:],
+                scalar=psi_inv_mean[:, band : band + 1],
+                in1=tile,
+                op0=MULT,
+                op1=SUBTRACT,
             )
-
-        def scale_sum(band):
-            nc.scalar.activation(
-                out=tile_of(("scaled", band), [P, K], F32)[:],
-                in_=tiles["sum", band, 0][:],
-                func=COPY,
-                scale=psi_inv_mean[:, band : band + 1],
-            )
-
-        def take_away(band):
-            before = tiles["result", band]
-            tiles["result", band] = tile_of(("ended", band), [P, K], F32)
-            nc.gpsimd.tensor_tensor(out=tiles["result", band][:], in0=tiles["scaled", band][:], in1=before[:], op=SUBTRACT)
-
-        def divide(band, engine):
-            tile, inverse = tiles["result", band], psi_inv[:, band : band + 1]
-            if engine == "vector":
-                nc.vector.tensor_scalar(out=tile[:], in0=tile[:], scalar1=inverse, scalar2=None, op0=MULT)
-            else:
-                nc.scalar.activation(out=tile[:], in_=tile[:], func=COPY, scale=inverse)
 
         def store(band, first, last):
             nc.sync.dma_start(out=out[band * P : (band + 1) * P, first:last], in_=tiles["result", band][:, first:last])
 
+        def w(side, g):
+            return ("w", side, g)
+
+        def y(group, side):
+            return ("y", group, side)
+
         def mix(slab, engine, first=0, last=WIDTH):
             return (interleave, slab, engine, first, last)
+
+        def rest(slab, engine):
+            return mix(slab, engine, GPSIMD_COLUMNS, WIDTH)
 
         def quant(slab, first=0, last=WIDTH):
             return (quantize, slab, first, last)
 
+        def quant_cut(slab):
+            return [quant(slab, GPSIMD_COLUMNS, WIDTH), quant(slab, 0, GPSIMD_COLUMNS)]
+
         def both(step, pair):
             return [(step, pair, g) for g in range(PASSES)]
 
-        def first_stage(group, block, rows=range(PACK)):
-            return [(multiply, PACK * group + j, block, g) for j in rows for g in range(PASSES)]
+        def by_unit(pair, *sides):
+            return [(multiply, 2 * pair + n, side, g) for side in sides for n in range(2) for g in range(PASSES)]
 
-        def strips(step, group, block, which=range(STRIPS)):
-            return [(step, group, block, strip) for strip in which]
+        def by_pass(pair, side):
+            return [(multiply, 2 * pair + n, side, g) for g in range(PASSES) for n in range(2)]
 
+        def duos(step, group):
+            return [(step, group, 1, duo) for duo in range(DUOS)]
 
-        def rotate(name, count, keys):
-            for n, key in enumerate(keys):
-                tenants.setdefault(f"{name}{n % count}", []).append(key)
+        halves = [(0, HALF), (HALF, WIDTH)]
+        ends = [(band, 0, K) for band in range(LAST_BAND)] + [(LAST_BAND, *half) for half in halves]
 
-        def sub(band, first=0, last=WIDTH):
-            return (subtract, band, first, last)
+        whole_slabs = {4: y(0, Z), 5: y(0, 0), 6: y(1, 0), 7: y(2, Z)}
+        gpsimd = [mix(w(Z, 0), "gpsimd", 0, GPSIMD_FIRST_COLUMNS)]
+        gpsimd += [mix(slab, "gpsimd", 0, GPSIMD_COLUMNS) for slab in (w(Z, 1), w(1, 0), w(1, 1))]
+        gpsimd += [mix(slab, "gpsimd") for slab in whole_slabs.values()]
+        gpsimd += [mix(slab, "gpsimd", 0, GPSIMD_COLUMNS) for slab in (y(2, 0), y(3, 0))]
+        for slab in (w(Z, 1), y(2, 0), y(3, 0)):
+            cut.add(slab)
 
-        def y(group, block):
-            return ("y", group, block)
+        tensor = [(warm, 0)]
+        for pair in range(4):
+            tensor += [(warm, pair + 1)] + both(turn, pair)
+        tensor += by_pass(0, Z) + by_unit(1, Z)
+        tensor += both(turn, 4) + by_unit(0, 0) + by_unit(1, 0) + by_pass(2, Z) + by_unit(2, 0)
+        tensor += both(turn, 5) + by_unit(3, Z, 0) + [(multiply_duo, 0, 1, 0)] + by_unit(2, 1)
+        tensor += both(turn, 6) + by_unit(4, Z) + [(multiply_duo, 0, 1, 1)] + by_unit(4, 0)
+        tensor += both(turn, 7) + by_unit(5, Z) + [(multiply_duo, 0, 1, 2)] + by_unit(5, 0) + by_unit(3, 1)
+        tensor += by_unit(6, Z) + [(multiply_duo, 0, 1, 3)] + by_unit(6, 0)
+        tensor += duos(multiply_duo, 2) + by_unit(7, Z, 0) + duos(multiply_duo, 3)
 
-        tenants, cuts = {}, {}
-        wz0, wz1, w00, w01, w10, w11 = [("w", block, g) for block in (Z, 0, 1) for g in range(PASSES)]
-
-        def rest(s, engine="scalar"):
-            return mix(s, engine, GC, WIDTH)
-
-        def q2(s):
-            return [quant(s, GC, WIDTH), quant(s, 0, GC)]
-
-        def pair_stage(pair, blocks=(Z, 0)):
-            return [step for block in blocks for step in first_stage(pair // 2, block, (2, 3) if pair % 2 else (0, 1))]
-
-        def by_pass(pair, block):
-            return [(multiply, 2 * pair + n, block, g) for g in range(PASSES) for n in range(2)]
-
-        def acc(group, band, first=0, last=K):
-            return (accumulate, group, band, first, last)
-
-        def w(n):
-            return [(warm, n)] if n in WARM else []
-
-        def g(s, first=0):
-            return ("grouped", *s, first)
-
-        def xg(pair, h):
-            return ("x_grouped", pair, h)
-
-        full = [y(0, Z), y(0, 0), y(1, 0), y(2, Z)]
-        gpsimd = [mix(wz0, "gpsimd", 0, G0)] + [mix(s, "gpsimd", 0, GC) for s in [wz1, w10, w11]] + [mix(s, "gpsimd") for s in full] + [mix(s, "gpsimd", 0, GC) for s in (y(2, 0), y(3, 0))]
-        for s in [wz1, y(2, 0), y(3, 0)]:
-            cuts[s] = (0, GC, WIDTH)
-
-        tensor = w(0) + w(1) + both(turn, 0) + w(2) + both(turn, 1) + w(3) + both(turn, 2) + w(4) + both(turn, 3) + w(5) + [(multiply, unit, Z, 0) for unit in range(2)]
-        tensor += [(multiply, unit, Z, 1) for unit in range(2)] + first_stage(0, Z, (2, 3))
-        tensor += both(turn, 4) + first_stage(0, 0) + by_pass(2, Z) + pair_stage(2, (0,))
-        tensor += both(turn, 5) + pair_stage(3) + strips(multiply_strip, 0, 1, (0,)) + pair_stage(2, (1,))
-        tensor += both(turn, 6) + pair_stage(4, (Z,)) + strips(multiply_strip, 0, 1, (1,)) + pair_stage(4, (0,))
-        tensor += both(turn, 7) + pair_stage(5, (Z,)) + strips(multiply_strip, 0, 1, (2,)) + pair_stage(5, (0,)) + pair_stage(3, (1,)) + pair_stage(6, (Z,)) + strips(multiply_strip, 0, 1, (3,)) + pair_stage(6, (0,))
-        tensor += strips(multiply_strip, 2, 1) + pair_stage(7) + strips(multiply_strip, 3, 1)
-
-        scalar = [(widen, 0, 1), (widen, 1, 1), mix(wz0, "scalar", G0, WIDTH), (widen, 2, None), rest(wz1), (widen, 3, None)]
-        scalar += [mix(w00, "scalar"), (widen_factor, Z), (widen, 4, None)]
-        extra = {(empty, 3, 0): [(widen, 5, None)], (empty, 5, 0): [(widen, 6, 0)], (empty, 7, 0): [(widen, 6, 1)], (empty, 5, 1): [(widen, 7, None)],
-                 (empty, 9, Z): [mix(y(1, Z), "scalar", 0, QUARTER)], (empty, 9, 0): [mix(y(1, Z), "scalar", QUARTER, WIDTH - QUARTER)], (empty, 11, Z): [mix(y(1, Z), "scalar", WIDTH - QUARTER, WIDTH)], (empty, 13, Z): [rest(y(2, 0))], (empty, 13, 0): [mix(y(1, 1), "scalar")]}
+        scalar = [(widen, 0, 1), (widen, 1, 1), mix(w(Z, 0), "scalar", GPSIMD_FIRST_COLUMNS, WIDTH), (widen, 2, None)]
+        scalar += [rest(w(Z, 1), "scalar"), (widen, 3, None), mix(w(0, 0), "scalar"), (widen_factor, Z), (widen, 4, None)]
+        behind = {
+            (empty, 2, Z): [(widen_factor, 0)],
+            (empty, 3, 0): [(widen, 5, None)],
+            (empty, 5, 0): [(widen, 6, 0)],
+            (empty, 7, 0): [(widen, 6, 1)],
+            (empty, 5, 1): [(widen, 7, None)],
+            (empty, 9, Z): [mix(y(1, Z), "scalar", 0, QUARTER)],
+            (empty, 9, 0): [mix(y(1, Z), "scalar", QUARTER, WIDTH - QUARTER)],
+            (empty, 11, Z): [mix(y(1, Z), "scalar", WIDTH - QUARTER, WIDTH)],
+            (empty, 13, Z): [rest(y(2, 0), "scalar")],
+            (empty, 13, 0): [mix(y(1, 1), "scalar")],
+            (empty, 15, 0): [mix(y(3, Z), "scalar"), rest(y(3, 0), "scalar")],
+        }
         for step in tensor:
-            if step == (multiply, 3, Z, 1):
-                scalar.append((widen_factor, 0))
             if step[0] is multiply and step[3] == PASSES - 1:
-                scalar.append((empty, *step[1:3]))
-                scalar += extra.get(scalar[-1], [])
-        scalar += [mix(y(3, Z), "scalar"), rest(y(3, 0))]
-        scalar += [(prepare, band) for band in range(8)]
+                scalar += [(empty, *step[1:3])] + behind.get((empty, *step[1:3]), [])
+        scalar += [(prepare, 0)] + [(join, 3, 1, half, "scalar") for half in range(2)]
+        scalar += [(prepare, band) for band in range(1, BANDS)]
 
-        tensor += [acc(group, band) for group in range(GROUPS) for band in range(BLOCK_BANDS)]
-        tensor += [acc(group, band) for band in (4, 5, 6) for group in (1, 2, 0, 3)]
-        tensor += [acc(group, 7, first, first + HALF) for first in (0, HALF) for group in range(4)]
-        freed = {(multiply, 10, 0, 0): [6], (multiply, 7, 1, 0): [7], (multiply, 13, 0, 0): [0], (multiply_strip, 2, 1, 1): [1]}
-        hold = {("strip", 0, 1, 1): 1}
-        group_order = {band: [step[1] for step in tensor if step[0] is accumulate and step[2:4] == (band, 0)] for band in range(BANDS)}
+        group_order = {band: (2, 0, 1, 3) if band in (4, 5) else tuple(range(GROUPS)) for band in range(BANDS)}
+        tensor += [(accumulate, group, band, 0, K) for group in range(GROUPS) for band in range(SIDE_BANDS)]
+        tensor += [(accumulate, group, band, 0, K) for group in group_order[4] for band in (4, 5)]
+        tensor += [(accumulate, group, *end) for end in ends[6:] for group in range(GROUPS)]
 
-        def made(step):
-            if step[0] is turn:
-                return ("turned", *step[1:])
-            if step[0] is warm:
-                return ("warm", step[1])
-            if step[0] is multiply and step[3] == 0:
-                return ("first", *step[1:3])
-            if step[0] is multiply_strip:
-                return ("strip", *step[1:])
-            if step[0] is accumulate and step[1] == group_order[step[2]][0]:
-                return ("sum", *step[2:4])
-            return None
+        vector = [(widen, *part) for part in VECTOR_WIDENS]
+        vector += both(product, 0) + [(x_quantize, 0, 0), quant(w(Z, 0)), (x_quantize, 0, 1)]
+        vector += both(product, 1) + quant_cut(w(Z, 1)) + both(x_quantize, 1)
+        vector += [mix(w(0, 1), "vector"), quant(w(0, 0)), quant(w(0, 1))]
+        vector += both(product, 2) + both(x_quantize, 2) + both(product, 3) + both(x_quantize, 3)
+        vector += [rest(w(1, 0), "vector"), rest(w(1, 1), "vector"), quant(w(1, 0)), quant(w(1, 1))]
+        small = {6: [(invert_psi,)], 7: [(mean_psi,)]}
+        for duo, (pair, slab) in enumerate(whole_slabs.items()):
+            vector += both(product, pair) + [(empty_duo, 0, 1, duo)] + small.get(pair, []) + [(x_quantize, pair, 0)]
+            vector += [(join, 0, 1, duo // 2, "vector")] if duo % 2 else []
+            vector += [(x_quantize, pair, 1), quant(slab)]
+        vector += duos(empty_duo, 2) + [(join, 2, 1, 0, "vector"), quant(y(1, Z)), (join, 2, 1, 1, "vector")]
+        vector += quant_cut(y(2, 0)) + [quant(y(2, 1))]
+        vector += duos(empty_duo, 3) + [quant(y(3, Z))] + quant_cut(y(3, 0))[::-1] + [quant(y(0, 1)), quant(y(1, 1))]
+        for end, half in zip(ends, halves):
+            vector += [(finish, *end), quant(y(3, 1), *half)]
+        vector += [(finish, *end) for end in ends[2:]]
 
-        ring = {"turned": list(TURN_RING), "sums": list(SUM_RING)}
-        held = []
+        sync = [(store, *end) for end in ends]
+
+        tenants = {}
+
+        def lodge(buffer, *keys):
+            tenants.setdefault(buffer, []).extend(keys)
+
+        ring = [2, 3]
+        enters = {
+            (multiply, 2, 0, 0): 4,
+            (multiply, 5, Z, 0): 5,
+            (multiply, 10, 0, 0): 6,
+            (multiply, 7, 1, 0): 7,
+            (multiply, 13, 0, 0): 0,
+            (multiply_duo, 2, 1, 1): 1,
+        }
         for step in tensor:
-            ring["sums"] = freed.get(step, []) + ring["sums"]
-            key = made(step)
-            if key is not None:
-                banks = ring["turned" if key[0] == "turned" else "sums"]
-                if key in HEAD_BANKS:
-                    bank = HEAD_BANKS[key]
-                else:
-                    bank = banks[0]
-                    banks.remove(bank)
-                    held.append([bank, hold.get(key, 0), banks])
-                    for entry in list(held):
-                        if entry[1] == 0:
-                            entry[2].append(entry[0])
-                            held.remove(entry)
-                        entry[1] = entry[1] - 1
-                tenants.setdefault(f"bank{bank}", []).append(key)
+            name, args = step[0], step[1:]
+            ring = ([enters[step]] if step in enters else []) + ring
+            if name is warm:
+                lodge(f"bank{6 + args[0] % 2}", ("warm", *args))
+            elif name is turn:
+                lodge(f"bank{(2 * args[0] if args[0] < 3 else 0 if args[0] % 2 else 6) + args[1]}", ("turned", *args))
+            elif name is multiply and args[0] < 2 and args[1:] == (Z, 0):
+                lodge(f"bank{6 + args[0]}", ("first", *args[:2]))
+            elif name is multiply_duo or (name is multiply and args[2] == 0):
+                lodge(f"bank{ring[0]}", ("duo", *args) if name is multiply_duo else ("first", *args[:2]))
+                ring = ring[1:] + ring[:1]
+            elif name is accumulate and args[0] == group_order[args[1]][0]:
+                lodge(f"bank{ring[0]}", ("sum", *args[1:3]))
+                ring = ring[1:] + ring[:1]
 
-        vector = [(widen, 0, 0), (widen, 1, 0)] + both(product, 0) + [(x_quantize, 0, 0), quant(wz0), (x_quantize, 0, 1)]
-        vector += both(product, 1) + q2(wz1) + both(x_quantize, 1) + [mix(w01, "vector"), quant(w00), quant(w01)]
-        vector += both(product, 2) + both(x_quantize, 2)
-        vector += both(product, 3) + both(x_quantize, 3) + [rest(w10, "vector"), rest(w11, "vector"), quant(w10), quant(w11)]
-        tail = {4: [quant(full[0])] + [], 5: [quant(full[1])], 6: [quant(full[2])], 7: [quant(full[3])]}
-        gates = {}
-        for pair in range(4, PAIRS):
-            steps = both(x_quantize, pair) + tail[pair]
-            if steps[-2][0] is widen:
-                steps = [steps[0], steps[-2]] + steps[1:-2] + steps[-1:]
-            gates[pair] = xg(*steps[-2][1:]) if steps[-2][0] is x_quantize else None
-            vector += both(product, pair) + strips(empty_strip, 0, 1, (pair - 4,)) + {6: [(invert_psi,)], 7: [(mean_psi,)]}.get(pair, []) + steps
-        vector += strips(empty_strip, 2, 1) + [quant(y(1, Z))] + q2(y(2, 0)) + [quant(y(1, 1)), quant(y(2, 1))]
-        vector += strips(empty_strip, 3, 1) + [quant(y(3, Z))] + q2(y(3, 0))[::-1] + [quant(y(0, 1)), quant(y(3, 1))]
-        vector += [sub(band) for band in range(7)]
-        vector += [sub(7, 0, HALF), sub(7, HALF, WIDTH)]
-        sync = [(store, band, 0, WIDTH) for band in range(7)] + [(store, 7, 0, HALF), (store, 7, HALF, WIDTH)]
-
-        whole_pairs = [step[1:] for step in scalar + vector if step[0] is widen and step[2] is None]
-        rotate("wide", 3, [("wide", *key) for key in sorted(whole_pairs)])
-        for step in scalar + vector:
-            if step[0] is widen and step[2] is not None:
-                tenants[f"wide_pass{step[1]}{step[2]}"] = [("wide", *step[1:])]
+        widened = sorted((step[1:] for step in scalar + vector if step[0] is widen), key=lambda part: part[0])
+        for n, part in enumerate(part for part in widened if part[1] is None):
+            lodge(f"wide{n % WIDE_BUFFERS}", ("wide", *part))
+        for part in widened:
+            if part[1] is not None:
+                lodge(f"wide_pass{part[0]}{part[1]}", ("wide", *part))
         for band, buffer in zip(range(BANDS), sorted(name for name in tenants if name.startswith("wide"))):
-            tenants[buffer].append(("result", band))
-        rotate("flat", 6, [("flat", step[1] // PACK, step[2]) for step in scalar if step[0] is empty and step[1] % PACK == 0])
-        after = dict(zip(range(4, PAIRS), full[1:] + [y(2, 0)]))
-        tenants["gate_z"] = [g(wz0), g(wz1), g(y(3, Z))]
-        tenants["gate_w"] = [g(w00), g(w10), g(y(0, Z))] + ([] if gates[4] else [g(after[4])])
-        tenants["gate_2"] = [xg(2, 0), g(w11)]
-        for pair in range(4, PAIRS):
-            if gates[pair]:
-                tenants[f"gate_{pair}"] = [gates[pair], g(after[pair])]
-        tenants["gate_y"] = tenants.get("gate_y", [g(y(1, 1))]) + [g(y(3, 0))]
-        tenants["late"] = [g(w01), g(y(0, 1))]
-        tenants["gate_2"].append(g(y(1, Z)))
-        tenants["gate_w"].append(g(y(2, 1)))
-        tenants["gate_4"].append(g(y(3, 1)))
-        used = [xg(2, 0)] + list(gates.values())
-        for h in range(PASSES):
-            tenants[f"xg{h}"] = [xg(pair, h) for pair in range(PAIRS) if xg(pair, h) not in used]
+            lodge(buffer, ("result", band))
+        for n, step in enumerate(step for step in scalar if step[0] is empty and step[1] % PACK == 0):
+            lodge(f"flat{n % FLAT_BUFFERS}", ("flat", step[1] // PACK, step[2]))
 
-        queues = [vector, scalar, tensor, gpsimd, sync]
+        lodge("gate_z", grouped_key(w(Z, 0)), grouped_key(w(Z, 1)), grouped_key(y(3, Z)))
+        lodge("gate_w", grouped_key(w(0, 0)), grouped_key(w(1, 0)), grouped_key(y(0, Z)), grouped_key(y(2, 1)))
+        lodge("gate_2", ("x_grouped", 2, 0), grouped_key(w(1, 1)), grouped_key(y(1, Z)))
+        for pair, slab in zip(whole_slabs, [*whole_slabs.values()][1:] + [y(2, 0)]):
+            lodge(f"gate_{pair}", ("x_grouped", pair, 1), grouped_key(slab))
+        lodge("gate_7", grouped_key(y(3, 0)))
+        lodge("gate_4", grouped_key(y(3, 1)))
+        lodge("late", grouped_key(w(0, 1)), grouped_key(y(0, 1)))
+        lodge("x_grouped0", *[("x_grouped", pair, 0) for pair in range(PAIRS) if pair != 2])
+        lodge("x_grouped1", *[("x_grouped", pair, 1) for pair in range(PAIRS) if pair not in whole_slabs])
+
         tenant_before = {}
         for buffer, keys in tenants.items():
             for before, key in zip([None] + keys, keys):
                 buffer_of[key], tenant_before[key] = buffer, before
 
-        group_order = {band: [step[1] for step in tensor if step[0] is accumulate and step[2] == band] for band in range(BANDS)}
         def touches(step):
             name, args = step[0], step[1:]
             whole = (0, WIDTH)
-            if name is widen:
-                return [], [(("wide", *args), *whole)]
             if name is warm:
                 return [], [(("warm", *args), *whole)]
+            if name is widen:
+                return [], [(("wide", *args), *whole)]
             if name is turn:
                 return [(("wide", args[0], None), *whole), (("wide", *args), *whole)], [(("turned", *args), *whole)]
             if name is product:
@@ -512,65 +485,59 @@ def tile_factoranalysisemloadinggradient_kernel(
             if name is interleave:
                 slab, first, last = args[0], args[2], args[3]
                 source = [(("flat", *slab[1:]), *whole)] if slab[0] == "y" else []
-                return source, [(("grouped", *slab, piece_of(slab, first)[0]), first, last)]
+                return source, [(grouped_key(slab, first), first, last)]
             if name is quantize:
-                return [(("grouped", *args[0], piece_of(*args[:2])[0]), *args[1:])], [args]
+                return [(grouped_key(*args[:2]), *args[1:])], [args]
             if name is multiply:
-                unit, block, g = args
-                before = [(("first", unit, block), 0, g)] if g else []
-                return before + [(("x", unit // 2, g), *whole), (("w", block, g), *whole)], [(("first", unit, block), g, g + 1)]
-            if name is multiply_strip:
-                group, block = args[:2]
-                x_keys = [("x", 2 * group + n, g) for n in range(2) for g in range(PASSES)]
-                w_keys = [("w", block, g) for g in range(PASSES)]
-                return [(key, *whole) for key in x_keys + w_keys], [(("strip", *args), *whole)]
-            if name is empty:
-                return [(("first", *args), *whole), (("factor", args[1] == Z), *whole)], [(("flat", args[0] // PACK, args[1]), *whole)]
-            if name is empty_strip:
-                group, block, strip = args
-                return [(("strip", *args), *whole), (("factor", block == Z), *whole)], [(("grouped", "y", group, block, piece_of(("y", group, block), strip * P)[0]), strip * P, (strip + 1) * P)]
+                unit, side, g = args
+                read = [(("first", unit, side), 0, g), (("x", unit // 2, g), *whole), (w(side, g), *whole)]
+                return read, [(("first", unit, side), g, g + 1)]
+            if name is multiply_duo:
+                group, side, duo = args
+                keys = [key for g in range(PASSES) for key in (("x", 2 * group + duo % 2, g), w(side, g))]
+                return [(key, *whole) for key in keys], [(("duo", *args), *whole)]
             if name is widen_factor:
                 return [], [(("factor", args[0] == Z), *whole)]
+            if name is empty:
+                read = [(("first", *args), *whole), (("factor", args[1] == Z), *whole)]
+                return read, [(("flat", args[0] // PACK, args[1]), *whole)]
+            if name is empty_duo:
+                read = [(("duo", *args), *whole), (("factor", args[1] == Z), *whole)]
+                return read, [(("paired", *args[:2], args[2] // 2), *whole)]
+            if name is join:
+                return [(("paired", *args[:3]), *whole)], [(grouped_key(y(*args[:2])), *halves[args[2]])]
             if name is accumulate:
                 group, band, first = args[:3]
-                block, place = divmod(band, BLOCK_BANDS)
+                side, place = divmod(band, SIDE_BANDS)
                 n = group_order[band].index(group)
-                before = [(("sum", band, first), 0, n)] if n else []
-                return before + [(("y", group, block), place * P, (place + 1) * P), (("y", group, Z), *whole)], [(("sum", band, first), n, n + 1)]
+                read = [(("sum", band, first), 0, n), (y(group, side), place * P, (place + 1) * P), (y(group, Z), *whole)]
+                return read, [(("sum", band, first), n, n + 1)]
             if name is invert_psi:
                 return [], [(("psi_inv",), *whole)]
             if name is mean_psi:
                 return [(("psi_inv",), *whole)], [(("psi_inv_mean",), *whole)]
             if name is prepare:
-                return [(("psi_inv",), *whole)], [(("prepared", args[0]), *whole), (("result", args[0]), 0, 0)]
-            if name is subtract:
-                band = args[0]
-                made = [(("prepared", band), *whole), (("psi_inv_mean",), *whole)] if band in PREPARED else []
-                return [(("sum", band, args[1]), *whole)] + made, [(("result" if band in PREPARED else "difference", band), *args[1:])]
-            if name is scale_sum:
-                return [(("sum", args[0], 0), *whole), (("psi_inv_mean",), *whole)], [(("scaled", args[0]), *whole)]
-            if name is take_away:
-                return [(("scaled", args[0]), *whole), (("prepared", args[0]), *whole)], [(("result", args[0]), *whole), (("ended", args[0]), *whole)]
-            if name is divide:
-                return [(("difference", args[0]), *whole), (("psi_inv",), *whole)], [(("result", args[0]), *whole)]
-            return [(("result", args[0]), *args[1:])], []
+                return [(("psi_inv",), *whole)], [(("result", *args), *whole)]
+            if name is finish:
+                read = [(("sum", *args[:2]), *whole), (("result", args[0]), *whole), (("psi_inv_mean",), *whole)]
+                return read, [(("finished", args[0]), *args[1:])]
+            return [(("finished", args[0]), *args[1:])], []
 
+        queues = [vector, scalar, tensor, gpsimd, sync]
         steps = [step for queue in queues for step in queue]
         waits = {step: set() for step in steps}
         for step in steps:
             read, written = touches(step)
             for other in steps:
                 other_read, other_written = touches(other)
-                for key, first, last in read:
-                    if any(key == k and first < b and a < last for k, a, b in other_written):
-                        waits[step].add(other)
-                for key, first, last in written:
-                    if any(k == tenant_before.get(key) for k, a, b in other_read + other_written):
-                        waits[step].add(other)
+                if any(key == k and first < b and a < last for key, first, last in read for k, a, b in other_written):
+                    waits[step].add(other)
+                if any(k == tenant_before.get(key) for key, a, b in written for k, c, d in other_read + other_written):
+                    waits[step].add(other)
         done = set()
         while any(queues):
-            ready = [queue for queue in queues if queue and all(wait in done for wait in waits[queue[0]])]
-            step = ready[0][0]
+            queue = [queue for queue in queues if queue and all(wait in done for wait in waits[queue[0]])][0]
+            step = queue[0]
             step[0](*step[1:])
             done.add(step)
-            ready[0].remove(step)
+            queue.remove(step)

@@ -26,6 +26,7 @@ GROUPS = N // K_PASS
 UNITS = N // P
 PAIRS = UNITS // 2
 WIDTH = 512
+BANKS = 8
 HALF = WIDTH // 2
 QUARTER = WIDTH // 4
 Z = 2
@@ -36,11 +37,7 @@ DUOS = 4
 RUN = 4
 ROW = 16
 GPSIMD_COLUMNS = 384
-GPSIMD_FIRST_COLUMNS = 320
-VECTOR_WIDENS = ((0, 0), (1, 0))
 WARM_WIDTH = 272
-WIDE_BUFFERS = 3
-FLAT_BUFFERS = 6
 
 
 def tile_factoranalysisemloadinggradient_kernel(
@@ -52,6 +49,8 @@ def tile_factoranalysisemloadinggradient_kernel(
         psum = ctx.enter_context(tc.psum_pool(name="psum", bufs=1))
         ctx.enter_context(tc.manual_schedule())
 
+        factor_rows = keep.tile([P, K_PASS], BF16, name="factor_rows")
+        nc.vector.memset(factor_rows[:].bitcast(U32), 0)
         zeros = keep.tile([P, WARM_WIDTH], F32, name="zeros")
         nc.vector.memset(zeros[:], 0.0)
         identity = keep.tile([P, P], F32, name="identity")
@@ -63,7 +62,9 @@ def tile_factoranalysisemloadinggradient_kernel(
         p_view = p.rearrange("(g q j) d -> g q j d", q=P, j=PACK)
         beta_view = beta.rearrange("(g q j) d -> g q j d", q=P, j=PACK)
         scale_view = x_scale.rearrange("o (g q j) -> (o g) q j", q=P, j=PACK)
-        x_raw, w_raw = {}, {}
+        x_raw = {}
+        tiles, buffer_of, cuts = {}, {}, {}
+        free_banks, held = list(range(BANKS)), {}
 
         def load_x(first_pair, pairs=1):
             raw = keep.tile([P, 2 * pairs, D], U8, name=f"x_raw{first_pair}")
@@ -73,77 +74,70 @@ def tile_factoranalysisemloadinggradient_kernel(
                 x_raw[first_pair + n] = raw[:, 2 * n : 2 * n + 2, :].rearrange("q j f -> q (j f)")
 
         def load_w(side, g):
-            raw = keep.tile([P, PACK, WIDTH], BF16, name=f"w_raw{side}{g}")
+            raw = tile_of(("flat", "w", side, g), [P, PACK, WIDTH], BF16)
             rows = beta_view[g] if side == Z else p_view[g][:, :, side * WIDTH : (side + 1) * WIDTH]
             nc.sync.dma_start(out=raw[:], in_=rows)
-            w_raw[side, g] = raw[:]
 
         def load_scale(g):
             nc.scalar.dma_start(out=scale[g][:], in_=scale_view[g])
 
-        def load_factor(tile, source):
-            nc.sync.dma_start(out=tile[:, :, :PACK], in_=source.rearrange("(g q j) -> q g j", q=P, j=PACK))
+        def load_factor(first, source):
+            nc.sync.dma_start(out=factor_rows[first : first + GROUPS, :], in_=source.rearrange("(g c) -> g c", g=GROUPS))
 
         scale = [keep.tile([P, PACK], F32, name=f"scale{g}") for g in range(PASSES)]
-        r16 = keep.tile([P, GROUPS, ROW], BF16, name="r16")
-        t16 = keep.tile([P, GROUPS, ROW], BF16, name="t16")
         v_raw = keep.tile([P, BANDS, K], BF16, name="v_raw")
         psi16 = keep.tile([P, BANDS, ROW], BF16, name="psi16")
-        load_x(0)
-        load_scale(0)
-        load_x(1)
-        load_scale(1)
-        load_w(Z, 0)
-        load_x(2)
-        load_w(Z, 1)
-        load_x(3)
-        load_w(0, 0)
-        load_factor(t16, t)
-        load_w(0, 1)
-        load_x(4)
-        load_factor(r16, r)
-        load_w(1, 0)
-        load_x(5)
-        load_w(1, 1)
-        load_x(6, pairs=2)
-        nc.sync.dma_start(out=v_raw[:], in_=v.rearrange("(b q) k -> q b k", q=P))
-        with nc.allow_non_contiguous_dma(reason="one noise variance for each partition and band"):
-            nc.sync.dma_start(out=psi16[:, :, 0], in_=psi.rearrange("(b q) -> q b", q=P))
-
         factor = {side: keep.tile([P, UNITS], F32, name=f"factor{side}") for side in (0, Z)}
         factor[1] = factor[0]
         psi_inv = keep.tile([P, BANDS], F32, name="psi_inv")
         psi_inv_mean = keep.tile([P, BANDS], F32, name="psi_inv_mean")
-        tiles, buffer_of, cut = {}, {}, set()
 
         def tile_of(key, shape, dtype):
             if key not in tiles:
                 name = buffer_of.get(key) or "_".join(str(part) for part in key)
-                if name.startswith("bank"):
-                    tiles[key] = psum.tile(shape, dtype, name=name)
-                else:
-                    tiles[key] = keep.tile(shape, dtype, name=name, align_bytes=256)
+                tiles[key] = keep.tile(shape, dtype, name=name, align_bytes=256)
             return tiles[key]
+
+        def bank_of(key, shape):
+            if key not in tiles:
+                held[key] = free_banks[0]
+                free_banks.remove(held[key])
+                tiles[key] = psum.tile(shape, F32, name=f"bank{held[key]}")
+            return tiles[key]
+
+        def release(key):
+            free_banks.append(held[key])
 
         def mx_tiles(key):
             return tile_of(("codes", *key), [P, WIDTH], U32), tile_of(("scales", *key), [P, WIDTH], U8)
 
         def grouped_key(slab, column=0):
-            return ("grouped", *slab, GPSIMD_COLUMNS if slab in cut and column >= GPSIMD_COLUMNS else 0)
+            return ("grouped", *slab, cuts[slab] if column >= cuts.get(slab, WIDTH) else 0)
 
         def grouped(slab, first, last):
             key = grouped_key(slab, first)
-            end = GPSIMD_COLUMNS if slab in cut and key[-1] == 0 else WIDTH
+            end = cuts.get(slab, WIDTH) if key[-1] == 0 else WIDTH
             return tile_of(key, [P, end - key[-1], PACK], BF16)[:, first - key[-1] : last - key[-1], :]
 
         def warm(n):
             nc.tensor.matmul(
-                out=tile_of(("warm", n), [P, WARM_WIDTH], F32)[:], lhsT=zeros[:, :P], rhs=zeros[:], start=True, stop=True
+                out=bank_of(("warm", n), [P, WARM_WIDTH])[:], lhsT=zeros[:, :P], rhs=zeros[:], start=True, stop=True
             )
+            release(("warm", n))
 
-        def widen_factor(side):
-            source = t16 if side == Z else r16
-            nc.scalar.copy(out=factor[side][:].rearrange("q (g j) -> q g j", j=PACK), in_=source[:, :, :PACK])
+        def turn_factors():
+            bank = bank_of(("factors",), [P, 2, P])
+            for u in range(2):
+                nc.tensor.transpose(bank[:, u, :], factor_rows[:].bitcast(F32)[:, u::2], identity[:])
+
+        def widen_factors():
+            for side, first in ((0, 0), (Z, GROUPS)):
+                source = tiles[("factors",)][:, :, first : first + GROUPS].bitcast(BF16)
+                nc.scalar.copy(
+                    out=factor[side][:].rearrange("q (g u e) -> q g u e", u=2, e=2),
+                    in_=source.rearrange("q u (g e) -> q g u e", e=2),
+                )
+            release(("factors",))
 
         def invert_psi():
             nc.vector.reciprocal(out=psi_inv[:], in_=psi16[:, :, 0])
@@ -151,9 +145,8 @@ def tile_factoranalysisemloadinggradient_kernel(
         def mean_psi():
             nc.vector.tensor_scalar(out=psi_inv_mean[:], in0=psi_inv[:], scalar1=1.0 / N, scalar2=None, op0=MULT)
 
-        def interleave(slab, engine, first, last):
-            kind, a, b = slab
-            source = (w_raw[a, b] if kind == "w" else tiles["flat", a, b][:])[:, :, first:last]
+        def interleave(slab, engine, first=0, last=WIDTH):
+            source = tiles[("flat", *slab)][:, :, first:last]
             target = grouped(slab, first, last).rearrange("q (c i) j -> q c j i", i=RUN)
             source = source.rearrange("q j (c i) -> q c j i", i=RUN)
             if engine == "gpsimd":
@@ -163,7 +156,7 @@ def tile_factoranalysisemloadinggradient_kernel(
             else:
                 nc.scalar.copy(out=target, in_=source)
 
-        def quantize(slab, first, last):
+        def quantize(slab, first=0, last=WIDTH):
             codes, scales = mx_tiles(slab)
             nc.vector.quantize_mx(
                 out=codes[:, first:last].bitcast(FP8X4),
@@ -171,14 +164,14 @@ def tile_factoranalysisemloadinggradient_kernel(
                 in_=grouped(slab, first, last).rearrange("q c j -> q (c j)"),
             )
 
-        def widen(pair, g):
+        def widen(pair, g, engine):
             passes = range(PASSES) if g is None else [g]
             tile = tile_of(("wide", pair, g), [P, 2 * len(passes) * K_PASS], BF16)
             whole = [(0, 0, 2 * D)]
             by_unit = [(unit * K_PASS, unit * D + passes[0] * K_PASS, K_PASS) for unit in range(2)]
             for place, first, count in whole if g is None else by_unit:
                 source = x_raw[pair][:, first : first + count].bitcast(FP8)
-                if (pair, g) in VECTOR_WIDENS:
+                if engine == "vector":
                     target = tile[:].rearrange("p (u w e) -> p w u e", u=2, e=2)
                     nc.vector.tensor_scalar(
                         out=target[:, place // PACK : (place + count) // PACK],
@@ -190,15 +183,16 @@ def tile_factoranalysisemloadinggradient_kernel(
                 else:
                     nc.scalar.copy(out=tile[:, place : place + count], in_=source)
             words = tile[:].bitcast(F32)
+            blocks = 2 * len(passes)
             for n, (unit, h) in enumerate((unit, h) for unit in range(2) for h in passes):
                 for u in range(2):
-                    if (pair, g) in VECTOR_WIDENS:
-                        tiles["words", pair, h, unit, u] = words[:, (2 * u + n) * P : (2 * u + n + 1) * P]
+                    if engine == "vector":
+                        tiles["words", pair, h, unit, u] = words[:, (blocks * u + n) * P : (blocks * u + n + 1) * P]
                     else:
                         tiles["words", pair, h, unit, u] = words[:, 2 * n * P + u : 2 * (n + 1) * P : 2]
 
         def turn(pair, g):
-            bank = tile_of(("turned", pair, g), [P, 2, 2 * P], F32)
+            bank = bank_of(("turned", pair, g), [P, 2, 2 * P])
             for unit in range(2):
                 for u in range(2):
                     nc.tensor.transpose(
@@ -210,6 +204,7 @@ def tile_factoranalysisemloadinggradient_kernel(
             values = tiles["turned", pair, g][:].bitcast(BF16).rearrange("q u (c e) -> q c u e", e=2)
             scales = scale[g][:].rearrange("q (o u e) -> q o u e", o=1, u=2)
             nc.vector.tensor_tensor(out=target[:], in0=values, in1=scales.to_broadcast([P, 2 * P, 2, 2]), op=MULT)
+            release(("turned", pair, g))
 
         def x_quantize(pair, g):
             codes, scales = mx_tiles(("x", pair))
@@ -235,23 +230,32 @@ def tile_factoranalysisemloadinggradient_kernel(
             )
 
         def multiply(unit, side, g):
-            first_pass(tile_of(("first", unit, side), [P, WIDTH], F32)[:], unit, side, g, slice(0, WIDTH))
+            first_pass(bank_of(("first", unit, side), [P, WIDTH])[:], unit, side, g, slice(0, WIDTH))
 
         def multiply_duo(group, side, duo):
             half, u = divmod(duo, 2)
-            bank = tile_of(("duo", group, side, duo), [P, 2, HALF], F32)
+            bank = bank_of(("duo", group, side, duo), [P, 2, HALF])
             for e in range(2):
                 for g in range(PASSES):
                     first_pass(bank[:, e, :], PACK * group + 2 * u + e, side, g, slice(half * HALF, (half + 1) * HALF))
 
+        def multiply_strips(group, side, half):
+            banks = [bank_of(("strip", group, side, 2 * half + s), [P, PACK, P]) for s in range(2)]
+            for j in range(PACK):
+                for g in range(PASSES):
+                    for s, bank in enumerate(banks):
+                        first = (2 * half + s) * P
+                        first_pass(bank[:, j, :], PACK * group + j, side, g, slice(first, first + P))
+
         def empty(unit, side):
             group, j = divmod(unit, PACK)
             nc.scalar.activation(
-                out=tile_of(("flat", group, side), [P, PACK, WIDTH], BF16)[:, j, :],
+                out=tile_of(("flat", "y", group, side), [P, PACK, WIDTH], BF16)[:, j, :],
                 in_=tiles["first", unit, side][:],
                 func=COPY,
                 scale=factor[side][:, unit : unit + 1],
             )
+            release(("first", unit, side))
 
         def empty_duo(group, side, duo):
             half, u = divmod(duo, 2)
@@ -263,6 +267,18 @@ def tile_factoranalysisemloadinggradient_kernel(
                 in1=factors.to_broadcast([P, HALF, 2]),
                 op=MULT,
             )
+            release(("duo", group, side, duo))
+
+        def empty_strip(group, side, strip):
+            first = PACK * group
+            factors = factor[side][:, first : first + PACK].rearrange("q (o j) -> q o j", o=1)
+            nc.vector.tensor_tensor(
+                out=grouped(("y", group, side), strip * P, (strip + 1) * P),
+                in0=tiles["strip", group, side, strip][:].rearrange("q j c -> q c j"),
+                in1=factors.to_broadcast([P, P, PACK]),
+                op=MULT,
+            )
+            release(("strip", group, side, strip))
 
         def join(group, side, half, engine):
             target = grouped(("y", group, side), half * HALF, (half + 1) * HALF)
@@ -283,7 +299,7 @@ def tile_factoranalysisemloadinggradient_kernel(
             e_codes, e_scales = mx_tiles(("y", group, side))
             z_codes, z_scales = mx_tiles(("y", group, Z))
             nc.tensor.matmul_mx(
-                out=tile_of(("sum", band, first), [P, last - first], F32)[:],
+                out=bank_of(("sum", band, first), [P, last - first])[:],
                 lhsT=e_codes[:, cols].bitcast(FP8X4),
                 lhsT_scale=e_scales[:, cols],
                 rhs=z_codes[:, first:last].bitcast(FP8X4),
@@ -292,13 +308,15 @@ def tile_factoranalysisemloadinggradient_kernel(
                 stop=(group == group_order[band][-1]),
             )
 
-        def prepare(band):
-            nc.scalar.activation(
-                out=tile_of(("result", band), [P, K], F32)[:],
-                in_=v_raw[:, band, :],
-                func=COPY,
-                scale=psi_inv[:, band : band + 1],
-            )
+        def prepare(band, engine):
+            target = tile_of(("result", band), [P, K], F32)[:]
+            inverse = psi_inv[:, band : band + 1]
+            if engine == "gpsimd":
+                nc.gpsimd.tensor_scalar(out=target, in0=v_raw[:, band, :], scalar1=inverse, scalar2=0.0, op0=MULT, op1=ADD)
+            elif engine == "vector":
+                nc.vector.tensor_scalar(out=target, in0=v_raw[:, band, :], scalar1=inverse, scalar2=None, op0=MULT)
+            else:
+                nc.scalar.activation(out=target, in_=v_raw[:, band, :], func=COPY, scale=inverse)
 
         def finish(band, first, last):
             tile = tiles["result", band][:, first:last]
@@ -310,9 +328,11 @@ def tile_factoranalysisemloadinggradient_kernel(
                 op0=MULT,
                 op1=SUBTRACT,
             )
-
-        def store(band, first, last):
+            release(("sum", band, first))
             nc.sync.dma_start(out=out[band * P : (band + 1) * P, first:last], in_=tiles["result", band][:, first:last])
+
+        S, V, G = "scalar", "vector", "gpsimd"
+        CUT = GPSIMD_COLUMNS
 
         def w(side, g):
             return ("w", side, g)
@@ -320,224 +340,241 @@ def tile_factoranalysisemloadinggradient_kernel(
         def y(group, side):
             return ("y", group, side)
 
-        def mix(slab, engine, first=0, last=WIDTH):
-            return (interleave, slab, engine, first, last)
-
-        def rest(slab, engine):
-            return mix(slab, engine, GPSIMD_COLUMNS, WIDTH)
-
-        def quant(slab, first=0, last=WIDTH):
-            return (quantize, slab, first, last)
-
-        def quant_cut(slab):
-            return [quant(slab, GPSIMD_COLUMNS, WIDTH), quant(slab, 0, GPSIMD_COLUMNS)]
-
         def both(step, pair):
-            return [(step, pair, g) for g in range(PASSES)]
+            for g in range(PASSES):
+                step(pair, g)
 
-        def by_unit(pair, *sides):
-            return [(multiply, 2 * pair + n, side, g) for side in sides for n in range(2) for g in range(PASSES)]
+        def unit_sums(unit, side):
+            for g in range(PASSES):
+                multiply(unit, side, g)
+            empty(unit, side)
+
+        def pair_sums(pair, *sides):
+            for side in sides:
+                for unit in (2 * pair, 2 * pair + 1):
+                    unit_sums(unit, side)
 
         def by_pass(pair, side):
-            return [(multiply, 2 * pair + n, side, g) for g in range(PASSES) for n in range(2)]
+            for g in range(PASSES):
+                for unit in (2 * pair, 2 * pair + 1):
+                    multiply(unit, side, g)
 
-        def duos(step, group):
-            return [(step, group, 1, duo) for duo in range(DUOS)]
-
-        halves = [(0, HALF), (HALF, WIDTH)]
-        ends = [(band, 0, K) for band in range(LAST_BAND)] + [(LAST_BAND, *half) for half in halves]
-
-        whole_slabs = {4: y(0, Z), 5: y(0, 0), 6: y(1, 0), 7: y(2, Z)}
-        gpsimd = [mix(w(Z, 0), "gpsimd", 0, GPSIMD_FIRST_COLUMNS)]
-        gpsimd += [mix(slab, "gpsimd", 0, GPSIMD_COLUMNS) for slab in (w(Z, 1), w(1, 0), w(1, 1))]
-        gpsimd += [mix(slab, "gpsimd") for slab in whole_slabs.values()]
-        gpsimd += [mix(slab, "gpsimd", 0, GPSIMD_COLUMNS) for slab in (y(2, 0), y(3, 0))]
-        for slab in (w(Z, 1), y(2, 0), y(3, 0)):
-            cut.add(slab)
-
-        tensor = [(warm, 0)]
-        for pair in range(4):
-            tensor += [(warm, pair + 1)] + both(turn, pair)
-        tensor += by_pass(0, Z) + by_unit(1, Z)
-        tensor += both(turn, 4) + by_unit(0, 0) + by_unit(1, 0) + by_pass(2, Z) + by_unit(2, 0)
-        tensor += both(turn, 5) + by_unit(3, Z, 0) + [(multiply_duo, 0, 1, 0)] + by_unit(2, 1)
-        tensor += both(turn, 6) + by_unit(4, Z) + [(multiply_duo, 0, 1, 1)] + by_unit(4, 0)
-        tensor += both(turn, 7) + by_unit(5, Z) + [(multiply_duo, 0, 1, 2)] + by_unit(5, 0) + by_unit(3, 1)
-        tensor += by_unit(6, Z) + [(multiply_duo, 0, 1, 3)] + by_unit(6, 0)
-        tensor += duos(multiply_duo, 2) + by_unit(7, Z, 0) + duos(multiply_duo, 3)
-
-        scalar = [(widen, 0, 1), (widen, 1, 1), mix(w(Z, 0), "scalar", GPSIMD_FIRST_COLUMNS, WIDTH), (widen, 2, None)]
-        scalar += [rest(w(Z, 1), "scalar"), (widen, 3, None), mix(w(0, 0), "scalar"), (widen_factor, Z), (widen, 4, None)]
-        behind = {
-            (empty, 2, Z): [(widen_factor, 0)],
-            (empty, 3, 0): [(widen, 5, None)],
-            (empty, 5, 0): [(widen, 6, 0)],
-            (empty, 7, 0): [(widen, 6, 1)],
-            (empty, 5, 1): [(widen, 7, None)],
-            (empty, 9, Z): [mix(y(1, Z), "scalar", 0, QUARTER)],
-            (empty, 9, 0): [mix(y(1, Z), "scalar", QUARTER, WIDTH - QUARTER)],
-            (empty, 11, Z): [mix(y(1, Z), "scalar", WIDTH - QUARTER, WIDTH)],
-            (empty, 13, Z): [rest(y(2, 0), "scalar")],
-            (empty, 13, 0): [mix(y(1, 1), "scalar")],
-            (empty, 15, 0): [mix(y(3, Z), "scalar"), rest(y(3, 0), "scalar")],
-        }
-        for step in tensor:
-            if step[0] is multiply and step[3] == PASSES - 1:
-                scalar += [(empty, *step[1:3])] + behind.get((empty, *step[1:3]), [])
-        scalar += [(prepare, 0)] + [(join, 3, 1, half, "scalar") for half in range(2)]
-        scalar += [(prepare, band) for band in range(1, BANDS)]
-
-        group_order = {band: (2, 0, 1, 3) if band in (4, 5) else tuple(range(GROUPS)) for band in range(BANDS)}
-        tensor += [(accumulate, group, band, 0, K) for group in range(GROUPS) for band in range(SIDE_BANDS)]
-        tensor += [(accumulate, group, band, 0, K) for group in group_order[4] for band in (4, 5)]
-        tensor += [(accumulate, group, *end) for end in ends[6:] for group in range(GROUPS)]
-
-        vector = [(widen, *part) for part in VECTOR_WIDENS]
-        vector += both(product, 0) + [(x_quantize, 0, 0), quant(w(Z, 0)), (x_quantize, 0, 1)]
-        vector += both(product, 1) + quant_cut(w(Z, 1)) + both(x_quantize, 1)
-        vector += [mix(w(0, 1), "vector"), quant(w(0, 0)), quant(w(0, 1))]
-        vector += both(product, 2) + both(x_quantize, 2) + both(product, 3) + both(x_quantize, 3)
-        vector += [rest(w(1, 0), "vector"), rest(w(1, 1), "vector"), quant(w(1, 0)), quant(w(1, 1))]
-        small = {6: [(invert_psi,)], 7: [(mean_psi,)]}
-        for duo, (pair, slab) in enumerate(whole_slabs.items()):
-            vector += both(product, pair) + [(empty_duo, 0, 1, duo)] + small.get(pair, []) + [(x_quantize, pair, 0)]
-            vector += [(join, 0, 1, duo // 2, "vector")] if duo % 2 else []
-            vector += [(x_quantize, pair, 1), quant(slab)]
-        vector += duos(empty_duo, 2) + [(join, 2, 1, 0, "vector"), quant(y(1, Z)), (join, 2, 1, 1, "vector")]
-        vector += quant_cut(y(2, 0)) + [quant(y(2, 1))]
-        vector += duos(empty_duo, 3) + [quant(y(3, Z))] + quant_cut(y(3, 0))[::-1] + [quant(y(0, 1)), quant(y(1, 1))]
-        for end, half in zip(ends, halves):
-            vector += [(finish, *end), quant(y(3, 1), *half)]
-        vector += [(finish, *end) for end in ends[2:]]
-
-        sync = [(store, *end) for end in ends]
-
-        tenants = {}
+        def quantize_cut(slab):
+            quantize(slab, cuts[slab], WIDTH)
+            quantize(slab, 0, cuts[slab])
 
         def lodge(buffer, *keys):
-            tenants.setdefault(buffer, []).extend(keys)
+            for key in keys:
+                buffer_of[key] = buffer
 
-        ring = [2, 3]
-        enters = {
-            (multiply, 2, 0, 0): 4,
-            (multiply, 5, Z, 0): 5,
-            (multiply, 10, 0, 0): 6,
-            (multiply, 7, 1, 0): 7,
-            (multiply, 13, 0, 0): 0,
-            (multiply_duo, 2, 1, 1): 1,
-        }
-        for step in tensor:
-            name, args = step[0], step[1:]
-            ring = ([enters[step]] if step in enters else []) + ring
-            if name is warm:
-                lodge(f"bank{6 + args[0] % 2}", ("warm", *args))
-            elif name is turn:
-                lodge(f"bank{(2 * args[0] if args[0] < 3 else 0 if args[0] % 2 else 6) + args[1]}", ("turned", *args))
-            elif name is multiply and args[0] < 2 and args[1:] == (Z, 0):
-                lodge(f"bank{6 + args[0]}", ("first", *args[:2]))
-            elif name is multiply_duo or (name is multiply and args[2] == 0):
-                lodge(f"bank{ring[0]}", ("duo", *args) if name is multiply_duo else ("first", *args[:2]))
-                ring = ring[1:] + ring[:1]
-            elif name is accumulate and args[0] == group_order[args[1]][0]:
-                lodge(f"bank{ring[0]}", ("sum", *args[1:3]))
-                ring = ring[1:] + ring[:1]
-
-        widened = sorted((step[1:] for step in scalar + vector if step[0] is widen), key=lambda part: part[0])
-        for n, part in enumerate(part for part in widened if part[1] is None):
-            lodge(f"wide{n % WIDE_BUFFERS}", ("wide", *part))
-        for part in widened:
-            if part[1] is not None:
-                lodge(f"wide_pass{part[0]}{part[1]}", ("wide", *part))
-        for band, buffer in zip(range(BANDS), sorted(name for name in tenants if name.startswith("wide"))):
-            lodge(buffer, ("result", band))
-        for n, step in enumerate(step for step in scalar if step[0] is empty and step[1] % PACK == 0):
-            lodge(f"flat{n % FLAT_BUFFERS}", ("flat", step[1] // PACK, step[2]))
-
-        lodge("gate_z", grouped_key(w(Z, 0)), grouped_key(w(Z, 1)), grouped_key(y(3, Z)))
-        lodge("gate_w", grouped_key(w(0, 0)), grouped_key(w(1, 0)), grouped_key(y(0, Z)), grouped_key(y(2, 1)))
-        lodge("gate_2", ("x_grouped", 2, 0), grouped_key(w(1, 1)), grouped_key(y(1, Z)))
-        for pair, slab in zip(whole_slabs, [*whole_slabs.values()][1:] + [y(2, 0)]):
-            lodge(f"gate_{pair}", ("x_grouped", pair, 1), grouped_key(slab))
-        lodge("gate_7", grouped_key(y(3, 0)))
-        lodge("gate_4", grouped_key(y(3, 1)))
+        LATE = 192
+        for slab in (w(Z, 1), y(0, Z), y(0, 0), y(1, Z), y(1, 0)):
+            cuts[slab] = CUT
+        cuts[y(2, 1)] = cuts[y(3, 1)] = HALF
+        lodge("gate_3", grouped_key(y(3, 1)), grouped_key(y(2, 1), HALF))
+        lodge("wide0", ("wide", 2, None), ("wide", 5, None), ("result", 0))
+        lodge("wide1", ("wide", 3, None), ("wide", 6, None), ("result", 1))
+        lodge("wide2", ("wide", 4, None), ("wide", 7, None), ("result", 2))
+        for band, part in zip(range(3, 7), [(0, 0), (0, 1), (1, 0), (1, 1)]):
+            lodge(f"wide_pass{band}", ("wide", *part), ("result", band))
+        lodge("flat0", ("flat", *w(Z, 0)), ("flat", *y(0, Z)), ("flat", *y(1, 1)))
+        lodge("flat1", ("flat", *w(Z, 1)), ("flat", *y(0, 0)), ("flat", *y(2, 1)))
+        lodge("flat2", ("flat", *w(0, 0)), ("flat", *y(1, Z)), ("flat", *y(3, 1)))
+        lodge("flat3", ("flat", *w(0, 1)), ("flat", *y(1, 0)))
+        lodge("flat5", ("flat", *w(1, 1)), ("flat", *y(2, 0)))
+        lodge("flat4", ("flat", *w(1, 0)), ("flat", *y(0, 1)))
+        lodge("gate_z", grouped_key(w(Z, 0)), grouped_key(w(Z, 1)), ("x_grouped", 3, 0), grouped_key(y(0, Z)))
+        lodge("gate_5", ("x_grouped", 5, 1), grouped_key(y(1, Z)))
+        lodge("gate_w", grouped_key(w(0, 0)), grouped_key(w(1, 0)), grouped_key(y(0, 0)))
+        lodge("gate_6", ("x_grouped", 6, 1), grouped_key(y(1, 0)), grouped_key(y(2, Z)))
+        lodge("gate_2", ("x_grouped", 2, 0), grouped_key(w(1, 1)))
         lodge("late", grouped_key(w(0, 1)), grouped_key(y(0, 1)))
-        lodge("x_grouped0", *[("x_grouped", pair, 0) for pair in range(PAIRS) if pair != 2])
-        lodge("x_grouped1", *[("x_grouped", pair, 1) for pair in range(PAIRS) if pair not in whole_slabs])
+        lodge("x_grouped0", *[("x_grouped", pair, 0) for pair in (0, 1, 4, 5, 6, 7)])
+        lodge("x_grouped1", *[("x_grouped", pair, 1) for pair in range(PAIRS) if pair not in (5, 6)])
+        load_x(0)
+        load_scale(0)
+        load_x(1)
+        load_scale(1)
+        load_w(Z, 0)
+        load_x(2)
+        load_factor(0, r)
+        load_factor(GROUPS, t)
+        load_w(Z, 1)
+        load_x(3)
+        load_w(0, 0)
+        load_w(0, 1)
+        load_x(4)
+        load_w(1, 0)
+        load_x(5)
+        load_w(1, 1)
+        load_x(6, pairs=2)
+        nc.sync.dma_start(out=v_raw[:], in_=v.rearrange("(b q) k -> q b k", q=P))
+        with nc.allow_non_contiguous_dma(reason="one noise variance for each partition and band"):
+            nc.sync.dma_start(out=psi16[:, :, 0], in_=psi.rearrange("(b q) -> q b", q=P))
 
-        tenant_before = {}
-        for buffer, keys in tenants.items():
-            for before, key in zip([None] + keys, keys):
-                buffer_of[key], tenant_before[key] = buffer, before
 
-        def touches(step):
-            name, args = step[0], step[1:]
-            whole = (0, WIDTH)
-            if name is warm:
-                return [], [(("warm", *args), *whole)]
-            if name is widen:
-                return [], [(("wide", *args), *whole)]
-            if name is turn:
-                return [(("wide", args[0], None), *whole), (("wide", *args), *whole)], [(("turned", *args), *whole)]
-            if name is product:
-                return [(("turned", *args), *whole)], [(("x_grouped", *args), *whole)]
-            if name is x_quantize:
-                return [(("x_grouped", *args), *whole)], [(("x", *args), *whole)]
-            if name is interleave:
-                slab, first, last = args[0], args[2], args[3]
-                source = [(("flat", *slab[1:]), *whole)] if slab[0] == "y" else []
-                return source, [(grouped_key(slab, first), first, last)]
-            if name is quantize:
-                return [(grouped_key(*args[:2]), *args[1:])], [args]
-            if name is multiply:
-                unit, side, g = args
-                read = [(("first", unit, side), 0, g), (("x", unit // 2, g), *whole), (w(side, g), *whole)]
-                return read, [(("first", unit, side), g, g + 1)]
-            if name is multiply_duo:
-                group, side, duo = args
-                keys = [key for g in range(PASSES) for key in (("x", 2 * group + duo % 2, g), w(side, g))]
-                return [(key, *whole) for key in keys], [(("duo", *args), *whole)]
-            if name is widen_factor:
-                return [], [(("factor", args[0] == Z), *whole)]
-            if name is empty:
-                read = [(("first", *args), *whole), (("factor", args[1] == Z), *whole)]
-                return read, [(("flat", args[0] // PACK, args[1]), *whole)]
-            if name is empty_duo:
-                read = [(("duo", *args), *whole), (("factor", args[1] == Z), *whole)]
-                return read, [(("paired", *args[:2], args[2] // 2), *whole)]
-            if name is join:
-                return [(("paired", *args[:3]), *whole)], [(grouped_key(y(*args[:2])), *halves[args[2]])]
-            if name is accumulate:
-                group, band, first = args[:3]
-                side, place = divmod(band, SIDE_BANDS)
-                n = group_order[band].index(group)
-                read = [(("sum", band, first), 0, n), (y(group, side), place * P, (place + 1) * P), (y(group, Z), *whole)]
-                return read, [(("sum", band, first), n, n + 1)]
-            if name is invert_psi:
-                return [], [(("psi_inv",), *whole)]
-            if name is mean_psi:
-                return [(("psi_inv",), *whole)], [(("psi_inv_mean",), *whole)]
-            if name is prepare:
-                return [(("psi_inv",), *whole)], [(("result", *args), *whole)]
-            if name is finish:
-                read = [(("sum", *args[:2]), *whole), (("result", args[0]), *whole), (("psi_inv_mean",), *whole)]
-                return read, [(("finished", args[0]), *args[1:])]
-            return [(("finished", args[0]), *args[1:])], []
-
-        queues = [vector, scalar, tensor, gpsimd, sync]
-        steps = [step for queue in queues for step in queue]
-        waits = {step: set() for step in steps}
-        for step in steps:
-            read, written = touches(step)
-            for other in steps:
-                other_read, other_written = touches(other)
-                if any(key == k and first < b and a < last for key, first, last in read for k, a, b in other_written):
-                    waits[step].add(other)
-                if any(k == tenant_before.get(key) for key, a, b in written for k, c, d in other_read + other_written):
-                    waits[step].add(other)
-        done = set()
-        while any(queues):
-            queue = [queue for queue in queues if queue and all(wait in done for wait in waits[queue[0]])][0]
-            step = queue[0]
-            step[0](*step[1:])
-            done.add(step)
-            queue.remove(step)
+        warm(0)
+        warm(1)
+        widen(0, 0, V)
+        widen(0, 1, S)
+        both(turn, 0)
+        widen(1, 0, V)
+        widen(1, 1, S)
+        warm(2)
+        both(turn, 1)
+        interleave(w(Z, 0), G, 0, 320)
+        interleave(w(Z, 0), S, 320)
+        widen(2, None, S)
+        warm(3)
+        turn_factors()
+        both(product, 0)
+        both(turn, 2)
+        x_quantize(0, 0)
+        quantize(w(Z, 0))
+        x_quantize(0, 1)
+        interleave(w(Z, 1), G, 0, CUT)
+        interleave(w(Z, 1), S, CUT)
+        widen_factors()
+        widen(3, None, S)
+        warm(4)
+        both(turn, 3)
+        both(product, 1)
+        quantize_cut(w(Z, 1))
+        both(x_quantize, 1)
+        interleave(w(0, 0), S)
+        widen(4, None, S)
+        by_pass(0, Z)
+        for unit in (2, 3):
+            for g in range(PASSES):
+                multiply(unit, Z, g)
+        for unit in range(4):
+            empty(unit, Z)
+        both(turn, 4)
+        interleave(w(0, 1), V)
+        quantize(w(0, 0))
+        quantize(w(0, 1))
+        interleave(w(1, 0), G, 0, CUT)
+        for g in range(PASSES):
+            multiply(0, 0, g)
+        for g in range(PASSES):
+            multiply(1, 0, g)
+        product(2, 0)
+        empty(0, 0)
+        empty(1, 0)
+        for unit in (2, 3):
+            for g in range(PASSES):
+                multiply(unit, 0, g)
+        product(2, 1)
+        empty(2, 0)
+        both(x_quantize, 2)
+        multiply(4, Z, 0)
+        multiply(5, Z, 0)
+        empty(3, 0)
+        widen(5, None, S)
+        multiply(4, Z, 1)
+        multiply(5, Z, 1)
+        interleave(w(1, 1), G, 0, CUT)
+        for unit in (4, 5):
+            for g in range(PASSES):
+                multiply(unit, 0, g)
+        both(product, 3)
+        both(x_quantize, 3)
+        both(turn, 5)
+        for side in (Z, 0):
+            empty(4, side)
+            empty(5, side)
+        interleave(y(0, Z), G, 0, CUT)
+        widen(6, None, S)
+        product(4, 0)
+        pair_sums(3, Z)
+        product(4, 1)
+        pair_sums(3, 0)
+        both(x_quantize, 4)
+        interleave(w(1, 0), V, CUT)
+        interleave(w(1, 1), V, CUT)
+        quantize(w(1, 0))
+        quantize(w(1, 1))
+        interleave(y(0, 0), G, 0, CUT)
+        pair_sums(4, Z, 0)
+        interleave(y(0, Z), S, CUT)
+        interleave(y(0, 0), S, CUT)
+        both(turn, 6)
+        both(product, 5)
+        pair_sums(0, 1)
+        both(x_quantize, 5)
+        widen(7, None, V)
+        quantize(y(0, Z), 0, CUT)
+        interleave(y(1, Z), G, 0, CUT)
+        pair_sums(5, Z, 0)
+        interleave(y(1, Z), S, CUT)
+        both(turn, 7)
+        both(product, 6)
+        x_quantize(6, 0)
+        invert_psi()
+        x_quantize(6, 1)
+        quantize(y(0, 0), 0, CUT)
+        interleave(y(1, 0), G, 0, CUT)
+        pair_sums(1, 1)
+        pair_sums(2, 1)
+        both(product, 7)
+        pair_sums(3, 1)
+        pair_sums(4, 1)
+        x_quantize(7, 0)
+        mean_psi()
+        x_quantize(7, 1)
+        for slab in (y(0, Z), y(0, 0), y(1, Z)):
+            quantize(slab, CUT, WIDTH)
+        prepare(0, V)
+        quantize(y(1, 0), 0, CUT)
+        quantize(y(1, Z), 0, CUT)
+        interleave(y(2, Z), G)
+        interleave(y(0, 1), G, 0, CUT)
+        interleave(y(1, 0), S, CUT)
+        interleave(y(2, 0), S)
+        interleave(y(0, 1), S, CUT)
+        interleave(y(1, 1), S, 0, HALF)
+        for side in (Z, 0):
+            for half in range(2):
+                multiply_strips(3, side, half)
+        for strip in range(PACK):
+            empty_strip(3, Z, strip)
+        pair_sums(5, 1)
+        for strip in range(PACK):
+            empty_strip(3, 0, strip)
+        interleave(y(1, 1), S, HALF)
+        pair_sums(6, 1)
+        pair_sums(7, 1)
+        quantize(y(1, 0), CUT, WIDTH)
+        for slab in (y(2, Z), y(2, 0), y(3, Z), y(3, 0)):
+            quantize(slab)
+        prepare(1, V)
+        quantize(y(0, 1))
+        interleave(y(2, 1), S, 0, HALF)
+        interleave(y(3, 1), S, 0, HALF)
+        interleave(y(3, 1), S, HALF)
+        group_order = {band: (0, 1, 3, 2) if band >= 6 else tuple(range(GROUPS)) for band in range(BANDS)}
+        for band in range(SIDE_BANDS):
+            for group in range(GROUPS):
+                accumulate(group, band, 0, K)
+        finish(0, 0, K)
+        prepare(2, V)
+        quantize(y(1, 1))
+        finish(1, 0, K)
+        prepare(3, V)
+        quantize(y(2, 1), 0, HALF)
+        finish(2, 0, K)
+        quantize(y(3, 1), 0, HALF)
+        prepare(4, V)
+        interleave(y(2, 1), G, HALF, HALF + LATE)
+        interleave(y(2, 1), S, HALF + LATE)
+        finish(3, 0, K)
+        for band, first, last in [(4, 0, K), (5, 0, K), (6, 0, K), (7, 0, HALF), (7, HALF, K)]:
+            for group in group_order[band]:
+                accumulate(group, band, first, last)
+            finish(band, first, last)
+            if band == 4:
+                quantize(y(3, 1), HALF, WIDTH)
+                quantize(y(2, 1), HALF, WIDTH)
+                prepare(5, S)
+                prepare(6, S)
+                prepare(7, S)

@@ -367,7 +367,7 @@ def tile_factoranalysisemloadinggradient_kernel(
             for key in keys:
                 buffer_of[key] = buffer
 
-        LATE = 192
+        LATE = 128
         for slab in (w(Z, 1), y(0, Z), y(0, 0), y(1, Z), y(1, 0)):
             cuts[slab] = CUT
         cuts[y(2, 1)] = cuts[y(3, 1)] = HALF
@@ -528,10 +528,10 @@ def tile_factoranalysisemloadinggradient_kernel(
         quantize(y(1, 0), 0, CUT)
         quantize(y(1, Z), 0, CUT)
         interleave(y(2, Z), G)
-        interleave(y(0, 1), G, 0, CUT)
+        interleave(y(0, 1), G, 0, CUT + 32)
         interleave(y(1, 0), S, CUT)
         interleave(y(2, 0), S)
-        interleave(y(0, 1), S, CUT)
+        interleave(y(0, 1), S, CUT + 32)
         interleave(y(1, 1), S, 0, HALF)
         for side in (Z, 0):
             for half in range(2):
@@ -568,13 +568,14 @@ def tile_factoranalysisemloadinggradient_kernel(
         interleave(y(2, 1), G, HALF, HALF + LATE)
         interleave(y(2, 1), S, HALF + LATE)
         finish(3, 0, K)
-        for band, first, last in [(4, 0, K), (5, 0, K), (6, 0, K), (7, 0, HALF), (7, HALF, K)]:
+        for band, first, last in [(4, 0, K), (5, 0, K)] + [(band, first, first + HALF) for band in (6, 7) for first in (0, HALF)]:
             for group in group_order[band]:
                 accumulate(group, band, first, last)
             finish(band, first, last)
+            if band in (4, 5):
+                place = (band - 2) * P
+                quantize(y(3, 1), place, place + P)
+                quantize(y(2, 1), place, place + P)
             if band == 4:
-                quantize(y(3, 1), HALF, WIDTH)
-                quantize(y(2, 1), HALF, WIDTH)
-                prepare(5, S)
-                prepare(6, S)
-                prepare(7, S)
+                for later in range(5, BANDS):
+                    prepare(later, S)

@@ -55,6 +55,7 @@ def tile_factoranalysisemloadinggradient_kernel(
         nc.vector.memset(zeros[:], 0.0)
         identity = keep.tile([P, P], F32, name="identity")
         make_identity(nc, identity[:])
+        identity16 = keep.tile([P, P], BF16, name="identity16")
         one = keep.tile([P, 1], F32, name="one")
         nc.vector.memset(one[:], 1.0)
 
@@ -84,9 +85,12 @@ def tile_factoranalysisemloadinggradient_kernel(
         def load_factor(first, source):
             nc.sync.dma_start(out=factor_rows[first : first + GROUPS, :], in_=source.rearrange("(g c) -> g c", g=GROUPS))
 
+        def load_psi():
+            rows = factor_rows[2 * GROUPS : 2 * GROUPS + BANDS, :P]
+            nc.sync.dma_start(out=rows, in_=psi.rearrange("(b q) -> b q", b=BANDS))
+
         scale = [keep.tile([P, PACK], F32, name=f"scale{g}") for g in range(PASSES)]
         v_raw = keep.tile([P, BANDS, K], BF16, name="v_raw")
-        psi16 = keep.tile([P, BANDS, ROW], BF16, name="psi16")
         factor = {side: keep.tile([P, UNITS], F32, name=f"factor{side}") for side in (0, Z)}
         factor[1] = factor[0]
         psi_inv = keep.tile([P, BANDS], F32, name="psi_inv")
@@ -126,13 +130,14 @@ def tile_factoranalysisemloadinggradient_kernel(
             release(("warm", n))
 
         def turn_factors():
-            bank = bank_of(("factors",), [P, 2, P])
+            bank = bank_of(("factors",), [P, 3, P])
             for u in range(2):
                 nc.tensor.transpose(bank[:, u, :], factor_rows[:].bitcast(F32)[:, u::2], identity[:])
+            nc.tensor.transpose(bank[:, 2, :].bitcast(BF16)[:, :P], factor_rows[:, :P], identity16[:])
 
         def widen_factors():
             for side, first in ((0, 0), (Z, GROUPS)):
-                source = tiles[("factors",)][:, :, first : first + GROUPS].bitcast(BF16)
+                source = tiles[("factors",)][:, :2, first : first + GROUPS].bitcast(BF16)
                 nc.scalar.copy(
                     out=factor[side][:].rearrange("q (g u e) -> q g u e", u=2, e=2),
                     in_=source.rearrange("q u (g e) -> q g u e", e=2),
@@ -140,10 +145,10 @@ def tile_factoranalysisemloadinggradient_kernel(
             release(("factors",))
 
         def invert_psi():
-            nc.vector.reciprocal(out=psi_inv[:], in_=psi16[:, :, 0])
+            nc.vector.reciprocal(out=psi_inv[:], in_=tiles[("factors",)][:, 2, :].bitcast(BF16)[:, 2 * GROUPS : 2 * GROUPS + BANDS])
 
         def mean_psi():
-            nc.vector.tensor_scalar(out=psi_inv_mean[:], in0=psi_inv[:], scalar1=1.0 / N, scalar2=None, op0=MULT)
+            nc.scalar.activation(out=psi_inv_mean[:], in_=psi_inv[:], func=COPY, scale=1.0 / N)
 
         def interleave(slab, engine, first=0, last=WIDTH):
             source = tiles[("flat", *slab)][:, :, first:last]
@@ -370,9 +375,9 @@ def tile_factoranalysisemloadinggradient_kernel(
         LATE = 128
         for slab in (w(Z, 1), y(0, Z), y(0, 0), y(1, Z), y(1, 0)):
             cuts[slab] = CUT
-        cuts[y(2, 1)] = cuts[y(3, 1)] = HALF
-        lodge("gate_3", grouped_key(y(3, 1)), grouped_key(y(2, 1), HALF))
-        lodge("wide0", ("wide", 2, None), ("wide", 5, None), ("result", 0))
+        cuts[y(2, 1)] = cuts[y(1, 1)] = HALF
+        lodge("gate_3", grouped_key(y(1, 1), HALF), grouped_key(y(2, 1), HALF))
+        lodge("wide0", ("wide", 2, None), ("result", 0))
         lodge("wide1", ("wide", 3, None), ("wide", 6, None), ("result", 1))
         lodge("wide2", ("wide", 4, None), ("wide", 7, None), ("result", 2))
         for band, part in zip(range(3, 7), [(0, 0), (0, 1), (1, 0), (1, 1)]):
@@ -396,9 +401,10 @@ def tile_factoranalysisemloadinggradient_kernel(
         load_x(1)
         load_scale(1)
         load_w(Z, 0)
-        load_x(2)
         load_factor(0, r)
         load_factor(GROUPS, t)
+        load_psi()
+        load_x(2)
         load_w(Z, 1)
         load_x(3)
         load_w(0, 0)
@@ -409,8 +415,6 @@ def tile_factoranalysisemloadinggradient_kernel(
         load_w(1, 1)
         load_x(6, pairs=2)
         nc.sync.dma_start(out=v_raw[:], in_=v.rearrange("(b q) k -> q b k", q=P))
-        with nc.allow_non_contiguous_dma(reason="one noise variance for each partition and band"):
-            nc.sync.dma_start(out=psi16[:, :, 0], in_=psi.rearrange("(b q) -> q b", q=P))
 
 
         warm(0)
@@ -421,13 +425,16 @@ def tile_factoranalysisemloadinggradient_kernel(
         widen(1, 0, V)
         widen(1, 1, S)
         warm(2)
-        both(turn, 1)
+        nc.scalar.copy(out=identity16[:], in_=identity[:])
+        turn(1, 0)
+        turn_factors()
+        turn(1, 1)
         interleave(w(Z, 0), G, 0, 320)
         interleave(w(Z, 0), S, 320)
         widen(2, None, S)
         warm(3)
-        turn_factors()
         both(product, 0)
+        invert_psi()
         both(turn, 2)
         x_quantize(0, 0)
         quantize(w(Z, 0))
@@ -435,6 +442,7 @@ def tile_factoranalysisemloadinggradient_kernel(
         interleave(w(Z, 1), G, 0, CUT)
         interleave(w(Z, 1), S, CUT)
         widen_factors()
+        mean_psi()
         widen(3, None, S)
         warm(4)
         both(turn, 3)
@@ -459,6 +467,7 @@ def tile_factoranalysisemloadinggradient_kernel(
         for g in range(PASSES):
             multiply(1, 0, g)
         product(2, 0)
+        widen(5, 0, S)
         empty(0, 0)
         empty(1, 0)
         for unit in (2, 3):
@@ -470,7 +479,7 @@ def tile_factoranalysisemloadinggradient_kernel(
         multiply(4, Z, 0)
         multiply(5, Z, 0)
         empty(3, 0)
-        widen(5, None, S)
+        widen(5, 1, S)
         multiply(4, Z, 1)
         multiply(5, Z, 1)
         interleave(w(1, 1), G, 0, CUT)
@@ -510,7 +519,6 @@ def tile_factoranalysisemloadinggradient_kernel(
         both(turn, 7)
         both(product, 6)
         x_quantize(6, 0)
-        invert_psi()
         x_quantize(6, 1)
         quantize(y(0, 0), 0, CUT)
         interleave(y(1, 0), G, 0, CUT)
@@ -520,7 +528,6 @@ def tile_factoranalysisemloadinggradient_kernel(
         pair_sums(3, 1)
         pair_sums(4, 1)
         x_quantize(7, 0)
-        mean_psi()
         x_quantize(7, 1)
         for slab in (y(0, Z), y(0, 0), y(1, Z)):
             quantize(slab, CUT, WIDTH)
@@ -528,10 +535,10 @@ def tile_factoranalysisemloadinggradient_kernel(
         quantize(y(1, 0), 0, CUT)
         quantize(y(1, Z), 0, CUT)
         interleave(y(2, Z), G)
-        interleave(y(0, 1), G, 0, CUT + 32)
+        interleave(y(0, 1), G, 0, 352)
         interleave(y(1, 0), S, CUT)
         interleave(y(2, 0), S)
-        interleave(y(0, 1), S, CUT + 32)
+        interleave(y(0, 1), S, 352)
         interleave(y(1, 1), S, 0, HALF)
         for side in (Z, 0):
             for half in range(2):
@@ -541,7 +548,6 @@ def tile_factoranalysisemloadinggradient_kernel(
         pair_sums(5, 1)
         for strip in range(PACK):
             empty_strip(3, 0, strip)
-        interleave(y(1, 1), S, HALF)
         pair_sums(6, 1)
         pair_sums(7, 1)
         quantize(y(1, 0), CUT, WIDTH)
@@ -551,6 +557,7 @@ def tile_factoranalysisemloadinggradient_kernel(
         quantize(y(0, 1))
         interleave(y(2, 1), S, 0, HALF)
         interleave(y(3, 1), S, 0, HALF)
+        interleave(y(1, 1), S, HALF)
         interleave(y(3, 1), S, HALF)
         group_order = {band: (0, 1, 3, 2) if band >= 6 else tuple(range(GROUPS)) for band in range(BANDS)}
         for band in range(SIDE_BANDS):
@@ -558,14 +565,16 @@ def tile_factoranalysisemloadinggradient_kernel(
                 accumulate(group, band, 0, K)
         finish(0, 0, K)
         prepare(2, V)
-        quantize(y(1, 1))
+        quantize(y(1, 1), 0, HALF)
         finish(1, 0, K)
         prepare(3, V)
         quantize(y(2, 1), 0, HALF)
-        finish(2, 0, K)
         quantize(y(3, 1), 0, HALF)
+        finish(2, 0, K)
+        quantize(y(1, 1), HALF, WIDTH)
         prepare(4, V)
         interleave(y(2, 1), G, HALF, HALF + LATE)
+        prepare(5, S)
         interleave(y(2, 1), S, HALF + LATE)
         finish(3, 0, K)
         for band, first, last in [(4, 0, K), (5, 0, K)] + [(band, first, first + HALF) for band in (6, 7) for first in (0, HALF)]:
@@ -577,5 +586,5 @@ def tile_factoranalysisemloadinggradient_kernel(
                 quantize(y(3, 1), place, place + P)
                 quantize(y(2, 1), place, place + P)
             if band == 4:
-                for later in range(5, BANDS):
+                for later in range(6, BANDS):
                     prepare(later, S)

@@ -113,7 +113,12 @@ def tile_factoranalysisemloadinggradient_kernel(
             free_banks.append(held[key])
 
         def mx_tiles(key):
-            return tile_of(("codes", *key), [P, WIDTH], U32), tile_of(("scales", *key), [P, WIDTH], U8)
+            stationary = key[0] == "x" or (key[0] == "y" and key[2] != Z)
+            code_shift = 32 if stationary else 0
+            scale_shift = 192 if stationary else 64
+            codes = tile_of(("codes", *key), [P, code_shift + WIDTH], U32)
+            scales = tile_of(("scales", *key), [P, scale_shift + WIDTH], U8)
+            return codes[:, code_shift:], scales[:, scale_shift:]
 
         def grouped_key(slab, column=0):
             return ("grouped", *slab, cuts[slab] if column >= cuts.get(slab, WIDTH) else 0)

@@ -393,12 +393,12 @@ def tile_factoranalysisemloadinggradient_kernel(
         lodge("flat3", ("flat", *w(0, 1)), ("flat", *y(1, 0)))
         lodge("flat5", ("flat", *w(1, 1)), ("flat", *y(2, 0)))
         lodge("flat4", ("flat", *w(1, 0)), ("flat", *y(0, 1)))
-        lodge("gate_z", grouped_key(w(Z, 0)), grouped_key(w(Z, 1)), ("x_grouped", 3, 0), grouped_key(y(0, Z)))
+        lodge("gate_z", grouped_key(w(Z, 0)), grouped_key(w(Z, 1)), grouped_key(w(0, 1)), ("x_grouped", 3, 0), grouped_key(y(0, Z)))
         lodge("gate_5", ("x_grouped", 5, 1), grouped_key(y(1, Z)))
         lodge("gate_w", grouped_key(w(0, 0)), grouped_key(w(1, 0)), grouped_key(y(0, 0)))
         lodge("gate_6", ("x_grouped", 6, 1), grouped_key(y(1, 0)), grouped_key(y(2, Z)))
         lodge("gate_2", ("x_grouped", 2, 0), grouped_key(w(1, 1)))
-        lodge("late", grouped_key(w(0, 1)), grouped_key(y(0, 1)))
+        lodge("late", grouped_key(y(0, 1)))
         lodge("x_grouped0", *[("x_grouped", pair, 0) for pair in (0, 1, 4, 5, 6, 7)])
         lodge("x_grouped1", *[("x_grouped", pair, 1) for pair in range(PAIRS) if pair not in (5, 6)])
         load_x(0)
@@ -434,8 +434,8 @@ def tile_factoranalysisemloadinggradient_kernel(
         turn(1, 0)
         turn_factors()
         turn(1, 1)
-        interleave(w(Z, 0), G, 0, 320)
-        interleave(w(Z, 0), S, 320)
+        interleave(w(Z, 0), G, 0, 288)
+        interleave(w(Z, 0), S, 288)
         widen(2, None, S)
         warm(3)
         both(product, 0)
@@ -452,40 +452,39 @@ def tile_factoranalysisemloadinggradient_kernel(
         warm(4)
         both(turn, 3)
         both(product, 1)
+        x_quantize(1, 0)
         quantize_cut(w(Z, 1))
-        both(x_quantize, 1)
+        x_quantize(1, 1)
         interleave(w(0, 0), S)
         widen(4, None, S)
-        by_pass(0, Z)
-        for unit in (2, 3):
-            for g in range(PASSES):
+        for g in range(PASSES):
+            for unit in range(4):
                 multiply(unit, Z, g)
+        interleave(w(0, 1), G, 0, 176)
+        product(2, 0)
         for unit in range(4):
             empty(unit, Z)
         both(turn, 4)
-        interleave(w(0, 1), V)
+        interleave(w(0, 1), V, 176)
         quantize(w(0, 0))
         quantize(w(0, 1))
-        interleave(w(1, 0), G, 0, CUT)
-        for g in range(PASSES):
-            multiply(0, 0, g)
-        for g in range(PASSES):
-            multiply(1, 0, g)
-        product(2, 0)
+        interleave(w(1, 0), G, 0, 176)
+        by_pass(0, 0)
+        product(2, 1)
         widen(5, 0, S)
+        interleave(w(1, 0), S, 464)
         empty(0, 0)
         empty(1, 0)
         for unit in (2, 3):
             for g in range(PASSES):
                 multiply(unit, 0, g)
-        product(2, 1)
         empty(2, 0)
         both(x_quantize, 2)
         multiply(4, Z, 0)
-        multiply(5, Z, 0)
+        multiply(4, Z, 1)
         empty(3, 0)
         widen(5, 1, S)
-        multiply(4, Z, 1)
+        multiply(5, Z, 0)
         multiply(5, Z, 1)
         interleave(w(1, 1), G, 0, CUT)
         for unit in (4, 5):
@@ -504,7 +503,7 @@ def tile_factoranalysisemloadinggradient_kernel(
         product(4, 1)
         pair_sums(3, 0)
         both(x_quantize, 4)
-        interleave(w(1, 0), V, CUT)
+        interleave(w(1, 0), V, 176, 464)
         interleave(w(1, 1), V, CUT)
         quantize(w(1, 0))
         quantize(w(1, 1))
@@ -515,6 +514,7 @@ def tile_factoranalysisemloadinggradient_kernel(
         both(turn, 6)
         both(product, 5)
         pair_sums(0, 1)
+        unit_sums(2, 1)
         both(x_quantize, 5)
         widen(7, None, V)
         quantize(y(0, Z), 0, CUT)
@@ -527,7 +527,7 @@ def tile_factoranalysisemloadinggradient_kernel(
         x_quantize(6, 1)
         quantize(y(0, 0), 0, CUT)
         interleave(y(1, 0), G, 0, CUT)
-        pair_sums(1, 1)
+        unit_sums(3, 1)
         pair_sums(2, 1)
         both(product, 7)
         pair_sums(3, 1)
@@ -536,14 +536,13 @@ def tile_factoranalysisemloadinggradient_kernel(
         x_quantize(7, 1)
         for slab in (y(0, Z), y(0, 0), y(1, Z)):
             quantize(slab, CUT, WIDTH)
-        prepare(0, V)
         quantize(y(1, 0), 0, CUT)
         quantize(y(1, Z), 0, CUT)
         interleave(y(2, Z), G)
-        interleave(y(0, 1), G, 0, 352)
+        interleave(y(0, 1), G, 0, 384)
         interleave(y(1, 0), S, CUT)
         interleave(y(2, 0), S)
-        interleave(y(0, 1), S, 352)
+        interleave(y(0, 1), S, 384)
         interleave(y(1, 1), S, 0, HALF)
         for side in (Z, 0):
             for half in range(2):
@@ -558,6 +557,7 @@ def tile_factoranalysisemloadinggradient_kernel(
         quantize(y(1, 0), CUT, WIDTH)
         for slab in (y(2, Z), y(2, 0), y(3, Z), y(3, 0)):
             quantize(slab)
+        prepare(0, V)
         prepare(1, V)
         quantize(y(0, 1))
         interleave(y(2, 1), S, 0, HALF)

@@ -121,11 +121,11 @@ def tile_factoranalysisemloadinggradient_kernel(
             return codes[:, code_shift:], scales[:, scale_shift:]
 
         def grouped_key(slab, column=0):
-            return ("grouped", *slab, cuts[slab] if column >= cuts.get(slab, WIDTH) else 0)
+            return ("grouped", *slab, max(cut for cut in (0, *cuts.get(slab, ())) if cut <= column))
 
         def grouped(slab, first, last):
             key = grouped_key(slab, first)
-            end = cuts.get(slab, WIDTH) if key[-1] == 0 else WIDTH
+            end = min(cut for cut in (*cuts.get(slab, ()), WIDTH) if cut > key[-1])
             return tile_of(key, [P, end - key[-1], PACK], BF16)[:, first - key[-1] : last - key[-1], :]
 
         def warm(n):
@@ -370,8 +370,8 @@ def tile_factoranalysisemloadinggradient_kernel(
                     multiply(unit, side, g)
 
         def quantize_cut(slab):
-            quantize(slab, cuts[slab], WIDTH)
-            quantize(slab, 0, cuts[slab])
+            quantize(slab, cuts[slab][0], WIDTH)
+            quantize(slab, 0, cuts[slab][0])
 
         def lodge(buffer, *keys):
             for key in keys:
@@ -379,9 +379,11 @@ def tile_factoranalysisemloadinggradient_kernel(
 
         LATE = 128
         for slab in (w(Z, 1), y(0, Z), y(0, 0), y(1, Z), y(1, 0)):
-            cuts[slab] = CUT
-        cuts[y(2, 1)] = cuts[y(1, 1)] = HALF
-        lodge("gate_3", grouped_key(y(1, 1), HALF), grouped_key(y(2, 1), HALF))
+            cuts[slab] = (CUT,)
+        cuts[y(1, 1)] = (HALF,)
+        cuts[y(2, 1)] = (HALF, HALF + P)
+        lodge("gate_3", grouped_key(y(1, 1)), grouped_key(y(2, 1), HALF))
+        lodge("gate_4", grouped_key(y(2, 1)), grouped_key(y(2, 1), HALF + P))
         lodge("wide0", ("wide", 2, None), ("result", 0))
         lodge("wide1", ("wide", 3, None), ("wide", 6, None), ("result", 1))
         lodge("wide2", ("wide", 4, None), ("wide", 7, None), ("result", 2))
@@ -396,11 +398,11 @@ def tile_factoranalysisemloadinggradient_kernel(
         lodge("gate_z", grouped_key(w(Z, 0)), grouped_key(w(Z, 1)), grouped_key(w(0, 1)), ("x_grouped", 3, 0), grouped_key(y(0, Z)))
         lodge("gate_5", ("x_grouped", 5, 1), grouped_key(y(1, Z)))
         lodge("gate_w", grouped_key(w(0, 0)), grouped_key(w(1, 0)), grouped_key(y(0, 0)))
-        lodge("gate_6", ("x_grouped", 6, 1), grouped_key(y(1, 0)), grouped_key(y(2, Z)))
+        lodge("gate_6", ("x_grouped", 6, 0), grouped_key(y(1, 0)), grouped_key(y(2, Z)))
         lodge("gate_2", ("x_grouped", 2, 0), grouped_key(w(1, 1)))
         lodge("late", grouped_key(y(0, 1)))
-        lodge("x_grouped0", *[("x_grouped", pair, 0) for pair in (0, 1, 4, 5, 6, 7)])
-        lodge("x_grouped1", *[("x_grouped", pair, 1) for pair in range(PAIRS) if pair not in (5, 6)])
+        lodge("x_grouped0", *[("x_grouped", pair, 0) for pair in (0, 1, 4, 5, 7)])
+        lodge("x_grouped1", *[("x_grouped", pair, 1) for pair in range(PAIRS) if pair != 5])
         load_x(0)
         load_scale(0)
         load_x(1)
@@ -497,7 +499,7 @@ def tile_factoranalysisemloadinggradient_kernel(
             empty(4, side)
             empty(5, side)
         interleave(y(0, Z), G, 0, CUT)
-        widen(6, None, S)
+        widen(6, 0, S)
         product(4, 0)
         pair_sums(3, Z)
         product(4, 1)
@@ -505,6 +507,7 @@ def tile_factoranalysisemloadinggradient_kernel(
         both(x_quantize, 4)
         interleave(w(1, 0), V, 176, 464)
         interleave(w(1, 1), V, CUT)
+        widen(6, 1, V)
         quantize(w(1, 0))
         quantize(w(1, 1))
         interleave(y(0, 0), G, 0, CUT)
@@ -514,10 +517,9 @@ def tile_factoranalysisemloadinggradient_kernel(
         both(turn, 6)
         both(product, 5)
         pair_sums(0, 1)
-        unit_sums(2, 1)
+        pair_sums(1, 1)
         both(x_quantize, 5)
         widen(7, None, V)
-        quantize(y(0, Z), 0, CUT)
         interleave(y(1, Z), G, 0, CUT)
         pair_sums(5, Z, 0)
         interleave(y(1, Z), S, CUT)
@@ -525,9 +527,7 @@ def tile_factoranalysisemloadinggradient_kernel(
         both(product, 6)
         x_quantize(6, 0)
         x_quantize(6, 1)
-        quantize(y(0, 0), 0, CUT)
         interleave(y(1, 0), G, 0, CUT)
-        unit_sums(3, 1)
         pair_sums(2, 1)
         both(product, 7)
         pair_sums(3, 1)
@@ -536,6 +536,8 @@ def tile_factoranalysisemloadinggradient_kernel(
         x_quantize(7, 1)
         for slab in (y(0, Z), y(0, 0), y(1, Z)):
             quantize(slab, CUT, WIDTH)
+        quantize(y(0, Z), 0, CUT)
+        quantize(y(0, 0), 0, CUT)
         quantize(y(1, 0), 0, CUT)
         quantize(y(1, Z), 0, CUT)
         interleave(y(2, Z), G)
@@ -555,41 +557,47 @@ def tile_factoranalysisemloadinggradient_kernel(
         pair_sums(6, 1)
         pair_sums(7, 1)
         quantize(y(1, 0), CUT, WIDTH)
-        for slab in (y(2, Z), y(2, 0), y(3, Z), y(3, 0)):
-            quantize(slab)
-        prepare(0, V)
-        prepare(1, V)
+        quantize(y(2, Z))
+        quantize(y(2, 0), 0, P)
+        quantize(y(3, Z))
+        quantize(y(3, 0), 0, P)
+        quantize(y(2, 0), P, WIDTH)
+        quantize(y(3, 0), P, WIDTH)
         quantize(y(0, 1))
+        prepare(0, V)
+        quantize(y(1, 1), 0, HALF)
+        prepare(1, V)
+        interleave(y(2, 1), G, HALF, HALF + P)
         interleave(y(2, 1), S, 0, HALF)
         interleave(y(3, 1), S, 0, HALF)
-        interleave(y(1, 1), S, HALF)
-        interleave(y(3, 1), S, HALF)
-        group_order = {band: (0, 1, 3, 2) if band >= 6 else tuple(range(GROUPS)) for band in range(BANDS)}
+        group_order = {band: (0, 1, 2, 3) if band >= 6 else tuple(range(GROUPS)) for band in range(BANDS)}
         for band in range(SIDE_BANDS):
             for group in range(GROUPS):
                 accumulate(group, band, 0, K)
         finish(0, 0, K)
-        prepare(2, V)
-        quantize(y(1, 1), 0, HALF)
         finish(1, 0, K)
-        prepare(3, V)
+        prepare(2, V)
         quantize(y(2, 1), 0, HALF)
         quantize(y(3, 1), 0, HALF)
-        finish(2, 0, K)
-        quantize(y(1, 1), HALF, WIDTH)
-        prepare(4, V)
-        interleave(y(2, 1), G, HALF, HALF + LATE)
+        prepare(3, S)
+        interleave(y(1, 1), S, HALF)
+        interleave(y(3, 1), S, HALF, HALF + P)
+        prepare(4, S)
         prepare(5, S)
-        interleave(y(2, 1), S, HALF + LATE)
+        interleave(y(3, 1), S, HALF + P)
+        interleave(y(2, 1), G, HALF + P)
+        finish(2, 0, K)
         finish(3, 0, K)
+        quantize(y(1, 1), HALF, WIDTH)
+        quantize(y(2, 1), HALF, HALF + P)
+        quantize(y(3, 1), HALF, HALF + P)
+        for later in range(6, BANDS):
+            prepare(later, S)
         for band, first, last in [(4, 0, K), (5, 0, K)] + [(band, first, first + HALF) for band in (6, 7) for first in (0, HALF)]:
             for group in group_order[band]:
                 accumulate(group, band, first, last)
             finish(band, first, last)
-            if band in (4, 5):
-                place = (band - 2) * P
-                quantize(y(3, 1), place, place + P)
-                quantize(y(2, 1), place, place + P)
             if band == 4:
-                for later in range(6, BANDS):
-                    prepare(later, S)
+                quantize(y(2, 1), HALF + P, WIDTH)
+            if band == 5:
+                quantize(y(3, 1), HALF + P, WIDTH)

from contextlib import ExitStack

import concourse.mybir as mybir
from concourse.masks import make_identity

N, D, K = 2048, 1024, 512

FLOPS = 2 * N * D * D + 2 * N * D * K + 2 * N * D * K

F32 = mybir.dt.float32
BF16 = mybir.dt.bfloat16
U32 = mybir.dt.uint32
U8 = mybir.dt.uint8
FP8 = mybir.dt.float8_e4m3fn
FP8X4 = mybir.dt.float8_e4m3fn_x4
MULT = mybir.AluOpType.mult
ADD = mybir.AluOpType.add
SUBTRACT = mybir.AluOpType.subtract
COPY = mybir.ActivationFunctionType.Copy

P = 128
PACK = 4
K_PASS = P * PACK
PASSES = D // K_PASS
GROUPS = N // K_PASS
UNITS = N // P
PAIRS = UNITS // 2
WIDTH = 512
BANKS = 8
HALF = WIDTH // 2
QUARTER = WIDTH // 4
Z = 2
BANDS = D // P
SIDE_BANDS = WIDTH // P
LAST_BAND = BANDS - 1
DUOS = 4
RUN = 4
ROW = 16
GPSIMD_COLUMNS = 384
WARM_WIDTH = 272


def tile_factoranalysisemloadinggradient_kernel(
    tc, x_bytes, x_scale, p, beta, r, t, v, psi, out
):
    nc = tc.nc
    with ExitStack() as ctx:
        keep = ctx.enter_context(tc.tile_pool(name="keep", bufs=1))
        psum = ctx.enter_context(tc.psum_pool(name="psum", bufs=1))
        ctx.enter_context(tc.manual_schedule())

        factor_rows = keep.tile([P, K_PASS], BF16, name="factor_rows")
        nc.vector.memset(factor_rows[:].bitcast(U32), 0)
        zeros = keep.tile([P, WARM_WIDTH], F32, name="zeros")
        nc.vector.memset(zeros[:], 0.0)
        identity = keep.tile([P, P], F32, name="identity")
        make_identity(nc, identity[:])
        identity16 = keep.tile([P, P], BF16, name="identity16")
        one = keep.tile([P, 1], F32, name="one")
        nc.vector.memset(one[:], 1.0)

        x_view = x_bytes.rearrange("(g q j) f -> g q j f", q=P, j=PACK)
        p_view = p.rearrange("(g q j) d -> g q j d", q=P, j=PACK)
        beta_view = beta.rearrange("(g q j) d -> g q j d", q=P, j=PACK)
        scale_view = x_scale.rearrange("o (g q j) -> (o g) q j", q=P, j=PACK)
        x_raw = {}
        tiles, buffer_of, cuts = {}, {}, {}
        free_banks, held = list(range(BANKS)), {}

        def load_x(first_pair, pairs=1):
            raw = keep.tile([P, 2 * pairs, D], U8, name=f"x_raw{first_pair}")
            group, j = divmod(2 * first_pair, PACK)
            nc.sync.dma_start(out=raw[:], in_=x_view[group][:, j : j + 2 * pairs, :])
            for n in range(pairs):
                x_raw[first_pair + n] = raw[:, 2 * n : 2 * n + 2, :].rearrange("q j f -> q (j f)")

        def load_w(side, g):
            raw = tile_of(("flat", "w", side, g), [P, PACK, WIDTH], BF16)
            rows = beta_view[g] if side == Z else p_view[g][:, :, side * WIDTH : (side + 1) * WIDTH]
            nc.sync.dma_start(out=raw[:], in_=rows)

        def load_scale(g):
            nc.scalar.dma_start(out=scale[g][:], in_=scale_view[g])

        def load_factor(first, source):
            nc.sync.dma_start(out=factor_rows[first : first + GROUPS, :], in_=source.rearrange("(g c) -> g c", g=GROUPS))

        def load_psi():
            rows = factor_rows[2 * GROUPS : 2 * GROUPS + BANDS, :P]
            nc.sync.dma_start(out=rows, in_=psi.rearrange("(b q) -> b q", b=BANDS))

        scale = [keep.tile([P, PACK], F32, name=f"scale{g}") for g in range(PASSES)]
        v_raw = keep.tile([P, BANDS, K], BF16, name="v_raw")
        factor = {side: keep.tile([P, UNITS], F32, name=f"factor{side}") for side in (0, Z)}
        factor[1] = factor[0]
        psi_inv = keep.tile([P, BANDS], F32, name="psi_inv")
        psi_inv_mean = keep.tile([P, BANDS], F32, name="psi_inv_mean")

        def tile_of(key, shape, dtype):
            if key not in tiles:
                name = buffer_of.get(key) or "_".join(str(part) for part in key)
                tiles[key] = keep.tile(shape, dtype, name=name, align_bytes=256)
            return tiles[key]

        def bank_of(key, shape):
            if key not in tiles:
                held[key] = free_banks[0]
                free_banks.remove(held[key])
                tiles[key] = psum.tile(shape, F32, name=f"bank{held[key]}")
            return tiles[key]

        def release(key):
            free_banks.append(held[key])

        def mx_tiles(key):
            stationary = key[0] == "x" or (key[0] == "y" and key[2] != Z)
            code_shift = 32 if stationary else 0
            scale_shift = 192 if stationary else 64
            codes = tile_of(("codes", *key), [P, code_shift + WIDTH], U32)
            scales = tile_of(("scales", *key), [P, scale_shift + WIDTH], U8)
            return codes[:, code_shift:], scales[:, scale_shift:]

        def grouped_key(slab, column=0):
            return ("grouped", *slab, max(cut for cut in (0, *cuts.get(slab, ())) if cut <= column))

        def grouped(slab, first, last):
            key = grouped_key(slab, first)
            end = min(cut for cut in (*cuts.get(slab, ()), WIDTH) if cut > key[-1])
            return tile_of(key, [P, end - key[-1], PACK], BF16)[:, first - key[-1] : last - key[-1], :]

        def warm(n):
            nc.tensor.matmul(
                out=bank_of(("warm", n), [P, WARM_WIDTH])[:], lhsT=zeros[:, :P], rhs=zeros[:], start=True, stop=True
            )
            release(("warm", n))

        def turn_factors():
            bank = bank_of(("factors",), [P, 3, P])
            for u in range(2):
                nc.tensor.transpose(bank[:, u, :], factor_rows[:].bitcast(F32)[:, u::2], identity[:])
            nc.tensor.transpose(bank[:, 2, :].bitcast(BF16)[:, :P], factor_rows[:, :P], identity16[:])

        def widen_factors():
            for side, first in ((0, 0), (Z, GROUPS)):
                source = tiles[("factors",)][:, :2, first : first + GROUPS].bitcast(BF16)
                nc.scalar.copy(
                    out=factor[side][:].rearrange("q (g u e) -> q g u e", u=2, e=2),
                    in_=source.rearrange("q u (g e) -> q g u e", e=2),
                )
            release(("factors",))

        def invert_psi():
            nc.vector.reciprocal(out=psi_inv[:], in_=tiles[("factors",)][:, 2, :].bitcast(BF16)[:, 2 * GROUPS : 2 * GROUPS + BANDS])

        def mean_psi():
            nc.scalar.activation(out=psi_inv_mean[:], in_=psi_inv[:], func=COPY, scale=1.0 / N)

        def interleave(slab, engine, first=0, last=WIDTH):
            source = tiles[("flat", *slab)][:, :, first:last]
            target = grouped(slab, first, last).rearrange("q (c i) j -> q c j i", i=RUN)
            source = source.rearrange("q j (c i) -> q c j i", i=RUN)
            if engine == "gpsimd":
                nc.gpsimd.tensor_scalar(out=target, in0=source, scalar1=1.0, scalar2=0.0, op0=MULT, op1=ADD)
            elif engine == "vector":
                nc.vector.tensor_copy(out=target, in_=source)
            else:
                nc.scalar.copy(out=target, in_=source)

        def quantize(slab, first=0, last=WIDTH):
            codes, scales = mx_tiles(slab)
            nc.vector.quantize_mx(
                out=codes[:, first:last].bitcast(FP8X4),
                scales=scales[:, first:last],
                in_=grouped(slab, first, last).rearrange("q c j -> q (c j)"),
            )

        def widen(pair, g, engine):
            passes = range(PASSES) if g is None else [g]
            tile = tile_of(("wide", pair, g), [P, 2 * len(passes) * K_PASS], BF16)
            whole = [(0, 0, 2 * D)]
            by_unit = [(unit * K_PASS, unit * D + passes[0] * K_PASS, K_PASS) for unit in range(2)]
            for place, first, count in whole if g is None else by_unit:
                source = x_raw[pair][:, first : first + count].bitcast(FP8)
                if engine == "vector":
                    target = tile[:].rearrange("p (u w e) -> p w u e", u=2, e=2)
                    nc.vector.tensor_scalar(
                        out=target[:, place // PACK : (place + count) // PACK],
                        in0=source.rearrange("p (w u e) -> p w u e", u=2, e=2),
                        scalar1=one[:],
                        scalar2=None,
                        op0=MULT,
                    )
                else:
                    nc.scalar.copy(out=tile[:, place : place + count], in_=source)
            words = tile[:].bitcast(F32)
            blocks = 2 * len(passes)
            for n, (unit, h) in enumerate((unit, h) for unit in range(2) for h in passes):
                for u in range(2):
                    if engine == "vector":
                        tiles["words", pair, h, unit, u] = words[:, (blocks * u + n) * P : (blocks * u + n + 1) * P]
                    else:
                        tiles["words", pair, h, unit, u] = words[:, 2 * n * P + u : 2 * (n + 1) * P : 2]

        def turn(pair, g):
            bank = bank_of(("turned", pair, g), [P, 2, 2 * P])
            for unit in range(2):
                for u in range(2):
                    nc.tensor.transpose(
                        bank[:, u, unit * P : (unit + 1) * P], tiles["words", pair, g, unit, u], identity[:]
                    )

        def product(pair, g):
            target = tile_of(("x_grouped", pair, g), [P, 2 * P, 2, 2], BF16)
            values = tiles["turned", pair, g][:].bitcast(BF16).rearrange("q u (c e) -> q c u e", e=2)
            scales = scale[g][:].rearrange("q (o u e) -> q o u e", o=1, u=2)
            nc.vector.tensor_tensor(out=target[:], in0=values, in1=scales.to_broadcast([P, 2 * P, 2, 2]), op=MULT)
            release(("turned", pair, g))

        def x_quantize(pair, g):
            codes, scales = mx_tiles(("x", pair))
            cols = slice(g * 2 * P, (g + 1) * 2 * P)
            nc.vector.quantize_mx(
                out=codes[:, cols].bitcast(FP8X4),
                scales=scales[:, cols],
                in_=tiles["x_grouped", pair, g][:].rearrange("q c u e -> q (c u e)"),
            )

        def first_pass(target, unit, side, g, w_cols):
            x_codes, x_scales = mx_tiles(("x", unit // 2))
            cols = slice((2 * g + unit % 2) * P, (2 * g + unit % 2 + 1) * P)
            w_codes, w_scales = mx_tiles(("w", side, g))
            nc.tensor.matmul_mx(
                out=target,
                lhsT=x_codes[:, cols].bitcast(FP8X4),
                lhsT_scale=x_scales[:, cols],
                rhs=w_codes[:, w_cols].bitcast(FP8X4),
                rhs_scale=w_scales[:, w_cols],
                start=(g == 0),
                stop=(g == PASSES - 1),
            )

        def multiply(unit, side, g):
            first_pass(bank_of(("first", unit, side), [P, WIDTH])[:], unit, side, g, slice(0, WIDTH))

        def multiply_duo(group, side, duo):
            half, u = divmod(duo, 2)
            bank = bank_of(("duo", group, side, duo), [P, 2, HALF])
            for e in range(2):
                for g in range(PASSES):
                    first_pass(bank[:, e, :], PACK * group + 2 * u + e, side, g, slice(half * HALF, (half + 1) * HALF))

        def multiply_strips(group, side, half):
            banks = [bank_of(("strip", group, side, 2 * half + s), [P, PACK, P]) for s in range(2)]
            for j in range(PACK):
                for g in range(PASSES):
                    for s, bank in enumerate(banks):
                        first = (2 * half + s) * P
                        first_pass(bank[:, j, :], PACK * group + j, side, g, slice(first, first + P))

        def empty(unit, side):
            group, j = divmod(unit, PACK)
            nc.scalar.activation(
                out=tile_of(("flat", "y", group, side), [P, PACK, WIDTH], BF16)[:, j, :],
                in_=tiles["first", unit, side][:],
                func=COPY,
                scale=factor[side][:, unit : unit + 1],
            )
            release(("first", unit, side))

        def empty_duo(group, side, duo):
            half, u = divmod(duo, 2)
            first = PACK * group + 2 * u
            factors = factor[side][:, first : first + 2].rearrange("q (o e) -> q o e", o=1)
            nc.vector.tensor_tensor(
                out=tile_of(("paired", group, side, half), [P, 2, HALF, 2], BF16)[:, u],
                in0=tiles["duo", group, side, duo][:].rearrange("q e c -> q c e"),
                in1=factors.to_broadcast([P, HALF, 2]),
                op=MULT,
            )
            release(("duo", group, side, duo))

        def empty_strip(group, side, strip):
            first = PACK * group
            factors = factor[side][:, first : first + PACK].rearrange("q (o j) -> q o j", o=1)
            nc.vector.tensor_tensor(
                out=grouped(("y", group, side), strip * P, (strip + 1) * P),
                in0=tiles["strip", group, side, strip][:].rearrange("q j c -> q c j"),
                in1=factors.to_broadcast([P, P, PACK]),
                op=MULT,
            )
            release(("strip", group, side, strip))

        def join(group, side, half, engine):
            target = grouped(("y", group, side), half * HALF, (half + 1) * HALF)
            source = tiles["paired", group, side, half][:]
            if engine == "vector":
                nc.vector.tensor_copy(
                    out=target.rearrange("q c (u e) -> q c u e", e=2), in_=source.rearrange("q u c e -> q c u e")
                )
            else:
                nc.scalar.copy(
                    out=target.rearrange("q c j -> q (c j)").bitcast(U32).rearrange("q (c u) -> q c u", u=2),
                    in_=source.rearrange("q u c e -> q u (c e)").bitcast(U32).rearrange("q u c -> q c u"),
                )

        def accumulate(group, band, first, last):
            side, place = divmod(band, SIDE_BANDS)
            cols = slice(place * P, (place + 1) * P)
            e_codes, e_scales = mx_tiles(("y", group, side))
            z_codes, z_scales = mx_tiles(("y", group, Z))
            nc.tensor.matmul_mx(
                out=bank_of(("sum", band, first), [P, last - first])[:],
                lhsT=e_codes[:, cols].bitcast(FP8X4),
                lhsT_scale=e_scales[:, cols],
                rhs=z_codes[:, first:last].bitcast(FP8X4),
                rhs_scale=z_scales[:, first:last],
                start=(group == group_order[band][0]),
                stop=(group == group_order[band][-1]),
            )

        def prepare(band, engine):
            target = tile_of(("result", band), [P, K], F32)[:]
            inverse = psi_inv[:, band : band + 1]
            if engine == "gpsimd":
                nc.gpsimd.tensor_scalar(out=target, in0=v_raw[:, band, :], scalar1=inverse, scalar2=0.0, op0=MULT, op1=ADD)
            elif engine == "vector":
                nc.vector.tensor_scalar(out=target, in0=v_raw[:, band, :], scalar1=inverse, scalar2=None, op0=MULT)
            else:
                nc.scalar.activation(out=target, in_=v_raw[:, band, :], func=COPY, scale=inverse)

        def finish(band, first, last):
            tile = tiles["result", band][:, first:last]
            nc.vector.scalar_tensor_tensor(
                out=tile,
                in0=tiles["sum", band, first][:],
                scalar=psi_inv_mean[:, band : band + 1],
                in1=tile,
                op0=MULT,
                op1=SUBTRACT,
            )
            release(("sum", band, first))
            nc.sync.dma_start(out=out[band * P : (band + 1) * P, first:last], in_=tiles["result", band][:, first:last])

        S, V, G = "scalar", "vector", "gpsimd"
        CUT = GPSIMD_COLUMNS

        def w(side, g):
            return ("w", side, g)

        def y(group, side):
            return ("y", group, side)

        def both(step, pair):
            for g in range(PASSES):
                step(pair, g)

        def unit_sums(unit, side):
            for g in range(PASSES):
                multiply(unit, side, g)
            empty(unit, side)

        def pair_sums(pair, *sides):
            for side in sides:
                for unit in (2 * pair, 2 * pair + 1):
                    unit_sums(unit, side)

        def by_pass(pair, side):
            for g in range(PASSES):
                for unit in (2 * pair, 2 * pair + 1):
                    multiply(unit, side, g)

        def quantize_cut(slab):
            quantize(slab, cuts[slab][0], WIDTH)
            quantize(slab, 0, cuts[slab][0])

        def lodge(buffer, *keys):
            for key in keys:
                buffer_of[key] = buffer

        LATE = 128
        for slab in (w(Z, 1), y(0, Z), y(0, 0), y(1, Z), y(1, 0)):
            cuts[slab] = (CUT,)
        cuts[y(1, 1)] = (HALF,)
        cuts[y(2, 1)] = (HALF, HALF + P)
        lodge("gate_3", grouped_key(y(1, 1)), grouped_key(y(2, 1), HALF))
        lodge("gate_4", grouped_key(y(2, 1)), grouped_key(y(2, 1), HALF + P))
        lodge("wide0", ("wide", 2, None), ("result", 0))
        lodge("wide1", ("wide", 3, None), ("wide", 6, None), ("result", 1))
        lodge("wide2", ("wide", 4, None), ("wide", 7, None), ("result", 2))
        for band, part in zip(range(3, 7), [(0, 0), (0, 1), (1, 0), (1, 1)]):
            lodge(f"wide_pass{band}", ("wide", *part), ("result", band))
        lodge("flat0", ("flat", *w(Z, 0)), ("flat", *y(0, Z)), ("flat", *y(1, 1)))
        lodge("flat1", ("flat", *w(Z, 1)), ("flat", *y(0, 0)), ("flat", *y(2, 1)))
        lodge("flat2", ("flat", *w(0, 0)), ("flat", *y(1, Z)), ("flat", *y(3, 1)))
        lodge("flat3", ("flat", *w(0, 1)), ("flat", *y(1, 0)))
        lodge("flat5", ("flat", *w(1, 1)), ("flat", *y(2, 0)))
        lodge("flat4", ("flat", *w(1, 0)), ("flat", *y(0, 1)))
        lodge("gate_z", grouped_key(w(Z, 0)), grouped_key(w(Z, 1)), grouped_key(w(0, 1)), ("x_grouped", 3, 0), grouped_key(y(0, Z)))
        lodge("gate_5", ("x_grouped", 5, 1), grouped_key(y(1, Z)))
        lodge("gate_w", grouped_key(w(0, 0)), grouped_key(w(1, 0)), grouped_key(y(0, 0)))
        lodge("gate_6", ("x_grouped", 6, 0), grouped_key(y(1, 0)), grouped_key(y(2, Z)))
        lodge("gate_2", ("x_grouped", 2, 0), grouped_key(w(1, 1)))
        lodge("late", grouped_key(y(0, 1)))
        lodge("x_grouped0", *[("x_grouped", pair, 0) for pair in (0, 1, 4, 5, 7)])
        lodge("x_grouped1", *[("x_grouped", pair, 1) for pair in range(PAIRS) if pair != 5])
        load_x(0)
        load_scale(0)
        load_x(1)
        load_scale(1)
        load_w(Z, 0)
        load_factor(0, r)
        load_factor(GROUPS, t)
        load_psi()
        load_x(2)
        load_w(Z, 1)
        load_x(3)
        load_w(0, 0)
        load_w(0, 1)
        load_x(4)
        load_w(1, 0)
        load_x(5)
        load_w(1, 1)
        load_x(6, pairs=2)
        nc.sync.dma_start(out=v_raw[:], in_=v.rearrange("(b q) k -> q b k", q=P))


        warm(0)
        warm(1)
        widen(0, 0, V)
        widen(0, 1, S)
        both(turn, 0)
        widen(1, 0, V)
        widen(1, 1, S)
        warm(2)
        nc.scalar.copy(out=identity16[:], in_=identity[:])
        turn(1, 0)
        turn_factors()
        turn(1, 1)
        interleave(w(Z, 0), G, 0, 288)
        interleave(w(Z, 0), S, 288)
        widen(2, None, S)
        warm(3)
        both(product, 0)
        invert_psi()
        both(turn, 2)
        x_quantize(0, 0)
        quantize(w(Z, 0))
        x_quantize(0, 1)
        interleave(w(Z, 1), G, 0, CUT)
        interleave(w(Z, 1), S, CUT)
        widen_factors()
        mean_psi()
        widen(3, None, S)
        warm(4)
        both(turn, 3)
        both(product, 1)
        x_quantize(1, 0)
        quantize_cut(w(Z, 1))
        x_quantize(1, 1)
        interleave(w(0, 0), S)
        widen(4, None, S)
        for g in range(PASSES):
            for unit in range(4):
                multiply(unit, Z, g)
        interleave(w(0, 1), G, 0, 176)
        product(2, 0)
        for unit in range(4):
            empty(unit, Z)
        both(turn, 4)
        interleave(w(0, 1), V, 176)
        quantize(w(0, 0))
        quantize(w(0, 1))
        interleave(w(1, 0), G, 0, 176)
        by_pass(0, 0)
        product(2, 1)
        widen(5, 0, S)
        interleave(w(1, 0), S, 464)
        empty(0, 0)
        empty(1, 0)
        for unit in (2, 3):
            for g in range(PASSES):
                multiply(unit, 0, g)
        empty(2, 0)
        both(x_quantize, 2)
        multiply(4, Z, 0)
        multiply(4, Z, 1)
        empty(3, 0)
        widen(5, 1, S)
        multiply(5, Z, 0)
        multiply(5, Z, 1)
        interleave(w(1, 1), G, 0, CUT)
        for unit in (4, 5):
            for g in range(PASSES):
                multiply(unit, 0, g)
        both(product, 3)
        both(x_quantize, 3)
        both(turn, 5)
        for side in (Z, 0):
            empty(4, side)
            empty(5, side)
        interleave(y(0, Z), G, 0, CUT)
        widen(6, 0, S)
        product(4, 0)
        pair_sums(3, Z)
        product(4, 1)
        pair_sums(3, 0)
        both(x_quantize, 4)
        interleave(w(1, 0), V, 176, 464)
        interleave(w(1, 1), V, CUT)
        widen(6, 1, V)
        quantize(w(1, 0))
        quantize(w(1, 1))
        interleave(y(0, 0), G, 0, CUT)
        pair_sums(4, Z, 0)
        interleave(y(0, Z), S, CUT)
        interleave(y(0, 0), S, CUT)
        both(turn, 6)
        both(product, 5)
        pair_sums(0, 1)
        pair_sums(1, 1)
        both(x_quantize, 5)
        widen(7, None, V)
        interleave(y(1, Z), G, 0, CUT)
        pair_sums(5, Z, 0)
        interleave(y(1, Z), S, CUT)
        both(turn, 7)
        both(product, 6)
        x_quantize(6, 0)
        x_quantize(6, 1)
        interleave(y(1, 0), G, 0, CUT)
        pair_sums(2, 1)
        both(product, 7)
        pair_sums(3, 1)
        pair_sums(4, 1)
        x_quantize(7, 0)
        x_quantize(7, 1)
        for slab in (y(0, Z), y(0, 0), y(1, Z)):
            quantize(slab, CUT, WIDTH)
        quantize(y(0, Z), 0, CUT)
        quantize(y(0, 0), 0, CUT)
        quantize(y(1, 0), 0, CUT)
        quantize(y(1, Z), 0, CUT)
        interleave(y(2, Z), G)
        interleave(y(0, 1), G, 0, 384)
        interleave(y(1, 0), S, CUT)
        interleave(y(2, 0), S)
        interleave(y(0, 1), S, 384)
        interleave(y(1, 1), S, 0, HALF)
        for side in (Z, 0):
            for half in range(2):
                multiply_strips(3, side, half)
        for strip in range(PACK):
            empty_strip(3, Z, strip)
        pair_sums(5, 1)
        for strip in range(PACK):
            empty_strip(3, 0, strip)
        pair_sums(6, 1)
        pair_sums(7, 1)
        quantize(y(1, 0), CUT, WIDTH)
        quantize(y(2, Z))
        quantize(y(2, 0), 0, P)
        quantize(y(3, Z))
        quantize(y(3, 0), 0, P)
        quantize(y(2, 0), P, WIDTH)
        quantize(y(3, 0), P, WIDTH)
        quantize(y(0, 1))
        prepare(0, V)
        quantize(y(1, 1), 0, HALF)
        prepare(1, V)
        interleave(y(2, 1), G, HALF, HALF + P)
        interleave(y(2, 1), S, 0, HALF)
        interleave(y(3, 1), S, 0, HALF)
        group_order = {band: (0, 1, 2, 3) if band >= 6 else tuple(range(GROUPS)) for band in range(BANDS)}
        for band in range(SIDE_BANDS):
            for group in range(GROUPS):
                accumulate(group, band, 0, K)
        finish(0, 0, K)
        finish(1, 0, K)
        prepare(2, V)
        quantize(y(2, 1), 0, HALF)
        quantize(y(3, 1), 0, HALF)
        prepare(3, S)
        interleave(y(1, 1), S, HALF)
        interleave(y(3, 1), S, HALF, HALF + P)
        prepare(4, S)
        prepare(5, S)
        interleave(y(3, 1), S, HALF + P)
        interleave(y(2, 1), G, HALF + P)
        finish(2, 0, K)
        finish(3, 0, K)
        quantize(y(1, 1), HALF, WIDTH)
        quantize(y(2, 1), HALF, HALF + P)
        quantize(y(3, 1), HALF, HALF + P)
        for later in range(6, BANDS):
            prepare(later, S)
        for band, first, last in [(4, 0, K), (5, 0, K)] + [(band, first, first + HALF) for band in (6, 7) for first in (0, HALF)]:
            for group in group_order[band]:
                accumulate(group, band, first, last)
            finish(band, first, last)
            if band == 4:
                quantize(y(2, 1), HALF + P, WIDTH)
            if band == 5:
                quantize(y(3, 1), HALF + P, WIDTH)
